import numpy as np, ml_dtypes
CORES = [6,15,38,47]
N = 4
BF = ml_dtypes.bfloat16
def gentries(a):
    return np.ascontiguousarray(a.reshape(8, 16, -1).transpose(0, 2, 1)).reshape(8, -1)
def gtable(e):
    e = np.asarray(e); return np.ascontiguousarray(e.reshape(8, -1, 16).transpose(0, 2, 1)).reshape(128, -1).astype(np.int32)
WX, WV, C, K, RO, TH = 4096, 4096, 256, 16, 4, 12
def flip(P, m):
    k = np.arange(K); m = np.asarray(m)[..., None]
    return np.take_along_axis(P, np.where(k <= m, m - k, k), -1)
def place(u):
    return (((u * u) >> 5) + 37 * u) & (WV - 1)
def slots(F, w):
    u = np.add.reduce(F * w[:, :, None], axis=1) & 4095
    return u, place(u)
def prints(X, Q):
    n, c = Q.shape[:2]; a = np.take_along_axis(X, Q.reshape(n, 1, c * K), 2).reshape(n, 16, c, K)
    return np.add.reduce(a * np.arange(K), axis=3) & 255
def parts(rng):
    X = rng.integers(0, 256, (N, 8, 16, WX)); w = rng.integers(0, 16, (N, 8, 16)); R = C >> 3; P = []; S = []; gg = np.arange(8)[:, None]
    a = rng.integers(0, WX, (8, R, K)); ma = rng.integers(1, K, (8, R))
    for q in range(N):
        roots = np.concatenate([a, rng.integers(0, WX, (8, R, K))], axis=1); ms = np.concatenate([ma, rng.integers(1, K, (8, R))], axis=1)
        fam = rng.integers(0, 2 * R, (8, C)); root = roots[gg, fam]; m = ms[gg, fam]
        kind = rng.integers(0, 4, (8, C)); m1 = rng.integers(1, K, (8, C)); m2 = rng.integers(0, K, (8, C))
        one = np.where(kind == 1, 0, np.where(kind == 2, m, m1))
        P.append(flip(flip(root, one), np.where(kind == 3, m2, 0)))
        S.append(np.where(kind == 0, m1, np.where(kind == 3, rng.integers(0, K, (8, C)), m)))
    return X, w, np.stack(P), np.stack(S)
def junk(rng, share):
    return np.where(rng.random((N, 8, 1, WV)) < share, rng.integers(0, 256, (N, 8, 16, WV)), 512)
def near(rng, F, tol, n):
    o = np.argsort(rng.random(F.shape), axis=1)
    d = np.where(o < n, np.where(rng.random(F.shape) < 0.5, tol, np.minimum(rng.integers(0, 6, F.shape), tol)), tol + 1 + rng.choice(np.array([0, 0, 1, 40]), F.shape))
    z = np.where(rng.random(F.shape) < 0.5, F + d, F - d)
    return np.where(z < 0, F + d, np.where(z > 255, F - d, z))
def sow(rng, X, V, w, P, s):
    E = 6
    for q in range(N):
        for t in range(RO):
            r = (q - t) % N; c = rng.permutation(C)[:C >> 2]; n = len(c)
            st = P[r][:, c]; m = np.maximum(s[r][:, c], 1)
            if t & 1: st = flip(st, m)
            F = prints(X[q], flip(st, m)); h = slots(F, w[q])[1]
            np.put_along_axis(V[q], h[:, None, :], near(rng, F, rng.integers(2, 6, (8, 1, n)), rng.choice(np.array([11, 12, 12, 13, 16]), (8, 1, n))), 2)
            Q = flip(np.broadcast_to(st[:, :E, None], (8, E, K - 1, K)), np.broadcast_to(np.arange(1, K), (8, E, K - 1))).reshape(8, E * (K - 1), K)
            F = prints(X[q], Q); h = slots(F, w[q])[1]; e = (E >> 1) * (K - 1)
            z = near(rng, F, 2, rng.choice(np.array([12, 13, 16]), (8, 1, E * (K - 1)))); z[:, :, :e] = F[:, :, :e]
            np.put_along_axis(V[q], h[:, None, :], z, 2)
    return V
def pack(X, V, P, s, w):
    return {"x": np.ascontiguousarray(X.reshape(N, 128, WX)).astype(np.float32).astype(BF), "v": np.ascontiguousarray(V.reshape(N, 128, WV)).astype(np.float32).astype(BF),
            "lanes": np.stack([gtable(a.reshape(8, C * K)) for a in P]), "s0": np.ascontiguousarray(s).astype(np.int32), "wt": np.ascontiguousarray(w.reshape(N, 128, 1)).astype(np.int32)}
def setup_inputs(rng):
    X, w, P, s = parts(rng)
    return pack(X, sow(rng, X, junk(rng, 0.2), w, P, s), P, s, w)
def setup_inputs_spread(rng):
    X, w, P, s = parts(rng)
    X = (np.exp2(8 * rng.random((N, 8, 1, WX))) * rng.random((N, 8, 16, WX))).astype(np.int64)
    w = (16 * rng.random((N, 8, 16)) ** 3).astype(np.int64); w[:, :, 5] = 1 + 2 * rng.integers(0, 8, (N, 8))
    tb = (WX * rng.random((8, WX)) ** 3).astype(np.int64); tb[:, 0] = WX - 1
    P = np.stack([tb[g][P[:, g]] for g in range(8)], axis=1)
    s = np.where(rng.random(s.shape) < 0.3, (K * rng.random(s.shape) ** 3).astype(np.int64), s)
    return pack(X, sow(rng, X, junk(rng, 0.5), w, P, s), P, s, w)
def setup_inputs_ends(rng):
    X = 255 * rng.integers(0, 2, (N, 8, 16, WX)); w = 15 * rng.integers(0, 2, (N, 8, 16))
    V = np.where(rng.random((N, 8, 1, WV)) < 0.25, 512 * rng.integers(0, 2, (N, 8, 16, WV)), 512 * rng.integers(0, 2, (N, 8, 1, WV)))
    for g in range(8):
        kind = 3 - (g & 3); o = rng.permutation(16)
        X[:, g, :, 0] = 255 if kind == 1 else 0; X[:, g, :, WX - 1] = 255 if kind == 0 else 0
        if kind == 0: w[:, g] = 15
        if kind == 1: w[:, g, o[0]] = 15; w[:, g, o[1]] = 0
        if kind == 2:
            for i in o[:4]: X[:, g, i, WX - 1] = 255; w[:, g, i] = 15
        if kind == 3:
            for i in o[:3]: X[:, g, i, 0] = 255; w[:, g, i] = 15
    P = np.where(rng.random((N, 8, C, K)) < rng.random((N, 8, C, 1)), WX - 1, 0); s = (K - 1) * rng.integers(0, 2, (N, 8, C))
    for c in (0, 1, C - 2, C - 1): P[:, :, c] = 0
    for c in (2, C - 3): P[:, :, c] = WX - 1
    for c in (3, C - 4): P[:, :, c] = 0; P[:, :, c, 0] = WX - 1; s[:, :, c] = 0
    for c in (4, C - 5): P[:, :, c] = 0; P[:, :, c, K - 1] = WX - 1; s[:, :, c] = K - 1
    V[1::2, :, :, 0] = 512; V[0::2, :, :, 0] = 0
    return pack(X, V, P, s, w)
def setup_inputs_corners(rng):
    X, w, P, s = parts(rng); top = int(np.argmax(place(np.arange(4096))))
    for q in range(N):
        for g in range(8):
            z = (q + g) & 7
            if z == 2: w[q, g] = 0
            if z == 3: w[q, g] = 15
            if z == 4:
                w[q, g] = 15; w[q, g, 0] = 1; X[q, g, :, 0] = 0; X[q, g, :, WX - 1] = 0
                b = top // 15; X[q, g, 0, WX - 1] = top - 15 * b; X[q, g, 1, WX - 1] = min(b, 255); X[q, g, 2, WX - 1] = b - min(b, 255)
                P[q, g, C - 1] = 0; P[q, g, C - 1, 0] = WX - 1; s[q, g, C - 1] = 1; P[q, g, 0] = 0; P[q, g, C - 2] = 0
                e = rng.integers(1, WX - 1, 8); h = slots(prints(X[q, g:g + 1], np.repeat(e, K).reshape(1, 8, K)), w[q, g:g + 1])[1][0]
                P[q, g, 1] = int(e[np.argmax((h != 0) & (h != int(place(np.int64(top)))))])
            if z == 5: P[q, g] = rng.integers(0, WX, (C, 1))
            if z == 7: s[q, g] = rng.choice(np.array([0, 1, K - 1]), C)
    V = sow(rng, X, junk(rng, 0.2), w, P, s)
    for q in range(N):
        for g in range(8):
            z = (q + g) & 7
            if z == 0: V[q, g] = 512
            if z == 1: V[q, g] = np.where(V[q, g] == 512, rng.integers(0, 256, (16, WV)), V[q, g])
            if z == 2:
                P[q, g, :8] = int(rng.integers(0, WX))
                V[q, g][:, 0] = prints(X[q, g:g + 1], P[q, g:g + 1, :1])[0, :, 0]
            if z == 4:
                V[q, g][:, 0] = 512; V[q, g][:, int(place(np.int64(top)))] = 512
                F = prints(X[q, g:g + 1], P[q, g:g + 1, 1:2]); V[q, g][:, int(slots(F, w[q, g:g + 1])[1][0, 0])] = F[0, :, 0]
            if z == 5:
                F = prints(X[q, g:g + 1], P[q, g:g + 1]); h = slots(F, w[q, g:g + 1])[1]
                V[q, g][:, h[0]] = near(rng, F, 2, 12)[0]
            if z == 6:
                F = prints(X[q, g:g + 1], flip(P[q, g:g + 1], np.maximum(s[q, g:g + 1], 1)))[:, :, C >> 1:]; h = slots(F, w[q, g:g + 1])[1][:, :]
                o = np.argsort(rng.random(F.shape), axis=1)
                V[q, g][:, h[0]] = np.where(o < rng.integers(11, 13, (1, 1, F.shape[2])), F, 512)[0]
    return pack(X, V, P, s, w)
def setup_inputs_crowd(rng):
    X, w, P, s = parts(rng); V = junk(rng, 0.2); w[:, :, 3] = 1 + 2 * rng.integers(0, 8, (N, 8))
    for g in range(8):
        root = rng.integers(0, WX, K); m = int(rng.integers(1, K)); mc = rng.integers(1, K, (N, C))
        if g in (0, 2, 4): P[:, g] = root; s[:, g] = rng.integers(0, K, (N, C)) if g == 4 else m
        if g == 2: P[:, g, C - 1] = rng.integers(0, WX, K)
        if g == 3: P[:, g, 0::2] = root; P[:, g, 1::2] = flip(root, m); s[:, g] = m
        if g in (5, 7): P[:, g] = flip(np.broadcast_to(root, (N, C, K)), mc); s[:, g] = mc
        if g in (1, 6): P[:, g] = int(rng.integers(0, WX))
        if g == 6: P[:, g, 0] = rng.integers(0, WX, K)
        if g == 1:
            P[1::2, g] = rng.integers(0, WX, P[1::2, g].shape); s[1::2, g] = rng.integers(1, K, s[1::2, g].shape)
            for q in range(0, N, 2):
                r = (q - 1) % N; F = prints(X[q, g:g + 1], P[r, g:g + 1]); h = slots(F, w[q, g:g + 1])[1]
                V[q, g][:, h[0]] = near(rng, F, rng.integers(3, 6, (1, 1, C)), rng.integers(12, 17, (1, 1, C)))[0]
        if g == 2:
            for q in range(N):
                F = prints(X[q, g:g + 1], flip(np.broadcast_to(root, (1, K - 1, K)), np.arange(1, K)[None, :])); h = slots(F, w[q, g:g + 1])[1]
                V[q, g][:, h[0]] = near(rng, F, 5, 12)[0]
        if g in (1, 6, 7):
            for q in range(N):
                Q = root if g == 7 else P[0, g, C - 1]
                F = prints(X[q, g:g + 1], Q.reshape(1, 1, K)); h = int(slots(F, w[q, g:g + 1])[1][0, 0])
                V[q, g][:, h] = 512 if g == 1 and q & 1 else F[0, :, 0]
    return pack(X, V, P, s, w)
def setup_inputs_kin(rng):
    X, w, P, s = parts(rng)
    for q in range(1, N):
        o = rng.permutation(C); P[q] = P[0][:, o]; s[q] = s[0][:, o]
    return pack(X, np.full((N, 8, 16, WV), 512), P, s, w)
def check_inputs(d):
    bad = []
    for k, lo, hi in (("x", 0, 255), ("v", 0, 512), ("lanes", 0, WX - 1), ("s0", 0, K - 1), ("wt", 0, 15)):
        a = np.asarray(d[k]).astype(np.float64)
        if not np.all((a >= lo) & (a <= hi) & (a == np.floor(a))): bad.append("range of " + k)
    a = np.asarray(d["v"]).astype(np.float64)
    if np.any((a > 255) & (a < 512)): bad.append("v between 255 and 512")
    return bad
def visit(X, V, P, s, w, A):
    a = np.take_along_axis(X, P.reshape(8, 1, C * K), 2).reshape(8, 16, C, K); k = np.arange(K, dtype=np.int32)
    ak = np.add.accumulate(a * k, axis=3, dtype=np.int32); b = np.add.accumulate(a, axis=3, dtype=np.int32)
    F = np.ascontiguousarray(((ak[..., K - 1:] - 2 * ak + k * b) & 255)[..., 1:])
    u, h = slots(F.reshape(8, 16, C * (K - 1)), w)
    D = np.abs(np.take_along_axis(V, h[:, None, :], 2).reshape(F.shape) - F)
    u = u.reshape(8, C, K - 1); h = h.reshape(8, C, K - 1)
    close = D <= (2 + (A & 3)).reshape(8, 1, 1, 1)
    seen = np.add.reduce(close, axis=1, dtype=np.int32) >= TH
    far = np.add.reduce(D, axis=1, dtype=np.int32)
    i = np.argmin(np.where(seen, K, (np.arange(1, K) - s[:, :, None]) & (K - 1)), axis=2); go = np.logical_not(np.all(seen, axis=2))
    hc = np.take_along_axis(h, i[:, :, None], 2)[:, :, 0]; won = np.zeros((8, C), bool)
    for g in range(8):
        c = np.flatnonzero(go[g]); c = c[np.unique(hc[g, c], return_index=True)[1]]
        won[g, c] = True; V[g][:, hc[g, c]] = F[g][:, c, i[g, c]]
    su = np.take_along_axis(u, np.argmin(far, axis=2)[:, :, None], 2)[:, :, 0] & (K - 1)
    return np.where(won[:, :, None], flip(P, i + 1), P), np.where(won, s, su), C - np.add.reduce(won, axis=1, dtype=np.int64)
def reference(x, v, lanes, s0, wt):
    X = x.astype(np.float32).astype(np.int32).reshape(N, 8, 16, WX); V = v.astype(np.float32).astype(np.int32).reshape(N, 8, 16, WV)
    P = np.stack([gentries(a) for a in lanes]).astype(np.int64).reshape(N, 8, C, K); s = s0.astype(np.int64); w = wt.astype(np.int32).reshape(N, 8, 16)
    A = np.zeros((N, 8), np.int64)
    for t in range(RO):
        for q in range(N):
            r = (q - t) % N
            P[r], s[r], A[q] = visit(X[q], V[q], P[r], s[r], w[q], A[q])
    return {"yl": np.stack([gtable(a.reshape(8, C * K)) for a in P]).astype(np.float32), "ys": s.astype(np.float32), "yv": V.reshape(N, 128, WV).astype(np.float32).astype(BF)}

@@ -1,0 +1,640 @@
+from concourse.bass import DstId, RemoteDMATransfer
+from concourse.mybir import dt, AluOpType, AxisListType, ActivationFunctionType
+
+ALU = AluOpType
+AF = ActivationFunctionType
+F32, BF, F16, I32, U16 = "float32", "bfloat16", "float16", "int32", "uint16"
+STEPS = 4
+KSPLIT = True
+SCANI = True
+HACT = True
+GAV = ((0, 0, 0, 1), (0, 0, 1, 1))
+FACT = (1, 1, 0, 0)
+CH = (8, 8)
+SUB = True
+NCH = len(CH)
+Q0 = [16 - sum(CH[:h + 1]) for h in range(NCH)]
+SEG = [[16 * (16 - (Q0[h] + q)) + 2 for q in range(CH[h])] for h in range(NCH)]
+TOT = [sum(s) for s in SEG]
+
+SCRATCH = {}
+PART = {}
+
+
+def _sb(name, n, d):
+    SCRATCH[name] = ("sbuf", [128, n], d)
+
+
+for _n, _w, _d in [
+    ("xs", 4096, BF), ("vs", 8208, BF), ("ctab", 4112, F32), ("lan", 256, I32), ("s0w", 256, I32), ("wti", 8, I32),
+    ("srow", 256, BF), ("ci", 16, I32), ("cf", 32, F32), ("t0", 256, F32), ("t1", 256, F32), ("t2", 256, F32),
+    ("t3", 256, F32), ("ti", 128, I32), ("tj", 32, I32), ("idb", 128, BF), ("idh", 128, F16), ("nid", 128, BF), ("i19", 128, BF),
+    ("tn", 120, BF), ("blk", 128, BF), ("sel", 144, BF), ("selw", 144, BF), ("selk", 144, F16), ("selb", 144, BF), ("wm", 128, F16),
+    ("iw", 32, BF), ("poff", 128, U16), ("pa", 2048, F16), ("ta", 128, BF), ("tb", 128, BF),
+    ("tc", 128, BF), ("mtab", 128, F32), ("rst", 120, F32), ("ltl", 16, U16), ("revl", 16, U16), ("rev", 16, U16),
+    ("ends", 8, U16), ("val", 8, F32), ("lst", 16, F32), ("tri", 16, BF), ("hrow", 272, F16), ("win", 16, BF), ("fsel", 256, BF),
+    ("thr", 8, F32), ("aq", 16, BF), ("ay", 8, F32), ("aj", 16, F32),
+]:
+    _sb(_n, _w, _d)
+for _h in range(NCH):
+    _c = CH[_h]
+    for _n, _w, _d in [
+        ("ld", 16 * _c, I32), ("lu", 16 * _c, U16), ("lh", 16 * _c, F16), ("a", 256 * _c, BF), ("at", 256 * _c, F16),
+        ("q", 240 * _c, BF), ("f", 240 * _c, BF), ("d", 240 * _c, F16), ("ab", 240 * _c, F16), ("cl", 240 * _c, BF),
+        ("lall", 1040 + 128 * _c, F32), ("w4", 256, F16), ("w1", 256, F32), ("w2", 256, I32), ("w3", 384, BF), ("hu", 128, U16),
+        ("sc", 240, I32 if SCANI else F32), ("k", 48, I32), ("m", 64, F32), ("ou", 32, U16), ("eq", TOT[_h], BF), ("es", TOT[_h], BF),
+        ("msk", TOT[_h], BF), ("snd", 144 * STEPS, I32), ("rcv", 144 * (STEPS + 1), I32), ("fo", 384, F32),
+    ]:
+        _o = SCRATCH[_n][1][1] if _h else 0
+        PART[_n + str(_h)] = (_n, _o, _w)
+        _sb(_n, _o + _w + (-_w) % 32, _d)
+for _n in ("pt0", "pt1"):
+    SCRATCH[_n] = ("psum", [128, 1024], BF)
+for _n in ("px0", "px1", "px2", "pu", "pc", "pk"):
+    SCRATCH[_n] = ("psum", [128, 512], F32)
+
+SEMAPHORES = ["sv", "sa", "sp", "sg", "gone"] + ["dm%d" % i for i in range(24)] + \
+    ["arr%d" % i for i in range(NCH * STEPS)]
+
+CYC, PCYC = 1.04, 0.6
+LAT_X, LAT_S, LAT_R = 130.0, 90.0, 3600.0
+SIZE = {F32: 4, I32: 4, BF: 2, F16: 2, U16: 2}
+
+
+def A(name, lo=0, hi=None, step=1, part=None):
+    name, o, w = PART.get(name) or (name, 0, SCRATCH[name][1][1])
+    return ("A", name, o + lo, o + (w if hi is None else hi), step, part)
+
+
+def IX(name, lo, hi, off, c, d):
+    w, l = A(name, lo, hi), A(off, c, d)
+    return ("I", w[1], w[2], w[3], l[1], l[2], l[3])
+
+
+def count(a):
+    if a[0] == "I":
+        return 16 * (a[6] - a[5])
+    return len(range(a[2], a[3], a[4]))
+
+
+def spans(a):
+    if a[0] == "I":
+        return [(a[1], a[2], a[3]), (a[4], a[5], a[6])]
+    if a[0] == "A":
+        return [(a[1], a[2], a[3])]
+    return []
+
+
+def psum(a):
+    return SCRATCH[a[1]][0] == "psum"
+
+
+def narrow(*xs):
+    return all(SIZE[SCRATCH[a[1]][2]] == 2 for a in xs)
+
+
+def plan():
+    ops = []
+    acc = {}
+    tag = [-9, 0, 0]
+
+    def add(eng, cost, call, reads, writes, kind="c", after=()):
+        i = len(ops)
+        deps = {}
+        for lst, wr in ((reads, False), (writes, True)):
+            for a in lst:
+                sp = spans(a)
+                for n, (name, lo, hi) in enumerate(sp):
+                    w = wr and n == 0
+                    ps = SCRATCH[name][0] == "psum"
+                    if ps:
+                        st = acc.setdefault(name, [eng, [], []])
+                        if st[0] != eng:
+                            st[:] = [eng, [], st[1]]
+                        for j in st[2]:
+                            deps[j] = True
+                        if eng == "P":
+                            for j in st[1][-2:]:
+                                if j != i:
+                                    deps.setdefault(j, False)
+                        if i not in st[1]:
+                            st[1].append(i)
+                        continue
+                    old = acc.setdefault(name, [])
+                    for (j, l2, h2, w2) in old:
+                        if j != i and (w or w2) and lo < h2 and l2 < hi:
+                            deps[j] = True
+                    if w:
+                        old[:] = [o for o in old if not (lo <= o[1] and o[2] <= hi)]
+                    old.append((i, lo, hi, w))
+        for j in after:
+            deps[j] = True
+        tag[2] += 1
+        ops.append(dict(eng=eng, cost=cost, call=call, deps=deps, kind=kind, tag=tuple(tag)))
+        return i
+
+    def aps(*xs):
+        return [x for x in xs if isinstance(x, tuple)]
+
+    def vcost(out, ins, two=False):
+        n = count(out)
+        if out[0] == "I":
+            return (60 + 3.8 * n) * CYC
+        if ins[0][0] == "I":
+            return (60 + 1.56 * n) * CYC
+        if two:
+            return max(64, n * (1 if any(psum(a) for a in ins) else 2)) * CYC
+        return max(64, n * (0.5 if narrow(out, *ins) else 1)) * CYC
+
+    def cp(out, in_):
+        return add("V", vcost(out, [in_]), ("cp", out, in_), [in_], [out])
+
+    def ts(out, in_, s1, op0, s2=None, op1=None):
+        return add("V", vcost(out, [in_]), ("ts", out, in_, s1, s2, op0, op1), [in_] + aps(s1, s2), [out])
+
+    def tt(out, a, b, op):
+        return add("V", vcost(out, [a, b], True), ("tt", out, a, b, op), [a, b], [out])
+
+    def scan(out, a, b, op0, op1):
+        return add("V", vcost(out, [a, b]), ("scan", out, a, b, op0, op1), [a, b], [out])
+
+    def ms(out, v):
+        return add("V", vcost(out, [out]), ("ms", out, v), [], [out])
+
+    def act(out, in_, f=AF.Identity, bias=0.0, scale=1.0, accum=None):
+        n = count(out)
+        c = (78 + 1.56 * n) if in_[0] == "I" else max(64, n)
+        return add("S", c * CYC, ("act", out, in_, f, bias, scale, accum), [in_] + aps(bias, scale), [out] + aps(accum))
+
+    def mm(lst):
+        c = 0
+        rd, wr = [], []
+        for m in lst:
+            c += max(64, count(m[0])) * (4 if SCRATCH[m[1][1]][2] == F32 else 1)
+            rd += [m[1], m[2]]
+            wr.append(m[0])
+        return add("P", c * PCYC, ("mm", lst), rd, wr)
+
+    def group(out, pairs):
+        return [(out, l, r, k == 0, k == len(pairs) - 1) for k, (l, r) in enumerate(pairs)]
+
+    def iota(out, pat, base, cm):
+        return add("G", 130 + 2 * count(out) * CYC, ("iota", out, pat, base, cm), [], [out])
+
+    def dma(eng, out, in_, nbytes):
+        return add(eng, 2000 + nbytes / 180.0, ("dma", out, in_), aps(in_) if in_[0] != "H" else [],
+                   aps(out) if out[0] != "H" else [], kind="d")
+
+    def H(name, *ix):
+        return ("H", name, ix)
+
+    al = slice(None)
+    dma("Y", A("lan"), H("lanes", al, al), 131072)
+    dma("S", A("xs", 0, 2048), H("x", al, slice(0, 2048)), 700000)
+    dma("Y", A("xs", 2048, 4096), H("x", al, slice(2048, 4096)), 700000)
+    ms(A("s0w"), 0)
+    dma("Y", A("wti", 0, 1), H("wt", al, al), 512)
+    dma("Y", A("s0w", part=slice(0, 128, 16)), H("s0", al, al), 8192)
+    dma("Y", A("vs", 0, 2048), H("v", al, slice(2048, 4096)), 1400000)
+    dma("Y", A("vs", 2048, 4096), H("v", al, slice(0, 2048)), 1400000)
+
+    def col(b, j):
+        return A(b, j, j + 1)
+    iota(col("ci", 0), [[0, 1]], 0, 1)
+    for h in range(NCH):
+        iota(A("tj", Q0[h], Q0[h] + CH[h]), [[-1, 2], [-32, CH[h] // 2]], 255 - 16 * Q0[h], -2)
+    iota(A("tj", 16, 32), [[-16, 16]], 255, -1)
+    iota(A("t0", 0, 144), [[1, 144]], 0, 0)
+    iota(A("t1", 0, 128), [[1, 16], [0, 8]], 0, 0)
+    iota(A("t1", 128, 256), [[0, 16], [1, 8]], 0, 0)
+    iota(A("t3", 0, 128), [[1, 8], [0, 16]], 0, 0)
+    iota(A("mtab", 0, 120), [[0, 8], [1, 15]], 1, 0)
+    iota(A("mtab", 120, 128), [[0, 8]], 0, 0)
+    iota(A("t3", 128, 136), [[16, 8]], 0, 0)
+    iota(A("ctab"), [[1, 4112]], -2048, 0)
+    ts(col("ci", 1), col("ci", 0), 15, ALU.bitwise_and)
+    ts(col("ci", 2), col("ci", 0), 4, ALU.arith_shift_right)
+    ts(col("ci", 3), col("ci", 0), 7, ALU.bitwise_and)
+    ts(col("ci", 4), col("ci", 0), 14, ALU.bitwise_and)
+    ts(col("ci", 5), col("ci", 0), 3, ALU.bitwise_and)
+    cp(A("cf", 0, 6), A("ci", 0, 6))
+    P_, J_, G_, J8, J14, J4 = (col("cf", j) for j in range(6))
+    ts(col("cf", 17), G_, 32.0, ALU.mult)
+    ts(col("cf", 6), G_, 16.0, ALU.mult)
+    ts(A("revl"), A("tj", 0, 16), col("cf", 17), ALU.add)
+    ts(A("rev"), A("tj", 16, 32), col("cf", 6), ALU.add)
+    ts(A("idb"), A("t0", 0, 128), P_, ALU.is_equal)
+    ts(A("t2", 0, 128), A("t1", 0, 128), J_, ALU.subtract)
+    ts(A("t2", 128, 256), A("t2", 0, 128), 0.0, ALU.is_ge)
+    ts(A("t2", 0, 128), A("t2", 0, 128), J_, ALU.subtract)
+    tt(A("t2", 0, 128), A("t2", 0, 128), A("t2", 128, 256), ALU.mult)
+    ts(A("t2", 0, 128), A("t2", 0, 128), J_, ALU.add)
+    ts(A("t1", 128, 256), A("t1", 128, 256), G_, ALU.is_equal)
+    tt(A("wm"), A("t2", 0, 128), A("t1", 128, 256), ALU.mult)
+    ts(col("cf", 7), G_, 16.0, ALU.mult, 15.0, ALU.add)
+    cp(col("cf", 8), col("wti", 0))
+    ts(A("selb"), A("t0", 0, 144), col("cf", 7), ALU.is_equal)
+    ts(A("selw"), A("t0", 0, 144), col("cf", 7), ALU.is_equal, col("cf", 8), ALU.mult)
+    act(A("sel"), A("selb"), scale=float(2 ** 20))
+    act(A("selk"), A("selb"), scale=1024.0)
+    act(A("nid"), A("idb"), scale=-1.0)
+    act(A("idh"), A("idb"))
+    act(A("i19"), A("idb"), scale=float(2 ** 19))
+    ms(A("tn"), -11.0 * 2 ** 20)
+    ts(col("cf", 16), J_, 8.0, ALU.is_ge, 65280.0, ALU.mult)
+    ts(A("tc", 0, 64), A("t0", 0, 64), 0.0, ALU.mult, col("cf", 16), ALU.add)
+    ts(A("tc", 64, 128), A("tc", 0, 64), 256.0, ALU.add)
+    act(A("ta", 0, 120), A("t0", 0, 120), scale=4096.0, bias=2048.0)
+    act(A("tb", 0, 120), A("mtab", 0, 120), scale=64.0, bias=12288.0)
+    ts(A("blk"), A("t3", 0, 128), G_, ALU.is_equal)
+    ms(A("rst", 0, 120), 0.0)
+    ms(A("rst", 0, 120, 15), float(2 ** 25))
+    ms(col("thr", 0), 2.0)
+    ts(A("t3", 136, 144), A("t3", 128, 136), J_, ALU.add, 0.5, ALU.add)
+    ts(A("t3", 144, 152), A("t3", 136, 144), 1.0 / 15.0, ALU.mult, -0.5, ALU.add)
+    cp(A("ti", 0, 8), A("t3", 144, 152))
+    for c in set(CH):
+        ts(A("ltl", 2 * c - 8, 3 * c - 8), A("ti", 0, c), c - 1.0, ALU.min)
+    ts(A("t2", 0, 128), A("t2", 0, 128), -16.0, ALU.add)
+    tt(A("t2", 128, 256), A("t2", 0, 128), A("t1", 128, 256), ALU.mult)
+    ts(A("poff"), A("t2", 128, 256), 16.0, ALU.add)
+    ts(A("iw"), A("t0", 0, 32), J_, ALU.is_equal)
+    for i in range(4):
+        act(A("pa", 512 * i, 512 * i + 512), IX("iw", 0, 32, "poff", 32 * i, 32 * i + 32))
+    ts(col("cf", 9), J_, 32.0, ALU.mult, 4128.0, ALU.add)
+    ts(A("val"), A("t3", 128, 136), 32.0, ALU.mult, col("cf", 9), ALU.add)
+    ts(col("cf", 10), J14, -2.0, ALU.mult)
+    for c in set(CH):
+        ts(A("lst", 2 * c - 8, 3 * c - 8), A("t3", 128, 128 + c), 30.0 * c - 2, ALU.mult, col("cf", 10), ALU.add)
+    ts(A("tri"), A("t0", 0, 16), J_, ALU.is_gt, 16384.0, ALU.mult)
+    ts(A("hrow", 256, 272), A("t0", 0, 16), 0.0, ALU.mult, 2048.0, ALU.add)
+    for h in range(NCH):
+        s, c = str(h), CH[h]
+        jc = J8 if c == 8 else J4
+        ts(col("cf", 18 + h), jc, -8.0, ALU.mult, float(SEG[h][0]), ALU.add)
+        ts(col("cf", 22 + h), jc, 1.0, ALU.add, col("cf", 18 + h), ALU.mult)
+        ts(A("ends", 2 * h, 2 * h + 1), col("cf", 22 + h), -1.0, ALU.add)
+        iota(A("msk" + s), [[0, TOT[h]]], 16384, 0)
+        o = 0
+        for q in range(c):
+            act(A("msk" + s, o, o + 16), A("tri"))
+            o += SEG[h][q]
+        iota(A("lall" + s, 120 * c, 1040 + 128 * c), [[0, 1040 + 8 * c]], 0, 0)
+        if c == 4:
+            ms(A("m" + s, 8, 16), 0.0)
+    cp(A("srow"), IX("s0w", 0, 256, "rev", 0, 16))
+    mm(group(A("pc", 0, 16), [(A("selb", 15 - j, 143 - j), A("srow", j, 256, 16)) for j in range(16)]))
+    for h in range(NCH):
+        cp(A("rcv%d" % h, 0, CH[h]), A("pc", Q0[h], Q0[h] + CH[h]))
+
+    rot = [0, 0]
+
+    def xbank():
+        rot[0] += 1
+        return "px%d" % (rot[0] % 3)
+
+    def arrive(t, h, sent):
+        return add("R", LAT_R, ("arr", t, h), [], [A("rcv%d" % h, 144 * t, 144 * t + 17 * CH[h])], kind="r", after=[sent])
+
+    def close_step(last):
+        for h in range(NCH):
+            cp(IX("vs", 0, 8208, "ou%d" % h, 16, 16 + CH[h]), A("fsel", 16 * Q0[h], 16 * (Q0[h] + CH[h])))
+        if not last:
+            mm(group(A("pk", 256, 272), [(A("blk"), A("win"))]))
+            act(A("aj"), A("pk", 256, 272), scale=-1.0, bias=48.375, accum=col("ay", 0))
+            act(col("aq", 0), col("ay", 0), bias=-3.5)
+            act(col("thr", 0), col("aq", 0), scale=-1.0, bias=col("ay", 0))
+
+    def selj(name, j):
+        return A(name, 15 - j, 143 - j)
+
+    def half(t, h):
+        s = str(h)
+        r0 = 144 * t
+        c = CH[h]
+        B, n2, nm, npc = 16 * Q0[h], 8 * c, 15 * c, c // 4
+        w1, w2, w3, w4 = "w1" + s, "w2" + s, "w3" + s, "w4" + s
+        tag[:] = [t, h, 0]
+        if t == 0:
+            cp(A("ld" + s), IX("lan", 0, 256, "revl", Q0[h], Q0[h] + c))
+        else:
+            ts(A("ld" + s, 0, n2), A("rcv" + s, r0 + c, r0 + 17 * c, 2), 4095, ALU.bitwise_and)
+            ts(A("ld" + s, n2, 2 * n2), A("rcv" + s, r0 + c + 1, r0 + 17 * c, 2), 12, ALU.arith_shift_right)
+        tag[:] = [t, h, 10]
+        cp(A("lu" + s), A("ld" + s))
+        ts(A("lh" + s, 0, n2), A("lu" + s, 0, n2), -2048.0, ALU.add, 1.0 / 4096, ALU.mult)
+        ts(A("lh" + s, n2, 2 * n2), A("lu" + s, n2, 2 * n2), -2048.0, ALU.add)
+        tt(A(w3, 0, 16 * c), IX("rcv" + s, r0, r0 + c, "ltl", 2 * c - 8, 3 * c - 8), A("mtab", 0, 16 * c), ALU.is_gt)
+
+        def slots(a, b):
+            act(A(w3, 128 + a, 128 + b), A("pu", a, b), bias=0.5)
+            tt(A(w4, a, b), A("pu", a, b), A(w3, 128 + a, 128 + b), ALU.subtract)
+            act(A("pu", 256 + a, 256 + b), A(w4, a, b), bias=5280.0)
+            tt(A(w2, a, b), A("pu", 256 + a, 256 + b), A(w4, a, b), ALU.mult)
+            ts(A(w2, 128 + a, 128 + b), A(w2, a, b), 5, ALU.arith_shift_right, 4095, ALU.bitwise_and)
+            cp(A("hu" + s, a, b), A(w2, 128 + a, 128 + b))
+        for pc in range(npc):
+            rot[1] += 1
+            pt = "pt%d" % (rot[1] % 2)
+            for b in range(2):
+                c0 = n2 * b + 32 * pc
+                o = 1024 * pc + 512 * b
+                (cp if (t, h, pc, b) in GAV or (h, pc, b) in GAV else act)(
+                    A("a" + s, o, o + 512), IX("xs", 0, 4096, "lu" + s, c0, c0 + 32))
+                lst = [("T", A(pt, 512 * b + 128 * i, 512 * b + 128 * i + 128), A("a" + s, o + 128 * i, o + 128 * i + 128))
+                       for i in range(4)]
+                add("P", 512 * PCYC, ("tr", lst), [m[2] for m in lst] + [A("idb")], [m[1] for m in lst])
+            ts(A("at" + s, 1024 * pc, 1024 * pc + 1024), A(pt), 288.0, ALU.add)
+            for u in range(2):
+                o = 480 * (2 * pc + u)
+                pi = ((16 - Q0[h] - c) // 2 + 2 * pc + u) % len(FACT)
+
+                def blocks(bank, first):
+                    r = []
+                    for ql in range(2):
+                        for b in range(2):
+                            a0 = 1024 * pc + 512 * b + 128 * (2 * u + ql)
+                            r.append((A(bank, 240 * ql + b, 240 * ql + 240, 2), A("at" + s, a0, a0 + 128), A("wm", 8, 128),
+                                      first, first or (ql == 1 and b == 1)))
+                    return r
+                bk = xbank()
+                mm(blocks(bk, True))
+                act(A("q" + s, o, o + 480), A(bk, 0, 480), bias=-127.5)
+                if FACT[pi]:
+                    mm([(A(bk, 0, 480), A("nid"), A("q" + s, o, o + 480), True, False)] + blocks(bk, False))
+                    act(A("f" + s, o, o + 480), A(bk, 0, 480))
+                else:
+                    tt(A("f" + s, o, o + 480), A(bk, 0, 480), A("q" + s, o, o + 480), ALU.subtract)
+            mm(group(A("pu", 60 * pc, 60 * pc + 60),
+                     [(A("blk"), A("tc", 64, 124))] +
+                     [(selj("selw", j), A("f" + s, 960 * pc + j, 960 * pc + 960, 16)) for j in range(16)]))
+            if SUB:
+                slots(60 * pc, 60 * pc + 60)
+        if not SUB:
+            slots(0, nm)
+        ts(A(w4, 128, 128 + nm), A("hu" + s, 0, nm), -2048.0, ALU.add)
+        act(A(w3, 256, 256 + nm), A(w4, 0, nm), bias=12288.0 - 31.5)
+        pre = [(A("idb"), A("ta", 0, nm)), (A("idh"), A(w4, 128, 128 + nm)), (A("i19"), A(w3, 0, nm))]
+        mm(group(A("pk", 0, nm), pre))
+        act(A(w1, 0, nm), A("pk", 0, nm))
+        mm([m[:4] + (False,) for m in group(A("pc", 0, nm), [(A("idb"), A("tn", 0, nm))] + pre)])
+        for bi in range(npc):
+            bk = xbank()
+            lst = []
+            for i in range(512 // n2):
+                m = (8 * bi + i + 1) % 16
+                lst += group(A(bk, n2 * i, n2 * i + n2), [(A("pa", 128 * m, 128 * m + 128), A("lh" + s, 0, n2)),
+                                                          (A("pa", 128 * m, 128 * m + 128), A("lh" + s, n2, 2 * n2))])
+            mm(lst)
+            n = 512 - n2 * (bi == npc - 1)
+            act(A("lall" + s, 512 * bi, 512 * bi + n), A(bk, 0, n), scale=4096.0, bias=2048.0 * 4097)
+            if bi == npc - 1:
+                for e in range(2):
+                    act(A("lall" + s, 1032 + 8 * e, 1032 + 128 * c, 16), A(bk, n, 512), scale=4096.0, bias=2048.0 * 4097)
+        if t and h == 0:
+            tag[:] = [t, 9, 0]
+            close_step(False)
+        tag[:] = [t, h, 500]
+        for pc in range(npc):
+            for u in range(2):
+                pi = 2 * pc + u
+                o = 480 * pi
+                tt(A("d" + s, o, o + 480), IX("vs", 0, 4096, "hu" + s, 30 * pi, 30 * pi + 30), A("f" + s, o, o + 480), ALU.subtract)
+                act(A("ab" + s, o, o + 480), A("d" + s, o, o + 480), AF.Abs)
+                ts(A("cl" + s, o, o + 480), A("ab" + s, o, o + 480), col("thr", 0), ALU.is_le)
+            c0, c1 = 60 * pc, 60 * pc + 60
+            mm([(A("pc", c0, c1), selj("sel", j), A("cl" + s, 960 * pc + j, 960 * pc + 960, 16), False, pc == npc - 1 and j == 15)
+                for j in range(16)])
+            mm(group(A("pk", 120 + c0, 120 + c1),
+                     [(A("idb"), A("tb", c0, c1)), (A("idh"), A(w4, c0, c1)), (A("nid"), A(w3, 256 + c0, 256 + c1))] +
+                     [(selj("selk", j), A("ab" + s, 960 * pc + j, 960 * pc + 960, 16)) for j in range(16)]))
+        tt(A(w1, 128, 128 + nm), A("pc", 0, nm), A(w1, 0, nm), ALU.max)
+        scan(A("sc" + s, 0, nm), A("rst", 0, nm), A(w1, 128, 128 + nm), ALU.add, ALU.min)
+        scan(A("sc" + s, nm, 2 * nm), A("rst", 0, nm), A("pk", 120, 120 + nm), ALU.add, ALU.min)
+        k, m_, ou = "k" + s, "m" + s, "ou" + s
+        k1, k2 = A(k, 0, c), A(k, c, 2 * c)
+        if SCANI:
+            k1, k2 = A("sc" + s, 14, nm, 15), A("sc" + s, nm + 14, 2 * nm, 15)
+        elif KSPLIT:
+            cp(k1, A("sc" + s, 14, nm, 15))
+            cp(k2, A("sc" + s, nm + 14, 2 * nm, 15))
+        else:
+            cp(A(k, 0, 2 * c), A("sc" + s, 14, 2 * nm, 15))
+        ts(A(k, 16, 16 + c), k1, 0x700FFF, ALU.bitwise_and)
+        ts(A(ou, 0, c), A(k, 16, 16 + c), 4096.0, ALU.min)
+        ts(A(m_, 16, 16 + c), A(k, 16, 16 + c), 4096.0, ALU.min, -2048.0, ALU.add)
+        act(A(m_, 0, c), A(m_, 16, 16 + c), bias=2048.0)
+        (act if HACT else cp)(A("hrow", B, B + 16 * c), IX("ctab", 0, 4112, ou, 0, c))
+        ts(A(k, 24, 24 + c), k1, 4 if c == 8 else 5, ALU.arith_shift_right, 127 * 32 * c, ALU.bitwise_and)
+        ts(A(k, 32, 32 + c), k2, 15, ALU.bitwise_and)
+        ts(A(ou, 8, 8 + c), A(k, 24, 24 + c), 0.5 / c, ALU.mult, J_, ALU.add)
+        tt(A(m_, c, 2 * c), A(k, 24, 24 + c), A("lst", 2 * c - 8, 3 * c - 8), ALU.subtract)
+        tt(A(m_, 24, 24 + c), A("rcv" + s, r0, r0 + c), A(k, 32, 32 + c), ALU.subtract)
+        o = 0
+        for q in range(c):
+            n = SEG[h][q]
+            ts(A("eq" + s, o, o + n), A("hrow", 258 - n, 258), col(m_, 16 + q), ALU.is_equal, col("val", q), ALU.mult)
+            o += n
+        scan(A("es" + s), A("eq" + s), A("msk" + s), ALU.max, ALU.min)
+        tt(A(m_, 32, 48), IX("es" + s, 0, TOT[h], "ends", 2 * h, 2 * h + 1), A(m_, 0, 16), ALU.max)
+        ts(A(ou, 24, 24 + c), A(m_, 32 + c, 32 + 2 * c), 0.25, ALU.mult)
+        cp(A("snd" + s, r0 + c, r0 + 17 * c), IX("lall" + s, 0, 1040 + 128 * c, ou, 24, 24 + c))
+        wn = A("win", Q0[h], Q0[h] + c)
+        ts(wn, A(m_, 32, 32 + c), 4096.0, ALU.is_lt)
+        tt(A(m_, 48, 48 + c), A(m_, 24, 24 + c), wn, ALU.mult)
+        tt(A("snd" + s, r0, r0 + c), A(m_, 48, 48 + c), A(k, 32, 32 + c), ALU.add)
+        src = A("snd" + s, r0, r0 + 17 * c)
+        sent = add("G", 300, ("send", t, h, src, A("rcv" + s, r0 + 144, r0 + 144 + 17 * c)), [src], [], kind="s")
+        arrive(t + 1, h, sent)
+        cp(A(ou, 16, 16 + c), A(m_, 32, 32 + c))
+        act(A("fsel", B, B + 16 * c), IX("f" + s, 0, 240 * c, ou, 8, 8 + c))
+
+    for t in range(STEPS):
+        for h in range(NCH):
+            half(t, h)
+    tag[:] = [STEPS, 9, 0]
+    close_step(True)
+    tag[:] = [99, 9, 0]
+    for k in range(4):
+        dma("YS"[k % 2], H("yv", al, slice((1024 * k + 2048) % 4096, (1024 * k + 2048) % 4096 + 1024)),
+            A("vs", 1024 * k, 1024 * k + 1024), 500000)
+    r0 = 144 * STEPS
+    for h in range(NCH):
+        s, c = str(h), CH[h]
+        n, l0 = 16 * c, 256 - 16 * (Q0[h] + c)
+        ts(A("ld" + s, 0, n, 2), A("rcv" + s, r0 + c, r0 + 17 * c, 2), 4095, ALU.bitwise_and)
+        ts(A("ld" + s, 1, n, 2), A("rcv" + s, r0 + c + 1, r0 + 17 * c, 2), 12, ALU.arith_shift_right)
+        cp(A("fo" + s, 0, n), IX("ld" + s, 0, n, "rev", 16 - c, 16))
+        dma("Y", H("yl", al, slice(l0, l0 + n)), A("fo" + s, 0, n), 65536)
+        cp(A("ou" + s, 0, c), A("rcv" + s, r0, r0 + c))
+        act(A("fo" + s, 128, 128 + n), IX("ctab", 0, 4112, "ou" + s, 0, c), bias=2048.0)
+        act(A("fo" + s, 256, 256 + n), IX("fo" + s, 128, 128 + n, "rev", 16 - c, 16))
+        dma("S", H("ys", al, slice(l0, l0 + n)), A("fo" + s, 256, 256 + n, part=slice(0, 128, 16)), 4096)
+    return ops
+
+
+def order(ops):
+    n = len(ops)
+    succ = [[] for _ in range(n)]
+    for i, o in enumerate(ops):
+        for j in o["deps"]:
+            succ[j].append(i)
+
+    def lat(j, i):
+        if not ops[i]["deps"][j] or ops[i]["kind"] == "r":
+            return 0.0
+        return LAT_S if ops[j]["eng"] == ops[i]["eng"] and ops[j]["kind"] == "c" else LAT_X
+    pr = [0.0] * n
+    for i in range(n - 1, -1, -1):
+        pr[i] = ops[i]["cost"] + max([pr[k] + lat(i, k) for k in succ[i]] + [0.0])
+    left = [len(o["deps"]) for o in ops]
+    rdy = [0.0] * n
+    cand = {}
+    free = {}
+    for i in range(n):
+        if left[i] == 0:
+            cand.setdefault(ops[i]["eng"], []).append(i)
+    seq = []
+    end = 0.0
+    while len(seq) < n:
+        best = None
+        for e, lst in cand.items():
+            if not lst:
+                continue
+            f = free.get(e, 0.0)
+            t0 = max(f, min(rdy[i] for i in lst))
+            i = max((i for i in lst if rdy[i] <= t0 + 40.0), key=lambda x: (pr[x], -x))
+            st = max(f, rdy[i])
+            if best is None or st < best[0]:
+                best = (st, i, e)
+        st, i, e = best
+        cand[e].remove(i)
+        o = ops[i]
+        fin = st + o["cost"]
+        free[e] = {"d": st + 100.0, "r": st}.get(o["kind"], fin)
+        o["t0"], o["t1"] = st, fin
+        end = max(end, fin)
+        seq.append(i)
+        for k in succ[i]:
+            rdy[k] = max(rdy[k], fin + lat(i, k))
+            left[k] -= 1
+            if left[k] == 0:
+                cand.setdefault(ops[k]["eng"], []).append(k)
+    return seq, end
+
+
+_PLAN = []
+ORDER = "010200060407080o0l0n0m0k1k0p1b0d0c090e0i0a260f0v1c0w1s0x120y100z0u110q1p140s1q1i1r0r1d19161f181u0b0g1g1v1j2x1e2y1x1z300305235r222g24130t252h5s20342i1l2t1y2z323335363o1m1n151h3m5w173n373b1a383c3p393q1o3d3a3e3r3u3f5x2u213s3v3t3g5y3h3w3i3j2f0h3k3l1t1w5z3x3y494i4j602w3z404a6g4f414b454g2j0j2s65612v4231434k44464q4n4h47664d4r484m5u5v674l4o2d4p4s4u4t5t4x544v4w4y534z504e62286i686364276h6j692e524c2a2b292c6a5157566k6l5c5b5d5e595f5a58555g6b5h6m6o6p5k5i5l6n6q2m2r732q6c6d5j5m6e6f6r2k2o742l5q6s755n5o796t7c7a6u76776z6v6w6x7d2n6y7k7h8l8m7e8n7b70727l712p787i7j7m5p8r8t7g7f7n8s8u7oa48o7p8p7q7s7x7t7z7u8v809b7w9d7v868584898883827r878w90919c8x8k9e7y8a92818b9f8e8c8j8f8d8g8y938z9g9j949h9k95a59y9i8h8i96979l98999aad9ma09z9nae9oaa9p9qbnbm9r9ua2abbo9s8q9tbs9v9wbu9xa6a7btalbvama8a3a9ccaibwacafahc1bxagbqanbrc2ajakc3apaobycec4bzc0bpasazaqaratayauavcdcfaxa1c5c6awb1b2cgb7b5b3b8b6b9b4bab0bbc7chckcic8clbcbfbdbgcjc9cmbecabhczcbd5cnd0blcod1bibjcpcqd8crd6csctd2d3d9cvcudgddcwdhcxcyeheidaejd7dcd4deenepdfdibkdbdjekdleldmdodteoeqdpdvdqf7erdwdkesewf8dse2e0e5e1e4dne3dzdydue6f9dretexegfadxe7fbeae8efebe9ecg0eueveyezfcfffdedeef0fufgf1g1fef2f3fhf4f5f6fifwg9fvfjgafkg6flfmhjhifnhkfoemfpfrfqfyg7hofshqftg2g3geghhphrhsgdhxhtgig4fzg5g8gbi8gfhmgjgghngchlglgogvhyhuhzgkgmgngpiahvi0hwi9ibgugqgrgtfxgygxich3h2h4h5h1gzh0h6i1i2gsidiggwh7i3h8iei4ihhbh9hcifi5iii6hai7hdj1ivijiwhhikilixhehfimj4inj2ioipiyizj5iriqjcj9isitiujdj8j6kdkekfj3j0jakjklj7jbjehgjflwjhkhjikkkmkgjkjpjljrjml3joknjsjgjwjxk0jyjvjuk1jjjzjqk2koksl4l5jnkpktkcl6jtk3l7k6k4kbk7k5k8kqkukrkvl8lbl9kwlqlckxlxlakykzk9kaldl0lelsl1l2m5lrlfm6lgm2lhlinfnelmlum3ljnglkkillnklnlonmlpnllymdmannlzmem0lvm1nom9o4mbm7m4npntm8nunqnimfmcnjmhnvmgnhmkmrmimjmlmqmmmnnro6o5nwnso7mpltnxnymomumto8o9mzmyn0n1mxmvmwn2msn3nzocn4oao0odorn7n5n8obo1oeo2n6o3n9oxofosndogohoip0oyojokolotoup1omp8nanboop9opoqp5ozp2p6pap7ncqjq9p3pbovqkpdpepgphplpopnpiqlonqmpkp4pcpuprpqpspxptpwpfpvpmpyowq8pjpppzq2q0q7q3q1q4qfqgq5q6qaqhqdqiqcqbqeqnqrqoqpqsqtqqqu"
+_OLD = "0102000604070c080n0k0m0l0o031b050p0d1k121c0e090i0q0u0v0w180r0a0g0f1f0x0s19260y0z1011141p1s1q1d0b0j1r2x1u2y1i1x1e131z1j2z30222g2321242h5r255s32343335362i370t2t151l201y1h1m1n3b3o3m3n3p0h383c5w3q1o393a3d3e5y2u3r2v2w3u3v3s313t3f5x3g3h1v3i2f5z3w3j603k3l1t1a173x3y4i3z4f2j49612s1w16404b4a454g624142434465464j4q4n471g4r294k4h48634m4o4s4p4u4l4t5v4v5t4w4y4x544z5753504d6i66676g4e2d64686h6j52514c2c2a282b69566k5c5a595f585e5b5d5u2e276a5g6b6l5h556m6c6o6p2m2o735k5i5l6n6d6q6e5m6f5j6r742r5q2q6s2p5n755o796t7c6z2l2k6u6v6w6x767d7a777k6y7h7e7072717l2n7g7i8l8m7b8n7m8q7j5p788r8t7f7n8s8u7oa47p7q9b7s8p7x7t7u7w9d7z8o808v8w909c9e7v8x918k8285877r89838486887y8a818b9f8e8y928z938c8j8f8d8g9g9j949h9k95a59y9i8h8i96979l98999za09aa19m9naaad9oabbnbm9pae9qbobs9r9s9tal9v9wbu9u9xbta6bvaia7aja8ama9a2cebwafacahbxc1apagc2byccanakaoc3bzcdcfbrasaqbparazataub2ayavb1cgc4c0axawc5a3c6chckb5b7b4bab3b9b6b8bqbbc7bcb0bfbdcic8clczbgcjc9cmbhcabecbcnd0blcod1bibjd5cpcvcqd8d6d3d9crcsctcudgcwcxd2dhcydcddd7deeiehejdadidfembkdbd4enepdjekdldmeldodtdqdpf7dseoeqdkdvdwerdye1e3dne5dze0e2e4duf9esewf8fae6dretexegeuevdxe7fbeae8ebg0e9ecefeyezfcfdedeefff0fufgf1fef2fhf3f4g1fwf5fvfxf6fig6fjg7fkg9hjhiflfmhkfqgahofnfofpfrfshqghfthpg2hrgeg3hsgdgfg4gig5hxgbg8glhtgcgjggfyiahyhui8gkhzi0hvi9hngogmhlgngvgpgqhwgtgygugribgxich3h1h0h6gzi1gsfzi2h5h2h4idigiehmh7i3h8gwi4hbh9ivihhcifi5iii6hdi7haijiwhhikixhehfj1ilj4iriminioipiyj5j2iziqjcisiuitjdj8j3j9jaj6kekdkfjejbhgj0kjkll5j7jfkglwjhkikkkmjgjijkkhjpjrjmjljol3jsknk1jzjujxjwjyk0jvjjk2jqkoksl4l6jnkpktkck3kqkukrkvjtl7k6k4kbk7k5k8l8lbl9kwlckxlxlalqkykzldl0k9kalslrltl1l2lem2lfm5lgm3nfnelhm6lingljnklklllnnlmdlonmlylmlzmalpnnmbm0mem1luo6nom9npntm7m4mhm8mfmcmgnunqo4nvnro5njmkminhmjmrmlmqmmmumno7nwnsmpmto8nxmolvo9nymwmxmzn2n1mvmyn0niocoan3nzn4o0odmsn7n5n8obo1oeoro2n9o3n6oxofosndognaotnbohp0oioup1oyovojokolomp8ooonopp5ozp2p9oqp6pap7qjncq9p4p3pbpdpeqkpgphqfplpcpipkqlqmpjowpnpoqgpqpvpxprpspupwptpfpypmpzppq2q7q3q0q4q1q8q5q6qaqhqiqbqcqdqeqnqrqoqsqpqtqqqu"
+
+
+def rank_program(g, core, T, topo):
+    rank = T.rank_of(core)
+    if rank is None:
+        return
+    if not _PLAN:
+        o_ = plan()
+        if len(ORDER) == 2 * len(o_):
+            q_ = [int(ORDER[i:i + 2], 36) for i in range(0, len(ORDER), 2)]
+        else:
+            q_ = order(o_)[0]
+        _PLAN.append((o_, q_))
+    ops, seq = _PLAN[0]
+    N = len(T.cores)
+    nxt, prv = T.cores[(rank + 1) % N], T.cores[(rank - 1) % N]
+    rid, pid, _se = topo.addr(nxt)
+    mask = topo.mask(core, nxt)
+    n_out, n_in = len(topo.engines(core, nxt)), len(topo.engines(prv, core))
+    Q = {"V": g.vector, "S": g.scalar, "P": g.tensor, "G": g, "Y": g.sync}
+    esem = {"V": "sv", "S": "sa", "P": "sp", "G": "sg"}
+
+    def ap(a):
+        if not isinstance(a, tuple):
+            return a
+        if a[0] == "H":
+            return T[a[1]][a[2]]
+        if a[0] == "I":
+            return T[a[1]][:, a[2]:a[3]].indirect(T[a[4]][:, a[5]:a[6]])
+        p = a[5] if a[5] is not None else slice(None)
+        if a[4] == 1:
+            return T[a[1]][p, a[2]:a[3]]
+        return T[a[1]][p, a[2]:a[3]:a[4]]
+
+    needed = set()
+    for o in ops:
+        if o["kind"] != "r":
+            needed.update(j for j, w in o["deps"].items() if w)
+    mark = {}
+    cnt = {}
+    seen = {}
+    known, clock = {}, {}
+    pos = {i: n for n, i in enumerate(seq)}
+    ndma = [0]
+    for i in seq:
+        o = ops[i]
+        e, c = o["eng"], o["call"]
+        if o["kind"] == "r":
+            mark[i] = ("arr%d" % (NCH * (c[1] - 1) + c[2]), n_in)
+            cnt[mark[i][0]] = n_in
+            continue
+        q = Q[e]
+        want = {}
+        kn = known.setdefault(e, {})
+        for j, w in o["deps"].items():
+            if w and mark[j][1] > want.get(mark[j][0], (0, 0))[0]:
+                want[mark[j][0]] = (mark[j][1], j)
+        for s_, (v, j) in sorted(want.items(), key=lambda x: -pos[x[1][1]]):
+            if kn.get(s_, 0) < v:
+                q.wait_ge(T.sem[s_], v)
+                seen[(e, s_)] = v
+                kn[s_] = v
+                for s2, v2 in clock.get(j, {}).items():
+                    kn[s2] = max(kn.get(s2, 0), v2)
+        clock[i] = dict(kn)
+        k = c[0]
+        if k == "cp":
+            r = q.tensor_copy(ap(c[1]), ap(c[2]))
+        elif k == "ts":
+            if c[6] is None:
+                r = q.tensor_scalar(ap(c[1]), ap(c[2]), ap(c[3]), None, c[5])
+            else:
+                r = q.tensor_scalar(ap(c[1]), ap(c[2]), ap(c[3]), ap(c[4]), c[5], c[6])
+        elif k == "tt":
+            r = q.tensor_tensor(ap(c[1]), ap(c[2]), ap(c[3]), c[4])
+        elif k == "scan":
+            r = q.tensor_tensor_scan(ap(c[1]), ap(c[2]), ap(c[3]), 0.0, c[4], c[5])
+        elif k == "ms":
+            r = q.memset(ap(c[1]), c[2])
+        elif k == "act":
+            r = q.activation(ap(c[1]), ap(c[2]), c[3], bias=ap(c[4]), scale=ap(c[5]), accum_out=ap(c[6]))
+        elif k == "mm":
+            for m in c[1]:
+                r = q.matmul(ap(m[0]), ap(m[1]), ap(m[2]), m[3], m[4])
+        elif k == "tr":
+            for m in c[1]:
+                r = q.transpose(ap(m[1]), ap(m[2]), T["idb"][:])
+        elif k == "iota":
+            if SCRATCH[c[1][1]][2] == I32:
+                r = q.iota(ap(c[1]), c[2], c[3], c[4])
+            else:
+                r = q.iota(ap(c[1]), c[2], c[3], c[4], allow_small_or_imprecise_dtypes=True)
+        elif k == "dma":
+            s_ = "dm%d" % ndma[0]
+            ndma[0] += 1
+            q.dma_start(ap(c[1]), ap(c[2])).then_inc(T.sem[s_], 16)
+            mark[i] = (s_, 16)
+            cnt[s_] = 16
+            continue
+        elif k == "send":
+            t, h = c[1], c[2]
+            q.remote_dma(ap(c[4]), ap(c[3]), T.sem["arr%d" % (NCH * t + h)], T.sem["gone"], pid, rid, mask)
+            cnt["gone"] = cnt.get("gone", 0) + n_out
+            continue
+        if i in needed:
+            s_ = esem[e]
+            cnt[s_] = cnt.get(s_, 0) + 1
+            r.then_inc(T.sem[s_], 1)
+            mark[i] = (s_, cnt[s_])
+    for s_, v in sorted(cnt.items()):
+        if max([0] + [w for (e, n_), w in seen.items() if n_ == s_]) < v:
+            g.wait_ge(T.sem[s_], v)

@@ -1,17 +1,13 @@
-from concourse.bass import DstId, RemoteDMATransfer
-from concourse.mybir import dt, AluOpType, AxisListType, ActivationFunctionType
+from concourse.mybir import AluOpType, ActivationFunctionType
 
 ALU = AluOpType
 AF = ActivationFunctionType
 F32, BF, F16, I32, U16 = "float32", "bfloat16", "float16", "int32", "uint16"
 STEPS = 4
-KSPLIT = True
-SCANI = True
-HACT = True
+SC = 16384.0
 GAV = ((0, 0, 0, 1), (0, 0, 1, 1))
-FACT = (1, 1, 0, 0)
+FACT = (1, 0, 0, 0, 0, 0, 0, 0)
 CH = (8, 8)
-SUB = True
 NCH = len(CH)
 Q0 = [16 - sum(CH[:h + 1]) for h in range(NCH)]
 SEG = [[16 * (16 - (Q0[h] + q)) + 2 for q in range(CH[h])] for h in range(NCH)]
@@ -28,12 +24,12 @@ def _sb(name, n, d):
 for _n, _w, _d in [
     ("xs", 4096, BF), ("vs", 8208, BF), ("ctab", 4112, F32), ("lan", 256, I32), ("s0w", 256, I32), ("wti", 8, I32),
     ("srow", 256, BF), ("ci", 16, I32), ("cf", 32, F32), ("t0", 256, F32), ("t1", 256, F32), ("t2", 256, F32),
-    ("t3", 256, F32), ("ti", 128, I32), ("tj", 32, I32), ("idb", 128, BF), ("idh", 128, F16), ("nid", 128, BF), ("i19", 128, BF),
-    ("tn", 120, BF), ("blk", 128, BF), ("sel", 144, BF), ("selw", 144, BF), ("selk", 144, F16), ("selb", 144, BF), ("wm", 128, F16),
-    ("iw", 32, BF), ("poff", 128, U16), ("pa", 2048, F16), ("ta", 128, BF), ("tb", 128, BF),
-    ("tc", 128, BF), ("mtab", 128, F32), ("rst", 120, F32), ("ltl", 16, U16), ("revl", 16, U16), ("rev", 16, U16),
-    ("ends", 8, U16), ("val", 8, F32), ("lst", 16, F32), ("tri", 16, BF), ("hrow", 272, F16), ("win", 16, BF), ("fsel", 256, BF),
-    ("thr", 8, F32), ("aq", 16, BF), ("ay", 8, F32), ("aj", 16, F32),
+    ("t3", 256, F32), ("ti", 128, I32), ("tj", 32, I32), ("idb", 128, BF), ("idh", 128, F16), ("nid", 128, BF),
+    ("i19", 128, BF), ("tn", 120, BF), ("blk", 128, BF), ("sel", 144, BF), ("selw", 144, BF), ("selk", 144, F16),
+    ("selb", 144, BF), ("wm", 128, F16), ("iw", 32, BF), ("poff", 128, U16), ("pa", 2048, F16), ("ta", 128, BF),
+    ("tb", 128, BF), ("tc", 128, BF), ("mtab", 128, F32), ("rst", 120, F32), ("ltl", 16, U16), ("revl", 16, U16),
+    ("rev", 16, U16), ("ends", 8, U16), ("val", 8, F32), ("lst", 16, F32), ("tri", 272, BF), ("hrow", 272, F16),
+    ("win", 16, BF), ("fsel", 256, BF), ("thr", 8, BF), ("hl", 64, BF), ("aq", 16, BF), ("ay", 8, F32), ("aj", 16, F32),
 ]:
     _sb(_n, _w, _d)
 for _h in range(NCH):
@@ -41,9 +37,10 @@ for _h in range(NCH):
     for _n, _w, _d in [
         ("ld", 16 * _c, I32), ("lu", 16 * _c, U16), ("lh", 16 * _c, F16), ("a", 256 * _c, BF), ("at", 256 * _c, F16),
         ("q", 240 * _c, BF), ("f", 240 * _c, BF), ("d", 240 * _c, F16), ("ab", 240 * _c, F16), ("cl", 240 * _c, BF),
-        ("lall", 1040 + 128 * _c, F32), ("w4", 256, F16), ("w1", 256, F32), ("w2", 256, I32), ("w3", 384, BF), ("hu", 128, U16),
-        ("sc", 240, I32 if SCANI else F32), ("k", 48, I32), ("m", 64, F32), ("ou", 32, U16), ("eq", TOT[_h], BF), ("es", TOT[_h], BF),
-        ("msk", TOT[_h], BF), ("snd", 144 * STEPS, I32), ("rcv", 144 * (STEPS + 1), I32), ("fo", 384, F32),
+        ("lall", 1040 + 128 * _c, F32), ("w4", 256, F16), ("w1", 256, F32), ("w2", 256, I32), ("w3", 384, BF),
+        ("hu", 128, U16), ("sc", 240, I32), ("k", 48, I32), ("m", 64, F32), ("ou", 32, U16), ("eq", TOT[_h], BF),
+        ("es", TOT[_h], BF), ("msk", TOT[_h], BF), ("snd", 144 * STEPS, I32), ("rcv", 144 * (STEPS + 1), I32),
+        ("fo", 384, F32),
     ]:
         _o = SCRATCH[_n][1][1] if _h else 0
         PART[_n + str(_h)] = (_n, _o, _w)
@@ -80,9 +77,7 @@ def count(a):
 def spans(a):
     if a[0] == "I":
         return [(a[1], a[2], a[3]), (a[4], a[5], a[6])]
-    if a[0] == "A":
-        return [(a[1], a[2], a[3])]
-    return []
+    return [(a[1], a[2], a[3])]
 
 
 def psum(a):
@@ -103,11 +98,9 @@ def plan():
         deps = {}
         for lst, wr in ((reads, False), (writes, True)):
             for a in lst:
-                sp = spans(a)
-                for n, (name, lo, hi) in enumerate(sp):
+                for n, (name, lo, hi) in enumerate(spans(a)):
                     w = wr and n == 0
-                    ps = SCRATCH[name][0] == "psum"
-                    if ps:
+                    if SCRATCH[name][0] == "psum":
                         st = acc.setdefault(name, [eng, [], []])
                         if st[0] != eng:
                             st[:] = [eng, [], st[1]]
@@ -150,7 +143,7 @@ def plan():
         return add("V", vcost(out, [in_]), ("cp", out, in_), [in_], [out])
 
     def ts(out, in_, s1, op0, s2=None, op1=None):
-        return add("V", vcost(out, [in_]), ("ts", out, in_, s1, s2, op0, op1), [in_] + aps(s1, s2), [out])
+        return add("V", vcost(out, [in_] + aps(s1, s2)), ("ts", out, in_, s1, s2, op0, op1), [in_] + aps(s1, s2), [out])
 
     def tt(out, a, b, op):
         return add("V", vcost(out, [a, b], True), ("tt", out, a, b, op), [a, b], [out])
@@ -167,13 +160,8 @@ def plan():
         return add("S", c * CYC, ("act", out, in_, f, bias, scale, accum), [in_] + aps(bias, scale), [out] + aps(accum))
 
     def mm(lst):
-        c = 0
-        rd, wr = [], []
-        for m in lst:
-            c += max(64, count(m[0])) * (4 if SCRATCH[m[1][1]][2] == F32 else 1)
-            rd += [m[1], m[2]]
-            wr.append(m[0])
-        return add("P", c * PCYC, ("mm", lst), rd, wr)
+        c = sum(max(64, count(m[0])) for m in lst)
+        return add("P", c * PCYC, ("mm", lst), [a for m in lst for a in m[1:3]], [m[0] for m in lst])
 
     def group(out, pairs):
         return [(out, l, r, k == 0, k == len(pairs) - 1) for k, (l, r) in enumerate(pairs)]
@@ -182,11 +170,14 @@ def plan():
         return add("G", 130 + 2 * count(out) * CYC, ("iota", out, pat, base, cm), [], [out])
 
     def dma(eng, out, in_, nbytes):
-        return add(eng, 2000 + nbytes / 180.0, ("dma", out, in_), aps(in_) if in_[0] != "H" else [],
-                   aps(out) if out[0] != "H" else [], kind="d")
+        return add(eng, 2000 + nbytes / 180.0, ("dma", out, in_), [in_] if in_[0] != "H" else [],
+                   [out] if out[0] != "H" else [], kind="d")
 
     def H(name, *ix):
         return ("H", name, ix)
+
+    def col(b, j):
+        return A(b, j, j + 1)
 
     al = slice(None)
     dma("Y", A("lan"), H("lanes", al, al), 131072)
@@ -198,8 +189,6 @@ def plan():
     dma("Y", A("vs", 0, 2048), H("v", al, slice(2048, 4096)), 1400000)
     dma("Y", A("vs", 2048, 4096), H("v", al, slice(0, 2048)), 1400000)
 
-    def col(b, j):
-        return A(b, j, j + 1)
     iota(col("ci", 0), [[0, 1]], 0, 1)
     for h in range(NCH):
         iota(A("tj", Q0[h], Q0[h] + CH[h]), [[-1, 2], [-32, CH[h] // 2]], 255 - 16 * Q0[h], -2)
@@ -235,12 +224,13 @@ def plan():
     cp(col("cf", 8), col("wti", 0))
     ts(A("selb"), A("t0", 0, 144), col("cf", 7), ALU.is_equal)
     ts(A("selw"), A("t0", 0, 144), col("cf", 7), ALU.is_equal, col("cf", 8), ALU.mult)
-    act(A("sel"), A("selb"), scale=float(2 ** 20))
+    act(A("sel"), A("selb"), scale=float(2 ** 19))
     act(A("selk"), A("selb"), scale=1024.0)
     act(A("nid"), A("idb"), scale=-1.0)
     act(A("idh"), A("idb"))
     act(A("i19"), A("idb"), scale=float(2 ** 19))
-    ms(A("tn"), -11.0 * 2 ** 20)
+    for i in range(2):
+        ms(A("tn", 60 * i, 60 * i + 60), -11.0 * 2 ** 20)
     ts(col("cf", 16), J_, 8.0, ALU.is_ge, 65280.0, ALU.mult)
     ts(A("tc", 0, 64), A("t0", 0, 64), 0.0, ALU.mult, col("cf", 16), ALU.add)
     ts(A("tc", 64, 128), A("tc", 0, 64), 256.0, ALU.add)
@@ -249,7 +239,7 @@ def plan():
     ts(A("blk"), A("t3", 0, 128), G_, ALU.is_equal)
     ms(A("rst", 0, 120), 0.0)
     ms(A("rst", 0, 120, 15), float(2 ** 25))
-    ms(col("thr", 0), 2.0)
+    ms(col("thr", 0), 2.5)
     ts(A("t3", 136, 144), A("t3", 128, 136), J_, ALU.add, 0.5, ALU.add)
     ts(A("t3", 144, 152), A("t3", 136, 144), 1.0 / 15.0, ALU.mult, -0.5, ALU.add)
     cp(A("ti", 0, 8), A("t3", 144, 152))
@@ -261,12 +251,13 @@ def plan():
     ts(A("iw"), A("t0", 0, 32), J_, ALU.is_equal)
     for i in range(4):
         act(A("pa", 512 * i, 512 * i + 512), IX("iw", 0, 32, "poff", 32 * i, 32 * i + 32))
-    ts(col("cf", 9), J_, 32.0, ALU.mult, 4128.0, ALU.add)
-    ts(A("val"), A("t3", 128, 136), 32.0, ALU.mult, col("cf", 9), ALU.add)
+    ts(col("cf", 9), J_, 32.0 / SC, ALU.mult, 4128.0 / SC, ALU.add)
+    ts(A("val"), A("t3", 128, 136), 32.0 / SC, ALU.mult, col("cf", 9), ALU.add)
     ts(col("cf", 10), J14, -2.0, ALU.mult)
     for c in set(CH):
         ts(A("lst", 2 * c - 8, 3 * c - 8), A("t3", 128, 128 + c), 30.0 * c - 2, ALU.mult, col("cf", 10), ALU.add)
-    ts(A("tri"), A("t0", 0, 16), J_, ALU.is_gt, 16384.0, ALU.mult)
+    ts(A("tri", 0, 16), A("t0", 0, 16), J_, ALU.is_gt)
+    ms(A("tri", 16, 272), 1.0)
     ts(A("hrow", 256, 272), A("t0", 0, 16), 0.0, ALU.mult, 2048.0, ALU.add)
     for h in range(NCH):
         s, c = str(h), CH[h]
@@ -274,10 +265,9 @@ def plan():
         ts(col("cf", 18 + h), jc, -8.0, ALU.mult, float(SEG[h][0]), ALU.add)
         ts(col("cf", 22 + h), jc, 1.0, ALU.add, col("cf", 18 + h), ALU.mult)
         ts(A("ends", 2 * h, 2 * h + 1), col("cf", 22 + h), -1.0, ALU.add)
-        iota(A("msk" + s), [[0, TOT[h]]], 16384, 0)
         o = 0
         for q in range(c):
-            act(A("msk" + s, o, o + 16), A("tri"))
+            act(A("msk" + s, o, o + SEG[h][q]), A("tri", 0, SEG[h][q]), scale=col("val", q))
             o += SEG[h][q]
         iota(A("lall" + s, 120 * c, 1040 + 128 * c), [[0, 1040 + 8 * c]], 0, 0)
         if c == 4:
@@ -293,20 +283,17 @@ def plan():
         rot[0] += 1
         return "px%d" % (rot[0] % 3)
 
-    def arrive(t, h, sent):
-        return add("R", LAT_R, ("arr", t, h), [], [A("rcv%d" % h, 144 * t, 144 * t + 17 * CH[h])], kind="r", after=[sent])
+    def selj(name, j):
+        return A(name, 15 - j, 143 - j)
 
     def close_step(last):
         for h in range(NCH):
             cp(IX("vs", 0, 8208, "ou%d" % h, 16, 16 + CH[h]), A("fsel", 16 * Q0[h], 16 * (Q0[h] + CH[h])))
         if not last:
             mm(group(A("pk", 256, 272), [(A("blk"), A("win"))]))
-            act(A("aj"), A("pk", 256, 272), scale=-1.0, bias=48.375, accum=col("ay", 0))
-            act(col("aq", 0), col("ay", 0), bias=-3.5)
+            act(A("aj"), A("pk", 256, 272), scale=-1.0, bias=48.40625, accum=col("ay", 0))
+            act(col("aq", 0), col("ay", 0), bias=-4.0)
             act(col("thr", 0), col("aq", 0), scale=-1.0, bias=col("ay", 0))
-
-    def selj(name, j):
-        return A(name, 15 - j, 143 - j)
 
     def half(t, h):
         s = str(h)
@@ -325,22 +312,13 @@ def plan():
         ts(A("lh" + s, 0, n2), A("lu" + s, 0, n2), -2048.0, ALU.add, 1.0 / 4096, ALU.mult)
         ts(A("lh" + s, n2, 2 * n2), A("lu" + s, n2, 2 * n2), -2048.0, ALU.add)
         tt(A(w3, 0, 16 * c), IX("rcv" + s, r0, r0 + c, "ltl", 2 * c - 8, 3 * c - 8), A("mtab", 0, 16 * c), ALU.is_gt)
-
-        def slots(a, b):
-            act(A(w3, 128 + a, 128 + b), A("pu", a, b), bias=0.5)
-            tt(A(w4, a, b), A("pu", a, b), A(w3, 128 + a, 128 + b), ALU.subtract)
-            act(A("pu", 256 + a, 256 + b), A(w4, a, b), bias=5280.0)
-            tt(A(w2, a, b), A("pu", 256 + a, 256 + b), A(w4, a, b), ALU.mult)
-            ts(A(w2, 128 + a, 128 + b), A(w2, a, b), 5, ALU.arith_shift_right, 4095, ALU.bitwise_and)
-            cp(A("hu" + s, a, b), A(w2, 128 + a, 128 + b))
         for pc in range(npc):
             rot[1] += 1
             pt = "pt%d" % (rot[1] % 2)
             for b in range(2):
                 c0 = n2 * b + 32 * pc
                 o = 1024 * pc + 512 * b
-                (cp if (t, h, pc, b) in GAV or (h, pc, b) in GAV else act)(
-                    A("a" + s, o, o + 512), IX("xs", 0, 4096, "lu" + s, c0, c0 + 32))
+                (cp if (t, h, pc, b) in GAV else act)(A("a" + s, o, o + 512), IX("xs", 0, 4096, "lu" + s, c0, c0 + 32))
                 lst = [("T", A(pt, 512 * b + 128 * i, 512 * b + 128 * i + 128), A("a" + s, o + 128 * i, o + 128 * i + 128))
                        for i in range(4)]
                 add("P", 512 * PCYC, ("tr", lst), [m[2] for m in lst] + [A("idb")], [m[1] for m in lst])
@@ -365,13 +343,15 @@ def plan():
                     act(A("f" + s, o, o + 480), A(bk, 0, 480))
                 else:
                     tt(A("f" + s, o, o + 480), A(bk, 0, 480), A("q" + s, o, o + 480), ALU.subtract)
-            mm(group(A("pu", 60 * pc, 60 * pc + 60),
-                     [(A("blk"), A("tc", 64, 124))] +
+            a, b = 60 * pc, 60 * pc + 60
+            mm(group(A("pu", a, b), [(A("blk"), A("tc", 64, 124))] +
                      [(selj("selw", j), A("f" + s, 960 * pc + j, 960 * pc + 960, 16)) for j in range(16)]))
-            if SUB:
-                slots(60 * pc, 60 * pc + 60)
-        if not SUB:
-            slots(0, nm)
+            act(A(w3, 128 + a, 128 + b), A("pu", a, b), bias=0.5)
+            tt(A(w4, a, b), A("pu", a, b), A(w3, 128 + a, 128 + b), ALU.subtract)
+            act(A("pu", 256 + a, 256 + b), A(w4, a, b), bias=5280.0)
+            tt(A(w2, a, b), A("pu", 256 + a, 256 + b), A(w4, a, b), ALU.mult)
+            ts(A(w2, 128 + a, 128 + b), A(w2, a, b), 5, ALU.arith_shift_right, 4095, ALU.bitwise_and)
+            cp(A("hu" + s, a, b), A(w2, 128 + a, 128 + b))
         ts(A(w4, 128, 128 + nm), A("hu" + s, 0, nm), -2048.0, ALU.add)
         act(A(w3, 256, 256 + nm), A(w4, 0, nm), bias=12288.0 - 31.5)
         pre = [(A("idb"), A("ta", 0, nm)), (A("idh"), A(w4, 128, 128 + nm)), (A("i19"), A(w3, 0, nm))]
@@ -401,10 +381,10 @@ def plan():
                 o = 480 * pi
                 tt(A("d" + s, o, o + 480), IX("vs", 0, 4096, "hu" + s, 30 * pi, 30 * pi + 30), A("f" + s, o, o + 480), ALU.subtract)
                 act(A("ab" + s, o, o + 480), A("d" + s, o, o + 480), AF.Abs)
-                ts(A("cl" + s, o, o + 480), A("ab" + s, o, o + 480), col("thr", 0), ALU.is_le)
+                ts(A("cl" + s, o, o + 480), A("ab" + s, o, o + 480), col("thr", 0), ALU.is_le, 2.0, ALU.mult)
             c0, c1 = 60 * pc, 60 * pc + 60
-            mm([(A("pc", c0, c1), selj("sel", j), A("cl" + s, 960 * pc + j, 960 * pc + 960, 16), False, pc == npc - 1 and j == 15)
-                for j in range(16)])
+            mm([(A("pc", c0, c1), selj("sel", j), A("cl" + s, 960 * pc + j, 960 * pc + 960, 16), False,
+                 pc == npc - 1 and j == 15) for j in range(16)])
             mm(group(A("pk", 120 + c0, 120 + c1),
                      [(A("idb"), A("tb", c0, c1)), (A("idh"), A(w4, c0, c1)), (A("nid"), A(w3, 256 + c0, 256 + c1))] +
                      [(selj("selk", j), A("ab" + s, 960 * pc + j, 960 * pc + 960, 16)) for j in range(16)]))
@@ -412,41 +392,38 @@ def plan():
         scan(A("sc" + s, 0, nm), A("rst", 0, nm), A(w1, 128, 128 + nm), ALU.add, ALU.min)
         scan(A("sc" + s, nm, 2 * nm), A("rst", 0, nm), A("pk", 120, 120 + nm), ALU.add, ALU.min)
         k, m_, ou = "k" + s, "m" + s, "ou" + s
-        k1, k2 = A(k, 0, c), A(k, c, 2 * c)
-        if SCANI:
-            k1, k2 = A("sc" + s, 14, nm, 15), A("sc" + s, nm + 14, 2 * nm, 15)
-        elif KSPLIT:
-            cp(k1, A("sc" + s, 14, nm, 15))
-            cp(k2, A("sc" + s, nm + 14, 2 * nm, 15))
-        else:
-            cp(A(k, 0, 2 * c), A("sc" + s, 14, 2 * nm, 15))
+        k1, k2 = A("sc" + s, 14, nm, 15), A("sc" + s, nm + 14, 2 * nm, 15)
         ts(A(k, 16, 16 + c), k1, 0x700FFF, ALU.bitwise_and)
         ts(A(ou, 0, c), A(k, 16, 16 + c), 4096.0, ALU.min)
         ts(A(m_, 16, 16 + c), A(k, 16, 16 + c), 4096.0, ALU.min, -2048.0, ALU.add)
-        act(A(m_, 0, c), A(m_, 16, 16 + c), bias=2048.0)
-        (act if HACT else cp)(A("hrow", B, B + 16 * c), IX("ctab", 0, 4112, ou, 0, c))
+        act(A(m_, 0, c), A(m_, 16, 16 + c), scale=1.0 / SC, bias=2048.0 / SC)
+        hi, lo = 16 * h, 16 * h + 8
+        ts(A("hl", hi, hi + c), A(k, 16, 16 + c), 4096.0, ALU.min, -2048.0, ALU.add)
+        tt(A("hl", lo, lo + c), A(m_, 16, 16 + c), A("hl", hi, hi + c), ALU.subtract)
+        act(A("hrow", B, B + 16 * c), IX("ctab", 0, 4112, ou, 0, c))
         ts(A(k, 24, 24 + c), k1, 4 if c == 8 else 5, ALU.arith_shift_right, 127 * 32 * c, ALU.bitwise_and)
         ts(A(k, 32, 32 + c), k2, 15, ALU.bitwise_and)
         ts(A(ou, 8, 8 + c), A(k, 24, 24 + c), 0.5 / c, ALU.mult, J_, ALU.add)
-        tt(A(m_, c, 2 * c), A(k, 24, 24 + c), A("lst", 2 * c - 8, 3 * c - 8), ALU.subtract)
+        tt(A(m_, 56, 56 + c), A(k, 24, 24 + c), A("lst", 2 * c - 8, 3 * c - 8), ALU.subtract)
+        act(A(m_, c, 2 * c), A(m_, 56, 56 + c), scale=1.0 / SC)
         tt(A(m_, 24, 24 + c), A("rcv" + s, r0, r0 + c), A(k, 32, 32 + c), ALU.subtract)
         o = 0
         for q in range(c):
             n = SEG[h][q]
-            ts(A("eq" + s, o, o + n), A("hrow", 258 - n, 258), col(m_, 16 + q), ALU.is_equal, col("val", q), ALU.mult)
+            ts(A("eq" + s, o, o + n), A("hrow", 258 - n, 258), col("hl", hi + q), ALU.subtract, col("hl", lo + q), ALU.is_equal)
             o += n
         scan(A("es" + s), A("eq" + s), A("msk" + s), ALU.max, ALU.min)
         tt(A(m_, 32, 48), IX("es" + s, 0, TOT[h], "ends", 2 * h, 2 * h + 1), A(m_, 0, 16), ALU.max)
-        ts(A(ou, 24, 24 + c), A(m_, 32 + c, 32 + 2 * c), 0.25, ALU.mult)
+        ts(A(ou, 24, 24 + c), A(m_, 32 + c, 32 + 2 * c), 0.25 * SC, ALU.mult)
         cp(A("snd" + s, r0 + c, r0 + 17 * c), IX("lall" + s, 0, 1040 + 128 * c, ou, 24, 24 + c))
         wn = A("win", Q0[h], Q0[h] + c)
-        ts(wn, A(m_, 32, 32 + c), 4096.0, ALU.is_lt)
+        ts(wn, A(m_, 32, 32 + c), 4096.0 / SC, ALU.is_lt)
         tt(A(m_, 48, 48 + c), A(m_, 24, 24 + c), wn, ALU.mult)
         tt(A("snd" + s, r0, r0 + c), A(m_, 48, 48 + c), A(k, 32, 32 + c), ALU.add)
-        src = A("snd" + s, r0, r0 + 17 * c)
-        sent = add("G", 300, ("send", t, h, src, A("rcv" + s, r0 + 144, r0 + 144 + 17 * c)), [src], [], kind="s")
-        arrive(t + 1, h, sent)
-        cp(A(ou, 16, 16 + c), A(m_, 32, 32 + c))
+        src, dst = A("snd" + s, r0, r0 + 17 * c), A("rcv" + s, r0 + 144, r0 + 144 + 17 * c)
+        sent = add("G", 300, ("send", t, h, src, dst), [src], [], kind="s")
+        add("R", LAT_R, ("arr", t + 1, h), [], [dst], kind="r", after=[sent])
+        ts(A(ou, 16, 16 + c), A(m_, 32, 32 + c), SC, ALU.mult)
         act(A("fsel", B, B + 16 * c), IX("f" + s, 0, 240 * c, ou, 8, 8 + c))
 
     for t in range(STEPS):
@@ -473,59 +450,8 @@ def plan():
     return ops
 
 
-def order(ops):
-    n = len(ops)
-    succ = [[] for _ in range(n)]
-    for i, o in enumerate(ops):
-        for j in o["deps"]:
-            succ[j].append(i)
-
-    def lat(j, i):
-        if not ops[i]["deps"][j] or ops[i]["kind"] == "r":
-            return 0.0
-        return LAT_S if ops[j]["eng"] == ops[i]["eng"] and ops[j]["kind"] == "c" else LAT_X
-    pr = [0.0] * n
-    for i in range(n - 1, -1, -1):
-        pr[i] = ops[i]["cost"] + max([pr[k] + lat(i, k) for k in succ[i]] + [0.0])
-    left = [len(o["deps"]) for o in ops]
-    rdy = [0.0] * n
-    cand = {}
-    free = {}
-    for i in range(n):
-        if left[i] == 0:
-            cand.setdefault(ops[i]["eng"], []).append(i)
-    seq = []
-    end = 0.0
-    while len(seq) < n:
-        best = None
-        for e, lst in cand.items():
-            if not lst:
-                continue
-            f = free.get(e, 0.0)
-            t0 = max(f, min(rdy[i] for i in lst))
-            i = max((i for i in lst if rdy[i] <= t0 + 40.0), key=lambda x: (pr[x], -x))
-            st = max(f, rdy[i])
-            if best is None or st < best[0]:
-                best = (st, i, e)
-        st, i, e = best
-        cand[e].remove(i)
-        o = ops[i]
-        fin = st + o["cost"]
-        free[e] = {"d": st + 100.0, "r": st}.get(o["kind"], fin)
-        o["t0"], o["t1"] = st, fin
-        end = max(end, fin)
-        seq.append(i)
-        for k in succ[i]:
-            rdy[k] = max(rdy[k], fin + lat(i, k))
-            left[k] -= 1
-            if left[k] == 0:
-                cand.setdefault(ops[k]["eng"], []).append(k)
-    return seq, end
-
-
+ORDER = "010207000604080d0o0l0n0k0m0p0e0a091c0v0q0w120c0f0x1d0y100z1e110g0b0i1t0j1q1r0s1s0u1j1u5t1k242x5u1f031b202y181w323l0525132h5y15343n3335363m373b1m0r26142i0t5z383c600h2g1i2j233o393a1l21272t221n1o2z303p3q613t3d3e2u1p621y2s3r1a3u3f193s3g3v173h1v1g3i3w3x1x3j2w2v313k3y3z484e1h44164f49404142434a45464h4p47664i674q634m4n644l4g4j4r4k6g6i5v4o68654s4u1z4v4t6h4x544y5w6j4z51694w5257555629535e5h5c5a5g6k5b5f5d502d2b282a2c4c2f582e4d4b6a6o6l5i5j596p5m5k6b6c6m5n5l5o6q6d6n6e735x6f792k2n2q6r742m6s6t5s7c5p5q756u766v6w6x6y7k70727a7d71772p6z7h7e7b787l2r7i2l2o7m8p8o8q8u8w7j7g7f7n8s5r7p7q8r7s7z7t7y7o8v8x827w7u7r7x808b8687888a89858c8y9d9f837v9e8z90938d818e848h8f8i8g8j948n9g91929h8k8l9i9l9j9m95a68t96979k8m989n99a0a19a9o9pa79bbrbs9c9qbtaca29r9s9t9u9vafan9xbxbz9wby9yadc0a8a9agaaaoabc1ak9zc5c2ajc6alc3cfchaeahapaibuamc7aqc4asarcgatavcic8bvawb2azaxb1aub5b0b3b4bcbbbfb8bacjb9bdbeaya4a3a5cnc9b6ckd2b7bgbhcacocbclbkbiblbjd3bmcccpcmcdcqcrbwced8csdbbnbod4bqctcud5cvcwcxdjdcd9czd0d6cyd1d7dkdgdddaeoendhepdldidfdedmeteverbpdodpeqdrdydse1dvdxdneuewdtdqdwdze8e7e9e6eae5e4ebexfcdue2fdfeeyezf2fff0ecede3e0egeeehefeifgf3emf1fhfkfiflejekf4g5f5f6fjeself7fmf8f9g6fafzfng0fofbfphqhrfqfvhsfrgbfsfthwhyfugeg1fwhxfxhzg7gcg8gmgfg9i0gjfyi4i1gngagii5gggdgoghgkhtgli2i6i3gpieiggrgsgqifihguh1gvgyhugwh0gxg3g2g4i7gtgzh4h2h3hbheh9h7hdiih8hchah5i8imijhfi9hgh6iniaikhjhhhkhihlibioj1j2ilicipiqhvidj7irjahmhnj3hpisj5j4j6itiujbj8iviwiyizixjij0jjjfjcj9knkmjgkojkjhkskujejdjljmkqhojnjokpjqjxjrk0jujsjpktjwjvkvjylbjtldk1k7k3k6k8k5k9k4kakwlckxkyl1lekzkbjzkck2kfkdkgkekhl2kll0lfkikjlglhljlkl3m4krl4l5kklil6lll7lylzl8lmlnm5l9lalonpnqlpnrlqlrmalsltm0mdmllunvnxlvnwlwmbnym6m7mem8nzmilxo3mmm9o0mhmfmcmgo4mjmnnsmko1o5o2moodmpoemqmrmtn0ntmumxofogmvmsmyn3n1mzn2ohn6nandn8ncn7nbn9mwm2m1m3o6n4o7oloiomn5neo8o9nfojnionoaokobp0p1nuocnjoop2opp6oqp9noorp3osngotouovphpapep7oxoyp4owpbp8p5pipfozpdpcpjpgpknnnhnknlnmpmpnpppqptpwpvplprpzpopupxq4q5q7q6q8q3q2q9psq0pyqaqbq1qeqcqfqdqgqrqlqvqjqsqkqwqxqmqtqhqiqpqqqoqyqzr3r0r4r1qnqur2r5r6"
 _PLAN = []
-ORDER = "010200060407080o0l0n0m0k1k0p1b0d0c090e0i0a260f0v1c0w1s0x120y100z0u110q1p140s1q1i1r0r1d19161f181u0b0g1g1v1j2x1e2y1x1z300305235r222g24130t252h5s20342i1l2t1y2z323335363o1m1n151h3m5w173n373b1a383c3p393q1o3d3a3e3r3u3f5x2u213s3v3t3g5y3h3w3i3j2f0h3k3l1t1w5z3x3y494i4j602w3z404a6g4f414b454g2j0j2s65612v4231434k44464q4n4h47664d4r484m5u5v674l4o2d4p4s4u4t5t4x544v4w4y534z504e62286i686364276h6j692e524c2a2b292c6a5157566k6l5c5b5d5e595f5a58555g6b5h6m6o6p5k5i5l6n6q2m2r732q6c6d5j5m6e6f6r2k2o742l5q6s755n5o796t7c7a6u76776z6v6w6x7d2n6y7k7h8l8m7e8n7b70727l712p787i7j7m5p8r8t7g7f7n8s8u7oa48o7p8p7q7s7x7t7z7u8v809b7w9d7v868584898883827r878w90919c8x8k9e7y8a92818b9f8e8c8j8f8d8g8y938z9g9j949h9k95a59y9i8h8i96979l98999aad9ma09z9nae9oaa9p9qbnbm9r9ua2abbo9s8q9tbs9v9wbu9xa6a7btalbvama8a3a9ccaibwacafahc1bxagbqanbrc2ajakc3apaobycec4bzc0bpasazaqaratayauavcdcfaxa1c5c6awb1b2cgb7b5b3b8b6b9b4bab0bbc7chckcic8clbcbfbdbgcjc9cmbecabhczcbd5cnd0blcod1bibjcpcqd8crd6csctd2d3d9cvcudgddcwdhcxcyeheidaejd7dcd4deenepdfdibkdbdjekdleldmdodteoeqdpdvdqf7erdwdkesewf8dse2e0e5e1e4dne3dzdydue6f9dretexegfadxe7fbeae8efebe9ecg0eueveyezfcfffdedeef0fufgf1g1fef2f3fhf4f5f6fifwg9fvfjgafkg6flfmhjhifnhkfoemfpfrfqfyg7hofshqftg2g3geghhphrhsgdhxhtgig4fzg5g8gbi8gfhmgjgghngchlglgogvhyhuhzgkgmgngpiahvi0hwi9ibgugqgrgtfxgygxich3h2h4h5h1gzh0h6i1i2gsidiggwh7i3h8iei4ihhbh9hcifi5iii6hai7hdj1ivijiwhhikilixhehfimj4inj2ioipiyizj5iriqjcj9isitiujdj8j6kdkekfj3j0jakjklj7jbjehgjflwjhkhjikkkmkgjkjpjljrjml3joknjsjgjwjxk0jyjvjuk1jjjzjqk2koksl4l5jnkpktkcl6jtk3l7k6k4kbk7k5k8kqkukrkvl8lbl9kwlqlckxlxlakykzk9kaldl0lelsl1l2m5lrlfm6lgm2lhlinfnelmlum3ljnglkkillnklnlonmlpnllymdmannlzmem0lvm1nom9o4mbm7m4npntm8nunqnimfmcnjmhnvmgnhmkmrmimjmlmqmmmnnro6o5nwnso7mpltnxnymomumto8o9mzmyn0n1mxmvmwn2msn3nzocn4oao0odorn7n5n8obo1oeo2n6o3n9oxofosndogohoip0oyojokolotoup1omp8nanboop9opoqp5ozp2p6pap7ncqjq9p3pbovqkpdpepgphplpopnpiqlonqmpkp4pcpuprpqpspxptpwpfpvpmpyowq8pjpppzq2q0q7q3q1q4qfqgq5q6qaqhqdqiqcqbqeqnqrqoqpqsqtqqqu"
-_OLD = "0102000604070c080n0k0m0l0o031b050p0d1k121c0e090i0q0u0v0w180r0a0g0f1f0x0s19260y0z1011141p1s1q1d0b0j1r2x1u2y1i1x1e131z1j2z30222g2321242h5r255s32343335362i370t2t151l201y1h1m1n3b3o3m3n3p0h383c5w3q1o393a3d3e5y2u3r2v2w3u3v3s313t3f5x3g3h1v3i2f5z3w3j603k3l1t1a173x3y4i3z4f2j49612s1w16404b4a454g624142434465464j4q4n471g4r294k4h48634m4o4s4p4u4l4t5v4v5t4w4y4x544z5753504d6i66676g4e2d64686h6j52514c2c2a282b69566k5c5a595f585e5b5d5u2e276a5g6b6l5h556m6c6o6p2m2o735k5i5l6n6d6q6e5m6f5j6r742r5q2q6s2p5n755o796t7c6z2l2k6u6v6w6x767d7a777k6y7h7e7072717l2n7g7i8l8m7b8n7m8q7j5p788r8t7f7n8s8u7oa47p7q9b7s8p7x7t7u7w9d7z8o808v8w909c9e7v8x918k8285877r89838486887y8a818b9f8e8y928z938c8j8f8d8g9g9j949h9k95a59y9i8h8i96979l98999za09aa19m9naaad9oabbnbm9pae9qbobs9r9s9tal9v9wbu9u9xbta6bvaia7aja8ama9a2cebwafacahbxc1apagc2byccanakaoc3bzcdcfbrasaqbparazataub2ayavb1cgc4c0axawc5a3c6chckb5b7b4bab3b9b6b8bqbbc7bcb0bfbdcic8clczbgcjc9cmbhcabecbcnd0blcod1bibjd5cpcvcqd8d6d3d9crcsctcudgcwcxd2dhcydcddd7deeiehejdadidfembkdbd4enepdjekdldmeldodtdqdpf7dseoeqdkdvdwerdye1e3dne5dze0e2e4duf9esewf8fae6dretexegeuevdxe7fbeae8ebg0e9ecefeyezfcfdedeefff0fufgf1fef2fhf3f4g1fwf5fvfxf6fig6fjg7fkg9hjhiflfmhkfqgahofnfofpfrfshqghfthpg2hrgeg3hsgdgfg4gig5hxgbg8glhtgcgjggfyiahyhui8gkhzi0hvi9hngogmhlgngvgpgqhwgtgygugribgxich3h1h0h6gzi1gsfzi2h5h2h4idigiehmh7i3h8gwi4hbh9ivihhcifi5iii6hdi7haijiwhhikixhehfj1ilj4iriminioipiyj5j2iziqjcisiuitjdj8j3j9jaj6kekdkfjejbhgj0kjkll5j7jfkglwjhkikkkmjgjijkkhjpjrjmjljol3jsknk1jzjujxjwjyk0jvjjk2jqkoksl4l6jnkpktkck3kqkukrkvjtl7k6k4kbk7k5k8l8lbl9kwlckxlxlalqkykzldl0k9kalslrltl1l2lem2lfm5lgm3nfnelhm6lingljnklklllnnlmdlonmlylmlzmalpnnmbm0mem1luo6nom9npntm7m4mhm8mfmcmgnunqo4nvnro5njmkminhmjmrmlmqmmmumno7nwnsmpmto8nxmolvo9nymwmxmzn2n1mvmyn0niocoan3nzn4o0odmsn7n5n8obo1oeoro2n9o3n6oxofosndognaotnbohp0oioup1oyovojokolomp8ooonopp5ozp2p9oqp6pap7qjncq9p4p3pbpdpeqkpgphqfplpcpipkqlqmpjowpnpoqgpqpvpxprpspupwptpfpypmpzppq2q7q3q0q4q1q8q5q6qaqhqiqbqcqdqeqnqrqoqsqpqtqqqu"
 
 
 def rank_program(g, core, T, topo):
@@ -533,12 +459,7 @@ def rank_program(g, core, T, topo):
     if rank is None:
         return
     if not _PLAN:
-        o_ = plan()
-        if len(ORDER) == 2 * len(o_):
-            q_ = [int(ORDER[i:i + 2], 36) for i in range(0, len(ORDER), 2)]
-        else:
-            q_ = order(o_)[0]
-        _PLAN.append((o_, q_))
+        _PLAN.append((plan(), [int(ORDER[i:i + 2], 36) for i in range(0, len(ORDER), 2)]))
     ops, seq = _PLAN[0]
     N = len(T.cores)
     nxt, prv = T.cores[(rank + 1) % N], T.cores[(rank - 1) % N]
@@ -564,10 +485,7 @@ def rank_program(g, core, T, topo):
     for o in ops:
         if o["kind"] != "r":
             needed.update(j for j, w in o["deps"].items() if w)
-    mark = {}
-    cnt = {}
-    seen = {}
-    known, clock = {}, {}
+    mark, cnt, seen, known, clock = {}, {}, {}, {}, {}
     pos = {i: n for n, i in enumerate(seq)}
     ndma = [0]
     for i in seq:
@@ -586,7 +504,7 @@ def rank_program(g, core, T, topo):
         for s_, (v, j) in sorted(want.items(), key=lambda x: -pos[x[1][1]]):
             if kn.get(s_, 0) < v:
                 q.wait_ge(T.sem[s_], v)
-                seen[(e, s_)] = v
+                seen[s_] = max(seen.get(s_, 0), v)
                 kn[s_] = v
                 for s2, v2 in clock.get(j, {}).items():
                     kn[s2] = max(kn.get(s2, 0), v2)
@@ -626,8 +544,7 @@ def rank_program(g, core, T, topo):
             cnt[s_] = 16
             continue
         elif k == "send":
-            t, h = c[1], c[2]
-            q.remote_dma(ap(c[4]), ap(c[3]), T.sem["arr%d" % (NCH * t + h)], T.sem["gone"], pid, rid, mask)
+            q.remote_dma(ap(c[4]), ap(c[3]), T.sem["arr%d" % (NCH * c[1] + c[2])], T.sem["gone"], pid, rid, mask)
             cnt["gone"] = cnt.get("gone", 0) + n_out
             continue
         if i in needed:
@@ -636,5 +553,5 @@ def rank_program(g, core, T, topo):
             r.then_inc(T.sem[s_], 1)
             mark[i] = (s_, cnt[s_])
     for s_, v in sorted(cnt.items()):
-        if max([0] + [w for (e, n_), w in seen.items() if n_ == s_]) < v:
+        if seen.get(s_, 0) < v:
             g.wait_ge(T.sem[s_], v)

@@ -4,9 +4,23 @@ ALU = AluOpType
 AF = ActivationFunctionType
 F32, BF, F16, I32, U16 = "float32", "bfloat16", "float16", "int32", "uint16"
 STEPS = 4
-SC = 16384.0
-GAV = ((0, 0, 0, 1), (0, 0, 1, 1))
-FACT = (1, 0, 0, 0, 0, 0, 0, 0)
+ROT = 2760
+OPT = dict(
+    mode="PVPVPVPV",
+    fev="SSSSSSSS",
+    gav=(),
+    ub=False,
+    col16=True,
+    seen="V",
+    near="D",
+    far="B",
+    u16=False,
+    ttu=True,
+    ssep=True,
+    eng={},
+)
+ENG = dict(lu0="V", lu1="V", hu="V", lh="S", h16="S", new="V", ou8="S", ou16="S", ou24="V", far="S", lall0="S", lall1="S",
+           same="S", w3="S", uq="S", m0="S", fsel="S", hrow="S")
 CH = (8, 8)
 NCH = len(CH)
 Q0 = [16 - sum(CH[:h + 1]) for h in range(NCH)]
@@ -25,11 +39,13 @@ for _n, _w, _d in [
     ("xs", 4096, BF), ("vs", 8208, BF), ("ctab", 4112, F32), ("lan", 256, I32), ("s0w", 256, I32), ("wti", 8, I32),
     ("srow", 256, BF), ("ci", 16, I32), ("cf", 32, F32), ("t0", 256, F32), ("t1", 256, F32), ("t2", 256, F32),
     ("t3", 256, F32), ("ti", 128, I32), ("tj", 32, I32), ("idb", 128, BF), ("idh", 128, F16), ("nid", 128, BF),
-    ("i19", 128, BF), ("tn", 120, BF), ("blk", 128, BF), ("sel", 144, BF), ("selw", 144, BF), ("selk", 144, F16),
-    ("selb", 144, BF), ("wm", 128, F16), ("iw", 32, BF), ("poff", 128, U16), ("pa", 2048, F16), ("ta", 128, BF),
+    ("idf", 128, F32), ("c31", 128, BF), ("n31", 128, BF), ("one", 480, BF), ("b8", 8, BF), ("b8k", 8, F16), ("b8w", 8, BF),
+    ("i19", 128, BF), ("blk", 128, BF), ("selw", 144, BF), ("selb", 144, BF), ("wm", 128, F16), ("wme", 128, F16),
+    ("nwm", 128, F16), ("iw", 32, BF), ("poff", 128, U16), ("pa", 2048, F16), ("pl", 2048, F16), ("ta", 128, BF),
     ("tb", 128, BF), ("tc", 128, BF), ("mtab", 128, F32), ("rst", 120, F32), ("ltl", 16, U16), ("revl", 16, U16),
     ("rev", 16, U16), ("ends", 8, U16), ("val", 8, F32), ("lst", 16, F32), ("tri", 272, BF), ("hrow", 272, F16),
-    ("win", 16, BF), ("fsel", 256, BF), ("thr", 8, BF), ("hl", 64, BF), ("aq", 16, BF), ("ay", 8, F32), ("aj", 16, F32),
+    ("win", 16, BF), ("fsel", 256, BF), ("thr", 8, BF), ("hl", 64, BF), ("hc", 64, F16), ("aq", 16, BF), ("ay", 8, F32),
+    ("aj", 16, F32), ("c43", 128, BF), ("n43", 128, BF), ("sel", 144, BF), ("selk", 144, F16),
 ]:
     _sb(_n, _w, _d)
 for _h in range(NCH):
@@ -37,8 +53,8 @@ for _h in range(NCH):
     for _n, _w, _d in [
         ("ld", 16 * _c, I32), ("lu", 16 * _c, U16), ("lh", 16 * _c, F16), ("a", 256 * _c, BF), ("at", 256 * _c, F16),
         ("q", 240 * _c, BF), ("f", 240 * _c, BF), ("d", 240 * _c, F16), ("ab", 240 * _c, F16), ("cl", 240 * _c, BF),
-        ("lall", 1040 + 128 * _c, F32), ("w4", 256, F16), ("w1", 256, F32), ("w2", 256, I32), ("w3", 384, BF),
-        ("hu", 128, U16), ("sc", 240, I32), ("k", 48, I32), ("m", 64, F32), ("ou", 32, U16), ("eq", TOT[_h], BF),
+        ("lall", 1040 + 128 * _c, F32), ("w4", 256, F16), ("w1", 128, F32), ("w2", 256, I32), ("w3", 512, BF),
+        ("hu", 128, U16), ("sc", 240, I32), ("k", 48, I32), ("m", 64, F32), ("ou", 48, U16), ("eq", TOT[_h], BF),
         ("es", TOT[_h], BF), ("msk", TOT[_h], BF), ("snd", 144 * STEPS, I32), ("rcv", 144 * (STEPS + 1), I32),
         ("fo", 384, F32),
     ]:
@@ -47,14 +63,14 @@ for _h in range(NCH):
         _sb(_n, _o + _w + (-_w) % 32, _d)
 for _n in ("pt0", "pt1"):
     SCRATCH[_n] = ("psum", [128, 1024], BF)
-for _n in ("px0", "px1", "px2", "pu", "pc", "pk"):
+for _n in ("px0", "px1", "px2", "pu", "pn", "pf"):
     SCRATCH[_n] = ("psum", [128, 512], F32)
 
 SEMAPHORES = ["sv", "sa", "sp", "sg", "gone"] + ["dm%d" % i for i in range(24)] + \
-    ["arr%d" % i for i in range(NCH * STEPS)]
+    ["arr%d" % i for i in range(2 * NCH * STEPS)]
 
-CYC, PCYC = 1.04, 0.6
-LAT_X, LAT_S, LAT_R = 130.0, 90.0, 3600.0
+CYC, PCYC = 1.04, 0.56
+LAT_X, LAT_S, LAT_R = 130.0, 90.0, 3000.0
 SIZE = {F32: 4, I32: 4, BF: 2, F16: 2, U16: 2}
 
 
@@ -91,7 +107,7 @@ def narrow(*xs):
 def plan():
     ops = []
     acc = {}
-    tag = [-9, 0, 0]
+    tag = [-9, 0, "c"]
 
     def add(eng, cost, call, reads, writes, kind="c", after=()):
         i = len(ops)
@@ -122,7 +138,6 @@ def plan():
                     old.append((i, lo, hi, w))
         for j in after:
             deps[j] = True
-        tag[2] += 1
         ops.append(dict(eng=eng, cost=cost, call=call, deps=deps, kind=kind, tag=tuple(tag)))
         return i
 
@@ -159,8 +174,25 @@ def plan():
         c = (78 + 1.56 * n) if in_[0] == "I" else max(64, n)
         return add("S", c * CYC, ("act", out, in_, f, bias, scale, accum), [in_] + aps(bias, scale), [out] + aps(accum))
 
+    def lin(eng, out, in_, scale, bias):
+        if eng == "S":
+            return act(out, in_, scale=scale, bias=bias)
+        return ts(out, in_, scale, ALU.mult, bias, ALU.add)
+
+    def flex(name, out, in_, scale=1.0, bias=0.0):
+        eng = OPT["eng"].get(name + str(tag[1]), ENG[name])
+        if eng == "V" and scale == 1.0 and bias == 0.0:
+            return cp(out, in_)
+        return lin(eng, out, in_, scale, bias)
+
+    def bits(name, out, tmp, in_, *a):
+        if OPT["u16"]:
+            return ts(out, in_, *a)
+        ts(tmp, in_, *a)
+        return flex(name, out, tmp)
+
     def mm(lst):
-        c = sum(max(64, count(m[0])) for m in lst)
+        c = sum(max(64, count(m[0])) * (4 if SCRATCH[m[1][1]][2] == F32 else 1) for m in lst)
         return add("P", c * PCYC, ("mm", lst), [a for m in lst for a in m[1:3]], [m[0] for m in lst])
 
     def group(out, pairs):
@@ -186,8 +218,8 @@ def plan():
     ms(A("s0w"), 0)
     dma("Y", A("wti", 0, 1), H("wt", al, al), 512)
     dma("Y", A("s0w", part=slice(0, 128, 16)), H("s0", al, al), 8192)
-    dma("Y", A("vs", 0, 2048), H("v", al, slice(2048, 4096)), 1400000)
-    dma("Y", A("vs", 2048, 4096), H("v", al, slice(0, 2048)), 1400000)
+    dma("Y", A("vs", 0, ROT), H("v", al, slice(4096 - ROT, 4096)), 1400000)
+    dma("Y", A("vs", ROT, 4096), H("v", al, slice(0, 4096 - ROT)), 1400000)
 
     iota(col("ci", 0), [[0, 1]], 0, 1)
     for h in range(NCH):
@@ -220,20 +252,34 @@ def plan():
     ts(A("t2", 0, 128), A("t2", 0, 128), J_, ALU.add)
     ts(A("t1", 128, 256), A("t1", 128, 256), G_, ALU.is_equal)
     tt(A("wm"), A("t2", 0, 128), A("t1", 128, 256), ALU.mult)
-    ts(col("cf", 7), G_, 16.0, ALU.mult, 15.0, ALU.add)
+    ts(A("t2", 128, 256), A("t1", 128, 256), 2.0 ** -10, ALU.mult)
+    tt(A("wme"), A("t2", 128, 256), A("wm"), ALU.max)
+    act(A("nwm"), A("wm"), scale=-1.0)
+    act(A("c31"), A("idb"), scale=2.0 ** 31)
+    act(A("n31"), A("idb"), scale=-2.0 ** 31)
+    ms(A("one"), 1.0)
     cp(col("cf", 8), col("wti", 0))
+    ts(col("cf", 7), G_, 16.0, ALU.mult, 15.0, ALU.add)
     ts(A("selb"), A("t0", 0, 144), col("cf", 7), ALU.is_equal)
-    ts(A("selw"), A("t0", 0, 144), col("cf", 7), ALU.is_equal, col("cf", 8), ALU.mult)
-    act(A("sel"), A("selb"), scale=float(2 ** 19))
-    act(A("selk"), A("selb"), scale=1024.0)
+    ts(A("b8"), A("t0", 0, 8), G_, ALU.is_equal)
+    ts(A("b8k"), A("t0", 0, 8), G_, ALU.is_equal, 1024.0, ALU.mult)
+    if OPT["ub"]:
+        ts(A("b8w"), A("t0", 0, 8), G_, ALU.is_equal, col("cf", 8), ALU.mult)
+    else:
+        ts(A("selw"), A("t0", 0, 144), col("cf", 7), ALU.is_equal, col("cf", 8), ALU.mult)
     act(A("nid"), A("idb"), scale=-1.0)
+    if OPT["near"] == "D":
+        act(A("c43"), A("idb"), scale=1.5 * 2.0 ** 43)
+        act(A("n43"), A("idb"), scale=-1.5 * 2.0 ** 43)
+        act(A("sel"), A("selb"), scale=2.0 ** 16)
+    if OPT["far"] == "D":
+        act(A("selk"), A("selb"), scale=1024.0)
     act(A("idh"), A("idb"))
+    act(A("idf"), A("idb"))
     act(A("i19"), A("idb"), scale=float(2 ** 19))
-    for i in range(2):
-        ms(A("tn", 60 * i, 60 * i + 60), -11.0 * 2 ** 20)
     ts(col("cf", 16), J_, 8.0, ALU.is_ge, 65280.0, ALU.mult)
-    ts(A("tc", 0, 64), A("t0", 0, 64), 0.0, ALU.mult, col("cf", 16), ALU.add)
-    ts(A("tc", 64, 128), A("tc", 0, 64), 256.0, ALU.add)
+    ts(col("cf", 16), col("cf", 16), 256.0, ALU.add)
+    ts(A("tc"), A("t0", 0, 128), 0.0, ALU.mult, col("cf", 16), ALU.add)
     act(A("ta", 0, 120), A("t0", 0, 120), scale=4096.0, bias=2048.0)
     act(A("tb", 0, 120), A("mtab", 0, 120), scale=64.0, bias=12288.0)
     ts(A("blk"), A("t3", 0, 128), G_, ALU.is_equal)
@@ -245,17 +291,23 @@ def plan():
     cp(A("ti", 0, 8), A("t3", 144, 152))
     for c in set(CH):
         ts(A("ltl", 2 * c - 8, 3 * c - 8), A("ti", 0, c), c - 1.0, ALU.min)
+    if OPT["ub"]:
+        ts(col("cf", 26), P_, 0.5, ALU.add, 1.0 / 15.0, ALU.mult)
+        ts(col("ci", 8), col("cf", 26), -0.5, ALU.add)
+        ts(col("cf", 27), col("ci", 8), -15.0, ALU.mult, P_, ALU.add)
+        ts(col("cf", 28), col("cf", 27), 64.0, ALU.mult, 12352.0, ALU.add)
     ts(A("t2", 0, 128), A("t2", 0, 128), -16.0, ALU.add)
     tt(A("t2", 128, 256), A("t2", 0, 128), A("t1", 128, 256), ALU.mult)
     ts(A("poff"), A("t2", 128, 256), 16.0, ALU.add)
     ts(A("iw"), A("t0", 0, 32), J_, ALU.is_equal)
     for i in range(4):
         act(A("pa", 512 * i, 512 * i + 512), IX("iw", 0, 32, "poff", 32 * i, 32 * i + 32))
-    ts(col("cf", 9), J_, 32.0 / SC, ALU.mult, 4128.0 / SC, ALU.add)
-    ts(A("val"), A("t3", 128, 136), 32.0 / SC, ALU.mult, col("cf", 9), ALU.add)
-    ts(col("cf", 10), J14, -2.0, ALU.mult)
+        ts(A("pl", 512 * i, 512 * i + 512), A("pa", 512 * i, 512 * i + 512), 1.0 / 4096, ALU.mult)
+    ts(col("cf", 9), J_, 8.0, ALU.mult, 1032.0, ALU.add)
+    ts(A("val"), A("t3", 128, 136), 8.0, ALU.mult, col("cf", 9), ALU.add)
+    ts(col("cf", 10), J14, -0.5, ALU.mult)
     for c in set(CH):
-        ts(A("lst", 2 * c - 8, 3 * c - 8), A("t3", 128, 128 + c), 30.0 * c - 2, ALU.mult, col("cf", 10), ALU.add)
+        ts(A("lst", 2 * c - 8, 3 * c - 8), A("t3", 128, 128 + c), 7.5 * c - 0.5, ALU.mult, col("cf", 10), ALU.add)
     ts(A("tri", 0, 16), A("t0", 0, 16), J_, ALU.is_gt)
     ms(A("tri", 16, 272), 1.0)
     ts(A("hrow", 256, 272), A("t0", 0, 16), 0.0, ALU.mult, 2048.0, ALU.add)
@@ -273,9 +325,9 @@ def plan():
         if c == 4:
             ms(A("m" + s, 8, 16), 0.0)
     cp(A("srow"), IX("s0w", 0, 256, "rev", 0, 16))
-    mm(group(A("pc", 0, 16), [(A("selb", 15 - j, 143 - j), A("srow", j, 256, 16)) for j in range(16)]))
+    mm(group(A("pn", 0, 16), [(A("selb", 15 - j, 143 - j), A("srow", j, 256, 16)) for j in range(16)]))
     for h in range(NCH):
-        cp(A("rcv%d" % h, 0, CH[h]), A("pc", Q0[h], Q0[h] + CH[h]))
+        cp(A("rcv%d" % h, 0, CH[h]), A("pn", Q0[h], Q0[h] + CH[h]))
 
     rot = [0, 0]
 
@@ -283,158 +335,228 @@ def plan():
         rot[0] += 1
         return "px%d" % (rot[0] % 3)
 
-    def selj(name, j):
-        return A(name, 15 - j, 143 - j)
-
-    def close_step(last):
+    def close_step(t):
+        tag[:] = [t, 9, "close"]
         for h in range(NCH):
             cp(IX("vs", 0, 8208, "ou%d" % h, 16, 16 + CH[h]), A("fsel", 16 * Q0[h], 16 * (Q0[h] + CH[h])))
-        if not last:
-            mm(group(A("pk", 256, 272), [(A("blk"), A("win"))]))
-            act(A("aj"), A("pk", 256, 272), scale=-1.0, bias=48.40625, accum=col("ay", 0))
+        if t < STEPS - 1:
+            mm(group(A("pn", 256, 272), [(A("blk"), A("win"))]))
+            act(A("aj"), A("pn", 256, 272), scale=-1.0, bias=48.40625, accum=col("ay", 0))
             act(col("aq", 0), col("ay", 0), bias=-4.0)
             act(col("thr", 0), col("aq", 0), scale=-1.0, bias=col("ay", 0))
 
-    def half(t, h):
+    def prints(t, h):
         s = str(h)
         r0 = 144 * t
         c = CH[h]
-        B, n2, nm, npc = 16 * Q0[h], 8 * c, 15 * c, c // 4
-        w1, w2, w3, w4 = "w1" + s, "w2" + s, "w3" + s, "w4" + s
-        tag[:] = [t, h, 0]
+        n2, nm, npc = 8 * c, 15 * c, c // 4
+        w2, w3, w4 = "w2" + s, "w3" + s, "w4" + s
+        rows = slice(0, nm)
+        tag[:] = [t, h, "list"]
         if t == 0:
             cp(A("ld" + s), IX("lan", 0, 256, "revl", Q0[h], Q0[h] + c))
+            cp(A("lu" + s), A("ld" + s))
         else:
-            ts(A("ld" + s, 0, n2), A("rcv" + s, r0 + c, r0 + 17 * c, 2), 4095, ALU.bitwise_and)
-            ts(A("ld" + s, n2, 2 * n2), A("rcv" + s, r0 + c + 1, r0 + 17 * c, 2), 12, ALU.arith_shift_right)
-        tag[:] = [t, h, 10]
-        cp(A("lu" + s), A("ld" + s))
-        ts(A("lh" + s, 0, n2), A("lu" + s, 0, n2), -2048.0, ALU.add, 1.0 / 4096, ALU.mult)
-        ts(A("lh" + s, n2, 2 * n2), A("lu" + s, n2, 2 * n2), -2048.0, ALU.add)
-        tt(A(w3, 0, 16 * c), IX("rcv" + s, r0, r0 + c, "ltl", 2 * c - 8, 3 * c - 8), A("mtab", 0, 16 * c), ALU.is_gt)
+            bits("lu0", A("lu" + s, 0, n2), A("ld" + s, 0, n2), A("rcv" + s, r0 + c, r0 + 17 * c, 2), 4095, ALU.bitwise_and)
+            bits("lu1", A("lu" + s, n2, 2 * n2), A("ld" + s, n2, 2 * n2), A("rcv" + s, r0 + c + 1, r0 + 17 * c, 2), 12,
+                 ALU.arith_shift_right)
         for pc in range(npc):
+            tag[:] = [t, h, "f%d" % pc]
             rot[1] += 1
             pt = "pt%d" % (rot[1] % 2)
             for b in range(2):
                 c0 = n2 * b + 32 * pc
                 o = 1024 * pc + 512 * b
-                (cp if (t, h, pc, b) in GAV else act)(A("a" + s, o, o + 512), IX("xs", 0, 4096, "lu" + s, c0, c0 + 32))
-                lst = [("T", A(pt, 512 * b + 128 * i, 512 * b + 128 * i + 128), A("a" + s, o + 128 * i, o + 128 * i + 128))
+                (cp if (t, h, pc, b) in OPT["gav"] else act)(A("a" + s, o, o + 512), IX("xs", 0, 4096, "lu" + s, c0, c0 + 32))
+                lst = [("T", A(pt, 256 * i + 128 * b, 256 * i + 128 * b + 128), A("a" + s, o + 128 * i, o + 128 * i + 128))
                        for i in range(4)]
                 add("P", 512 * PCYC, ("tr", lst), [m[2] for m in lst] + [A("idb")], [m[1] for m in lst])
-            ts(A("at" + s, 1024 * pc, 1024 * pc + 1024), A(pt), 288.0, ALU.add)
+            pi0 = (16 - Q0[h] - c) // 2 + 2 * pc
+            lift = [272.0 if OPT["mode"][pi0 + u] == "P" else 288.0 for u in range(2)]
+            if lift[0] == lift[1]:
+                ts(A("at" + s, 1024 * pc, 1024 * pc + 1024), A(pt), lift[0], ALU.add)
+            else:
+                for u in range(2):
+                    ts(A("at" + s, 1024 * pc + 512 * u, 1024 * pc + 512 * u + 512), A(pt, 512 * u, 512 * u + 512), lift[u], ALU.add)
             for u in range(2):
                 o = 480 * (2 * pc + u)
-                pi = ((16 - Q0[h] - c) // 2 + 2 * pc + u) % len(FACT)
-
-                def blocks(bank, first):
-                    r = []
-                    for ql in range(2):
-                        for b in range(2):
-                            a0 = 1024 * pc + 512 * b + 128 * (2 * u + ql)
-                            r.append((A(bank, 240 * ql + b, 240 * ql + 240, 2), A("at" + s, a0, a0 + 128), A("wm", 8, 128),
-                                      first, first or (ql == 1 and b == 1)))
-                    return r
                 bk = xbank()
-                mm(blocks(bk, True))
-                act(A("q" + s, o, o + 480), A(bk, 0, 480), bias=-127.5)
-                if FACT[pi]:
-                    mm([(A(bk, 0, 480), A("nid"), A("q" + s, o, o + 480), True, False)] + blocks(bk, False))
-                    act(A("f" + s, o, o + 480), A(bk, 0, 480))
+
+                def blocks(w, first, last):
+                    return [(A(bk, 240 * (i // 2) + i % 2, 240 * (i // 2) + 240, 2),
+                             A("at" + s, 1024 * pc + 512 * u + 128 * i, 1024 * pc + 512 * u + 128 * i + 128), A(w, 8, 128),
+                             first, first or (last and i == 3)) for i in range(4)]
+                if OPT["mode"][pi0 + u] == "P":
+                    mm([(A(bk, 0, 480), A("c31"), A("one"), True, False)] + blocks("wme", False, False) +
+                       [(A(bk, 0, 480), A("n31"), A("one"), False, False)] + blocks("nwm", False, True))
+                    lin(OPT["fev"][pi0 + u], A("f" + s, o, o + 480), A(bk, 0, 480), -1.0, 128.0)
                 else:
+                    mm(blocks("wm", True, True))
+                    act(A("q" + s, o, o + 480), A(bk, 0, 480), bias=-127.5)
                     tt(A("f" + s, o, o + 480), A(bk, 0, 480), A("q" + s, o, o + 480), ALU.subtract)
-            a, b = 60 * pc, 60 * pc + 60
-            mm(group(A("pu", a, b), [(A("blk"), A("tc", 64, 124))] +
-                     [(selj("selw", j), A("f" + s, 960 * pc + j, 960 * pc + 960, 16)) for j in range(16)]))
-            act(A(w3, 128 + a, 128 + b), A("pu", a, b), bias=0.5)
-            tt(A(w4, a, b), A("pu", a, b), A(w3, 128 + a, 128 + b), ALU.subtract)
-            act(A("pu", 256 + a, 256 + b), A(w4, a, b), bias=5280.0)
-            tt(A(w2, a, b), A("pu", 256 + a, 256 + b), A(w4, a, b), ALU.mult)
-            ts(A(w2, 128 + a, 128 + b), A(w2, a, b), 5, ALU.arith_shift_right, 4095, ALU.bitwise_and)
-            cp(A("hu" + s, a, b), A(w2, 128 + a, 128 + b))
-        ts(A(w4, 128, 128 + nm), A("hu" + s, 0, nm), -2048.0, ALU.add)
-        act(A(w3, 256, 256 + nm), A(w4, 0, nm), bias=12288.0 - 31.5)
-        pre = [(A("idb"), A("ta", 0, nm)), (A("idh"), A(w4, 128, 128 + nm)), (A("i19"), A(w3, 0, nm))]
-        mm(group(A("pk", 0, nm), pre))
-        act(A(w1, 0, nm), A("pk", 0, nm))
-        mm([m[:4] + (False,) for m in group(A("pc", 0, nm), [(A("idb"), A("tn", 0, nm))] + pre)])
+            if not OPT["ub"]:
+                tag[:] = [t, h, "u%d" % pc]
+                a, b = 60 * pc, 60 * pc + 60
+                mm(group(A("pu", a, b), [(A("blk"), A("tc", 0, 60))] +
+                         [(A("selw", 15 - j, 143 - j), A("f" + s, 960 * pc + j, 960 * pc + 960, 16)) for j in range(16)]))
+                flex("uq", A(w3, 128 + a, 128 + b), A("pu", a, b), bias=0.5)
+                tt(A(w4, a, b), A("pu", a, b), A(w3, 128 + a, 128 + b), ALU.subtract)
+                act(A(w2, a, b), A(w4, a, b), AF.Square, bias=2640.0)
+                bits("hu", A("hu" + s, a, b), A(w2, 128 + a, 128 + b), A(w2, a, b), 5, ALU.arith_shift_right, 4095, ALU.bitwise_and)
+        if OPT["ub"]:
+            tag[:] = [t, h, "u0"]
+            mm([(A("pu", 0, 128, part=rows), A("blk", 0, nm), A("tc"), True, False)] +
+               [(A("pu", j, 128, 16, rows), A("f" + s, j, 240 * c, 16), A("b8w"), False, j == 15) for j in range(16)])
+            act(A(w3, 128, 256, part=rows), A("pu", 0, 128, part=rows), bias=0.5)
+            tt(A(w4, 0, 128, part=rows), A("pu", 0, 128, part=rows), A(w3, 128, 256, part=rows), ALU.subtract)
+            mm(group(A("pu", 128, 128 + nm), [(A(w4, 0, 128, part=rows), A("idh", 0, nm, part=rows))]))
+            act(A(w2, 0, nm), A("pu", 128, 128 + nm), AF.Square, bias=2640.0)
+            bits("hu", A("hu" + s, 0, nm), A(w2, 128, 128 + nm), A(w2, 0, nm), 5, ALU.arith_shift_right, 4095, ALU.bitwise_and)
+        tag[:] = [t, h, "key"]
+        tt(A(w3, 0, 16 * c), IX("rcv" + s, r0, r0 + c, "ltl", 2 * c - 8, 3 * c - 8), A("mtab", 0, 16 * c), ALU.is_gt)
+        flex("h16", A(w4, 128, 128 + nm), A("hu" + s, 0, nm), bias=-2048.0)
+        if OPT["ub"]:
+            flex("w3", A(w3, 256, 384, part=rows), A(w4, 0, 128, part=rows), bias=12288.0 - 31.5)
+        else:
+            flex("w3", A(w3, 256, 256 + nm), A(w4, 0, nm), bias=12288.0 - 31.5)
+        tag[:] = [t, h, "flip"]
+        flex("lh", A("lh" + s), A("lu" + s), bias=-2048.0)
         for bi in range(npc):
             bk = xbank()
             lst = []
             for i in range(512 // n2):
                 m = (8 * bi + i + 1) % 16
-                lst += group(A(bk, n2 * i, n2 * i + n2), [(A("pa", 128 * m, 128 * m + 128), A("lh" + s, 0, n2)),
+                lst += group(A(bk, n2 * i, n2 * i + n2), [(A("pl", 128 * m, 128 * m + 128), A("lh" + s, 0, n2)),
                                                           (A("pa", 128 * m, 128 * m + 128), A("lh" + s, n2, 2 * n2))])
             mm(lst)
             n = 512 - n2 * (bi == npc - 1)
-            act(A("lall" + s, 512 * bi, 512 * bi + n), A(bk, 0, n), scale=4096.0, bias=2048.0 * 4097)
+            flex("lall%d" % (bi % 2), A("lall" + s, 512 * bi, 512 * bi + n), A(bk, 0, n), 4096.0, 2048.0 * 4097)
             if bi == npc - 1:
                 for e in range(2):
-                    act(A("lall" + s, 1032 + 8 * e, 1032 + 128 * c, 16), A(bk, n, 512), scale=4096.0, bias=2048.0 * 4097)
-        if t and h == 0:
-            tag[:] = [t, 9, 0]
-            close_step(False)
-        tag[:] = [t, h, 500]
-        for pc in range(npc):
-            for u in range(2):
-                pi = 2 * pc + u
-                o = 480 * pi
-                tt(A("d" + s, o, o + 480), IX("vs", 0, 4096, "hu" + s, 30 * pi, 30 * pi + 30), A("f" + s, o, o + 480), ALU.subtract)
-                act(A("ab" + s, o, o + 480), A("d" + s, o, o + 480), AF.Abs)
-                ts(A("cl" + s, o, o + 480), A("ab" + s, o, o + 480), col("thr", 0), ALU.is_le, 2.0, ALU.mult)
-            c0, c1 = 60 * pc, 60 * pc + 60
-            mm([(A("pc", c0, c1), selj("sel", j), A("cl" + s, 960 * pc + j, 960 * pc + 960, 16), False,
-                 pc == npc - 1 and j == 15) for j in range(16)])
-            mm(group(A("pk", 120 + c0, 120 + c1),
-                     [(A("idb"), A("tb", c0, c1)), (A("idh"), A(w4, c0, c1)), (A("nid"), A(w3, 256 + c0, 256 + c1))] +
-                     [(selj("selk", j), A("ab" + s, 960 * pc + j, 960 * pc + 960, 16)) for j in range(16)]))
-        tt(A(w1, 128, 128 + nm), A("pc", 0, nm), A(w1, 0, nm), ALU.max)
-        scan(A("sc" + s, 0, nm), A("rst", 0, nm), A(w1, 128, 128 + nm), ALU.add, ALU.min)
-        scan(A("sc" + s, nm, 2 * nm), A("rst", 0, nm), A("pk", 120, 120 + nm), ALU.add, ALU.min)
+                    flex("same", A("lall" + s, 1032 + 8 * e, 1032 + 128 * c, 16), A(bk, n, 512), 4096.0, 2048.0 * 4097)
+
+    def decide(t, h):
+        s = str(h)
+        r0 = 144 * t
+        c = CH[h]
+        B, nm = 16 * Q0[h], 15 * c
+        w1, w3, w4 = "w1" + s, "w3" + s, "w4" + s
+        rows = slice(0, nm)
+        for pi in range(c // 2):
+            tag[:] = [t, h, "d%d" % pi]
+            o = 480 * pi
+            tt(A("d" + s, o, o + 480), IX("vs", 0, 4096, "hu" + s, 30 * pi, 30 * pi + 30), A("f" + s, o, o + 480), ALU.subtract)
+            act(A("ab" + s, o, o + 480), A("d" + s, o, o + 480), AF.Abs)
+            if OPT["near"] == "D":
+                ts(A("cl" + s, o, o + 480), A("ab" + s, o, o + 480), col("thr", 0), ALU.is_le, -3.5 / 16, ALU.add)
+            else:
+                ts(A("cl" + s, o, o + 480), A("ab" + s, o, o + 480), col("thr", 0), ALU.is_le)
+            if pi % 2:
+                c0, c1, o = 30 * pi - 30, 30 * pi + 30, o - 480
+                if OPT["near"] == "D":
+                    tag[:] = [t, h, "n%d" % pi]
+                    mm([(A("pn", 0, nm), A("c43"), A("one", 0, nm), True, False)] * (pi == 1) +
+                       [(A("pn", c0, c1), A("sel", 15 - j, 143 - j), A("cl" + s, o + j, o + 960, 16), False, False) for j in range(16)])
+                if OPT["far"] == "D":
+                    tag[:] = [t, h, "r%d" % pi]
+                    mm(group(A("pf", c0, c1), [(A("idb"), A("tb", c0, c1)), (A("idh"), A(w4, c0, c1)), (A("nid"), A(w3, 256 + c0, 256 + c1))] +
+                             [(A("selk", 15 - j, 143 - j), A("ab" + s, o + j, o + 960, 16)) for j in range(16)]))
+        tag[:] = [t, h, "near"]
+        pre = [(A("idb"), A("ta", 0, nm)), (A("idh"), A(w4, 128, 128 + nm)), (A("i19"), A(w3, 0, nm))]
+        if OPT["near"] == "D":
+            mm([(A("pn", 0, nm), l, r, False, k == 3) for k, (l, r) in enumerate([(A("n43"), A("one", 0, nm))] + pre)])
+            key = A("pn", 0, nm)
+        else:
+            mm([(A("pn", j, 128, 16, rows), A("cl" + s, j, 240 * c, 16), A("b8"), True, True) for j in range(16)])
+            seen = A(w3, 384, 512, part=rows)
+            if OPT["seen"] == "V":
+                ts(seen, A("pn", 0, 128, part=rows), 11.5, ALU.is_ge, 2.0 ** 20, ALU.mult)
+            else:
+                act(seen, A("pn", 0, 128, part=rows), AF.Relu, scale=2.0 ** 20, bias=-11.0 * 2 ** 20)
+            key = A("pn", 128, 128 + nm)
+            mm(group(key, pre + [(seen, A("idb", 0, nm, part=rows))]))
+        scan(A("sc" + s, 0, nm), A("rst", 0, nm), key, ALU.add, ALU.min)
+        tag[:] = [t, h, "far"]
+        far = A(w1, 0, 128, part=rows)
+        turn = [(far, A("idf", 0, nm, part=rows))]
+        key = A("pf", 128, 128 + nm)
+        if OPT["far"] == "D":
+            key = A("pf", 0, nm)
+        elif OPT["ub"]:
+            pay = [(A("idh", 0, nm, part=rows), A(w4, 0, 128, part=rows)), (A("nid", 0, nm, part=rows), A(w3, 256, 384, part=rows))]
+            mm([(A("pf", 0, 128, part=rows), l, r, k == 0, False) for k, (l, r) in enumerate(pay)] +
+               [(A("pf", j, 128, 16, rows), A("ab" + s, j, 240 * c, 16), A("b8k"), False, j == 15) for j in range(16)])
+            act(far, A("pf", 0, 128, part=rows), bias=A("cf", 28, 29, part=rows))
+        else:
+            mm([(A("pf", j, 128, 16, rows), A("ab" + s, j, 240 * c, 16), A("b8k"), True, True) for j in range(16)])
+            flex("far", far, A("pf", 0, 128, part=rows))
+            turn = [(A("idb"), A("tb", 0, nm)), (A("idh"), A(w4, 0, nm)), (A("nid"), A(w3, 256, 256 + nm))] + turn
+        if OPT["far"] != "D":
+            mm(group(key, turn))
+        scan(A("sc" + s, nm, 2 * nm), A("rst", 0, nm), key, ALU.add, ALU.min)
         k, m_, ou = "k" + s, "m" + s, "ou" + s
         k1, k2 = A("sc" + s, 14, nm, 15), A("sc" + s, nm + 14, 2 * nm, 15)
+        ts(A(k, 32, 32 + c), k2, 15, ALU.bitwise_and)
+        tt(A(m_, 24, 24 + c), A("rcv" + s, r0, r0 + c), A(k, 32, 32 + c), ALU.subtract)
+        tag[:] = [t, h, "pick"]
         ts(A(k, 16, 16 + c), k1, 0x700FFF, ALU.bitwise_and)
         ts(A(ou, 0, c), A(k, 16, 16 + c), 4096.0, ALU.min)
-        ts(A(m_, 16, 16 + c), A(k, 16, 16 + c), 4096.0, ALU.min, -2048.0, ALU.add)
-        act(A(m_, 0, c), A(m_, 16, 16 + c), scale=1.0 / SC, bias=2048.0 / SC)
-        hi, lo = 16 * h, 16 * h + 8
-        ts(A("hl", hi, hi + c), A(k, 16, 16 + c), 4096.0, ALU.min, -2048.0, ALU.add)
-        tt(A("hl", lo, lo + c), A(m_, 16, 16 + c), A("hl", hi, hi + c), ALU.subtract)
-        act(A("hrow", B, B + 16 * c), IX("ctab", 0, 4112, ou, 0, c))
-        ts(A(k, 24, 24 + c), k1, 4 if c == 8 else 5, ALU.arith_shift_right, 127 * 32 * c, ALU.bitwise_and)
-        ts(A(k, 32, 32 + c), k2, 15, ALU.bitwise_and)
-        ts(A(ou, 8, 8 + c), A(k, 24, 24 + c), 0.5 / c, ALU.mult, J_, ALU.add)
-        tt(A(m_, 56, 56 + c), A(k, 24, 24 + c), A("lst", 2 * c - 8, 3 * c - 8), ALU.subtract)
-        act(A(m_, c, 2 * c), A(m_, 56, 56 + c), scale=1.0 / SC)
-        tt(A(m_, 24, 24 + c), A("rcv" + s, r0, r0 + c), A(k, 32, 32 + c), ALU.subtract)
+        flex("hrow", A("hrow", B, B + 16 * c), IX("ctab", 0, 4112, ou, 0, c))
+        hi = 16 * h
+        ts(A("hc", hi, hi + c), A(k, 16, 16 + c), 4096.0, ALU.min, -2048.0, ALU.add)
+        ts(A(k, 24, 24 + c), k1, 6 if c == 8 else 7, ALU.arith_shift_right, 127 * 8 * c, ALU.bitwise_and)
+        flex("m0", A(m_, 0, c), A("hc", hi, hi + c), 0.25, 512.0)
+        tt(A(m_, c, 2 * c), A(k, 24, 24 + c), A("lst", 2 * c - 8, 3 * c - 8), ALU.subtract)
+        flex("ou8", A(ou, 8, 8 + c), A(k, 24, 24 + c), 2.0 / c, J_)
+        flex("fsel", A("fsel", B, B + 16 * c), IX("f" + s, 0, 240 * c, ou, 8, 8 + c))
+        tag[:] = [t, h, "win"]
         o = 0
         for q in range(c):
             n = SEG[h][q]
-            ts(A("eq" + s, o, o + n), A("hrow", 258 - n, 258), col("hl", hi + q), ALU.subtract, col("hl", lo + q), ALU.is_equal)
+            ts(A("eq" + s, o, o + n), A("hrow", 258 - n, 258), col("hc", hi + q), ALU.is_equal, 4096.0, ALU.mult)
             o += n
         scan(A("es" + s), A("eq" + s), A("msk" + s), ALU.max, ALU.min)
-        tt(A(m_, 32, 48), IX("es" + s, 0, TOT[h], "ends", 2 * h, 2 * h + 1), A(m_, 0, 16), ALU.max)
-        ts(A(ou, 24, 24 + c), A(m_, 32 + c, 32 + 2 * c), 0.25 * SC, ALU.mult)
-        cp(A("snd" + s, r0 + c, r0 + 17 * c), IX("lall" + s, 0, 1040 + 128 * c, ou, 24, 24 + c))
+        ends = IX("es" + s, 0, TOT[h], "ends", 2 * h, 2 * h + 1)
+        tag[:] = [t, h, "send"]
+        if OPT["ttu"]:
+            tt(A(ou, 32, 48), ends, A(m_, 0, 16), ALU.max)
+            new = 32 + c
+        else:
+            tt(A(m_, 32, 48), ends, A(m_, 0, 16), ALU.max)
+            flex("ou24", A(ou, 24, 24 + c), A(m_, 32 + c, 32 + 2 * c))
+            new = 24
+        flex("new", A("snd" + s, r0 + c, r0 + 17 * c), IX("lall" + s, 0, 1040 + 128 * c, ou, new, new + c))
+
+        def send(n, lo, hi):
+            src, dst = A("snd" + s, r0 + lo, r0 + hi), A("rcv" + s, r0 + 144 + lo, r0 + 144 + hi)
+            sent = add("G", 300, ("send", "arr%d" % n, h, src, dst), [src], [], kind="s")
+            add("R", 0, ("arr", "arr%d" % n), [], [dst], kind="r", after=[sent])
+        if OPT["ssep"]:
+            send(NCH * t + h, c, 17 * c)
+            tag[:] = [t, h, "s"]
+        if OPT["ttu"]:
+            tt(A(m_, 32, 48), ends, A(m_, 0, 16), ALU.max)
         wn = A("win", Q0[h], Q0[h] + c)
-        ts(wn, A(m_, 32, 32 + c), 4096.0 / SC, ALU.is_lt)
+        ts(wn, A(m_, 32, 32 + c), 1024.5, ALU.is_lt)
         tt(A(m_, 48, 48 + c), A(m_, 24, 24 + c), wn, ALU.mult)
         tt(A("snd" + s, r0, r0 + c), A(m_, 48, 48 + c), A(k, 32, 32 + c), ALU.add)
-        src, dst = A("snd" + s, r0, r0 + 17 * c), A("rcv" + s, r0 + 144, r0 + 144 + 17 * c)
-        sent = add("G", 300, ("send", t, h, src, dst), [src], [], kind="s")
-        add("R", LAT_R, ("arr", t + 1, h), [], [dst], kind="r", after=[sent])
-        ts(A(ou, 16, 16 + c), A(m_, 32, 32 + c), SC, ALU.mult)
-        act(A("fsel", B, B + 16 * c), IX("f" + s, 0, 240 * c, ou, 8, 8 + c))
+        if OPT["ssep"]:
+            send(NCH * (STEPS + t) + h, 0, c)
+        else:
+            send(NCH * t + h, 0, 17 * c)
+        flex("ou16", A(ou, 16, 16 + c), A(m_, 32, 32 + c), 4.0)
 
     for t in range(STEPS):
         for h in range(NCH):
-            half(t, h)
-    tag[:] = [STEPS, 9, 0]
-    close_step(True)
-    tag[:] = [99, 9, 0]
+            prints(t, h)
+        for h in range(NCH):
+            decide(t, h)
+        close_step(t)
+    tag[:] = [99, 9, "out"]
+    cut = [0, 920, 1840, ROT, 4096]
     for k in range(4):
-        dma("YS"[k % 2], H("yv", al, slice((1024 * k + 2048) % 4096, (1024 * k + 2048) % 4096 + 1024)),
-            A("vs", 1024 * k, 1024 * k + 1024), 500000)
+        o = (cut[k] - ROT) % 4096
+        dma("YS"[k % 2], H("yv", al, slice(o, o + cut[k + 1] - cut[k])), A("vs", cut[k], cut[k + 1]), 500000)
     r0 = 144 * STEPS
     for h in range(NCH):
         s, c = str(h), CH[h]
@@ -450,7 +572,59 @@ def plan():
     return ops
 
 
-ORDER = "010207000604080d0o0l0n0k0m0p0e0a091c0v0q0w120c0f0x1d0y100z1e110g0b0i1t0j1q1r0s1s0u1j1u5t1k242x5u1f031b202y181w323l0525132h5y15343n3335363m373b1m0r26142i0t5z383c600h2g1i2j233o393a1l21272t221n1o2z303p3q613t3d3e2u1p621y2s3r1a3u3f193s3g3v173h1v1g3i3w3x1x3j2w2v313k3y3z484e1h44164f49404142434a45464h4p47664i674q634m4n644l4g4j4r4k6g6i5v4o68654s4u1z4v4t6h4x544y5w6j4z51694w5257555629535e5h5c5a5g6k5b5f5d502d2b282a2c4c2f582e4d4b6a6o6l5i5j596p5m5k6b6c6m5n5l5o6q6d6n6e735x6f792k2n2q6r742m6s6t5s7c5p5q756u766v6w6x6y7k70727a7d71772p6z7h7e7b787l2r7i2l2o7m8p8o8q8u8w7j7g7f7n8s5r7p7q8r7s7z7t7y7o8v8x827w7u7r7x808b8687888a89858c8y9d9f837v9e8z90938d818e848h8f8i8g8j948n9g91929h8k8l9i9l9j9m95a68t96979k8m989n99a0a19a9o9pa79bbrbs9c9qbtaca29r9s9t9u9vafan9xbxbz9wby9yadc0a8a9agaaaoabc1ak9zc5c2ajc6alc3cfchaeahapaibuamc7aqc4asarcgatavcic8bvawb2azaxb1aub5b0b3b4bcbbbfb8bacjb9bdbeaya4a3a5cnc9b6ckd2b7bgbhcacocbclbkbiblbjd3bmcccpcmcdcqcrbwced8csdbbnbod4bqctcud5cvcwcxdjdcd9czd0d6cyd1d7dkdgdddaeoendhepdldidfdedmeteverbpdodpeqdrdydse1dvdxdneuewdtdqdwdze8e7e9e6eae5e4ebexfcdue2fdfeeyezf2fff0ecede3e0egeeehefeifgf3emf1fhfkfiflejekf4g5f5f6fjeself7fmf8f9g6fafzfng0fofbfphqhrfqfvhsfrgbfsfthwhyfugeg1fwhxfxhzg7gcg8gmgfg9i0gjfyi4i1gngagii5gggdgoghgkhtgli2i6i3gpieiggrgsgqifihguh1gvgyhugwh0gxg3g2g4i7gtgzh4h2h3hbheh9h7hdiih8hchah5i8imijhfi9hgh6iniaikhjhhhkhihlibioj1j2ilicipiqhvidj7irjahmhnj3hpisj5j4j6itiujbj8iviwiyizixjij0jjjfjcj9knkmjgkojkjhkskujejdjljmkqhojnjokpjqjxjrk0jujsjpktjwjvkvjylbjtldk1k7k3k6k8k5k9k4kakwlckxkyl1lekzkbjzkck2kfkdkgkekhl2kll0lfkikjlglhljlkl3m4krl4l5kklil6lll7lylzl8lmlnm5l9lalonpnqlpnrlqlrmalsltm0mdmllunvnxlvnwlwmbnym6m7mem8nzmilxo3mmm9o0mhmfmcmgo4mjmnnsmko1o5o2moodmpoemqmrmtn0ntmumxofogmvmsmyn3n1mzn2ohn6nandn8ncn7nbn9mwm2m1m3o6n4o7oloiomn5neo8o9nfojnionoaokobp0p1nuocnjoop2opp6oqp9noorp3osngotouovphpapep7oxoyp4owpbp8p5pipfozpdpcpjpgpknnnhnknlnmpmpnpppqptpwpvplprpzpopupxq4q5q7q6q8q3q2q9psq0pyqaqbq1qeqcqfqdqgqrqlqvqjqsqkqwqxqmqtqhqiqpqqqoqyqzr3r0r4r1qnqur2r5r6"
+def place(order, before, eng, hold, first):
+    busy, st = {}, {}
+    for i in order:
+        t = first[i]
+        for j, d in before[i]:
+            t = max(t, st[j] + d)
+        if eng[i] != "R":
+            b = busy.setdefault(eng[i], [])
+            k = len(b)
+            while k and b[k - 1][1] > t:
+                k -= 1
+            while k < len(b) and b[k][0] < t + hold[i]:
+                t = max(t, b[k][1])
+                k += 1
+            b.insert(k, (t, t + hold[i]))
+        st[i] = t
+    return st
+
+
+def issue_order(ops, shift=None, rounds=3):
+    n = len(ops)
+    eng = [o["eng"] for o in ops]
+    lat = [LAT_R if o["kind"] == "r" else o["cost"] for o in ops]
+    hold = [60 if o["kind"] == "d" else o["cost"] for o in ops]
+    pred, succ = [[] for _ in ops], [[] for _ in ops]
+    for i, o in enumerate(ops):
+        for j, w in o["deps"].items():
+            gap = (LAT_S if eng[j] == eng[i] else LAT_X) if w else 0
+            pred[i].append((j, lat[j] + gap))
+            succ[j].append((i, hold[i] + gap + lat[j] - hold[j]))
+    tail = [0.0] * n
+    for i in range(n - 1, -1, -1):
+        tail[i] = max([tail[j] + d - hold[j] + hold[i] for j, d in succ[i]] or [lat[i]])
+    if shift:
+        tail = [tail[i] + shift(ops[i]) for i in range(n)]
+        for i in range(n - 1, -1, -1):
+            tail[i] = max([tail[i]] + [tail[j] + 1 for j, d in succ[i]])
+    order = sorted(range(n), key=lambda i: (-tail[i], i))
+    best = None
+    for r in range(rounds):
+        st = place(order, pred, eng, hold, [0.0] * n)
+        end = max(st[i] + lat[i] for i in range(n))
+        if best is None or end < best[0]:
+            best = (end, sorted(range(n), key=lambda i: (st[i], i)))
+        late = place(sorted(range(n), key=lambda i: (-st[i] - lat[i], -i)), succ, eng, hold, [lat[i] - hold[i] for i in range(n)])
+        order = sorted(range(n), key=lambda i: (-late[i] - hold[i], i))
+    return best
+
+
+OPT.update({'mode': 'PVPVPVPV', 'fev': 'SVSVSVSS', 'gav': ((0, 0, 0, 1), (0, 1, 0, 1)), 'eng': {'h161': 'V', 'fsel0': 'S', 'ou81': 'S', 'ou161': 'S', 'lh0': 'S', 'w30': 'V', 'hrow0': 'V', 'ou241': 'V', 'ou160': 'V', 'hu0': 'S', 'lu10': 'V', 'lu00': 'S', 'ou240': 'S', 'lh1': 'V'}})
+SHIFT = {(0, 'd0'): 4000, (0, 'd1'): 4250, (0, 'd2'): 3750, (0, 'd3'): 4250, (0, 'f0'): 3000, (0, 'f1'): 3750, (0, 'far'): 250, (0, 'flip'): 5000, (0, 'key'): 5500, (0, 'list'): -7500, (0, 'n1'): -6000, (0, 'n3'): -7250, (0, 'near'): -4000, (0, 'pick'): -5500, (0, 'send'): 6000, (0, 'u0'): 1250, (0, 'u1'): 4250, (0, 'win'): -6000, (1, 'd0'): -5500, (1, 'd1'): -3000, (1, 'd2'): -8000, (1, 'd3'): 1000, (1, 'f0'): 1500, (1, 'f1'): -500, (1, 'far'): 4250, (1, 'flip'): 750, (1, 'key'): -5750, (1, 'list'): -3750, (1, 'n1'): -4000, (1, 'n3'): 3750, (1, 'near'): 2500, (1, 'pick'): 6250, (1, 'send'): -500, (1, 'u0'): 1500, (1, 'u1'): -6000, (1, 'win'): -7500, (9, 'close'): -1000, (1, 's'): -4000, (0, 's'): 250}
+OPT.update({'mode': 'PVPVPVPV', 'fev': 'SSSSSSSS', 'gav': ((0, 0, 0, 1), (0, 1, 0, 0), (0, 1, 0, 1), (1, 0, 0, 1), (2, 0, 0, 1), (3, 0, 0, 1)), 'eng': {'h161': 'V', 'fsel0': 'S', 'ou81': 'V', 'ou161': 'S', 'lh0': 'S', 'w30': 'S', 'hrow0': 'V', 'ou241': 'V', 'ou160': 'S', 'hu0': 'V', 'lu10': 'V', 'lu00': 'S', 'ou240': 'V', 'lh1': 'V', 'new1': 'S', 'new0': 'S', 'far0': 'V'}})
+SHIFT = {(0, 'd0'): 4250, (0, 'd1'): 4500, (0, 'd2'): 3750, (0, 'd3'): 3750, (0, 'f0'): 4500, (0, 'f1'): 4250, (0, 'far'): -2250, (0, 'flip'): 5250, (0, 'key'): 7000, (0, 'list'): -7750, (0, 'n1'): -4000, (0, 'n3'): 3000, (0, 'near'): -1000, (0, 'pick'): -8000, (0, 'send'): 4500, (0, 'u0'): 1500, (0, 'u1'): 4500, (0, 'win'): 1500, (1, 'd0'): -6000, (1, 'd1'): -6000, (1, 'd2'): -6000, (1, 'd3'): -8000, (1, 'f0'): 1250, (1, 'f1'): -1250, (1, 'far'): -7000, (1, 'flip'): 1000, (1, 'key'): -2000, (1, 'list'): -6750, (1, 'n1'): -7750, (1, 'n3'): 2500, (1, 'near'): -3500, (1, 'pick'): 5500, (1, 'send'): 1250, (1, 'u0'): -3000, (1, 'u1'): -3750, (1, 'win'): -7000, (9, 'close'): -1250, (1, 's'): 0, (0, 's'): 3250}
 _PLAN = []
 
 
@@ -459,7 +633,8 @@ def rank_program(g, core, T, topo):
     if rank is None:
         return
     if not _PLAN:
-        _PLAN.append((plan(), [int(ORDER[i:i + 2], 36) for i in range(0, len(ORDER), 2)]))
+        ops = plan()
+        _PLAN.append((ops, issue_order(ops, lambda o: SHIFT.get(o["tag"][1:], 0), 2)[1]))
     ops, seq = _PLAN[0]
     N = len(T.cores)
     nxt, prv = T.cores[(rank + 1) % N], T.cores[(rank - 1) % N]
@@ -492,7 +667,7 @@ def rank_program(g, core, T, topo):
         o = ops[i]
         e, c = o["eng"], o["call"]
         if o["kind"] == "r":
-            mark[i] = ("arr%d" % (NCH * (c[1] - 1) + c[2]), n_in)
+            mark[i] = (c[1], n_in)
             cnt[mark[i][0]] = n_in
             continue
         q = Q[e]
@@ -544,7 +719,7 @@ def rank_program(g, core, T, topo):
             cnt[s_] = 16
             continue
         elif k == "send":
-            q.remote_dma(ap(c[4]), ap(c[3]), T.sem["arr%d" % (NCH * c[1] + c[2])], T.sem["gone"], pid, rid, mask)
+            q.remote_dma(ap(c[4]), ap(c[3]), T.sem[c[1]], T.sem["gone"], pid, rid, mask)
             cnt["gone"] = cnt.get("gone", 0) + n_out
             continue
         if i in needed:

@@ -1,3 +1,5 @@
+import math
+
 from concourse.mybir import AluOpType, ActivationFunctionType
 
 ALU = AluOpType
@@ -7,24 +9,14 @@ STEPS = 4
 ROT = 2760
 OPT = dict(
     mode="PVPVPVPV",
-    fev="SSSSSSSS",
-    gav=(),
-    ub=False,
-    col16=True,
-    seen="V",
-    near="D",
-    far="B",
-    u16=False,
-    ttu=True,
-    ssep=True,
-    eng={},
+    lead=3000.0,
+    tries=200000,
+    temp=250.0,
+    neg=True,
 )
-ENG = dict(lu0="V", lu1="V", hu="V", lh="S", h16="S", new="V", ou8="S", ou16="S", ou24="V", far="S", lall0="S", lall1="S",
-           same="S", w3="S", uq="S", m0="S", fsel="S", hrow="S")
-CH = (8, 8)
-NCH = len(CH)
-Q0 = [16 - sum(CH[:h + 1]) for h in range(NCH)]
-SEG = [[16 * (16 - (Q0[h] + q)) + 2 for q in range(CH[h])] for h in range(NCH)]
+C = 8
+Q0 = (8, 0)
+SEG = [[16 * (16 - (Q0[h] + q)) + 2 for q in range(C)] for h in range(2)]
 TOT = [sum(s) for s in SEG]
 
 SCRATCH = {}
@@ -37,26 +29,24 @@ def _sb(name, n, d):
 
 for _n, _w, _d in [
     ("xs", 4096, BF), ("vs", 8208, BF), ("ctab", 4112, F32), ("lan", 256, I32), ("s0w", 256, I32), ("wti", 8, I32),
-    ("srow", 256, BF), ("ci", 16, I32), ("cf", 32, F32), ("t0", 256, F32), ("t1", 256, F32), ("t2", 256, F32),
-    ("t3", 256, F32), ("ti", 128, I32), ("tj", 32, I32), ("idb", 128, BF), ("idh", 128, F16), ("nid", 128, BF),
-    ("idf", 128, F32), ("c31", 128, BF), ("n31", 128, BF), ("one", 480, BF), ("b8", 8, BF), ("b8k", 8, F16), ("b8w", 8, BF),
-    ("i19", 128, BF), ("blk", 128, BF), ("selw", 144, BF), ("selb", 144, BF), ("wm", 128, F16), ("wme", 128, F16),
-    ("nwm", 128, F16), ("iw", 32, BF), ("poff", 128, U16), ("pa", 2048, F16), ("pl", 2048, F16), ("ta", 128, BF),
-    ("tb", 128, BF), ("tc", 128, BF), ("mtab", 128, F32), ("rst", 120, F32), ("ltl", 16, U16), ("revl", 16, U16),
-    ("rev", 16, U16), ("ends", 8, U16), ("val", 8, F32), ("lst", 16, F32), ("tri", 272, BF), ("hrow", 272, F16),
-    ("win", 16, BF), ("fsel", 256, BF), ("thr", 8, BF), ("hl", 64, BF), ("hc", 64, F16), ("aq", 16, BF), ("ay", 8, F32),
-    ("aj", 16, F32), ("c43", 128, BF), ("n43", 128, BF), ("sel", 144, BF), ("selk", 144, F16),
+    ("srow", 256, BF), ("ci", 16, I32), ("cf", 32, F32), ("t0", 144, F32), ("t1", 256, F32), ("t2", 384, F32),
+    ("t3", 256, F32), ("ti", 8, I32), ("tj", 32, I32), ("tn", 128, BF), ("idb", 128, BF), ("idh", 128, F16),
+    ("nid", 128, BF), ("c31", 128, BF), ("n31", 128, BF), ("c43", 128, BF), ("n43", 128, BF), ("i19", 128, BF),
+    ("one", 480, BF), ("blk", 128, BF), ("sel", 144, BF), ("selk", 144, F16), ("selw", 144, BF), ("selb", 144, BF),
+    ("wm", 128, F16), ("wme", 128, F16), ("nwm", 128, F16), ("wx", 128, F16), ("pcol", 16, BF), ("pa", 2048, F16),
+    ("ta", 128, BF), ("tb", 128, BF), ("tc", 64, BF), ("mtab", 128, F32), ("rst", 120, F32), ("ltl", 8, U16),
+    ("revl", 16, U16), ("rev", 16, U16), ("ends", 8, U16), ("val", 8, F16), ("lst", 8, F32), ("tri", 272, BF),
+    ("hrow", 272, F16), ("win", 16, BF), ("fsel", 256, BF), ("thr", 8, BF), ("hc", 32, F16), ("aq", 16, BF),
+    ("ay", 8, F32), ("aj", 16, F32),
 ]:
     _sb(_n, _w, _d)
-for _h in range(NCH):
-    _c = CH[_h]
+for _h in range(2):
     for _n, _w, _d in [
-        ("ld", 16 * _c, I32), ("lu", 16 * _c, U16), ("lh", 16 * _c, F16), ("a", 256 * _c, BF), ("at", 256 * _c, F16),
-        ("q", 240 * _c, BF), ("f", 240 * _c, BF), ("d", 240 * _c, F16), ("ab", 240 * _c, F16), ("cl", 240 * _c, BF),
-        ("lall", 1040 + 128 * _c, F32), ("w4", 256, F16), ("w1", 128, F32), ("w2", 256, I32), ("w3", 512, BF),
-        ("hu", 128, U16), ("sc", 240, I32), ("k", 48, I32), ("m", 64, F32), ("ou", 48, U16), ("eq", TOT[_h], BF),
-        ("es", TOT[_h], BF), ("msk", TOT[_h], BF), ("snd", 144 * STEPS, I32), ("rcv", 144 * (STEPS + 1), I32),
-        ("fo", 384, F32),
+        ("ld", 256, I32), ("lu", 128 * STEPS, U16), ("su", 128 * STEPS, U16), ("home", 256, F32), ("lh", 128, F16),
+        ("a", 2048, BF), ("at", 2048, F16), ("q", 1920, BF), ("f", 1920, BF), ("d", 1920, F16), ("ab", 1920, F16),
+        ("cl", 1920, BF), ("lall", 2064, F32), ("w4", 256, F16), ("w2", 256, I32), ("w3", 384, BF), ("hu", 128, U16),
+        ("sc", 240, I32), ("k", 48, I32), ("m", 64, F32), ("ou", 64, U16), ("eq", TOT[_h], BF), ("es", TOT[_h], BF),
+        ("msk", TOT[_h], BF), ("snd", 8 * STEPS, I32), ("rcv", 8 * STEPS, I32), ("fo", 256, F32), ("sl", 16, U16),
     ]:
         _o = SCRATCH[_n][1][1] if _h else 0
         PART[_n + str(_h)] = (_n, _o, _w)
@@ -66,8 +56,7 @@ for _n in ("pt0", "pt1"):
 for _n in ("px0", "px1", "px2", "pu", "pn", "pf"):
     SCRATCH[_n] = ("psum", [128, 512], F32)
 
-SEMAPHORES = ["sv", "sa", "sp", "sg", "gone"] + ["dm%d" % i for i in range(24)] + \
-    ["arr%d" % i for i in range(2 * NCH * STEPS)]
+SEMAPHORES = ["sv", "sa", "sp", "sg", "gone"] + ["dm%d" % i for i in range(40)] + ["arr%d" % i for i in range(4 * STEPS)]
 
 CYC, PCYC = 1.04, 0.56
 LAT_X, LAT_S, LAT_R = 130.0, 90.0, 3000.0
@@ -87,7 +76,7 @@ def IX(name, lo, hi, off, c, d):
 def count(a):
     if a[0] == "I":
         return 16 * (a[6] - a[5])
-    return len(range(a[2], a[3], a[4]))
+    return len(range(a[2], a[3], abs(a[4])))
 
 
 def spans(a):
@@ -109,17 +98,18 @@ def plan():
     acc = {}
     tag = [-9, 0, "c"]
 
-    def add(eng, cost, call, reads, writes, kind="c", after=()):
+    def add(eng, cost, call, reads, writes, kind="c", after=(), alt=None):
         i = len(ops)
         deps = {}
+        user = i if alt else eng
         for lst, wr in ((reads, False), (writes, True)):
             for a in lst:
                 for n, (name, lo, hi) in enumerate(spans(a)):
                     w = wr and n == 0
                     if SCRATCH[name][0] == "psum":
-                        st = acc.setdefault(name, [eng, [], []])
-                        if st[0] != eng:
-                            st[:] = [eng, [], st[1]]
+                        st = acc.setdefault(name, [user, [], []])
+                        if st[0] != user:
+                            st[:] = [user, [], st[1]]
                         for j in st[2]:
                             deps[j] = True
                         if eng == "P":
@@ -138,7 +128,7 @@ def plan():
                     old.append((i, lo, hi, w))
         for j in after:
             deps[j] = True
-        ops.append(dict(eng=eng, cost=cost, call=call, deps=deps, kind=kind, tag=tuple(tag)))
+        ops.append(dict(eng=eng, cost=cost, call=call, deps=deps, kind=kind, tag=tuple(tag), alt=alt))
         return i
 
     def aps(*xs):
@@ -153,6 +143,9 @@ def plan():
         if two:
             return max(64, n * (1 if any(psum(a) for a in ins) else 2)) * CYC
         return max(64, n * (0.5 if narrow(out, *ins) else 1)) * CYC
+
+    def scost(out, in_):
+        return ((78 + 1.56 * count(out)) if in_[0] == "I" else max(64, count(out))) * CYC
 
     def cp(out, in_):
         return add("V", vcost(out, [in_]), ("cp", out, in_), [in_], [out])
@@ -170,40 +163,27 @@ def plan():
         return add("V", vcost(out, [out]), ("ms", out, v), [], [out])
 
     def act(out, in_, f=AF.Identity, bias=0.0, scale=1.0, accum=None):
-        n = count(out)
-        c = (78 + 1.56 * n) if in_[0] == "I" else max(64, n)
-        return add("S", c * CYC, ("act", out, in_, f, bias, scale, accum), [in_] + aps(bias, scale), [out] + aps(accum))
+        return add("S", scost(out, in_), ("act", out, in_, f, bias, scale, accum), [in_] + aps(bias, scale), [out] + aps(accum))
 
-    def lin(eng, out, in_, scale, bias):
-        if eng == "S":
-            return act(out, in_, scale=scale, bias=bias)
-        return ts(out, in_, scale, ALU.mult, bias, ALU.add)
-
-    def flex(name, out, in_, scale=1.0, bias=0.0):
-        eng = OPT["eng"].get(name + str(tag[1]), ENG[name])
-        if eng == "V" and scale == 1.0 and bias == 0.0:
-            return cp(out, in_)
-        return lin(eng, out, in_, scale, bias)
-
-    def bits(name, out, tmp, in_, *a):
-        if OPT["u16"]:
-            return ts(out, in_, *a)
-        ts(tmp, in_, *a)
-        return flex(name, out, tmp)
+    def lin(eng, out, in_, scale=1.0, bias=0.0):
+        ins = [in_] + aps(bias)
+        v = ("cp", out, in_) if (scale, bias) == (1.0, 0.0) else ("ts", out, in_, scale, bias, ALU.mult, ALU.add)
+        ways = {"V": ("V", vcost(out, ins), v), "S": ("S", scost(out, in_), ("act", out, in_, AF.Identity, bias, scale, None))}
+        return add(*ways[eng], ins, [out], alt=ways["V" if eng == "S" else "S"])
 
     def mm(lst):
-        c = sum(max(64, count(m[0])) * (4 if SCRATCH[m[1][1]][2] == F32 else 1) for m in lst)
+        c = sum(max(64, count(m[0])) for m in lst)
         return add("P", c * PCYC, ("mm", lst), [a for m in lst for a in m[1:3]], [m[0] for m in lst])
 
-    def group(out, pairs):
-        return [(out, l, r, k == 0, k == len(pairs) - 1) for k, (l, r) in enumerate(pairs)]
+    def group(out, pairs, first=True, last=True):
+        return [(out, l, r, first and k == 0, last and k == len(pairs) - 1) for k, (l, r) in enumerate(pairs)]
 
     def iota(out, pat, base, cm):
         return add("G", 130 + 2 * count(out) * CYC, ("iota", out, pat, base, cm), [], [out])
 
-    def dma(eng, out, in_, nbytes):
+    def dma(eng, out, in_, nbytes, after=()):
         return add(eng, 2000 + nbytes / 180.0, ("dma", out, in_), [in_] if in_[0] != "H" else [],
-                   [out] if out[0] != "H" else [], kind="d")
+                   [out] if out[0] != "H" else [], kind="d", after=after)
 
     def H(name, *ix):
         return ("H", name, ix)
@@ -211,21 +191,25 @@ def plan():
     def col(b, j):
         return A(b, j, j + 1)
 
+    def selj(name, j):
+        return A(name, 15 - j, 143 - j)
+
     al = slice(None)
     dma("Y", A("lan"), H("lanes", al, al), 131072)
-    dma("S", A("xs", 0, 2048), H("x", al, slice(0, 2048)), 700000)
-    dma("Y", A("xs", 2048, 4096), H("x", al, slice(2048, 4096)), 700000)
-    ms(A("s0w"), 0)
+    first = [dma("S", A("xs", 0, 2048), H("x", al, slice(0, 2048)), 700000),
+             dma("Y", A("xs", 2048, 4096), H("x", al, slice(2048, 4096)), 700000)]
+    iota(A("s0w"), [[0, 256]], 0, 0)
     dma("Y", A("wti", 0, 1), H("wt", al, al), 512)
     dma("Y", A("s0w", part=slice(0, 128, 16)), H("s0", al, al), 8192)
-    dma("Y", A("vs", 0, ROT), H("v", al, slice(4096 - ROT, 4096)), 1400000)
-    dma("Y", A("vs", ROT, 4096), H("v", al, slice(0, 4096 - ROT)), 1400000)
+    dma("Y", A("vs", 0, ROT), H("v", al, slice(4096 - ROT, 4096)), 700000, first)
+    dma("Y", A("vs", ROT, 4096), H("v", al, slice(0, 4096 - ROT)), 700000, first)
 
     iota(col("ci", 0), [[0, 1]], 0, 1)
-    for h in range(NCH):
-        iota(A("tj", Q0[h], Q0[h] + CH[h]), [[-1, 2], [-32, CH[h] // 2]], 255 - 16 * Q0[h], -2)
+    for h in range(2):
+        iota(A("tj", Q0[h], Q0[h] + C), [[-1, 2], [-32, C // 2]], 255 - 16 * Q0[h], -2)
     iota(A("tj", 16, 32), [[-16, 16]], 255, -1)
-    iota(A("t0", 0, 144), [[1, 144]], 0, 0)
+    iota(A("t0"), [[1, 144]], 0, 0)
+    iota(A("tn"), [[1, 128]], 128, 0)
     iota(A("t1", 0, 128), [[1, 16], [0, 8]], 0, 0)
     iota(A("t1", 128, 256), [[0, 16], [1, 8]], 0, 0)
     iota(A("t3", 0, 128), [[1, 8], [0, 16]], 0, 0)
@@ -237,97 +221,65 @@ def plan():
     ts(col("ci", 2), col("ci", 0), 4, ALU.arith_shift_right)
     ts(col("ci", 3), col("ci", 0), 7, ALU.bitwise_and)
     ts(col("ci", 4), col("ci", 0), 14, ALU.bitwise_and)
-    ts(col("ci", 5), col("ci", 0), 3, ALU.bitwise_and)
-    cp(A("cf", 0, 6), A("ci", 0, 6))
-    P_, J_, G_, J8, J14, J4 = (col("cf", j) for j in range(6))
-    ts(col("cf", 17), G_, 32.0, ALU.mult)
-    ts(col("cf", 6), G_, 16.0, ALU.mult)
-    ts(A("revl"), A("tj", 0, 16), col("cf", 17), ALU.add)
-    ts(A("rev"), A("tj", 16, 32), col("cf", 6), ALU.add)
+    cp(A("cf", 0, 5), A("ci", 0, 5))
+    P_, J_, G_, J8, J14 = (col("cf", j) for j in range(5))
+    lin("S", col("cf", 17), G_, 32.0)
+    lin("S", col("cf", 6), G_, 16.0)
+    lin("V", A("revl"), A("tj", 0, 16), 1.0, col("cf", 17))
+    lin("V", A("rev"), A("tj", 16, 32), 1.0, col("cf", 6))
     ts(A("idb"), A("t0", 0, 128), P_, ALU.is_equal)
-    ts(A("t2", 0, 128), A("t1", 0, 128), J_, ALU.subtract)
-    ts(A("t2", 128, 256), A("t2", 0, 128), 0.0, ALU.is_ge)
-    ts(A("t2", 0, 128), A("t2", 0, 128), J_, ALU.subtract)
-    tt(A("t2", 0, 128), A("t2", 0, 128), A("t2", 128, 256), ALU.mult)
-    ts(A("t2", 0, 128), A("t2", 0, 128), J_, ALU.add)
-    ts(A("t1", 128, 256), A("t1", 128, 256), G_, ALU.is_equal)
-    tt(A("wm"), A("t2", 0, 128), A("t1", 128, 256), ALU.mult)
-    ts(A("t2", 128, 256), A("t1", 128, 256), 2.0 ** -10, ALU.mult)
-    tt(A("wme"), A("t2", 128, 256), A("wm"), ALU.max)
-    act(A("nwm"), A("wm"), scale=-1.0)
-    act(A("c31"), A("idb"), scale=2.0 ** 31)
-    act(A("n31"), A("idb"), scale=-2.0 ** 31)
+    ts(A("t2", 0, 128), A("t1", 0, 128), J_, ALU.subtract, 2.0 ** -10, ALU.max)
+    ts(A("t2", 128, 256), A("t1", 0, 128), J_, ALU.is_lt, J_, ALU.mult)
+    tt(A("t2", 256, 384), A("t2", 0, 128), A("t2", 128, 256), ALU.max)
+    ts(A("t2", 0, 128), A("t1", 128, 256), G_, ALU.is_equal)
+    tt(A("wme"), A("t2", 256, 384), A("t2", 0, 128), ALU.mult)
+    lin("S", A("wx"), A("wme"), 1.0, 1024.0)
+    lin("S", A("wm"), A("wx"), 1.0, -1024.0)
+    lin("S", A("nwm"), A("wx"), -1.0, 1024.0)
+    for name, f in (("c31", 2.0 ** 31), ("n31", -2.0 ** 31), ("c43", 1.5 * 2.0 ** 43), ("n43", -1.5 * 2.0 ** 43),
+                    ("nid", -1.0), ("idh", 1.0), ("i19", 2.0 ** 19)):
+        lin("S", A(name), A("idb"), f)
     ms(A("one"), 1.0)
-    cp(col("cf", 8), col("wti", 0))
-    ts(col("cf", 7), G_, 16.0, ALU.mult, 15.0, ALU.add)
-    ts(A("selb"), A("t0", 0, 144), col("cf", 7), ALU.is_equal)
-    ts(A("b8"), A("t0", 0, 8), G_, ALU.is_equal)
-    ts(A("b8k"), A("t0", 0, 8), G_, ALU.is_equal, 1024.0, ALU.mult)
-    if OPT["ub"]:
-        ts(A("b8w"), A("t0", 0, 8), G_, ALU.is_equal, col("cf", 8), ALU.mult)
-    else:
-        ts(A("selw"), A("t0", 0, 144), col("cf", 7), ALU.is_equal, col("cf", 8), ALU.mult)
-    act(A("nid"), A("idb"), scale=-1.0)
-    if OPT["near"] == "D":
-        act(A("c43"), A("idb"), scale=1.5 * 2.0 ** 43)
-        act(A("n43"), A("idb"), scale=-1.5 * 2.0 ** 43)
-        act(A("sel"), A("selb"), scale=2.0 ** 16)
-    if OPT["far"] == "D":
-        act(A("selk"), A("selb"), scale=1024.0)
-    act(A("idh"), A("idb"))
-    act(A("idf"), A("idb"))
-    act(A("i19"), A("idb"), scale=float(2 ** 19))
+    lin("S", col("cf", 8), col("wti", 0))
+    lin("S", col("cf", 7), G_, 16.0, 15.0)
+    ts(A("selb"), A("t0"), col("cf", 7), ALU.is_equal)
+    ts(A("selw"), A("selb"), col("cf", 8), ALU.mult)
+    lin("S", A("sel"), A("selb"), 2.0 ** 16)
+    lin("S", A("selk"), A("selb"), 1024.0)
     ts(col("cf", 16), J_, 8.0, ALU.is_ge, 65280.0, ALU.mult)
-    ts(col("cf", 16), col("cf", 16), 256.0, ALU.add)
-    ts(A("tc"), A("t0", 0, 128), 0.0, ALU.mult, col("cf", 16), ALU.add)
-    act(A("ta", 0, 120), A("t0", 0, 120), scale=4096.0, bias=2048.0)
-    act(A("tb", 0, 120), A("mtab", 0, 120), scale=64.0, bias=12288.0)
+    lin("S", A("tc"), A("one", 0, 64), 256.0, col("cf", 16))
+    lin("S", A("ta", 0, 120), A("t0", 0, 120), 4096.0, 2048.0)
+    lin("S", A("tb", 0, 120), A("mtab", 0, 120), 64.0, 12288.0)
     ts(A("blk"), A("t3", 0, 128), G_, ALU.is_equal)
-    ms(A("rst", 0, 120), 0.0)
-    ms(A("rst", 0, 120, 15), float(2 ** 25))
+    ts(A("rst"), A("mtab", 0, 120), 1.0, ALU.is_equal, 2.0 ** 25, ALU.mult)
     ms(col("thr", 0), 2.5)
-    ts(A("t3", 136, 144), A("t3", 128, 136), J_, ALU.add, 0.5, ALU.add)
-    ts(A("t3", 144, 152), A("t3", 136, 144), 1.0 / 15.0, ALU.mult, -0.5, ALU.add)
-    cp(A("ti", 0, 8), A("t3", 144, 152))
-    for c in set(CH):
-        ts(A("ltl", 2 * c - 8, 3 * c - 8), A("ti", 0, c), c - 1.0, ALU.min)
-    if OPT["ub"]:
-        ts(col("cf", 26), P_, 0.5, ALU.add, 1.0 / 15.0, ALU.mult)
-        ts(col("ci", 8), col("cf", 26), -0.5, ALU.add)
-        ts(col("cf", 27), col("ci", 8), -15.0, ALU.mult, P_, ALU.add)
-        ts(col("cf", 28), col("cf", 27), 64.0, ALU.mult, 12352.0, ALU.add)
-    ts(A("t2", 0, 128), A("t2", 0, 128), -16.0, ALU.add)
-    tt(A("t2", 128, 256), A("t2", 0, 128), A("t1", 128, 256), ALU.mult)
-    ts(A("poff"), A("t2", 128, 256), 16.0, ALU.add)
-    ts(A("iw"), A("t0", 0, 32), J_, ALU.is_equal)
-    for i in range(4):
-        act(A("pa", 512 * i, 512 * i + 512), IX("iw", 0, 32, "poff", 32 * i, 32 * i + 32))
-        ts(A("pl", 512 * i, 512 * i + 512), A("pa", 512 * i, 512 * i + 512), 1.0 / 4096, ALU.mult)
-    ts(col("cf", 9), J_, 8.0, ALU.mult, 1032.0, ALU.add)
-    ts(A("val"), A("t3", 128, 136), 8.0, ALU.mult, col("cf", 9), ALU.add)
-    ts(col("cf", 10), J14, -0.5, ALU.mult)
-    for c in set(CH):
-        ts(A("lst", 2 * c - 8, 3 * c - 8), A("t3", 128, 128 + c), 7.5 * c - 0.5, ALU.mult, col("cf", 10), ALU.add)
-    ts(A("tri", 0, 16), A("t0", 0, 16), J_, ALU.is_gt)
-    ms(A("tri", 16, 272), 1.0)
-    ts(A("hrow", 256, 272), A("t0", 0, 16), 0.0, ALU.mult, 2048.0, ALU.add)
-    for h in range(NCH):
-        s, c = str(h), CH[h]
-        jc = J8 if c == 8 else J4
-        ts(col("cf", 18 + h), jc, -8.0, ALU.mult, float(SEG[h][0]), ALU.add)
-        ts(col("cf", 22 + h), jc, 1.0, ALU.add, col("cf", 18 + h), ALU.mult)
-        ts(A("ends", 2 * h, 2 * h + 1), col("cf", 22 + h), -1.0, ALU.add)
-        o = 0
-        for q in range(c):
-            act(A("msk" + s, o, o + SEG[h][q]), A("tri", 0, SEG[h][q]), scale=col("val", q))
-            o += SEG[h][q]
-        iota(A("lall" + s, 120 * c, 1040 + 128 * c), [[0, 1040 + 8 * c]], 0, 0)
-        if c == 4:
-            ms(A("m" + s, 8, 16), 0.0)
-    cp(A("srow"), IX("s0w", 0, 256, "rev", 0, 16))
-    mm(group(A("pn", 0, 16), [(A("selb", 15 - j, 143 - j), A("srow", j, 256, 16)) for j in range(16)]))
-    for h in range(NCH):
-        cp(A("rcv%d" % h, 0, CH[h]), A("pn", Q0[h], Q0[h] + CH[h]))
+    lin("S", col("cf", 9), J_, 1.0 / 15.0, 0.5 / 15.0 - 0.5)
+    lin("S", A("ti"), A("t3", 128, 136), 1.0 / 15.0, col("cf", 9))
+    ts(A("ltl"), A("ti"), C - 1.0, ALU.min)
+    lin("S", col("cf", 11), G_, 16.0, 128.0)
+    lin("S", A("pcol"), A("t2", 256, 384, 8), 1.0, col("cf", 11))
+    for m in range(16):
+        ts(A("pa", 128 * m, 128 * m + 128), A("tn"), col("pcol", m), ALU.is_equal)
+    lin("S", col("cf", 12), J_, 8.0, 1032.0)
+    lin("S", A("val"), A("t3", 128, 136), 8.0, col("cf", 12))
+    lin("S", col("cf", 10), J14, -0.5)
+    lin("S", A("lst"), A("t3", 128, 136), 59.5, col("cf", 10))
+    ts(A("tri", 0, 16), A("t0", 0, 16), J_, ALU.is_gt, 4096.0, ALU.mult)
+    lin("S", A("tri", 16, 272), A("one", 0, 256), 4096.0)
+    lin("S", A("hrow", 256, 272), A("one", 0, 16), 2048.0)
+    for h in range(2):
+        s = str(h)
+        lin("S", col("cf", 18 + h), J8, -8.0, float(SEG[h][0]))
+        ts(col("cf", 22 + h), J8, 1.0, ALU.add, col("cf", 18 + h), ALU.mult)
+        lin("S", A("ends", 2 * h, 2 * h + 1), col("cf", 22 + h), 1.0, -1.0)
+        for q in range(C):
+            o = sum(SEG[h][:q])
+            dma("Y", A("msk" + s, o, o + SEG[h][q]), A("tri", 0, SEG[h][q]), 60000, first)
+        iota(A("lall" + s, 960, 2064), [[0, 1104]], 0, 0)
+    lin("S", A("srow"), IX("s0w", 0, 256, "rev", 0, 16))
+    mm(group(A("pn", 0, 16), [(selj("selb", j), A("srow", j, 256, 16)) for j in range(16)]))
+    for h in range(2):
+        lin("S", A("rcv%d" % h, 0, C), A("pn", Q0[h], Q0[h] + C))
 
     rot = [0, 0]
 
@@ -337,47 +289,37 @@ def plan():
 
     def close_step(t):
         tag[:] = [t, 9, "close"]
-        for h in range(NCH):
-            cp(IX("vs", 0, 8208, "ou%d" % h, 16, 16 + CH[h]), A("fsel", 16 * Q0[h], 16 * (Q0[h] + CH[h])))
+        for h in range(2):
+            cp(IX("vs", 0, 8208, "ou%d" % h, 16, 24), A("fsel", 16 * Q0[h], 16 * Q0[h] + 128))
         if t < STEPS - 1:
             mm(group(A("pn", 256, 272), [(A("blk"), A("win"))]))
             act(A("aj"), A("pn", 256, 272), scale=-1.0, bias=48.40625, accum=col("ay", 0))
-            act(col("aq", 0), col("ay", 0), bias=-4.0)
-            act(col("thr", 0), col("aq", 0), scale=-1.0, bias=col("ay", 0))
+            lin("S", col("aq", 0), col("ay", 0), 1.0, -4.0)
+            lin("S", col("thr", 0), col("aq", 0), -1.0, col("ay", 0))
 
     def prints(t, h):
         s = str(h)
-        r0 = 144 * t
-        c = CH[h]
-        n2, nm, npc = 8 * c, 15 * c, c // 4
+        l0 = 128 * t
         w2, w3, w4 = "w2" + s, "w3" + s, "w4" + s
-        rows = slice(0, nm)
         tag[:] = [t, h, "list"]
         if t == 0:
-            cp(A("ld" + s), IX("lan", 0, 256, "revl", Q0[h], Q0[h] + c))
-            cp(A("lu" + s), A("ld" + s))
-        else:
-            bits("lu0", A("lu" + s, 0, n2), A("ld" + s, 0, n2), A("rcv" + s, r0 + c, r0 + 17 * c, 2), 4095, ALU.bitwise_and)
-            bits("lu1", A("lu" + s, n2, 2 * n2), A("ld" + s, n2, 2 * n2), A("rcv" + s, r0 + c + 1, r0 + 17 * c, 2), 12,
-                 ALU.arith_shift_right)
-        for pc in range(npc):
+            lin("V", A("ld" + s, 0, 128), IX("lan", 0, 256, "revl", Q0[h], Q0[h] + C))
+            lin("V", A("lu" + s, 0, 128), A("ld" + s, 0, 128))
+        for pc in range(2):
             tag[:] = [t, h, "f%d" % pc]
             rot[1] += 1
             pt = "pt%d" % (rot[1] % 2)
             for b in range(2):
-                c0 = n2 * b + 32 * pc
+                c0 = l0 + 64 * b + 32 * pc
                 o = 1024 * pc + 512 * b
-                (cp if (t, h, pc, b) in OPT["gav"] else act)(A("a" + s, o, o + 512), IX("xs", 0, 4096, "lu" + s, c0, c0 + 32))
+                lin("S", A("a" + s, o, o + 512), IX("xs", 0, 4096, "lu" + s, c0, c0 + 32))
                 lst = [("T", A(pt, 256 * i + 128 * b, 256 * i + 128 * b + 128), A("a" + s, o + 128 * i, o + 128 * i + 128))
                        for i in range(4)]
                 add("P", 512 * PCYC, ("tr", lst), [m[2] for m in lst] + [A("idb")], [m[1] for m in lst])
-            pi0 = (16 - Q0[h] - c) // 2 + 2 * pc
-            lift = [272.0 if OPT["mode"][pi0 + u] == "P" else 288.0 for u in range(2)]
-            if lift[0] == lift[1]:
-                ts(A("at" + s, 1024 * pc, 1024 * pc + 1024), A(pt), lift[0], ALU.add)
-            else:
-                for u in range(2):
-                    ts(A("at" + s, 1024 * pc + 512 * u, 1024 * pc + 512 * u + 512), A(pt, 512 * u, 512 * u + 512), lift[u], ALU.add)
+            mode = OPT["mode"][4 * h + 2 * pc:4 * h + 2 * pc + 2]
+            for u in range(2):
+                ts(A("at" + s, 1024 * pc + 512 * u, 1024 * pc + 512 * u + 512), A(pt, 512 * u, 512 * u + 512),
+                   272.0 if mode[u] == "P" else 288.0, ALU.add)
             for u in range(2):
                 o = 480 * (2 * pc + u)
                 bk = xbank()
@@ -386,170 +328,125 @@ def plan():
                     return [(A(bk, 240 * (i // 2) + i % 2, 240 * (i // 2) + 240, 2),
                              A("at" + s, 1024 * pc + 512 * u + 128 * i, 1024 * pc + 512 * u + 128 * i + 128), A(w, 8, 128),
                              first, first or (last and i == 3)) for i in range(4)]
-                if OPT["mode"][pi0 + u] == "P":
-                    mm([(A(bk, 0, 480), A("c31"), A("one"), True, False)] + blocks("wme", False, False) +
-                       [(A(bk, 0, 480), A("n31"), A("one"), False, False)] + blocks("nwm", False, True))
-                    lin(OPT["fev"][pi0 + u], A("f" + s, o, o + 480), A(bk, 0, 480), -1.0, 128.0)
+                if mode[u] == "P":
+                    mm([(A(bk, 0, 480), A("c31"), A("one"), True, False)])
+                    mm(blocks("wme", False, False) + [(A(bk, 0, 480), A("n31"), A("one"), False, False)] + blocks("nwm", False, True))
+                    lin("S", A("f" + s, o, o + 480), A(bk, 0, 480), -1.0, 128.0)
                 else:
                     mm(blocks("wm", True, True))
-                    act(A("q" + s, o, o + 480), A(bk, 0, 480), bias=-127.5)
+                    lin("S", A("q" + s, o, o + 480), A(bk, 0, 480), 1.0, -127.5)
                     tt(A("f" + s, o, o + 480), A(bk, 0, 480), A("q" + s, o, o + 480), ALU.subtract)
-            if not OPT["ub"]:
-                tag[:] = [t, h, "u%d" % pc]
-                a, b = 60 * pc, 60 * pc + 60
-                mm(group(A("pu", a, b), [(A("blk"), A("tc", 0, 60))] +
-                         [(A("selw", 15 - j, 143 - j), A("f" + s, 960 * pc + j, 960 * pc + 960, 16)) for j in range(16)]))
-                flex("uq", A(w3, 128 + a, 128 + b), A("pu", a, b), bias=0.5)
-                tt(A(w4, a, b), A("pu", a, b), A(w3, 128 + a, 128 + b), ALU.subtract)
-                act(A(w2, a, b), A(w4, a, b), AF.Square, bias=2640.0)
-                bits("hu", A("hu" + s, a, b), A(w2, 128 + a, 128 + b), A(w2, a, b), 5, ALU.arith_shift_right, 4095, ALU.bitwise_and)
-        if OPT["ub"]:
-            tag[:] = [t, h, "u0"]
-            mm([(A("pu", 0, 128, part=rows), A("blk", 0, nm), A("tc"), True, False)] +
-               [(A("pu", j, 128, 16, rows), A("f" + s, j, 240 * c, 16), A("b8w"), False, j == 15) for j in range(16)])
-            act(A(w3, 128, 256, part=rows), A("pu", 0, 128, part=rows), bias=0.5)
-            tt(A(w4, 0, 128, part=rows), A("pu", 0, 128, part=rows), A(w3, 128, 256, part=rows), ALU.subtract)
-            mm(group(A("pu", 128, 128 + nm), [(A(w4, 0, 128, part=rows), A("idh", 0, nm, part=rows))]))
-            act(A(w2, 0, nm), A("pu", 128, 128 + nm), AF.Square, bias=2640.0)
-            bits("hu", A("hu" + s, 0, nm), A(w2, 128, 128 + nm), A(w2, 0, nm), 5, ALU.arith_shift_right, 4095, ALU.bitwise_and)
+            tag[:] = [t, h, "u%d" % pc]
+            a, b = 60 * pc, 60 * pc + 60
+            mm(group(A("pu", a, b), [(A("blk"), A("tc", 0, 60))] +
+                     [(selj("selw", j), A("f" + s, 960 * pc + j, 960 * pc + 960, 16)) for j in range(16)]))
+            lin("S", A(w3, 128 + a, 128 + b), A("pu", a, b), 1.0, 0.5)
+            tt(A(w4, a, b), A("pu", a, b), A(w3, 128 + a, 128 + b), ALU.subtract)
+            act(A(w2, a, b), A(w4, a, b), AF.Square, bias=2640.0)
+            ts(A(w2, 128 + a, 128 + b), A(w2, a, b), 5, ALU.arith_shift_right, 4095, ALU.bitwise_and)
+            lin("V", A("hu" + s, a, b), A(w2, 128 + a, 128 + b))
         tag[:] = [t, h, "key"]
-        tt(A(w3, 0, 16 * c), IX("rcv" + s, r0, r0 + c, "ltl", 2 * c - 8, 3 * c - 8), A("mtab", 0, 16 * c), ALU.is_gt)
-        flex("h16", A(w4, 128, 128 + nm), A("hu" + s, 0, nm), bias=-2048.0)
-        if OPT["ub"]:
-            flex("w3", A(w3, 256, 384, part=rows), A(w4, 0, 128, part=rows), bias=12288.0 - 31.5)
-        else:
-            flex("w3", A(w3, 256, 256 + nm), A(w4, 0, nm), bias=12288.0 - 31.5)
+        tt(A(w3, 0, 128), IX("rcv" + s, 8 * t, 8 * t + 8, "ltl", 0, 8), A("mtab"), ALU.is_gt)
+        lin("S", A(w4, 128, 248), A("hu" + s, 0, 120), 1.0, -2048.0)
+        lin("S", A(w3, 256, 376), A(w4, 0, 120), 1.0, 12288.0 - 31.5)
         tag[:] = [t, h, "flip"]
-        flex("lh", A("lh" + s), A("lu" + s), bias=-2048.0)
-        for bi in range(npc):
+        lin("S", A("lh" + s, 0, 64), A("lu" + s, l0, l0 + 64), 1.0 / 4096, -0.5)
+        lin("S", A("lh" + s, 64, 128), A("lu" + s, l0 + 64, l0 + 128), 1.0, -2048.0)
+        for bi in range(2):
             bk = xbank()
             lst = []
-            for i in range(512 // n2):
+            for i in range(8):
                 m = (8 * bi + i + 1) % 16
-                lst += group(A(bk, n2 * i, n2 * i + n2), [(A("pl", 128 * m, 128 * m + 128), A("lh" + s, 0, n2)),
-                                                          (A("pa", 128 * m, 128 * m + 128), A("lh" + s, n2, 2 * n2))])
+                lst += group(A(bk, 64 * i, 64 * i + 64), [(A("pa", 128 * m, 128 * m + 128), A("lh" + s, 0, 64)),
+                                                          (A("pa", 128 * m, 128 * m + 128), A("lh" + s, 64, 128))])
             mm(lst)
-            n = 512 - n2 * (bi == npc - 1)
-            flex("lall%d" % (bi % 2), A("lall" + s, 512 * bi, 512 * bi + n), A(bk, 0, n), 4096.0, 2048.0 * 4097)
-            if bi == npc - 1:
+            n = 512 - 64 * bi
+            lin("S", A("lall" + s, 512 * bi, 512 * bi + n), A(bk, 0, n), 4096.0, 2048.0 * 4097)
+            if bi:
                 for e in range(2):
-                    flex("same", A("lall" + s, 1032 + 8 * e, 1032 + 128 * c, 16), A(bk, n, 512), 4096.0, 2048.0 * 4097)
+                    lin("S", A("lall" + s, 1032 + 8 * e, 2056, 16), A(bk, n, 512), 4096.0, 2048.0 * 4097)
+
+    def send(sem, src, dst):
+        sent = add("G", 300, ("send", "arr%d" % sem, 0, src, dst), [src], [], kind="s")
+        add("R", 0, ("arr", "arr%d" % sem), [], [dst], kind="r", after=[sent])
 
     def decide(t, h):
         s = str(h)
-        r0 = 144 * t
-        c = CH[h]
-        B, nm = 16 * Q0[h], 15 * c
-        w1, w3, w4 = "w1" + s, "w3" + s, "w4" + s
-        rows = slice(0, nm)
-        for pi in range(c // 2):
+        B = 16 * Q0[h]
+        w3, w4, k, m_, ou, ld = "w3" + s, "w4" + s, "k" + s, "m" + s, "ou" + s, "ld" + s
+        tag[:] = [t, h, "pre"]
+        mm(group(A("pn", 0, 120), [(A("c43"), A("one", 0, 120))], last=False))
+        mm(group(A("pf", 0, 120), [(A("idb"), A("tb", 0, 120)), (A("idh"), A(w4, 0, 120)), (A("nid"), A(w3, 256, 376))], last=False))
+        for pi in range(4):
             tag[:] = [t, h, "d%d" % pi]
             o = 480 * pi
             tt(A("d" + s, o, o + 480), IX("vs", 0, 4096, "hu" + s, 30 * pi, 30 * pi + 30), A("f" + s, o, o + 480), ALU.subtract)
             act(A("ab" + s, o, o + 480), A("d" + s, o, o + 480), AF.Abs)
-            if OPT["near"] == "D":
-                ts(A("cl" + s, o, o + 480), A("ab" + s, o, o + 480), col("thr", 0), ALU.is_le, -3.5 / 16, ALU.add)
-            else:
-                ts(A("cl" + s, o, o + 480), A("ab" + s, o, o + 480), col("thr", 0), ALU.is_le)
+            ts(A("cl" + s, o, o + 480), A("ab" + s, o, o + 480), col("thr", 0), ALU.is_le, -3.5 / 16, ALU.add)
             if pi % 2:
                 c0, c1, o = 30 * pi - 30, 30 * pi + 30, o - 480
-                if OPT["near"] == "D":
-                    tag[:] = [t, h, "n%d" % pi]
-                    mm([(A("pn", 0, nm), A("c43"), A("one", 0, nm), True, False)] * (pi == 1) +
-                       [(A("pn", c0, c1), A("sel", 15 - j, 143 - j), A("cl" + s, o + j, o + 960, 16), False, False) for j in range(16)])
-                if OPT["far"] == "D":
-                    tag[:] = [t, h, "r%d" % pi]
-                    mm(group(A("pf", c0, c1), [(A("idb"), A("tb", c0, c1)), (A("idh"), A(w4, c0, c1)), (A("nid"), A(w3, 256 + c0, 256 + c1))] +
-                             [(A("selk", 15 - j, 143 - j), A("ab" + s, o + j, o + 960, 16)) for j in range(16)]))
+                tag[:] = [t, h, "n%d" % pi]
+                mm(group(A("pn", c0, c1), [(selj("sel", j), A("cl" + s, o + j, o + 960, 16)) for j in range(16)], False, False))
+                tag[:] = [t, h, "r%d" % pi]
+                mm(group(A("pf", c0, c1), [(selj("selk", j), A("ab" + s, o + j, o + 960, 16)) for j in range(16)], False, pi == 3))
         tag[:] = [t, h, "near"]
-        pre = [(A("idb"), A("ta", 0, nm)), (A("idh"), A(w4, 128, 128 + nm)), (A("i19"), A(w3, 0, nm))]
-        if OPT["near"] == "D":
-            mm([(A("pn", 0, nm), l, r, False, k == 3) for k, (l, r) in enumerate([(A("n43"), A("one", 0, nm))] + pre)])
-            key = A("pn", 0, nm)
-        else:
-            mm([(A("pn", j, 128, 16, rows), A("cl" + s, j, 240 * c, 16), A("b8"), True, True) for j in range(16)])
-            seen = A(w3, 384, 512, part=rows)
-            if OPT["seen"] == "V":
-                ts(seen, A("pn", 0, 128, part=rows), 11.5, ALU.is_ge, 2.0 ** 20, ALU.mult)
-            else:
-                act(seen, A("pn", 0, 128, part=rows), AF.Relu, scale=2.0 ** 20, bias=-11.0 * 2 ** 20)
-            key = A("pn", 128, 128 + nm)
-            mm(group(key, pre + [(seen, A("idb", 0, nm, part=rows))]))
-        scan(A("sc" + s, 0, nm), A("rst", 0, nm), key, ALU.add, ALU.min)
+        mm(group(A("pn", 0, 120), [(A("n43"), A("one", 0, 120)), (A("idb"), A("ta", 0, 120)), (A("idh"), A(w4, 128, 248)),
+                                   (A("i19"), A(w3, 0, 120))], first=False))
+        scan(A("sc" + s, 0, 120), A("rst"), A("pn", 0, 120), ALU.add, ALU.min)
         tag[:] = [t, h, "far"]
-        far = A(w1, 0, 128, part=rows)
-        turn = [(far, A("idf", 0, nm, part=rows))]
-        key = A("pf", 128, 128 + nm)
-        if OPT["far"] == "D":
-            key = A("pf", 0, nm)
-        elif OPT["ub"]:
-            pay = [(A("idh", 0, nm, part=rows), A(w4, 0, 128, part=rows)), (A("nid", 0, nm, part=rows), A(w3, 256, 384, part=rows))]
-            mm([(A("pf", 0, 128, part=rows), l, r, k == 0, False) for k, (l, r) in enumerate(pay)] +
-               [(A("pf", j, 128, 16, rows), A("ab" + s, j, 240 * c, 16), A("b8k"), False, j == 15) for j in range(16)])
-            act(far, A("pf", 0, 128, part=rows), bias=A("cf", 28, 29, part=rows))
-        else:
-            mm([(A("pf", j, 128, 16, rows), A("ab" + s, j, 240 * c, 16), A("b8k"), True, True) for j in range(16)])
-            flex("far", far, A("pf", 0, 128, part=rows))
-            turn = [(A("idb"), A("tb", 0, nm)), (A("idh"), A(w4, 0, nm)), (A("nid"), A(w3, 256, 256 + nm))] + turn
-        if OPT["far"] != "D":
-            mm(group(key, turn))
-        scan(A("sc" + s, nm, 2 * nm), A("rst", 0, nm), key, ALU.add, ALU.min)
-        k, m_, ou = "k" + s, "m" + s, "ou" + s
-        k1, k2 = A("sc" + s, 14, nm, 15), A("sc" + s, nm + 14, 2 * nm, 15)
-        ts(A(k, 32, 32 + c), k2, 15, ALU.bitwise_and)
-        tt(A(m_, 24, 24 + c), A("rcv" + s, r0, r0 + c), A(k, 32, 32 + c), ALU.subtract)
+        scan(A("sc" + s, 120, 240), A("rst"), A("pf", 0, 120), ALU.add, ALU.min)
+        k1, k2 = A("sc" + s, 14, 120, 15), A("sc" + s, 134, 240, 15)
+        ts(A(k, 32, 40), k2, 15, ALU.bitwise_and)
+        tt(A(m_, 24, 32), A("rcv" + s, 8 * t, 8 * t + 8), A(k, 32, 40), ALU.subtract)
         tag[:] = [t, h, "pick"]
-        ts(A(k, 16, 16 + c), k1, 0x700FFF, ALU.bitwise_and)
-        ts(A(ou, 0, c), A(k, 16, 16 + c), 4096.0, ALU.min)
-        flex("hrow", A("hrow", B, B + 16 * c), IX("ctab", 0, 4112, ou, 0, c))
+        ts(A(k, 16, 24), k1, 0x100FFF, ALU.bitwise_and)
+        ts(A(ou, 0, 8), A(k, 16, 24), 4096.0, ALU.min)
+        lin("S", A("hrow", B, B + 128), IX("ctab", 0, 4112, ou, 0, 8))
         hi = 16 * h
-        ts(A("hc", hi, hi + c), A(k, 16, 16 + c), 4096.0, ALU.min, -2048.0, ALU.add)
-        ts(A(k, 24, 24 + c), k1, 6 if c == 8 else 7, ALU.arith_shift_right, 127 * 8 * c, ALU.bitwise_and)
-        flex("m0", A(m_, 0, c), A("hc", hi, hi + c), 0.25, 512.0)
-        tt(A(m_, c, 2 * c), A(k, 24, 24 + c), A("lst", 2 * c - 8, 3 * c - 8), ALU.subtract)
-        flex("ou8", A(ou, 8, 8 + c), A(k, 24, 24 + c), 2.0 / c, J_)
-        flex("fsel", A("fsel", B, B + 16 * c), IX("f" + s, 0, 240 * c, ou, 8, 8 + c))
+        lin("V", A("hc", hi, hi + 8), A(ou, 0, 8), 1.0, -2048.0)
+        ts(A(k, 24, 32), k1, 6, ALU.arith_shift_right, 127 * 64, ALU.bitwise_and)
+        lin("S", A(m_, 0, 8), A(ou, 0, 8), 0.25)
+        tt(A(m_, 8, 16), A(k, 24, 32), A("lst"), ALU.subtract)
+        lin("S", A(ou, 8, 16), A(k, 24, 32), 0.25, J_)
+        lin("S", A("fsel", B, B + 128), IX("f" + s, 0, 1920, ou, 8, 16))
         tag[:] = [t, h, "win"]
-        o = 0
-        for q in range(c):
-            n = SEG[h][q]
-            ts(A("eq" + s, o, o + n), A("hrow", 258 - n, 258), col("hc", hi + q), ALU.is_equal, 4096.0, ALU.mult)
-            o += n
+        for q in range(C):
+            o, w = sum(SEG[h][:q]), SEG[h][q]
+            ts(A("eq" + s, o, o + w), A("hrow", 258 - w, 258), col("hc", hi + q), ALU.is_equal, col("val", q), ALU.mult)
         scan(A("es" + s), A("eq" + s), A("msk" + s), ALU.max, ALU.min)
         ends = IX("es" + s, 0, TOT[h], "ends", 2 * h, 2 * h + 1)
         tag[:] = [t, h, "send"]
-        if OPT["ttu"]:
-            tt(A(ou, 32, 48), ends, A(m_, 0, 16), ALU.max)
-            new = 32 + c
+        tt(A(ou, 32, 48), ends, A(m_, 0, 16), ALU.max)
+        lin("S", A(ld, 128, 256), IX("lall" + s, 0, 2064, ou, 40, 48))
+        if t < STEPS - 1:
+            ts(A(ld, 0, 64), A(ld, 128, 256, 2), 4095, ALU.bitwise_and)
+            ts(A(ld, 64, 128), A(ld, 129, 256, 2), 12, ALU.arith_shift_right)
+            lin("V", A("su" + s, 128 * t, 128 * t + 128), A(ld, 0, 128))
+            send(2 * t + h, A("su" + s, 128 * t, 128 * t + 128), A("lu" + s, 128 * t + 128, 128 * t + 256))
         else:
-            tt(A(m_, 32, 48), ends, A(m_, 0, 16), ALU.max)
-            flex("ou24", A(ou, 24, 24 + c), A(m_, 32 + c, 32 + 2 * c))
-            new = 24
-        flex("new", A("snd" + s, r0 + c, r0 + 17 * c), IX("lall" + s, 0, 1040 + 128 * c, ou, new, new + c))
-
-        def send(n, lo, hi):
-            src, dst = A("snd" + s, r0 + lo, r0 + hi), A("rcv" + s, r0 + 144 + lo, r0 + 144 + hi)
-            sent = add("G", 300, ("send", "arr%d" % n, h, src, dst), [src], [], kind="s")
-            add("R", 0, ("arr", "arr%d" % n), [], [dst], kind="r", after=[sent])
-        if OPT["ssep"]:
-            send(NCH * t + h, c, 17 * c)
-            tag[:] = [t, h, "s"]
-        if OPT["ttu"]:
-            tt(A(m_, 32, 48), ends, A(m_, 0, 16), ALU.max)
-        wn = A("win", Q0[h], Q0[h] + c)
-        ts(wn, A(m_, 32, 32 + c), 1024.5, ALU.is_lt)
-        tt(A(m_, 48, 48 + c), A(m_, 24, 24 + c), wn, ALU.mult)
-        tt(A("snd" + s, r0, r0 + c), A(m_, 48, 48 + c), A(k, 32, 32 + c), ALU.add)
-        if OPT["ssep"]:
-            send(NCH * (STEPS + t) + h, 0, c)
-        else:
-            send(NCH * t + h, 0, 17 * c)
-        flex("ou16", A(ou, 16, 16 + c), A(m_, 32, 32 + c), 4.0)
+            ts(A(ld, 0, 128, 2), A(ld, 128, 256, 2), 4095, ALU.bitwise_and)
+            ts(A(ld, 1, 128, 2), A(ld, 129, 256, 2), 12, ALU.arith_shift_right)
+            if OPT["neg"]:
+                lin("V", A("home" + s, 0, 128), A(ld, 0, 128, -1))
+            else:
+                lin("V", A("home" + s, 0, 128), IX(ld, 0, 128, "rev", 8, 16))
+            send(2 * t + h, A("home" + s, 0, 128), A("home" + s, 128, 256))
+        tag[:] = [t, h, "s"]
+        tt(A(m_, 32, 48), ends, A(m_, 0, 16), ALU.max)
+        lin("S", A(ou, 16, 24), A(m_, 32, 40), 4.0)
+        wn = A("win", Q0[h], Q0[h] + C)
+        ts(wn, A(m_, 32, 40), 1024.5, ALU.is_lt)
+        tt(A(m_, 48, 56), A(m_, 24, 32), wn, ALU.mult)
+        src, dst = A("snd" + s, 8 * t, 8 * t + 8), A("rcv" + s, 8 * t + 8, 8 * t + 16)
+        if t == STEPS - 1:
+            src, dst = A("sl" + s, 0, 8), A("sl" + s, 8, 16)
+        tt(src, A(m_, 48, 56), A(k, 32, 40), ALU.add)
+        send(2 * (STEPS + t) + h, src, dst)
 
     for t in range(STEPS):
-        for h in range(NCH):
+        for h in range(2):
             prints(t, h)
-        for h in range(NCH):
+        for h in range(2):
             decide(t, h)
         close_step(t)
     tag[:] = [99, 9, "out"]
@@ -557,74 +454,162 @@ def plan():
     for k in range(4):
         o = (cut[k] - ROT) % 4096
         dma("YS"[k % 2], H("yv", al, slice(o, o + cut[k + 1] - cut[k])), A("vs", cut[k], cut[k + 1]), 500000)
-    r0 = 144 * STEPS
-    for h in range(NCH):
-        s, c = str(h), CH[h]
-        n, l0 = 16 * c, 256 - 16 * (Q0[h] + c)
-        ts(A("ld" + s, 0, n, 2), A("rcv" + s, r0 + c, r0 + 17 * c, 2), 4095, ALU.bitwise_and)
-        ts(A("ld" + s, 1, n, 2), A("rcv" + s, r0 + c + 1, r0 + 17 * c, 2), 12, ALU.arith_shift_right)
-        cp(A("fo" + s, 0, n), IX("ld" + s, 0, n, "rev", 16 - c, 16))
-        dma("Y", H("yl", al, slice(l0, l0 + n)), A("fo" + s, 0, n), 65536)
-        cp(A("ou" + s, 0, c), A("rcv" + s, r0, r0 + c))
-        act(A("fo" + s, 128, 128 + n), IX("ctab", 0, 4112, "ou" + s, 0, c), bias=2048.0)
-        act(A("fo" + s, 256, 256 + n), IX("fo" + s, 128, 128 + n, "rev", 16 - c, 16))
-        dma("S", H("ys", al, slice(l0, l0 + n)), A("fo" + s, 256, 256 + n, part=slice(0, 128, 16)), 4096)
+    for h in range(2):
+        s, l0 = str(h), 128 * h
+        dma("Y", H("yl", al, slice(l0, l0 + 128)), A("home" + s, 128, 256), 65536)
+        if OPT["neg"]:
+            lin("S", A("fo" + s, 128, 256, -1), IX("ctab", 0, 4112, "sl" + s, 8, 16), 1.0, 2048.0)
+        else:
+            lin("S", A("fo" + s, 0, 128), IX("ctab", 0, 4112, "sl" + s, 8, 16), 1.0, 2048.0)
+            lin("S", A("fo" + s, 128, 256), IX("fo" + s, 0, 128, "rev", 8, 16))
+        dma("S", H("ys", al, slice(l0, l0 + 128)), A("fo" + s, 128, 256, part=slice(0, 128, 16)), 4096)
     return ops
 
 
-def place(order, before, eng, hold, first):
-    busy, st = {}, {}
-    for i in order:
-        t = first[i]
-        for j, d in before[i]:
-            t = max(t, st[j] + d)
-        if eng[i] != "R":
-            b = busy.setdefault(eng[i], [])
+def first_order(ops):
+    n = len(ops)
+    tail = [0.0] * n
+    for i in range(n - 1, -1, -1):
+        o = ops[i]
+        tail[i] += LAT_R if o["kind"] == "r" else o["cost"]
+        for j in o["deps"]:
+            tail[j] = max(tail[j], tail[i] + LAT_X)
+    tail = [tail[i] + (OPT["lead"] if o["tag"][1] == 0 and 0 <= o["tag"][0] < STEPS else 0) for i, o in enumerate(ops)]
+    for i in range(n - 1, -1, -1):
+        for j in ops[i]["deps"]:
+            tail[j] = max(tail[j], tail[i] + 1)
+    busy, st, end = {}, {}, {}
+    for i in sorted(range(n), key=lambda i: (-tail[i], i)):
+        o = ops[i]
+        t = max([end[j] + LAT_X for j in o["deps"]] or [0.0])
+        hold = 60 if o["kind"] == "d" else o["cost"]
+        if o["kind"] != "r":
+            b = busy.setdefault(o["eng"], [])
             k = len(b)
             while k and b[k - 1][1] > t:
                 k -= 1
-            while k < len(b) and b[k][0] < t + hold[i]:
+            while k < len(b) and b[k][0] < t + hold:
                 t = max(t, b[k][1])
                 k += 1
-            b.insert(k, (t, t + hold[i]))
-        st[i] = t
-    return st
+            b.insert(k, (t, t + hold))
+        st[i], end[i] = t, t + (LAT_R if o["kind"] == "r" else o["cost"])
+    return sorted(range(n), key=lambda i: (st[i], i))
 
 
-def issue_order(ops, shift=None, rounds=3):
-    n = len(ops)
+def improve(ops, seq):
+    n, tries = len(ops), OPT["tries"]
     eng = [o["eng"] for o in ops]
     lat = [LAT_R if o["kind"] == "r" else o["cost"] for o in ops]
     hold = [60 if o["kind"] == "d" else o["cost"] for o in ops]
-    pred, succ = [[] for _ in ops], [[] for _ in ops]
+    other = [o["alt"][:2] if o["alt"] else None for o in ops]
+    keep, anc, succ = [], [], [[] for _ in ops]
     for i, o in enumerate(ops):
-        for j, w in o["deps"].items():
-            gap = (LAT_S if eng[j] == eng[i] else LAT_X) if w else 0
-            pred[i].append((j, lat[j] + gap))
-            succ[j].append((i, hold[i] + gap + lat[j] - hold[j]))
-    tail = [0.0] * n
-    for i in range(n - 1, -1, -1):
-        tail[i] = max([tail[j] + d - hold[j] + hold[i] for j, d in succ[i]] or [lat[i]])
-    if shift:
-        tail = [tail[i] + shift(ops[i]) for i in range(n)]
-        for i in range(n - 1, -1, -1):
-            tail[i] = max([tail[i]] + [tail[j] + 1 for j, d in succ[i]])
-    order = sorted(range(n), key=lambda i: (-tail[i], i))
-    best = None
-    for r in range(rounds):
-        st = place(order, pred, eng, hold, [0.0] * n)
-        end = max(st[i] + lat[i] for i in range(n))
-        if best is None or end < best[0]:
-            best = (end, sorted(range(n), key=lambda i: (st[i], i)))
-        late = place(sorted(range(n), key=lambda i: (-st[i] - lat[i], -i)), succ, eng, hold, [lat[i] - hold[i] for i in range(n)])
-        order = sorted(range(n), key=lambda i: (-late[i] - hold[i], i))
-    return best
+        a, k = 0, []
+        for j in sorted(o["deps"], reverse=True):
+            if not (a >> j) & 1:
+                k.append(j)
+                succ[j].append(i)
+            a |= anc[j] | (1 << j)
+        anc.append(a)
+        keep.append(k)
+
+    def waits(i):
+        return [(j, lat[j] + ((LAT_S if eng[j] == eng[i] else LAT_X) if ops[i]["deps"][j] else 0)) for j in keep[i]]
+    pred = [waits(i) for i in range(n)]
+    order = list(seq)
+    prev, nxt, last = [None] * n, [None] * n, {}
+
+    def link(*row):
+        for a, b in zip(row, row[1:]):
+            if a is not None:
+                nxt[a] = b
+            if b is not None:
+                prev[b] = a
+    for i in order:
+        if eng[i] != "R":
+            link(last.get(eng[i]), i)
+            last[eng[i]] = i
+    st, why = [0.0] * n, [None] * n
+
+    def starts(k0):
+        for i in order[k0:]:
+            p = prev[i]
+            t, w = (0.0, None) if p is None else (st[p] + hold[p], p)
+            for j, d in pred[i]:
+                if st[j] + d >= t:
+                    t, w = st[j] + d, -1 - j
+            st[i], why[i] = t, w
+        return max(st[e] + lat[e] for e in ends)
+
+    def hand(i):
+        link(prev[i], nxt[i])
+        (eng[i], lat[i]), other[i] = other[i], (eng[i], lat[i])
+        hold[i] = lat[i]
+        a = b = pos[i]
+        while a >= 0 and (order[a] == i or eng[order[a]] != eng[i]):
+            a -= 1
+        while b < n and (order[b] == i or eng[order[b]] != eng[i]):
+            b += 1
+        link(order[a] if a >= 0 else None, i, order[b] if b < n else None)
+        for e in [i] + succ[i]:
+            pred[e] = waits(e)
+    ends = [i for i in range(n) if ops[i]["tag"][0] == 99]
+    cur = starts(0)
+    best, x, moves = (cur, list(order), list(eng)), 1, []
+    pos = {i: k for k, i in enumerate(order)}
+    for it in range(tries):
+        if not moves:
+            i = max(ends, key=lambda e: st[e] + lat[e])
+            while why[i] is not None:
+                w = why[i]
+                if w >= 0 and not (anc[i] >> w) & 1:
+                    moves.append((w, i))
+                if other[i]:
+                    moves.append((i, i))
+                i = w if w >= 0 else -1 - w
+        x = (x * 1103515245 + 12345) % 2147483648
+        j, i = moves[x * len(moves) >> 31]
+        a, b = pos[j], pos[i]
+        seg = order[a:b + 1]
+        old = st[:], why[:]
+        if i == j:
+            hand(i)
+            while a and order[a - 1] != prev[i] and prev[i] is not None:
+                a -= 1
+        else:
+            mark = {i}
+            for e in reversed(seg):
+                if e in mark:
+                    mark.update(keep[e])
+                    if e != i:
+                        mark.add(prev[e])
+            if j in mark:
+                moves.remove((j, i))
+                continue
+            p, q = prev[j], nxt[i]
+            link(p, i, j, q)
+            order[a:b + 1] = [e for e in seg if e in mark] + [e for e in seg if e not in mark]
+        new = starts(a)
+        x = (x * 1103515245 + 12345) % 2147483648
+        if new <= cur or x / 2147483648.0 < math.exp((cur - new) / (OPT["temp"] * (1 - it / tries) + 1)):
+            cur, moves = new, []
+            for k in range(a, b + 1):
+                pos[order[k]] = k
+            if cur < best[0]:
+                best = (cur, list(order), list(eng))
+        else:
+            if i == j:
+                hand(i)
+            else:
+                order[a:b + 1] = seg
+                link(p, j, i, q)
+            st[:], why[:] = old
+    for o, e in zip(ops, best[2]):
+        if e != o["eng"]:
+            (o["eng"], o["cost"], o["call"]), o["alt"] = o["alt"], (o["eng"], o["cost"], o["call"])
+    return best[:2]
 
 
-OPT.update({'mode': 'PVPVPVPV', 'fev': 'SVSVSVSS', 'gav': ((0, 0, 0, 1), (0, 1, 0, 1)), 'eng': {'h161': 'V', 'fsel0': 'S', 'ou81': 'S', 'ou161': 'S', 'lh0': 'S', 'w30': 'V', 'hrow0': 'V', 'ou241': 'V', 'ou160': 'V', 'hu0': 'S', 'lu10': 'V', 'lu00': 'S', 'ou240': 'S', 'lh1': 'V'}})
-SHIFT = {(0, 'd0'): 4000, (0, 'd1'): 4250, (0, 'd2'): 3750, (0, 'd3'): 4250, (0, 'f0'): 3000, (0, 'f1'): 3750, (0, 'far'): 250, (0, 'flip'): 5000, (0, 'key'): 5500, (0, 'list'): -7500, (0, 'n1'): -6000, (0, 'n3'): -7250, (0, 'near'): -4000, (0, 'pick'): -5500, (0, 'send'): 6000, (0, 'u0'): 1250, (0, 'u1'): 4250, (0, 'win'): -6000, (1, 'd0'): -5500, (1, 'd1'): -3000, (1, 'd2'): -8000, (1, 'd3'): 1000, (1, 'f0'): 1500, (1, 'f1'): -500, (1, 'far'): 4250, (1, 'flip'): 750, (1, 'key'): -5750, (1, 'list'): -3750, (1, 'n1'): -4000, (1, 'n3'): 3750, (1, 'near'): 2500, (1, 'pick'): 6250, (1, 'send'): -500, (1, 'u0'): 1500, (1, 'u1'): -6000, (1, 'win'): -7500, (9, 'close'): -1000, (1, 's'): -4000, (0, 's'): 250}
-OPT.update({'mode': 'PVPVPVPV', 'fev': 'SSSSSSSS', 'gav': ((0, 0, 0, 1), (0, 1, 0, 0), (0, 1, 0, 1), (1, 0, 0, 1), (2, 0, 0, 1), (3, 0, 0, 1)), 'eng': {'h161': 'V', 'fsel0': 'S', 'ou81': 'V', 'ou161': 'S', 'lh0': 'S', 'w30': 'S', 'hrow0': 'V', 'ou241': 'V', 'ou160': 'S', 'hu0': 'V', 'lu10': 'V', 'lu00': 'S', 'ou240': 'V', 'lh1': 'V', 'new1': 'S', 'new0': 'S', 'far0': 'V'}})
-SHIFT = {(0, 'd0'): 4250, (0, 'd1'): 4500, (0, 'd2'): 3750, (0, 'd3'): 3750, (0, 'f0'): 4500, (0, 'f1'): 4250, (0, 'far'): -2250, (0, 'flip'): 5250, (0, 'key'): 7000, (0, 'list'): -7750, (0, 'n1'): -4000, (0, 'n3'): 3000, (0, 'near'): -1000, (0, 'pick'): -8000, (0, 'send'): 4500, (0, 'u0'): 1500, (0, 'u1'): 4500, (0, 'win'): 1500, (1, 'd0'): -6000, (1, 'd1'): -6000, (1, 'd2'): -6000, (1, 'd3'): -8000, (1, 'f0'): 1250, (1, 'f1'): -1250, (1, 'far'): -7000, (1, 'flip'): 1000, (1, 'key'): -2000, (1, 'list'): -6750, (1, 'n1'): -7750, (1, 'n3'): 2500, (1, 'near'): -3500, (1, 'pick'): 5500, (1, 'send'): 1250, (1, 'u0'): -3000, (1, 'u1'): -3750, (1, 'win'): -7000, (9, 'close'): -1250, (1, 's'): 0, (0, 's'): 3250}
 _PLAN = []
 
 
@@ -634,7 +619,7 @@ def rank_program(g, core, T, topo):
         return
     if not _PLAN:
         ops = plan()
-        _PLAN.append((ops, issue_order(ops, lambda o: SHIFT.get(o["tag"][1:], 0), 2)[1]))
+        _PLAN.append((ops, improve(ops, first_order(ops))[1]))
     ops, seq = _PLAN[0]
     N = len(T.cores)
     nxt, prv = T.cores[(rank + 1) % N], T.cores[(rank - 1) % N]
@@ -654,6 +639,8 @@ def rank_program(g, core, T, topo):
         p = a[5] if a[5] is not None else slice(None)
         if a[4] == 1:
             return T[a[1]][p, a[2]:a[3]]
+        if a[4] < 0:
+            return T[a[1]][p, a[3] - 1:(a[2] - 1 if a[2] else None):a[4]]
         return T[a[1]][p, a[2]:a[3]:a[4]]
 
     needed = set()

@@ -12,7 +12,17 @@ OPT = dict(
     lead=3000.0,
     tries=200000,
     temp=250.0,
-    neg=True,
+    share=(1, 1, 1, 1),
+    seed=1,
+    run=40,
+    lazy=4,
+    shift={},
+    gs=((), ()),
+    cross=False,
+    big=9999,
+    far=3,
+    dflip=True,
+    free=5,
 )
 C = 8
 Q0 = (8, 0)
@@ -28,14 +38,14 @@ def _sb(name, n, d):
 
 
 for _n, _w, _d in [
-    ("xs", 4096, BF), ("vs", 8208, BF), ("ctab", 4112, F32), ("lan", 256, I32), ("s0w", 256, I32), ("wti", 8, I32),
+    ("xs", 4096, BF), ("vs", 4224, BF), ("ctab", 4240, F32), ("lan", 256, I32), ("s0w", 256, I32), ("wti", 8, I32),
     ("srow", 256, BF), ("ci", 16, I32), ("cf", 32, F32), ("t0", 144, F32), ("t1", 256, F32), ("t2", 384, F32),
     ("t3", 256, F32), ("ti", 8, I32), ("tj", 32, I32), ("tn", 128, BF), ("idb", 128, BF), ("idh", 128, F16),
     ("nid", 128, BF), ("c31", 128, BF), ("n31", 128, BF), ("c43", 128, BF), ("n43", 128, BF), ("i19", 128, BF),
     ("one", 480, BF), ("blk", 128, BF), ("sel", 144, BF), ("selk", 144, F16), ("selw", 144, BF), ("selb", 144, BF),
     ("wm", 128, F16), ("wme", 128, F16), ("nwm", 128, F16), ("wx", 128, F16), ("pcol", 16, BF), ("pa", 2048, F16),
-    ("ta", 128, BF), ("tb", 128, BF), ("tc", 64, BF), ("mtab", 128, F32), ("rst", 120, F32), ("ltl", 8, U16),
-    ("revl", 16, U16), ("rev", 16, U16), ("ends", 8, U16), ("val", 8, F16), ("lst", 8, F32), ("tri", 272, BF),
+    ("ta", 128, BF), ("tb", 128, BF), ("tc", 96, BF), ("mtab", 128, F32), ("rst", 120, F32), ("ltl", 8, U16),
+    ("ends", 8, U16), ("val", 8, BF), ("lst", 8, F32), ("tri", 272, BF),
     ("hrow", 272, F16), ("win", 16, BF), ("fsel", 256, BF), ("thr", 8, BF), ("hc", 32, F16), ("aq", 16, BF),
     ("ay", 8, F32), ("aj", 16, F32),
 ]:
@@ -44,22 +54,28 @@ for _h in range(2):
     for _n, _w, _d in [
         ("ld", 256, I32), ("lu", 128 * STEPS, U16), ("su", 128 * STEPS, U16), ("home", 256, F32), ("lh", 128, F16),
         ("a", 2048, BF), ("at", 2048, F16), ("q", 1920, BF), ("f", 1920, BF), ("d", 1920, F16), ("ab", 1920, F16),
-        ("cl", 1920, BF), ("lall", 2064, F32), ("w4", 256, F16), ("w2", 256, I32), ("w3", 384, BF), ("hu", 128, U16),
+        ("cl", 1920, BF), ("lall", 1088, I32), ("w4", 256, F16), ("w2", 256, I32), ("w3", 384, BF), ("hu", 128, U16),
         ("sc", 240, I32), ("k", 48, I32), ("m", 64, F32), ("ou", 64, U16), ("eq", TOT[_h], BF), ("es", TOT[_h], BF),
         ("msk", TOT[_h], BF), ("snd", 8 * STEPS, I32), ("rcv", 8 * STEPS, I32), ("fo", 256, F32), ("sl", 16, U16),
+        ("own", 64, I32),
     ]:
         _o = SCRATCH[_n][1][1] if _h else 0
         PART[_n + str(_h)] = (_n, _o, _w)
         _sb(_n, _o + _w + (-_w) % 32, _d)
+for _n in ("dl0", "dl1"):
+    SCRATCH[_n] = ("dram", [8, 1024], I32)
 for _n in ("pt0", "pt1"):
     SCRATCH[_n] = ("psum", [128, 1024], BF)
-for _n in ("px0", "px1", "px2", "pu", "pn", "pf"):
+for _n in ("px0", "px1", "px2"):
+    SCRATCH[_n] = ("psum", [128, 32, 16], F32)
+for _n in ("pu", "pn", "pf"):
     SCRATCH[_n] = ("psum", [128, 512], F32)
+HALF_ROWS = 0
 
-SEMAPHORES = ["sv", "sa", "sp", "sg", "gone"] + ["dm%d" % i for i in range(40)] + ["arr%d" % i for i in range(4 * STEPS)]
+SEMAPHORES = ["sv", "sa", "sp", "sg", "gone"] + ["dm%d" % i for i in range(70)] + ["arr%d" % i for i in range(4 * STEPS)]
 
 CYC, PCYC = 1.04, 0.56
-LAT_X, LAT_S, LAT_R = 130.0, 90.0, 3000.0
+LAT_X, LAT_S, LAT_R = 130.0, 90.0, 2600.0
 SIZE = {F32: 4, I32: 4, BF: 2, F16: 2, U16: 2}
 
 
@@ -76,6 +92,8 @@ def IX(name, lo, hi, off, c, d):
 def count(a):
     if a[0] == "I":
         return 16 * (a[6] - a[5])
+    if a[4] == HALF_ROWS:
+        return 120
     return len(range(a[2], a[3], abs(a[4])))
 
 
@@ -201,32 +219,24 @@ def plan():
     iota(A("s0w"), [[0, 256]], 0, 0)
     dma("Y", A("wti", 0, 1), H("wt", al, al), 512)
     dma("Y", A("s0w", part=slice(0, 128, 16)), H("s0", al, al), 8192)
-    dma("Y", A("vs", 0, ROT), H("v", al, slice(4096 - ROT, 4096)), 700000, first)
-    dma("Y", A("vs", ROT, 4096), H("v", al, slice(0, 4096 - ROT)), 700000, first)
+    dma("Y", A("vs", 128, 128 + ROT), H("v", al, slice(4096 - ROT, 4096)), 700000, first)
+    dma("Y", A("vs", 128 + ROT, 4224), H("v", al, slice(0, 4096 - ROT)), 700000, first)
 
     iota(col("ci", 0), [[0, 1]], 0, 1)
-    for h in range(2):
-        iota(A("tj", Q0[h], Q0[h] + C), [[-1, 2], [-32, C // 2]], 255 - 16 * Q0[h], -2)
-    iota(A("tj", 16, 32), [[-16, 16]], 255, -1)
+    iota(A("t3", 136, 144), [[3840, 2], [944, 4]], -128, 0)
     iota(A("t0"), [[1, 144]], 0, 0)
-    iota(A("tn"), [[1, 128]], 128, 0)
     iota(A("t1", 0, 128), [[1, 16], [0, 8]], 0, 0)
     iota(A("t1", 128, 256), [[0, 16], [1, 8]], 0, 0)
     iota(A("t3", 0, 128), [[1, 8], [0, 16]], 0, 0)
     iota(A("mtab", 0, 120), [[0, 8], [1, 15]], 1, 0)
     iota(A("mtab", 120, 128), [[0, 8]], 0, 0)
     iota(A("t3", 128, 136), [[16, 8]], 0, 0)
-    iota(A("ctab"), [[1, 4112]], -2048, 0)
+    iota(A("ctab"), [[1, 4240]], -2176, 0)
     ts(col("ci", 1), col("ci", 0), 15, ALU.bitwise_and)
     ts(col("ci", 2), col("ci", 0), 4, ALU.arith_shift_right)
     ts(col("ci", 3), col("ci", 0), 7, ALU.bitwise_and)
-    ts(col("ci", 4), col("ci", 0), 14, ALU.bitwise_and)
-    cp(A("cf", 0, 5), A("ci", 0, 5))
-    P_, J_, G_, J8, J14 = (col("cf", j) for j in range(5))
-    lin("S", col("cf", 17), G_, 32.0)
-    lin("S", col("cf", 6), G_, 16.0)
-    lin("V", A("revl"), A("tj", 0, 16), 1.0, col("cf", 17))
-    lin("V", A("rev"), A("tj", 16, 32), 1.0, col("cf", 6))
+    cp(A("cf", 0, 4), A("ci", 0, 4))
+    P_, J_, G_, J8 = (col("cf", j) for j in range(4))
     ts(A("idb"), A("t0", 0, 128), P_, ALU.is_equal)
     ts(A("t2", 0, 128), A("t1", 0, 128), J_, ALU.subtract, 2.0 ** -10, ALU.max)
     ts(A("t2", 128, 256), A("t1", 0, 128), J_, ALU.is_lt, J_, ALU.mult)
@@ -247,7 +257,7 @@ def plan():
     lin("S", A("sel"), A("selb"), 2.0 ** 16)
     lin("S", A("selk"), A("selb"), 1024.0)
     ts(col("cf", 16), J_, 8.0, ALU.is_ge, 65280.0, ALU.mult)
-    lin("S", A("tc"), A("one", 0, 64), 256.0, col("cf", 16))
+    lin("S", A("tc"), A("one", 0, 96), 256.0, col("cf", 16))
     lin("S", A("ta", 0, 120), A("t0", 0, 120), 4096.0, 2048.0)
     lin("S", A("tb", 0, 120), A("mtab", 0, 120), 64.0, 12288.0)
     ts(A("blk"), A("t3", 0, 128), G_, ALU.is_equal)
@@ -256,16 +266,16 @@ def plan():
     lin("S", col("cf", 9), J_, 1.0 / 15.0, 0.5 / 15.0 - 0.5)
     lin("S", A("ti"), A("t3", 128, 136), 1.0 / 15.0, col("cf", 9))
     ts(A("ltl"), A("ti"), C - 1.0, ALU.min)
-    lin("S", col("cf", 11), G_, 16.0, 128.0)
-    lin("S", A("pcol"), A("t2", 256, 384, 8), 1.0, col("cf", 11))
-    for m in range(16):
-        ts(A("pa", 128 * m, 128 * m + 128), A("tn"), col("pcol", m), ALU.is_equal)
-    lin("S", col("cf", 12), J_, 8.0, 1032.0)
-    lin("S", A("val"), A("t3", 128, 136), 8.0, col("cf", 12))
-    lin("S", col("cf", 10), J14, -0.5)
-    lin("S", A("lst"), A("t3", 128, 136), 59.5, col("cf", 10))
-    ts(A("tri", 0, 16), A("t0", 0, 16), J_, ALU.is_gt, 4096.0, ALU.mult)
-    lin("S", A("tri", 16, 272), A("one", 0, 256), 4096.0)
+    if not OPT["dflip"]:
+        iota(A("tn"), [[1, 128]], 128, 0)
+        lin("S", col("cf", 11), G_, 16.0, 128.0)
+        lin("S", A("pcol"), A("t2", 256, 384, 8), 1.0, col("cf", 11))
+        for m in range(16):
+            ts(A("pa", 128 * m, 128 * m + 128), A("tn"), col("pcol", m), ALU.is_equal)
+    lin("S", A("val"), A("t3", 128, 136), 1.0, J_)
+    ts(A("lst"), A("t3", 136, 144), J_, ALU.subtract)
+    ts(A("tri", 0, 16), A("t0", 0, 16), J_, ALU.is_le, 8192.0, ALU.mult)
+    lin("S", A("tri", 16, 272), A("one", 0, 256), 0.0)
     lin("S", A("hrow", 256, 272), A("one", 0, 16), 2048.0)
     for h in range(2):
         s = str(h)
@@ -274,9 +284,8 @@ def plan():
         lin("S", A("ends", 2 * h, 2 * h + 1), col("cf", 22 + h), 1.0, -1.0)
         for q in range(C):
             o = sum(SEG[h][:q])
-            dma("Y", A("msk" + s, o, o + SEG[h][q]), A("tri", 0, SEG[h][q]), 60000, first)
-        iota(A("lall" + s, 960, 2064), [[0, 1104]], 0, 0)
-    lin("S", A("srow"), IX("s0w", 0, 256, "rev", 0, 16))
+            ts(A("msk" + s, o, o + SEG[h][q]), A("tri", 0, SEG[h][q]), col("val", q), ALU.max)
+    lin("S", A("srow"), A("s0w", 0, 256, -1))
     mm(group(A("pn", 0, 16), [(selj("selb", j), A("srow", j, 256, 16)) for j in range(16)]))
     for h in range(2):
         lin("S", A("rcv%d" % h, 0, C), A("pn", Q0[h], Q0[h] + C))
@@ -290,7 +299,7 @@ def plan():
     def close_step(t):
         tag[:] = [t, 9, "close"]
         for h in range(2):
-            cp(IX("vs", 0, 8208, "ou%d" % h, 16, 24), A("fsel", 16 * Q0[h], 16 * Q0[h] + 128))
+            cp(IX("vs", 0, 4224, "ou%d" % h, 32, 40), A("fsel", 16 * Q0[h], 16 * Q0[h] + 128))
         if t < STEPS - 1:
             mm(group(A("pn", 256, 272), [(A("blk"), A("win"))]))
             act(A("aj"), A("pn", 256, 272), scale=-1.0, bias=48.40625, accum=col("ay", 0))
@@ -303,31 +312,28 @@ def plan():
         w2, w3, w4 = "w2" + s, "w3" + s, "w4" + s
         tag[:] = [t, h, "list"]
         if t == 0:
-            lin("V", A("ld" + s, 0, 128), IX("lan", 0, 256, "revl", Q0[h], Q0[h] + C))
-            lin("V", A("lu" + s, 0, 128), A("ld" + s, 0, 128))
+            lin("V", A("lu" + s, 0, 128), A("lan", 128 * h, 128 * h + 128, -1))
         for pc in range(2):
-            tag[:] = [t, h, "f%d" % pc]
-            rot[1] += 1
-            pt = "pt%d" % (rot[1] % 2)
-            for b in range(2):
-                c0 = l0 + 64 * b + 32 * pc
-                o = 1024 * pc + 512 * b
-                lin("S", A("a" + s, o, o + 512), IX("xs", 0, 4096, "lu" + s, c0, c0 + 32))
-                lst = [("T", A(pt, 256 * i + 128 * b, 256 * i + 128 * b + 128), A("a" + s, o + 128 * i, o + 128 * i + 128))
-                       for i in range(4)]
-                add("P", 512 * PCYC, ("tr", lst), [m[2] for m in lst] + [A("idb")], [m[1] for m in lst])
             mode = OPT["mode"][4 * h + 2 * pc:4 * h + 2 * pc + 2]
             for u in range(2):
-                ts(A("at" + s, 1024 * pc + 512 * u, 1024 * pc + 512 * u + 512), A(pt, 512 * u, 512 * u + 512),
-                   272.0 if mode[u] == "P" else 288.0, ALU.add)
-            for u in range(2):
+                tag[:] = [t, h, "f%d" % (2 * pc + u)]
+                rot[1] += 1
+                pt = "pt%d" % (rot[1] % 2)
+                c0 = l0 + 64 * pc + 32 * u
+                o = 1024 * pc + 512 * u
+                cuts = (0, 16, 32) if 2 * pc + u in OPT["g2"] else (0, 32)
+                for a, b in zip(cuts, cuts[1:]):
+                    lin("S", A("a" + s, o + 16 * a, o + 16 * b), IX("xs", 0, 4096, "lu" + s, c0 + a, c0 + b))
+                lst = [("T", A(pt, 128 * i, 128 * i + 128), A("a" + s, o + 128 * i, o + 128 * i + 128)) for i in range(4)]
+                add("P", 512 * PCYC, ("tr", lst), [m[2] for m in lst] + [A("idb")], [m[1] for m in lst])
+                lin("V", A("at" + s, o, o + 512), A(pt, 0, 512), 1.0, 272.0 if mode[u] == "P" else 288.0)
                 o = 480 * (2 * pc + u)
                 bk = xbank()
 
                 def blocks(w, first, last):
-                    return [(A(bk, 240 * (i // 2) + i % 2, 240 * (i // 2) + 240, 2),
+                    return [(A(bk, 240 * (i // 2) + 8 * (i % 2), 240 * (i // 2) + 240, HALF_ROWS),
                              A("at" + s, 1024 * pc + 512 * u + 128 * i, 1024 * pc + 512 * u + 128 * i + 128), A(w, 8, 128),
-                             first, first or (last and i == 3)) for i in range(4)]
+                             first and i == 0, last and i == 3) for i in range(4)]
                 if mode[u] == "P":
                     mm([(A(bk, 0, 480), A("c31"), A("one"), True, False)])
                     mm(blocks("wme", False, False) + [(A(bk, 0, 480), A("n31"), A("one"), False, False)] + blocks("nwm", False, True))
@@ -335,21 +341,40 @@ def plan():
                 else:
                     mm(blocks("wm", True, True))
                     lin("S", A("q" + s, o, o + 480), A(bk, 0, 480), 1.0, -127.5)
-                    tt(A("f" + s, o, o + 480), A(bk, 0, 480), A("q" + s, o, o + 480), ALU.subtract)
-            tag[:] = [t, h, "u%d" % pc]
-            a, b = 60 * pc, 60 * pc + 60
-            mm(group(A("pu", a, b), [(A("blk"), A("tc", 0, 60))] +
-                     [(selj("selw", j), A("f" + s, 960 * pc + j, 960 * pc + 960, 16)) for j in range(16)]))
-            lin("S", A(w3, 128 + a, 128 + b), A("pu", a, b), 1.0, 0.5)
-            tt(A(w4, a, b), A("pu", a, b), A(w3, 128 + a, 128 + b), ALU.subtract)
-            act(A(w2, a, b), A(w4, a, b), AF.Square, bias=2640.0)
-            ts(A(w2, 128 + a, 128 + b), A(w2, a, b), 5, ALU.arith_shift_right, 4095, ALU.bitwise_and)
-            lin("V", A("hu" + s, a, b), A(w2, 128 + a, 128 + b))
+                    if mode[u] == "V":
+                        tt(A("f" + s, o, o + 480), A(bk, 0, 480), A("q" + s, o, o + 480), ALU.subtract)
+                    else:
+                        mm([(A(bk, 0, 480), A("nid"), A("q" + s, o, o + 480), False, True)])
+                        lin("S", A("f" + s, o, o + 480), A(bk, 0, 480))
+                if 2 * pc + u + 1 not in OPT["up"]:
+                    continue
+                n = OPT["up"].index(2 * pc + u + 1)
+                tag[:] = [t, h, "u%d" % n]
+                a, b = 30 * OPT["up"][n - 1], 30 * OPT["up"][n]
+                mm(group(A("pu", a, b), [(A("blk"), A("tc", 0, b - a))] +
+                         [(selj("selw", j), A("f" + s, 16 * a + j, 16 * b, 16)) for j in range(16)]))
+                lin("S", A(w3, 128 + a, 128 + b), A("pu", a, b), 1.0, 0.5)
+                tt(A(w4, a, b), A("pu", a, b), A(w3, 128 + a, 128 + b), ALU.subtract)
+                act(A(w2, a, b), A(w4, a, b), AF.Square, bias=2640.0)
+                ts(A(w2, 128 + a, 128 + b), A(w2, a, b), 5, ALU.arith_shift_right, 4095, ALU.bitwise_and)
+                lin("V", A("hu" + s, a, b), A(w2, 128 + a, 128 + b))
         tag[:] = [t, h, "key"]
         tt(A(w3, 0, 128), IX("rcv" + s, 8 * t, 8 * t + 8, "ltl", 0, 8), A("mtab"), ALU.is_gt)
         lin("S", A(w4, 128, 248), A("hu" + s, 0, 120), 1.0, -2048.0)
         lin("S", A(w3, 256, 376), A(w4, 0, 120), 1.0, 12288.0 - 31.5)
         tag[:] = [t, h, "flip"]
+        if OPT["dflip"]:
+            lall = "lall" + s
+            lin("S", A("own" + s), A("lu" + s, l0 + 64, l0 + 128), 4096.0)
+            tt(A(lall, 0, 64), A("own" + s), A("lu" + s, l0, l0 + 64), ALU.add)
+            dma("Y", A("dl" + s), A(lall, 0, 64), 270000)
+            for w in (64, 256):
+                add("Y", 3500, ("dmas", [(A(lall, w * i, w * i + w), A(lall, 0, w)) for i in (1, 2, 3)]),
+                    [A(lall, 0, w)], [A(lall, w, 4 * w)], kind="d")
+            moves = [(A(lall, 64 * max(k, 1) + 64, 1088, part=slice(k, 128, 16)), A("dl" + s, 64 * (k == 0), 1024 - 64 * k))
+                     for k in range(16)]
+            add("Y", 6000, ("dmas", moves), [A("dl" + s)], [A(lall, 128, 1088)], kind="d")
+            return
         lin("S", A("lh" + s, 0, 64), A("lu" + s, l0, l0 + 64), 1.0 / 4096, -0.5)
         lin("S", A("lh" + s, 64, 128), A("lu" + s, l0 + 64, l0 + 128), 1.0, -2048.0)
         for bi in range(2):
@@ -361,10 +386,10 @@ def plan():
                                                           (A("pa", 128 * m, 128 * m + 128), A("lh" + s, 64, 128))])
             mm(lst)
             n = 512 - 64 * bi
-            lin("S", A("lall" + s, 512 * bi, 512 * bi + n), A(bk, 0, n), 4096.0, 2048.0 * 4097)
+            lin("S", A("lall" + s, 128 + 512 * bi, 128 + 512 * bi + n), A(bk, 0, n), 4096.0, 2048.0 * 4097)
             if bi:
                 for e in range(2):
-                    lin("S", A("lall" + s, 1032 + 8 * e, 2056, 16), A(bk, n, 512), 4096.0, 2048.0 * 4097)
+                    lin("S", A("lall" + s, 64 * e, 64 * e + 64), A(bk, n, 512), 4096.0, 2048.0 * 4097)
 
     def send(sem, src, dst):
         sent = add("G", 300, ("send", "arr%d" % sem, 0, src, dst), [src], [], kind="s")
@@ -376,19 +401,33 @@ def plan():
         w3, w4, k, m_, ou, ld = "w3" + s, "w4" + s, "k" + s, "m" + s, "ou" + s, "ld" + s
         tag[:] = [t, h, "pre"]
         mm(group(A("pn", 0, 120), [(A("c43"), A("one", 0, 120))], last=False))
-        mm(group(A("pf", 0, 120), [(A("idb"), A("tb", 0, 120)), (A("idh"), A(w4, 0, 120)), (A("nid"), A(w3, 256, 376))], last=False))
         for pi in range(4):
             tag[:] = [t, h, "d%d" % pi]
             o = 480 * pi
-            tt(A("d" + s, o, o + 480), IX("vs", 0, 4096, "hu" + s, 30 * pi, 30 * pi + 30), A("f" + s, o, o + 480), ALU.subtract)
-            act(A("ab" + s, o, o + 480), A("d" + s, o, o + 480), AF.Abs)
-            ts(A("cl" + s, o, o + 480), A("ab" + s, o, o + 480), col("thr", 0), ALU.is_le, -3.5 / 16, ALU.add)
+            marks = IX("vs", 128, 4224, "hu" + s, 30 * pi, 30 * pi + 30)
+            if pi in OPT["gs"][h]:
+                lin("S", A("q" + s, o, o + 480), marks)
+                mm(group(A("pf", 0, 480), [(A("idb"), A("q" + s, o, o + 480)), (A("nid"), A("f" + s, o, o + 480))]))
+                act(A("ab" + s, o, o + 480), A("pf", 0, 480), AF.Abs)
+                ts(A("cl" + s, o, o + 480), A("ab" + s, o, o + 480), col("thr", 0), ALU.is_le, -3.5 / 16, ALU.add)
+            else:
+                cuts = (0, 16, 30) if pi in OPT["ds"] else (0, 30)
+                for a, b in zip(cuts, cuts[1:]):
+                    marks = IX("vs", 128, 4224, "hu" + s, 30 * pi + a, 30 * pi + b)
+                    a, b = o + 16 * a, o + 16 * b
+                    tt(A("d" + s, a, b), marks, A("f" + s, a, b), ALU.subtract)
+                    act(A("ab" + s, a, b), A("d" + s, a, b), AF.Abs)
+                    ts(A("cl" + s, a, b), A("ab" + s, a, b), col("thr", 0), ALU.is_le, -3.5 / 16, ALU.add)
             if pi % 2:
                 c0, c1, o = 30 * pi - 30, 30 * pi + 30, o - 480
                 tag[:] = [t, h, "n%d" % pi]
                 mm(group(A("pn", c0, c1), [(selj("sel", j), A("cl" + s, o + j, o + 960, 16)) for j in range(16)], False, False))
-                tag[:] = [t, h, "r%d" % pi]
-                mm(group(A("pf", c0, c1), [(selj("selk", j), A("ab" + s, o + j, o + 960, 16)) for j in range(16)], False, pi == 3))
+        tag[:] = [t, h, "pre"]
+        mm(group(A("pf", 0, 120), [(A("idb"), A("tb", 0, 120)), (A("idh"), A(w4, 0, 120)), (A("nid"), A(w3, 256, 376))], last=False))
+        for pc in range(2):
+            tag[:] = [t, h, "r%d" % pc]
+            mm(group(A("pf", 60 * pc, 60 * pc + 60), [(selj("selk", j), A("ab" + s, 960 * pc + j, 960 * pc + 960, 16)) for j in range(16)],
+                     False, pc == 1))
         tag[:] = [t, h, "near"]
         mm(group(A("pn", 0, 120), [(A("n43"), A("one", 0, 120)), (A("idb"), A("ta", 0, 120)), (A("idh"), A(w4, 128, 248)),
                                    (A("i19"), A(w3, 0, 120))], first=False))
@@ -400,42 +439,34 @@ def plan():
         tt(A(m_, 24, 32), A("rcv" + s, 8 * t, 8 * t + 8), A(k, 32, 40), ALU.subtract)
         tag[:] = [t, h, "pick"]
         ts(A(k, 16, 24), k1, 0x100FFF, ALU.bitwise_and)
-        ts(A(ou, 0, 8), A(k, 16, 24), 4096.0, ALU.min)
-        lin("S", A("hrow", B, B + 128), IX("ctab", 0, 4112, ou, 0, 8))
+        ts(A(ou, 0, 8), A(k, 16, 24), 4096.0, ALU.min, 128.0, ALU.add)
+        lin("S", A("hrow", B, B + 128), IX("ctab", 0, 4240, ou, 0, 8))
         hi = 16 * h
-        lin("V", A("hc", hi, hi + 8), A(ou, 0, 8), 1.0, -2048.0)
+        ts(A("hc", hi, hi + 8), A(k, 16, 24), 4096.0, ALU.min, -2048.0, ALU.add)
         ts(A(k, 24, 32), k1, 6, ALU.arith_shift_right, 127 * 64, ALU.bitwise_and)
-        lin("S", A(m_, 0, 8), A(ou, 0, 8), 0.25)
-        tt(A(m_, 8, 16), A(k, 24, 32), A("lst"), ALU.subtract)
-        lin("S", A(ou, 8, 16), A(k, 24, 32), 0.25, J_)
-        lin("S", A("fsel", B, B + 128), IX("f" + s, 0, 1920, ou, 8, 16))
+        tt(A(ou, 8, 16), A(k, 24, 32), A("lst"), ALU.subtract)
+        lin("S", A(ou, 16, 24), A(k, 24, 32), 0.25, J_)
+        lin("S", A("fsel", B, B + 128), IX("f" + s, 0, 1920, ou, 16, 24))
         tag[:] = [t, h, "win"]
         for q in range(C):
             o, w = sum(SEG[h][:q]), SEG[h][q]
-            ts(A("eq" + s, o, o + w), A("hrow", 258 - w, 258), col("hc", hi + q), ALU.is_equal, col("val", q), ALU.mult)
-        scan(A("es" + s), A("eq" + s), A("msk" + s), ALU.max, ALU.min)
-        ends = IX("es" + s, 0, TOT[h], "ends", 2 * h, 2 * h + 1)
+            cuts = (0, w - 130, w) if h and OPT["cross"] else (0, w)
+            for a, b in zip(cuts, cuts[1:]):
+                ts(A("eq" + s, o + a, o + b), A("hrow", 258 - w + a, 258 - w + b), col("hc", hi + q), ALU.not_equal, 8192.0, ALU.mult)
+        scan(A("es" + s), A("eq" + s), A("msk" + s), ALU.min, ALU.max)
         tag[:] = [t, h, "send"]
-        tt(A(ou, 32, 48), ends, A(m_, 0, 16), ALU.max)
-        lin("S", A(ld, 128, 256), IX("lall" + s, 0, 2064, ou, 40, 48))
+        tt(A(ou, 32, 48), IX("es" + s, 0, TOT[h], "ends", 2 * h, 2 * h + 1), A(ou, 0, 16), ALU.min)
+        ts(A(ld, 0, 64), IX("lall" + s, 0, 1088, ou, 40, 44), 4095, ALU.bitwise_and)
+        ts(A(ld, 64, 128), IX("lall" + s, 0, 1088, ou, 44, 48), 12, ALU.arith_shift_right)
         if t < STEPS - 1:
-            ts(A(ld, 0, 64), A(ld, 128, 256, 2), 4095, ALU.bitwise_and)
-            ts(A(ld, 64, 128), A(ld, 129, 256, 2), 12, ALU.arith_shift_right)
             lin("V", A("su" + s, 128 * t, 128 * t + 128), A(ld, 0, 128))
             send(2 * t + h, A("su" + s, 128 * t, 128 * t + 128), A("lu" + s, 128 * t + 128, 128 * t + 256))
         else:
-            ts(A(ld, 0, 128, 2), A(ld, 128, 256, 2), 4095, ALU.bitwise_and)
-            ts(A(ld, 1, 128, 2), A(ld, 129, 256, 2), 12, ALU.arith_shift_right)
-            if OPT["neg"]:
-                lin("V", A("home" + s, 0, 128), A(ld, 0, 128, -1))
-            else:
-                lin("V", A("home" + s, 0, 128), IX(ld, 0, 128, "rev", 8, 16))
+            lin("V", A("home" + s, 0, 128), A(ld, 0, 128, -1))
             send(2 * t + h, A("home" + s, 0, 128), A("home" + s, 128, 256))
         tag[:] = [t, h, "s"]
-        tt(A(m_, 32, 48), ends, A(m_, 0, 16), ALU.max)
-        lin("S", A(ou, 16, 24), A(m_, 32, 40), 4.0)
         wn = A("win", Q0[h], Q0[h] + C)
-        ts(wn, A(m_, 32, 40), 1024.5, ALU.is_lt)
+        ts(wn, A(ou, 32, 40), 127.5, ALU.is_gt)
         tt(A(m_, 48, 56), A(m_, 24, 32), wn, ALU.mult)
         src, dst = A("snd" + s, 8 * t, 8 * t + 8), A("rcv" + s, 8 * t + 8, 8 * t + 16)
         if t == STEPS - 1:
@@ -453,15 +484,11 @@ def plan():
     cut = [0, 920, 1840, ROT, 4096]
     for k in range(4):
         o = (cut[k] - ROT) % 4096
-        dma("YS"[k % 2], H("yv", al, slice(o, o + cut[k + 1] - cut[k])), A("vs", cut[k], cut[k + 1]), 500000)
+        dma("YS"[k % 2], H("yv", al, slice(o, o + cut[k + 1] - cut[k])), A("vs", 128 + cut[k], 128 + cut[k + 1]), 500000)
     for h in range(2):
         s, l0 = str(h), 128 * h
         dma("Y", H("yl", al, slice(l0, l0 + 128)), A("home" + s, 128, 256), 65536)
-        if OPT["neg"]:
-            lin("S", A("fo" + s, 128, 256, -1), IX("ctab", 0, 4112, "sl" + s, 8, 16), 1.0, 2048.0)
-        else:
-            lin("S", A("fo" + s, 0, 128), IX("ctab", 0, 4112, "sl" + s, 8, 16), 1.0, 2048.0)
-            lin("S", A("fo" + s, 128, 256), IX("fo" + s, 0, 128, "rev", 8, 16))
+        lin("S", A("fo" + s, 128, 256, -1), IX("ctab", 0, 4240, "sl" + s, 8, 16), 1.0, 2176.0)
         dma("S", H("ys", al, slice(l0, l0 + 128)), A("fo" + s, 128, 256, part=slice(0, 128, 16)), 4096)
     return ops
 
@@ -474,7 +501,8 @@ def first_order(ops):
         tail[i] += LAT_R if o["kind"] == "r" else o["cost"]
         for j in o["deps"]:
             tail[j] = max(tail[j], tail[i] + LAT_X)
-    tail = [tail[i] + (OPT["lead"] if o["tag"][1] == 0 and 0 <= o["tag"][0] < STEPS else 0) for i, o in enumerate(ops)]
+    tail = [tail[i] + OPT["shift"].get(o["tag"][1:], 0) + (OPT["lead"] * OPT["share"][o["tag"][0]] if o["tag"][1] == 0 and 0 <= o["tag"][0] < STEPS else 0)
+            for i, o in enumerate(ops)]
     for i in range(n - 1, -1, -1):
         for j in ops[i]["deps"]:
             tail[j] = max(tail[j], tail[i] + 1)
@@ -501,7 +529,7 @@ def improve(ops, seq):
     eng = [o["eng"] for o in ops]
     lat = [LAT_R if o["kind"] == "r" else o["cost"] for o in ops]
     hold = [60 if o["kind"] == "d" else o["cost"] for o in ops]
-    other = [o["alt"][:2] if o["alt"] else None for o in ops]
+    other = [o["alt"][:2] if o["alt"] and (o["tag"][0] < 1 or min(o["cost"], o["alt"][1]) < OPT["big"]) else None for o in ops]
     keep, anc, succ = [], [], [[] for _ in ops]
     for i, o in enumerate(ops):
         a, k = 0, []
@@ -531,15 +559,27 @@ def improve(ops, seq):
             last[eng[i]] = i
     st, why = [0.0] * n, [None] * n
 
-    def starts(k0):
-        for i in order[k0:]:
+    def starts(k0, k1=n):
+        run, by = 0, 0.0
+        for k in range(k0, n):
+            i = order[k]
             p = prev[i]
             t, w = (0.0, None) if p is None else (st[p] + hold[p], p)
             for j, d in pred[i]:
                 if st[j] + d >= t:
                     t, w = st[j] + d, -1 - j
+            if -0.01 < t - st[i] - by < 0.01:
+                run += 1
+                if run > RUN and k > k1:
+                    if by:
+                        for e in order[k:]:
+                            st[e] += by
+                    break
+            else:
+                run, by = 0, t - st[i]
             st[i], why[i] = t, w
         return max(st[e] + lat[e] for e in ends)
+    RUN = OPT["run"]
 
     def hand(i):
         link(prev[i], nxt[i])
@@ -554,8 +594,9 @@ def improve(ops, seq):
         for e in [i] + succ[i]:
             pred[e] = waits(e)
     ends = [i for i in range(n) if ops[i]["tag"][0] == 99]
+    either = [i for i in range(n) if other[i]]
     cur = starts(0)
-    best, x, moves = (cur, list(order), list(eng)), 1, []
+    best, x, moves = (cur, list(order), list(eng)), OPT["seed"], []
     pos = {i: k for k, i in enumerate(order)}
     for it in range(tries):
         if not moves:
@@ -569,32 +610,56 @@ def improve(ops, seq):
                 i = w if w >= 0 else -1 - w
         x = (x * 1103515245 + 12345) % 2147483648
         j, i = moves[x * len(moves) >> 31]
+        if it % OPT["free"] == 0:
+            i = j = either[x * len(either) >> 31]
+            if eng[i] == "S" and x % 4:
+                continue
+        far, ahead = (x >> 8) % OPT["far"], (x >> 12) & 1
+        if i != j:
+            if nxt[j] != i:
+                moves = []
+                continue
+            for _ in range(far):
+                if ahead and prev[j] is not None:
+                    j = prev[j]
+                if not ahead and nxt[i] is not None:
+                    i = nxt[i]
         a, b = pos[j], pos[i]
         seg = order[a:b + 1]
-        old = st[:], why[:]
         if i == j:
             hand(i)
-            while a and order[a - 1] != prev[i] and prev[i] is not None:
-                a -= 1
         else:
-            mark = {i}
-            for e in reversed(seg):
+            e0, way, deps = (i, prev, keep) if ahead else (j, nxt, succ)
+            mark = {e0}
+            for e in (reversed(seg) if ahead else seg):
                 if e in mark:
-                    mark.update(keep[e])
-                    if e != i:
-                        mark.add(prev[e])
-            if j in mark:
-                moves.remove((j, i))
+                    if e != e0 and eng[e] == eng[e0]:
+                        break
+                    mark.update(deps[e])
+                    if e != e0:
+                        mark.add(way[e])
+            else:
+                e = None
+            if e is not None:
                 continue
-            p, q = prev[j], nxt[i]
-            link(p, i, j, q)
-            order[a:b + 1] = [e for e in seg if e in mark] + [e for e in seg if e not in mark]
-        new = starts(a)
+            p, q = prev[e0], nxt[e0]
+            link(p, q)
+            if ahead:
+                link(prev[j], i, j)
+            else:
+                link(i, j, nxt[i])
+            order[a:b + 1] = [e for e in seg if (e in mark) == ahead] + [e for e in seg if (e in mark) != ahead]
+        old = st[:], why[:]
+        new = starts(a, b)
         x = (x * 1103515245 + 12345) % 2147483648
         if new <= cur or x / 2147483648.0 < math.exp((cur - new) / (OPT["temp"] * (1 - it / tries) + 1)):
-            cur, moves = new, []
+            if abs(new - cur) > 0.01 or x % OPT["lazy"] == 0:
+                moves = []
+            cur = new
             for k in range(a, b + 1):
                 pos[order[k]] = k
+            if cur < best[0] or x % 64 == 0:
+                cur = starts(0)
             if cur < best[0]:
                 best = (cur, list(order), list(eng))
         else:
@@ -602,7 +667,8 @@ def improve(ops, seq):
                 hand(i)
             else:
                 order[a:b + 1] = seg
-                link(p, j, i, q)
+                link(prev[e0], nxt[e0])
+                link(p, e0, q)
             st[:], why[:] = old
     for o, e in zip(ops, best[2]):
         if e != o["eng"]:
@@ -610,6 +676,8 @@ def improve(ops, seq):
     return best[:2]
 
 
+OPT.update(free=10, mode="VPVPVPVP", dflip=2, far=3, lead=6000, passes=((50000, 400), (580000, 200)), gs=((1,), (1,)),
+           up=(0, 2, 4), g2=(), ds=())
 _PLAN = []
 
 
@@ -619,7 +687,11 @@ def rank_program(g, core, T, topo):
         return
     if not _PLAN:
         ops = plan()
-        _PLAN.append((ops, improve(ops, first_order(ops))[1]))
+        seq = first_order(ops)
+        for tries, temp in OPT["passes"]:
+            OPT.update(tries=tries, temp=temp)
+            seq = improve(ops, seq)[1]
+        _PLAN.append((ops, seq))
     ops, seq = _PLAN[0]
     N = len(T.cores)
     nxt, prv = T.cores[(rank + 1) % N], T.cores[(rank - 1) % N]
@@ -637,6 +709,10 @@ def rank_program(g, core, T, topo):
         if a[0] == "I":
             return T[a[1]][:, a[2]:a[3]].indirect(T[a[4]][:, a[5]:a[6]])
         p = a[5] if a[5] is not None else slice(None)
+        if a[4] == HALF_ROWS:
+            return T[a[1]][p, a[2] // 16:a[2] // 16 + 15, a[2] % 16:a[2] % 16 + 8]
+        if len(SCRATCH[a[1]][1]) == 3:
+            return T[a[1]][p, a[2] // 16:a[3] // 16, :]
         if a[4] == 1:
             return T[a[1]][p, a[2]:a[3]]
         if a[4] < 0:
@@ -698,12 +774,14 @@ def rank_program(g, core, T, topo):
                 r = q.iota(ap(c[1]), c[2], c[3], c[4])
             else:
                 r = q.iota(ap(c[1]), c[2], c[3], c[4], allow_small_or_imprecise_dtypes=True)
-        elif k == "dma":
+        elif k in ("dma", "dmas"):
             s_ = "dm%d" % ndma[0]
             ndma[0] += 1
-            q.dma_start(ap(c[1]), ap(c[2])).then_inc(T.sem[s_], 16)
-            mark[i] = (s_, 16)
-            cnt[s_] = 16
+            moves = c[1] if k == "dmas" else [c[1:3]]
+            for out, in_ in moves:
+                q.dma_start(ap(out), ap(in_)).then_inc(T.sem[s_], 16)
+            cnt[s_] = 16 * len(moves)
+            mark[i] = (s_, cnt[s_])
             continue
         elif k == "send":
             q.remote_dma(ap(c[4]), ap(c[3]), T.sem[c[1]], T.sem["gone"], pid, rid, mask)

@@ -7,27 +7,11 @@ AF = ActivationFunctionType
 F32, BF, F16, I32, U16 = "float32", "bfloat16", "float16", "int32", "uint16"
 STEPS = 4
 ROT = 2760
-OPT = dict(
-    mode="PVPVPVPV",
-    lead=3000.0,
-    tries=200000,
-    temp=250.0,
-    share=(1, 1, 1, 1),
-    seed=1,
-    run=40,
-    lazy=4,
-    shift={},
-    gs=((), ()),
-    cross=False,
-    big=9999,
-    far=3,
-    dflip=True,
-    free=5,
-)
 C = 8
 Q0 = (8, 0)
 SEG = [[16 * (16 - (Q0[h] + q)) + 2 for q in range(C)] for h in range(2)]
 TOT = [sum(s) for s in SEG]
+OPT = dict(lead=3000.0, seed=1, passes=((50000, 400), (600000, 200)))
 
 SCRATCH = {}
 PART = {}
@@ -40,24 +24,21 @@ def _sb(name, n, d):
 for _n, _w, _d in [
     ("xs", 4096, BF), ("vs", 4224, BF), ("ctab", 4240, F32), ("lan", 256, I32), ("s0w", 256, I32), ("wti", 8, I32),
     ("srow", 256, BF), ("ci", 16, I32), ("cf", 32, F32), ("t0", 144, F32), ("t1", 256, F32), ("t2", 384, F32),
-    ("t3", 256, F32), ("ti", 8, I32), ("tj", 32, I32), ("tn", 128, BF), ("idb", 128, BF), ("idh", 128, F16),
-    ("nid", 128, BF), ("c31", 128, BF), ("n31", 128, BF), ("c43", 128, BF), ("n43", 128, BF), ("i19", 128, BF),
-    ("one", 480, BF), ("blk", 128, BF), ("sel", 144, BF), ("selk", 144, F16), ("selw", 144, BF), ("selb", 144, BF),
-    ("wm", 128, F16), ("wme", 128, F16), ("nwm", 128, F16), ("wx", 128, F16), ("pcol", 16, BF), ("pa", 2048, F16),
-    ("ta", 128, BF), ("tb", 128, BF), ("tc", 96, BF), ("mtab", 128, F32), ("rst", 120, F32), ("ltl", 8, U16),
-    ("ends", 8, U16), ("val", 8, BF), ("lst", 8, F32), ("tri", 272, BF),
-    ("hrow", 272, F16), ("win", 16, BF), ("fsel", 256, BF), ("thr", 8, BF), ("hc", 32, F16), ("aq", 16, BF),
-    ("ay", 8, F32), ("aj", 16, F32),
+    ("t3", 144, F32), ("ti", 8, I32), ("idb", 128, BF), ("idh", 128, F16), ("nid", 128, BF), ("c31", 128, BF),
+    ("n31", 128, BF), ("c43", 128, BF), ("n43", 128, BF), ("i19", 128, BF), ("one", 480, BF), ("blk", 128, BF),
+    ("sel", 144, BF), ("selk", 144, F16), ("selw", 144, BF), ("selb", 144, BF), ("wme", 128, F16), ("nwm", 128, F16),
+    ("wx", 128, F16), ("ta", 128, BF), ("tb", 128, BF), ("tc", 64, BF), ("mtab", 128, F32), ("rst", 120, F32),
+    ("ltl", 8, U16), ("ends", 8, U16), ("val", 8, BF), ("lst", 8, F32), ("tri", 272, BF), ("hrow", 272, F16),
+    ("win", 16, BF), ("fsel", 256, BF), ("thr", 8, BF), ("hc", 32, F16), ("aq", 16, BF), ("ay", 8, F32), ("aj", 16, F32),
 ]:
     _sb(_n, _w, _d)
 for _h in range(2):
     for _n, _w, _d in [
-        ("ld", 256, I32), ("lu", 128 * STEPS, U16), ("su", 128 * STEPS, U16), ("home", 256, F32), ("lh", 128, F16),
-        ("a", 2048, BF), ("at", 2048, F16), ("q", 1920, BF), ("f", 1920, BF), ("d", 1920, F16), ("ab", 1920, F16),
-        ("cl", 1920, BF), ("lall", 1088, I32), ("w4", 256, F16), ("w2", 256, I32), ("w3", 384, BF), ("hu", 128, U16),
-        ("sc", 240, I32), ("k", 48, I32), ("m", 64, F32), ("ou", 64, U16), ("eq", TOT[_h], BF), ("es", TOT[_h], BF),
-        ("msk", TOT[_h], BF), ("snd", 8 * STEPS, I32), ("rcv", 8 * STEPS, I32), ("fo", 256, F32), ("sl", 16, U16),
-        ("own", 64, I32),
+        ("ld", 128, I32), ("lu", 128 * STEPS, U16), ("su", 128 * STEPS, U16), ("home", 256, F32), ("a", 2048, BF),
+        ("at", 2048, F16), ("f", 1920, BF), ("d", 1920, F16), ("ab", 1920, F16), ("cl", 1920, BF), ("lall", 1088, I32),
+        ("w4", 256, F16), ("w2", 256, I32), ("w3", 384, BF), ("hu", 128, U16), ("sc", 240, I32), ("k", 48, I32),
+        ("m", 16, F32), ("ou", 64, U16), ("eq", TOT[_h], BF), ("es", TOT[_h], BF), ("msk", TOT[_h], BF),
+        ("snd", 8 * STEPS, I32), ("rcv", 8 * STEPS, I32), ("fo", 128, F32), ("sl", 16, U16), ("own", 64, I32),
     ]:
         _o = SCRATCH[_n][1][1] if _h else 0
         PART[_n + str(_h)] = (_n, _o, _w)
@@ -66,22 +47,25 @@ for _n in ("dl0", "dl1"):
     SCRATCH[_n] = ("dram", [8, 1024], I32)
 for _n in ("pt0", "pt1"):
     SCRATCH[_n] = ("psum", [128, 1024], BF)
-for _n in ("px0", "px1", "px2"):
+for _n in ("px0", "px1", "px2", "px3"):
     SCRATCH[_n] = ("psum", [128, 32, 16], F32)
-for _n in ("pu", "pn", "pf"):
+for _n in ("pn", "pf"):
     SCRATCH[_n] = ("psum", [128, 512], F32)
-HALF_ROWS = 0
 
-SEMAPHORES = ["sv", "sa", "sp", "sg", "gone"] + ["dm%d" % i for i in range(70)] + ["arr%d" % i for i in range(4 * STEPS)]
+SEMAPHORES = ["sv", "sa", "sp", "sg", "gone"] + ["dm%d" % i for i in range(50)] + ["arr%d" % i for i in range(6 * STEPS)]
 
 CYC, PCYC = 1.04, 0.56
-LAT_X, LAT_S, LAT_R = 130.0, 90.0, 2600.0
+MIDDLE, CAUTIOUS = (1.56, 3.8, 130.0, 90.0, 2400.0), (1.62, 4.1, 140.0, 95.0, 2800.0)
 SIZE = {F32: 4, I32: 4, BF: 2, F16: 2, U16: 2}
 
 
 def A(name, lo=0, hi=None, step=1, part=None):
     name, o, w = PART.get(name) or (name, 0, SCRATCH[name][1][1])
     return ("A", name, o + lo, o + (w if hi is None else hi), step, part)
+
+
+def rows(name, lo, w):
+    return ("A", name, lo, lo + 240, (w,), None)
 
 
 def IX(name, lo, hi, off, c, d):
@@ -92,8 +76,8 @@ def IX(name, lo, hi, off, c, d):
 def count(a):
     if a[0] == "I":
         return 16 * (a[6] - a[5])
-    if a[4] == HALF_ROWS:
-        return 120
+    if isinstance(a[4], tuple):
+        return 15 * a[4][0]
     return len(range(a[2], a[3], abs(a[4])))
 
 
@@ -111,7 +95,8 @@ def narrow(*xs):
     return all(SIZE[SCRATCH[a[1]][2]] == 2 for a in xs)
 
 
-def plan():
+def plan(costs=MIDDLE):
+    GATHER, SCATTER = costs[:2]
     ops = []
     acc = {}
     tag = [-9, 0, "c"]
@@ -155,15 +140,15 @@ def plan():
     def vcost(out, ins, two=False):
         n = count(out)
         if out[0] == "I":
-            return (60 + 3.8 * n) * CYC
+            return (60 + SCATTER * n) * CYC
         if ins[0][0] == "I":
-            return (60 + 1.56 * n) * CYC
+            return (60 + GATHER * n) * CYC
         if two:
             return max(64, n * (1 if any(psum(a) for a in ins) else 2)) * CYC
         return max(64, n * (0.5 if narrow(out, *ins) else 1)) * CYC
 
     def scost(out, in_):
-        return ((78 + 1.56 * count(out)) if in_[0] == "I" else max(64, count(out))) * CYC
+        return ((78 + GATHER * count(out)) if in_[0] == "I" else max(64, count(out))) * CYC
 
     def cp(out, in_):
         return add("V", vcost(out, [in_]), ("cp", out, in_), [in_], [out])
@@ -196,12 +181,14 @@ def plan():
     def group(out, pairs, first=True, last=True):
         return [(out, l, r, first and k == 0, last and k == len(pairs) - 1) for k, (l, r) in enumerate(pairs)]
 
+    def sums(name, src, pc):
+        return [(A(name, 15 - j, 143 - j), A(src, 960 * pc + j, 960 * pc + 960, 16)) for j in range(16)]
+
     def iota(out, pat, base, cm):
         return add("G", 130 + 2 * count(out) * CYC, ("iota", out, pat, base, cm), [], [out])
 
-    def dma(eng, out, in_, nbytes, after=()):
-        return add(eng, 2000 + nbytes / 180.0, ("dma", out, in_), [in_] if in_[0] != "H" else [],
-                   [out] if out[0] != "H" else [], kind="d", after=after)
+    def dma(eng, out, in_, ns, after=()):
+        return add(eng, ns, ("dma", out, in_), [in_] if in_[0] != "H" else [], [out] if out[0] != "H" else [], kind="d", after=after)
 
     def H(name, *ix):
         return ("H", name, ix)
@@ -209,28 +196,28 @@ def plan():
     def col(b, j):
         return A(b, j, j + 1)
 
-    def selj(name, j):
-        return A(name, 15 - j, 143 - j)
+    def seg0(h, q):
+        return (sum(SEG[h][:q]) - sum(SEG[h][:4])) % TOT[h]
 
     al = slice(None)
-    dma("Y", A("lan"), H("lanes", al, al), 131072)
-    first = [dma("S", A("xs", 0, 2048), H("x", al, slice(0, 2048)), 700000),
-             dma("Y", A("xs", 2048, 4096), H("x", al, slice(2048, 4096)), 700000)]
+    dma("Y", A("lan"), H("lanes", al, al), 2700)
+    first = [dma("S", A("xs", 0, 2048), H("x", al, slice(0, 2048)), 5900),
+             dma("Y", A("xs", 2048, 4096), H("x", al, slice(2048, 4096)), 5900)]
     iota(A("s0w"), [[0, 256]], 0, 0)
-    dma("Y", A("wti", 0, 1), H("wt", al, al), 512)
-    dma("Y", A("s0w", part=slice(0, 128, 16)), H("s0", al, al), 8192)
-    dma("Y", A("vs", 128, 128 + ROT), H("v", al, slice(4096 - ROT, 4096)), 700000, first)
-    dma("Y", A("vs", 128 + ROT, 4224), H("v", al, slice(0, 4096 - ROT)), 700000, first)
+    dma("Y", A("wti", 0, 1), H("wt", al, al), 2000)
+    dma("Y", A("s0w", part=slice(0, 128, 16)), H("s0", al, al), 2000)
+    dma("Y", A("vs", 128, 128 + ROT), H("v", al, slice(4096 - ROT, 4096)), 5900, first)
+    dma("Y", A("vs", 128 + ROT, 4224), H("v", al, slice(0, 4096 - ROT)), 5900, first)
 
     iota(col("ci", 0), [[0, 1]], 0, 1)
-    iota(A("t3", 136, 144), [[3840, 2], [944, 4]], -128, 0)
     iota(A("t0"), [[1, 144]], 0, 0)
     iota(A("t1", 0, 128), [[1, 16], [0, 8]], 0, 0)
     iota(A("t1", 128, 256), [[0, 16], [1, 8]], 0, 0)
     iota(A("t3", 0, 128), [[1, 8], [0, 16]], 0, 0)
+    iota(A("t3", 128, 136), [[16, 8]], 0, 0)
+    iota(A("t3", 136, 144), [[3840, 2], [944, 4]], -128, 0)
     iota(A("mtab", 0, 120), [[0, 8], [1, 15]], 1, 0)
     iota(A("mtab", 120, 128), [[0, 8]], 0, 0)
-    iota(A("t3", 128, 136), [[16, 8]], 0, 0)
     iota(A("ctab"), [[1, 4240]], -2176, 0)
     ts(col("ci", 1), col("ci", 0), 15, ALU.bitwise_and)
     ts(col("ci", 2), col("ci", 0), 4, ALU.arith_shift_right)
@@ -244,7 +231,6 @@ def plan():
     ts(A("t2", 0, 128), A("t1", 128, 256), G_, ALU.is_equal)
     tt(A("wme"), A("t2", 256, 384), A("t2", 0, 128), ALU.mult)
     lin("S", A("wx"), A("wme"), 1.0, 1024.0)
-    lin("S", A("wm"), A("wx"), 1.0, -1024.0)
     lin("S", A("nwm"), A("wx"), -1.0, 1024.0)
     for name, f in (("c31", 2.0 ** 31), ("n31", -2.0 ** 31), ("c43", 1.5 * 2.0 ** 43), ("n43", -1.5 * 2.0 ** 43),
                     ("nid", -1.0), ("idh", 1.0), ("i19", 2.0 ** 19)):
@@ -257,7 +243,7 @@ def plan():
     lin("S", A("sel"), A("selb"), 2.0 ** 16)
     lin("S", A("selk"), A("selb"), 1024.0)
     ts(col("cf", 16), J_, 8.0, ALU.is_ge, 65280.0, ALU.mult)
-    lin("S", A("tc"), A("one", 0, 96), 256.0, col("cf", 16))
+    lin("S", A("tc"), A("one", 0, 64), 256.0, col("cf", 16))
     lin("S", A("ta", 0, 120), A("t0", 0, 120), 4096.0, 2048.0)
     lin("S", A("tb", 0, 120), A("mtab", 0, 120), 64.0, 12288.0)
     ts(A("blk"), A("t3", 0, 128), G_, ALU.is_equal)
@@ -266,12 +252,6 @@ def plan():
     lin("S", col("cf", 9), J_, 1.0 / 15.0, 0.5 / 15.0 - 0.5)
     lin("S", A("ti"), A("t3", 128, 136), 1.0 / 15.0, col("cf", 9))
     ts(A("ltl"), A("ti"), C - 1.0, ALU.min)
-    if not OPT["dflip"]:
-        iota(A("tn"), [[1, 128]], 128, 0)
-        lin("S", col("cf", 11), G_, 16.0, 128.0)
-        lin("S", A("pcol"), A("t2", 256, 384, 8), 1.0, col("cf", 11))
-        for m in range(16):
-            ts(A("pa", 128 * m, 128 * m + 128), A("tn"), col("pcol", m), ALU.is_equal)
     lin("S", A("val"), A("t3", 128, 136), 1.0, J_)
     ts(A("lst"), A("t3", 136, 144), J_, ALU.subtract)
     ts(A("tri", 0, 16), A("t0", 0, 16), J_, ALU.is_le, 8192.0, ALU.mult)
@@ -281,20 +261,137 @@ def plan():
         s = str(h)
         lin("S", col("cf", 18 + h), J8, -8.0, float(SEG[h][0]))
         ts(col("cf", 22 + h), J8, 1.0, ALU.add, col("cf", 18 + h), ALU.mult)
-        lin("S", A("ends", 2 * h, 2 * h + 1), col("cf", 22 + h), 1.0, -1.0)
+        ts(A("ends", 4 + 2 * h, 5 + 2 * h), col("cf", 22 + h), -1.0 - sum(SEG[h][:4]), ALU.add, 0.0, ALU.max)
+        ts(col("cf", 24 + h), J8, 4.0, ALU.is_lt, float(TOT[h]), ALU.mult)
+        ts(A("ends", 2 * h, 2 * h + 1), col("cf", 22 + h), -1.0 - sum(SEG[h][:4]), ALU.add, col("cf", 24 + h), ALU.add)
+        ms(A("ou" + s, 0, 16), 0)
         for q in range(C):
-            o = sum(SEG[h][:q])
+            o = seg0(h, q)
             ts(A("msk" + s, o, o + SEG[h][q]), A("tri", 0, SEG[h][q]), col("val", q), ALU.max)
     lin("S", A("srow"), A("s0w", 0, 256, -1))
-    mm(group(A("pn", 0, 16), [(selj("selb", j), A("srow", j, 256, 16)) for j in range(16)]))
+    mm(group(A("pn", 0, 16), [(A("selb", 15 - j, 143 - j), A("srow", j, 256, 16)) for j in range(16)]))
     for h in range(2):
         lin("S", A("rcv%d" % h, 0, C), A("pn", Q0[h], Q0[h] + C))
 
-    rot = [0, 0]
+    def prints(t, h):
+        s = str(h)
+        l0 = 128 * t
+        w2, w3, w4, lall = "w2" + s, "w3" + s, "w4" + s, "lall" + s
+        tag[:] = [t, h, "list"]
+        if t == 0:
+            lin("V", A("lu" + s, 0, 128), A("lan", 128 * h, 128 * h + 128, -1))
+        for pc in (1, 0):
+            for u in range(2):
+                tag[:] = [t, h, "f%d" % (2 * pc + u)]
+                pt, bk = "pt%d" % u, "px%d" % (2 * pc + u)
+                o = 1024 * pc + 512 * u
+                if pc or not u:
+                    n = 32 if pc else 64
+                    lin("S", A("a" + s, o, o + 16 * n), IX("xs", 0, 4096, "lu" + s, l0 + o // 16, l0 + o // 16 + n))
+                lst = [("T", A(pt, 128 * i, 128 * i + 128), A("a" + s, o + 128 * i, o + 128 * i + 128)) for i in range(4)]
+                add("P", 512 * PCYC, ("tr", lst), [m[2] for m in lst] + [A("idb")], [m[1] for m in lst])
+                lin("V", A("at" + s, o, o + 512), A(pt, 0, 512), 1.0, 272.0)
 
-    def xbank():
-        rot[0] += 1
-        return "px%d" % (rot[0] % 3)
+                def blocks(w, last):
+                    return [(rows(bk, 240 * (i // 2) + 8 * (i % 2), 8), A("at" + s, o + 128 * i, o + 128 * i + 128), A(w, 8, 128),
+                             False, last and i == 3) for i in range(4)]
+                mm([(A(bk, 0, 480), A("c31"), A("one"), True, False)])
+                mm(blocks("wme", False) + [(A(bk, 0, 480), A("n31"), A("one"), False, False)] + blocks("nwm", True))
+                lin("S", A("f" + s, 960 * pc + 480 * u, 960 * pc + 480 * u + 480), A(bk, 0, 480), -1.0, 128.0)
+            tag[:] = [t, h, "u%d" % pc]
+            a, b = 60 * pc, 60 * pc + 60
+            pu = rows(bk, 0, 4)
+            mm(group(pu, [(A("blk"), A("tc", 0, 60))] + sums("selw", "f" + s, pc)))
+            lin("S", A(w3, 128 + a, 128 + b), pu, 1.0, 0.5)
+            tt(A(w4, a, b), pu, A(w3, 128 + a, 128 + b), ALU.subtract)
+            act(A(w2, a, b), A(w4, a, b), AF.Square, bias=2640.0)
+            ts(A(w2, 128 + a, 128 + b), A(w2, a, b), 5, ALU.arith_shift_right, 4095, ALU.bitwise_and)
+            lin("V", A("hu" + s, a, b), A(w2, 128 + a, 128 + b))
+            lin("S", A(w4, 128 + a, 128 + b), A(w2, 128 + a, 128 + b), 1.0, -2048.0)
+        tag[:] = [t, h, "key"]
+        tt(A(w3, 0, 128), IX("rcv" + s, 8 * t, 8 * t + 8, "ltl", 0, 8), A("mtab"), ALU.is_gt)
+        lin("S", A(w3, 256, 376), A(w4, 0, 120), 1.0, 12288.0 - 31.5)
+        tag[:] = [t, h, "flip"]
+        lin("S", A("own" + s), A("lu" + s, l0 + 64, l0 + 128), 4096.0)
+        tt(A(lall, 0, 64), A("own" + s), A("lu" + s, l0, l0 + 64), ALU.add)
+        dma("Y", A("dl" + s), A(lall, 0, 64), 3500)
+        for w in (64, 256):
+            add("Y", 3500, ("dmas", [(A(lall, w * i, w * i + w), A(lall, 0, w)) for i in (1, 2, 3)]),
+                [A(lall, 0, w)], [A(lall, w, 4 * w)], kind="d")
+        moves = [(A(lall, 64 * max(k, 1) + 64, 1088, part=slice(k, 128, 16)), A("dl" + s, 64 * (k == 0), 1024 - 64 * k))
+                 for k in range(16)]
+        add("Y", 6000, ("dmas", moves), [A("dl" + s)], [A(lall, 128, 1088)], kind="d")
+
+    def send(sem, src, dst):
+        sent = add("G", 300, ("send", "arr%d" % sem, 0, src, dst), [src], [], kind="s")
+        add("R", 0, ("arr", "arr%d" % sem), [], [dst], kind="r", after=[sent])
+
+    def decide(t, h):
+        s = str(h)
+        B, cut = 16 * Q0[h], sum(SEG[h][4:])
+        w3, w4, k, m_, ou, ld, sc = "w3" + s, "w4" + s, "k" + s, "m" + s, "ou" + s, "ld" + s, "sc" + s
+        for q0, q1 in ((4, 8), (0, 4)) if t < STEPS - 1 else ((0, 8),):
+            c0, c1, early = 15 * q0, 15 * q1, q0 // 4
+            tag[:] = [t, h, "near"]
+            mm(group(A("pn", c0, c1), [(A("c43"), A("one", c0, c1))], last=False))
+            for pc in range(q1 // 4 - 1, q0 // 4 - 1, -1):
+                for pi in (2 * pc, 2 * pc + 1):
+                    tag[:] = [t, h, "d%d" % pi]
+                    a, b = 480 * pi, 480 * pi + 480
+                    tt(A("d" + s, a, b), IX("vs", 128, 4224, "hu" + s, 30 * pi, 30 * pi + 30), A("f" + s, a, b), ALU.subtract)
+                    act(A("ab" + s, a, b), A("d" + s, a, b), AF.Abs)
+                    ts(A("cl" + s, a, b), A("ab" + s, a, b), col("thr", 0), ALU.is_le, -3.5 / 16, ALU.add)
+                mm(group(A("pn", 60 * pc, 60 * pc + 60), sums("sel", "cl" + s, pc), False, False))
+            tag[:] = [t, h, "pick"]
+            mm(group(A("pn", c0, c1), [(A("n43"), A("one", c0, c1)), (A("idb"), A("ta", c0, c1)),
+                                       (A("idh"), A(w4, 128 + c0, 128 + c1)), (A("i19"), A(w3, c0, c1))], first=False))
+            scan(A(sc, c0, c1), A("rst", c0, c1), A("pn", c0, c1), ALU.add, ALU.min)
+            k1 = A(sc, c0 + 14, c1, 15)
+            ts(A(k, 16 + q0, 16 + q1), k1, 0x100FFF, ALU.bitwise_and)
+            ts(A(ou, q0, q1), A(k, 16 + q0, 16 + q1), 4096.0, ALU.min, 128.0, ALU.add)
+            lin("S", A("hrow", B + 16 * q0, B + 16 * q1), IX("ctab", 0, 4240, ou, q0, q1))
+            lin("V", A("hc", 16 * h + q0, 16 * h + q1), A(ou, q0, q1), 1.0, -2176.0)
+            ts(A(k, 24 + q0, 24 + q1), k1, 6, ALU.arith_shift_right, 127 * 64, ALU.bitwise_and)
+            tt(A(ou, 8 + q0, 8 + q1), A(k, 24 + q0, 24 + q1), A("lst", q0, q1), ALU.subtract)
+            tag[:] = [t, h, "win"]
+            for q in range(q0, q1):
+                o, w = seg0(h, q), SEG[h][q]
+                ts(A("eq" + s, o, o + w), A("hrow", 258 - w, 258), col("hc", 16 * h + q), ALU.not_equal, 8192.0, ALU.mult)
+            a, b = 0 if q1 == 8 else cut, cut if early else TOT[h]
+            scan(A("es" + s, a, b), A("eq" + s, a, b), A("msk" + s, a, b), ALU.min, ALU.max)
+            tag[:] = [t, h, "send"]
+            a = 32 + 16 * early
+            tt(A(ou, a, a + 16), IX("es" + s, 0, b, "ends", 4 * early + 2 * h, 4 * early + 2 * h + 1), A(ou, 0, 16), ALU.min)
+            for q in range(q0, q1, 4):
+                ts(A(ld, 16 * q, 16 * q + 64), IX("lall" + s, 0, 1088, ou, a + 8 + q, a + 12 + q),
+                   *((12, ALU.arith_shift_right) if q else (4095, ALU.bitwise_and)))
+            if t < STEPS - 1:
+                o = 128 * t + 16 * q0
+                src, dst = A("su" + s, o, o + 64), A("lu" + s, o + 128, o + 192)
+                lin("V", src, A(ld, 16 * q0, 16 * q1))
+            else:
+                src, dst = A("home" + s, 0, 128), A("home" + s, 128, 256)
+                lin("V", src, A(ld, 0, 128, -1))
+            send(2 * t + h + 4 * STEPS * early, src, dst)
+        tag[:] = [t, h, "mark"]
+        lin("S", A(ou, 16, 24), A(k, 24, 32), 0.25, J_)
+        lin("S", A("fsel", B, B + 128), IX("f" + s, 0, 1920, ou, 16, 24))
+        tag[:] = [t, h, "far"]
+        mm(group(A("pf", 0, 120), [(A("idb"), A("tb", 0, 120)), (A("idh"), A(w4, 0, 120)), (A("nid"), A(w3, 256, 376))], last=False))
+        for pc in (1, 0):
+            mm(group(A("pf", 60 * pc, 60 * pc + 60), sums("selk", "ab" + s, pc), False, pc == 0))
+        scan(A(sc, 120, 240), A("rst"), A("pf", 0, 120), ALU.add, ALU.min)
+        ts(A(k, 32, 40), A(sc, 134, 240, 15), 15, ALU.bitwise_and)
+        tt(A(m_, 0, 8), A("rcv" + s, 8 * t, 8 * t + 8), A(k, 32, 40), ALU.subtract)
+        tag[:] = [t, h, "s"]
+        wn = A("win", Q0[h], Q0[h] + C)
+        ts(wn, A(ou, 32, 40), 127.5, ALU.is_gt)
+        tt(A(m_, 8, 16), A(m_, 0, 8), wn, ALU.mult)
+        src, dst = A("snd" + s, 8 * t, 8 * t + 8), A("rcv" + s, 8 * t + 8, 8 * t + 16)
+        if t == STEPS - 1:
+            src, dst = A("sl" + s, 0, 8), A("sl" + s, 8, 16)
+        tt(src, A(m_, 8, 16), A(k, 32, 40), ALU.add)
+        send(2 * (STEPS + t) + h, src, dst)
 
     def close_step(t):
         tag[:] = [t, 9, "close"]
@@ -306,174 +403,6 @@ def plan():
             lin("S", col("aq", 0), col("ay", 0), 1.0, -4.0)
             lin("S", col("thr", 0), col("aq", 0), -1.0, col("ay", 0))
 
-    def prints(t, h):
-        s = str(h)
-        l0 = 128 * t
-        w2, w3, w4 = "w2" + s, "w3" + s, "w4" + s
-        tag[:] = [t, h, "list"]
-        if t == 0:
-            lin("V", A("lu" + s, 0, 128), A("lan", 128 * h, 128 * h + 128, -1))
-        for pc in range(2):
-            mode = OPT["mode"][4 * h + 2 * pc:4 * h + 2 * pc + 2]
-            for u in range(2):
-                tag[:] = [t, h, "f%d" % (2 * pc + u)]
-                rot[1] += 1
-                pt = "pt%d" % (rot[1] % 2)
-                c0 = l0 + 64 * pc + 32 * u
-                o = 1024 * pc + 512 * u
-                cuts = (0, 16, 32) if 2 * pc + u in OPT["g2"] else (0, 32)
-                for a, b in zip(cuts, cuts[1:]):
-                    lin("S", A("a" + s, o + 16 * a, o + 16 * b), IX("xs", 0, 4096, "lu" + s, c0 + a, c0 + b))
-                lst = [("T", A(pt, 128 * i, 128 * i + 128), A("a" + s, o + 128 * i, o + 128 * i + 128)) for i in range(4)]
-                add("P", 512 * PCYC, ("tr", lst), [m[2] for m in lst] + [A("idb")], [m[1] for m in lst])
-                lin("V", A("at" + s, o, o + 512), A(pt, 0, 512), 1.0, 272.0 if mode[u] == "P" else 288.0)
-                o = 480 * (2 * pc + u)
-                bk = xbank()
-
-                def blocks(w, first, last):
-                    return [(A(bk, 240 * (i // 2) + 8 * (i % 2), 240 * (i // 2) + 240, HALF_ROWS),
-                             A("at" + s, 1024 * pc + 512 * u + 128 * i, 1024 * pc + 512 * u + 128 * i + 128), A(w, 8, 128),
-                             first and i == 0, last and i == 3) for i in range(4)]
-                if mode[u] == "P":
-                    mm([(A(bk, 0, 480), A("c31"), A("one"), True, False)])
-                    mm(blocks("wme", False, False) + [(A(bk, 0, 480), A("n31"), A("one"), False, False)] + blocks("nwm", False, True))
-                    lin("S", A("f" + s, o, o + 480), A(bk, 0, 480), -1.0, 128.0)
-                else:
-                    mm(blocks("wm", True, True))
-                    lin("S", A("q" + s, o, o + 480), A(bk, 0, 480), 1.0, -127.5)
-                    if mode[u] == "V":
-                        tt(A("f" + s, o, o + 480), A(bk, 0, 480), A("q" + s, o, o + 480), ALU.subtract)
-                    else:
-                        mm([(A(bk, 0, 480), A("nid"), A("q" + s, o, o + 480), False, True)])
-                        lin("S", A("f" + s, o, o + 480), A(bk, 0, 480))
-                if 2 * pc + u + 1 not in OPT["up"]:
-                    continue
-                n = OPT["up"].index(2 * pc + u + 1)
-                tag[:] = [t, h, "u%d" % n]
-                a, b = 30 * OPT["up"][n - 1], 30 * OPT["up"][n]
-                mm(group(A("pu", a, b), [(A("blk"), A("tc", 0, b - a))] +
-                         [(selj("selw", j), A("f" + s, 16 * a + j, 16 * b, 16)) for j in range(16)]))
-                lin("S", A(w3, 128 + a, 128 + b), A("pu", a, b), 1.0, 0.5)
-                tt(A(w4, a, b), A("pu", a, b), A(w3, 128 + a, 128 + b), ALU.subtract)
-                act(A(w2, a, b), A(w4, a, b), AF.Square, bias=2640.0)
-                ts(A(w2, 128 + a, 128 + b), A(w2, a, b), 5, ALU.arith_shift_right, 4095, ALU.bitwise_and)
-                lin("V", A("hu" + s, a, b), A(w2, 128 + a, 128 + b))
-        tag[:] = [t, h, "key"]
-        tt(A(w3, 0, 128), IX("rcv" + s, 8 * t, 8 * t + 8, "ltl", 0, 8), A("mtab"), ALU.is_gt)
-        lin("S", A(w4, 128, 248), A("hu" + s, 0, 120), 1.0, -2048.0)
-        lin("S", A(w3, 256, 376), A(w4, 0, 120), 1.0, 12288.0 - 31.5)
-        tag[:] = [t, h, "flip"]
-        if OPT["dflip"]:
-            lall = "lall" + s
-            lin("S", A("own" + s), A("lu" + s, l0 + 64, l0 + 128), 4096.0)
-            tt(A(lall, 0, 64), A("own" + s), A("lu" + s, l0, l0 + 64), ALU.add)
-            dma("Y", A("dl" + s), A(lall, 0, 64), 270000)
-            for w in (64, 256):
-                add("Y", 3500, ("dmas", [(A(lall, w * i, w * i + w), A(lall, 0, w)) for i in (1, 2, 3)]),
-                    [A(lall, 0, w)], [A(lall, w, 4 * w)], kind="d")
-            moves = [(A(lall, 64 * max(k, 1) + 64, 1088, part=slice(k, 128, 16)), A("dl" + s, 64 * (k == 0), 1024 - 64 * k))
-                     for k in range(16)]
-            add("Y", 6000, ("dmas", moves), [A("dl" + s)], [A(lall, 128, 1088)], kind="d")
-            return
-        lin("S", A("lh" + s, 0, 64), A("lu" + s, l0, l0 + 64), 1.0 / 4096, -0.5)
-        lin("S", A("lh" + s, 64, 128), A("lu" + s, l0 + 64, l0 + 128), 1.0, -2048.0)
-        for bi in range(2):
-            bk = xbank()
-            lst = []
-            for i in range(8):
-                m = (8 * bi + i + 1) % 16
-                lst += group(A(bk, 64 * i, 64 * i + 64), [(A("pa", 128 * m, 128 * m + 128), A("lh" + s, 0, 64)),
-                                                          (A("pa", 128 * m, 128 * m + 128), A("lh" + s, 64, 128))])
-            mm(lst)
-            n = 512 - 64 * bi
-            lin("S", A("lall" + s, 128 + 512 * bi, 128 + 512 * bi + n), A(bk, 0, n), 4096.0, 2048.0 * 4097)
-            if bi:
-                for e in range(2):
-                    lin("S", A("lall" + s, 64 * e, 64 * e + 64), A(bk, n, 512), 4096.0, 2048.0 * 4097)
-
-    def send(sem, src, dst):
-        sent = add("G", 300, ("send", "arr%d" % sem, 0, src, dst), [src], [], kind="s")
-        add("R", 0, ("arr", "arr%d" % sem), [], [dst], kind="r", after=[sent])
-
-    def decide(t, h):
-        s = str(h)
-        B = 16 * Q0[h]
-        w3, w4, k, m_, ou, ld = "w3" + s, "w4" + s, "k" + s, "m" + s, "ou" + s, "ld" + s
-        tag[:] = [t, h, "pre"]
-        mm(group(A("pn", 0, 120), [(A("c43"), A("one", 0, 120))], last=False))
-        for pi in range(4):
-            tag[:] = [t, h, "d%d" % pi]
-            o = 480 * pi
-            marks = IX("vs", 128, 4224, "hu" + s, 30 * pi, 30 * pi + 30)
-            if pi in OPT["gs"][h]:
-                lin("S", A("q" + s, o, o + 480), marks)
-                mm(group(A("pf", 0, 480), [(A("idb"), A("q" + s, o, o + 480)), (A("nid"), A("f" + s, o, o + 480))]))
-                act(A("ab" + s, o, o + 480), A("pf", 0, 480), AF.Abs)
-                ts(A("cl" + s, o, o + 480), A("ab" + s, o, o + 480), col("thr", 0), ALU.is_le, -3.5 / 16, ALU.add)
-            else:
-                cuts = (0, 16, 30) if pi in OPT["ds"] else (0, 30)
-                for a, b in zip(cuts, cuts[1:]):
-                    marks = IX("vs", 128, 4224, "hu" + s, 30 * pi + a, 30 * pi + b)
-                    a, b = o + 16 * a, o + 16 * b
-                    tt(A("d" + s, a, b), marks, A("f" + s, a, b), ALU.subtract)
-                    act(A("ab" + s, a, b), A("d" + s, a, b), AF.Abs)
-                    ts(A("cl" + s, a, b), A("ab" + s, a, b), col("thr", 0), ALU.is_le, -3.5 / 16, ALU.add)
-            if pi % 2:
-                c0, c1, o = 30 * pi - 30, 30 * pi + 30, o - 480
-                tag[:] = [t, h, "n%d" % pi]
-                mm(group(A("pn", c0, c1), [(selj("sel", j), A("cl" + s, o + j, o + 960, 16)) for j in range(16)], False, False))
-        tag[:] = [t, h, "pre"]
-        mm(group(A("pf", 0, 120), [(A("idb"), A("tb", 0, 120)), (A("idh"), A(w4, 0, 120)), (A("nid"), A(w3, 256, 376))], last=False))
-        for pc in range(2):
-            tag[:] = [t, h, "r%d" % pc]
-            mm(group(A("pf", 60 * pc, 60 * pc + 60), [(selj("selk", j), A("ab" + s, 960 * pc + j, 960 * pc + 960, 16)) for j in range(16)],
-                     False, pc == 1))
-        tag[:] = [t, h, "near"]
-        mm(group(A("pn", 0, 120), [(A("n43"), A("one", 0, 120)), (A("idb"), A("ta", 0, 120)), (A("idh"), A(w4, 128, 248)),
-                                   (A("i19"), A(w3, 0, 120))], first=False))
-        scan(A("sc" + s, 0, 120), A("rst"), A("pn", 0, 120), ALU.add, ALU.min)
-        tag[:] = [t, h, "far"]
-        scan(A("sc" + s, 120, 240), A("rst"), A("pf", 0, 120), ALU.add, ALU.min)
-        k1, k2 = A("sc" + s, 14, 120, 15), A("sc" + s, 134, 240, 15)
-        ts(A(k, 32, 40), k2, 15, ALU.bitwise_and)
-        tt(A(m_, 24, 32), A("rcv" + s, 8 * t, 8 * t + 8), A(k, 32, 40), ALU.subtract)
-        tag[:] = [t, h, "pick"]
-        ts(A(k, 16, 24), k1, 0x100FFF, ALU.bitwise_and)
-        ts(A(ou, 0, 8), A(k, 16, 24), 4096.0, ALU.min, 128.0, ALU.add)
-        lin("S", A("hrow", B, B + 128), IX("ctab", 0, 4240, ou, 0, 8))
-        hi = 16 * h
-        ts(A("hc", hi, hi + 8), A(k, 16, 24), 4096.0, ALU.min, -2048.0, ALU.add)
-        ts(A(k, 24, 32), k1, 6, ALU.arith_shift_right, 127 * 64, ALU.bitwise_and)
-        tt(A(ou, 8, 16), A(k, 24, 32), A("lst"), ALU.subtract)
-        lin("S", A(ou, 16, 24), A(k, 24, 32), 0.25, J_)
-        lin("S", A("fsel", B, B + 128), IX("f" + s, 0, 1920, ou, 16, 24))
-        tag[:] = [t, h, "win"]
-        for q in range(C):
-            o, w = sum(SEG[h][:q]), SEG[h][q]
-            cuts = (0, w - 130, w) if h and OPT["cross"] else (0, w)
-            for a, b in zip(cuts, cuts[1:]):
-                ts(A("eq" + s, o + a, o + b), A("hrow", 258 - w + a, 258 - w + b), col("hc", hi + q), ALU.not_equal, 8192.0, ALU.mult)
-        scan(A("es" + s), A("eq" + s), A("msk" + s), ALU.min, ALU.max)
-        tag[:] = [t, h, "send"]
-        tt(A(ou, 32, 48), IX("es" + s, 0, TOT[h], "ends", 2 * h, 2 * h + 1), A(ou, 0, 16), ALU.min)
-        ts(A(ld, 0, 64), IX("lall" + s, 0, 1088, ou, 40, 44), 4095, ALU.bitwise_and)
-        ts(A(ld, 64, 128), IX("lall" + s, 0, 1088, ou, 44, 48), 12, ALU.arith_shift_right)
-        if t < STEPS - 1:
-            lin("V", A("su" + s, 128 * t, 128 * t + 128), A(ld, 0, 128))
-            send(2 * t + h, A("su" + s, 128 * t, 128 * t + 128), A("lu" + s, 128 * t + 128, 128 * t + 256))
-        else:
-            lin("V", A("home" + s, 0, 128), A(ld, 0, 128, -1))
-            send(2 * t + h, A("home" + s, 0, 128), A("home" + s, 128, 256))
-        tag[:] = [t, h, "s"]
-        wn = A("win", Q0[h], Q0[h] + C)
-        ts(wn, A(ou, 32, 40), 127.5, ALU.is_gt)
-        tt(A(m_, 48, 56), A(m_, 24, 32), wn, ALU.mult)
-        src, dst = A("snd" + s, 8 * t, 8 * t + 8), A("rcv" + s, 8 * t + 8, 8 * t + 16)
-        if t == STEPS - 1:
-            src, dst = A("sl" + s, 0, 8), A("sl" + s, 8, 16)
-        tt(src, A(m_, 48, 56), A(k, 32, 40), ALU.add)
-        send(2 * (STEPS + t) + h, src, dst)
-
     for t in range(STEPS):
         for h in range(2):
             prints(t, h)
@@ -484,25 +413,25 @@ def plan():
     cut = [0, 920, 1840, ROT, 4096]
     for k in range(4):
         o = (cut[k] - ROT) % 4096
-        dma("YS"[k % 2], H("yv", al, slice(o, o + cut[k + 1] - cut[k])), A("vs", 128 + cut[k], 128 + cut[k + 1]), 500000)
+        dma("YS"[k % 2], H("yv", al, slice(o, o + cut[k + 1] - cut[k])), A("vs", 128 + cut[k], 128 + cut[k + 1]), 4800)
     for h in range(2):
         s, l0 = str(h), 128 * h
-        dma("Y", H("yl", al, slice(l0, l0 + 128)), A("home" + s, 128, 256), 65536)
-        lin("S", A("fo" + s, 128, 256, -1), IX("ctab", 0, 4240, "sl" + s, 8, 16), 1.0, 2176.0)
-        dma("S", H("ys", al, slice(l0, l0 + 128)), A("fo" + s, 128, 256, part=slice(0, 128, 16)), 4096)
+        dma("Y", H("yl", al, slice(l0, l0 + 128)), A("home" + s, 128, 256), 2400)
+        lin("S", A("fo" + s, 0, 128, -1), IX("ctab", 0, 4240, "sl" + s, 8, 16), 1.0, 2176.0)
+        dma("S", H("ys", al, slice(l0, l0 + 128)), A("fo" + s, 0, 128, part=slice(0, 128, 16)), 2000)
     return ops
 
 
 def first_order(ops):
     n = len(ops)
+    LAT_X, LAT_S, LAT_R = MIDDLE[2:]
     tail = [0.0] * n
     for i in range(n - 1, -1, -1):
         o = ops[i]
         tail[i] += LAT_R if o["kind"] == "r" else o["cost"]
         for j in o["deps"]:
             tail[j] = max(tail[j], tail[i] + LAT_X)
-    tail = [tail[i] + OPT["shift"].get(o["tag"][1:], 0) + (OPT["lead"] * OPT["share"][o["tag"][0]] if o["tag"][1] == 0 and 0 <= o["tag"][0] < STEPS else 0)
-            for i, o in enumerate(ops)]
+    tail = [tail[i] + (OPT["lead"] if o["tag"][1] == 0 and 0 <= o["tag"][0] < STEPS else 0) for i, o in enumerate(ops)]
     for i in range(n - 1, -1, -1):
         for j in ops[i]["deps"]:
             tail[j] = max(tail[j], tail[i] + 1)
@@ -524,12 +453,17 @@ def first_order(ops):
     return sorted(range(n), key=lambda i: (st[i], i))
 
 
-def improve(ops, seq):
-    n, tries = len(ops), OPT["tries"]
+def swap(o):
+    (o["eng"], o["cost"], o["call"]), o["alt"] = o["alt"], (o["eng"], o["cost"], o["call"])
+
+
+def improve(ops, seq, tries, temp, costs=MIDDLE):
+    n = len(ops)
+    LAT_X, LAT_S, LAT_R = costs[2:]
     eng = [o["eng"] for o in ops]
     lat = [LAT_R if o["kind"] == "r" else o["cost"] for o in ops]
     hold = [60 if o["kind"] == "d" else o["cost"] for o in ops]
-    other = [o["alt"][:2] if o["alt"] and (o["tag"][0] < 1 or min(o["cost"], o["alt"][1]) < OPT["big"]) else None for o in ops]
+    other = [o["alt"][:2] if o["alt"] else None for o in ops]
     keep, anc, succ = [], [], [[] for _ in ops]
     for i, o in enumerate(ops):
         a, k = 0, []
@@ -570,7 +504,7 @@ def improve(ops, seq):
                     t, w = st[j] + d, -1 - j
             if -0.01 < t - st[i] - by < 0.01:
                 run += 1
-                if run > RUN and k > k1:
+                if run > 40 and k > k1:
                     if by:
                         for e in order[k:]:
                             st[e] += by
@@ -579,7 +513,6 @@ def improve(ops, seq):
                 run, by = 0, t - st[i]
             st[i], why[i] = t, w
         return max(st[e] + lat[e] for e in ends)
-    RUN = OPT["run"]
 
     def hand(i):
         link(prev[i], nxt[i])
@@ -610,11 +543,11 @@ def improve(ops, seq):
                 i = w if w >= 0 else -1 - w
         x = (x * 1103515245 + 12345) % 2147483648
         j, i = moves[x * len(moves) >> 31]
-        if it % OPT["free"] == 0:
+        if it % 10 == 0:
             i = j = either[x * len(either) >> 31]
             if eng[i] == "S" and x % 4:
                 continue
-        far, ahead = (x >> 8) % OPT["far"], (x >> 12) & 1
+        far, ahead = (x >> 8) % 3, (x >> 12) & 1
         if i != j:
             if nxt[j] != i:
                 moves = []
@@ -652,8 +585,8 @@ def improve(ops, seq):
         old = st[:], why[:]
         new = starts(a, b)
         x = (x * 1103515245 + 12345) % 2147483648
-        if new <= cur or x / 2147483648.0 < math.exp((cur - new) / (OPT["temp"] * (1 - it / tries) + 1)):
-            if abs(new - cur) > 0.01 or x % OPT["lazy"] == 0:
+        if new <= cur or x / 2147483648.0 < math.exp((cur - new) / (temp * (1 - it / tries) + 1)):
+            if abs(new - cur) > 0.01 or x % 4 == 0:
                 moves = []
             cur = new
             for k in range(a, b + 1):
@@ -672,12 +605,22 @@ def improve(ops, seq):
             st[:], why[:] = old
     for o, e in zip(ops, best[2]):
         if e != o["eng"]:
-            (o["eng"], o["cost"], o["call"]), o["alt"] = o["alt"], (o["eng"], o["cost"], o["call"])
+            swap(o)
     return best[:2]
 
 
-OPT.update(free=10, mode="VPVPVPVP", dflip=2, far=3, lead=6000, passes=((50000, 400), (580000, 200)), gs=((1,), (1,)),
-           up=(0, 2, 4), g2=(), ds=())
+def program():
+    ops = plan()
+    seq = first_order(ops)
+    for tries, temp in OPT["passes"]:
+        seq = improve(ops, seq, tries, temp)[1]
+    slow = plan(CAUTIOUS)
+    for o, first in zip(slow, ops):
+        if o["eng"] != first["eng"]:
+            swap(o)
+    return slow, improve(slow, seq, 150000, 40, CAUTIOUS)[1]
+
+
 _PLAN = []
 
 
@@ -686,12 +629,7 @@ def rank_program(g, core, T, topo):
     if rank is None:
         return
     if not _PLAN:
-        ops = plan()
-        seq = first_order(ops)
-        for tries, temp in OPT["passes"]:
-            OPT.update(tries=tries, temp=temp)
-            seq = improve(ops, seq)[1]
-        _PLAN.append((ops, seq))
+        _PLAN.append(program())
     ops, seq = _PLAN[0]
     N = len(T.cores)
     nxt, prv = T.cores[(rank + 1) % N], T.cores[(rank - 1) % N]
@@ -709,8 +647,8 @@ def rank_program(g, core, T, topo):
         if a[0] == "I":
             return T[a[1]][:, a[2]:a[3]].indirect(T[a[4]][:, a[5]:a[6]])
         p = a[5] if a[5] is not None else slice(None)
-        if a[4] == HALF_ROWS:
-            return T[a[1]][p, a[2] // 16:a[2] // 16 + 15, a[2] % 16:a[2] % 16 + 8]
+        if isinstance(a[4], tuple):
+            return T[a[1]][p, a[2] // 16:a[2] // 16 + 15, a[2] % 16:a[2] % 16 + a[4][0]]
         if len(SCRATCH[a[1]][1]) == 3:
             return T[a[1]][p, a[2] // 16:a[3] // 16, :]
         if a[4] == 1:

@@ -11,7 +11,8 @@ C = 8
 Q0 = (8, 0)
 SEG = [[16 * (16 - (Q0[h] + q)) + 2 for q in range(C)] for h in range(2)]
 TOT = [sum(s) for s in SEG]
-OPT = dict(lead=3000.0, seed=1, passes=((50000, 400), (600000, 200)))
+OPT = dict(lead=3000.0, seed=1, passes=((1, 40, 300), (4, 190, 150)), split=(0, 1), tensor=(), fine=(0, 1), two=False,
+           off=((1, 0),), wrap="P", cand="P")
 
 SCRATCH = {}
 PART = {}
@@ -24,21 +25,22 @@ def _sb(name, n, d):
 for _n, _w, _d in [
     ("xs", 4096, BF), ("vs", 4224, BF), ("ctab", 4240, F32), ("lan", 256, I32), ("s0w", 256, I32), ("wti", 8, I32),
     ("srow", 256, BF), ("ci", 16, I32), ("cf", 32, F32), ("t0", 144, F32), ("t1", 256, F32), ("t2", 384, F32),
-    ("t3", 144, F32), ("ti", 8, I32), ("idb", 128, BF), ("idh", 128, F16), ("nid", 128, BF), ("c31", 128, BF),
-    ("n31", 128, BF), ("c43", 128, BF), ("n43", 128, BF), ("i19", 128, BF), ("one", 480, BF), ("blk", 128, BF),
+    ("t3", 144, F32), ("t4", 128, F32), ("idb", 128, BF), ("idh", 128, F16), ("nid", 128, BF), ("c31", 128, BF),
+    ("n31", 128, BF), ("c45", 128, BF), ("n45", 128, BF), ("n43", 128, BF), ("i15", 128, BF), ("i24", 128, BF),
+    ("one", 480, BF), ("blk", 128, BF), ("cont", 120, BF), ("rsf", 120, F32),
     ("sel", 144, BF), ("selk", 144, F16), ("selw", 144, BF), ("selb", 144, BF), ("wme", 128, F16), ("nwm", 128, F16),
-    ("wx", 128, F16), ("ta", 128, BF), ("tb", 128, BF), ("tc", 64, BF), ("mtab", 128, F32), ("rst", 120, F32),
-    ("ltl", 8, U16), ("ends", 8, U16), ("val", 8, BF), ("lst", 8, F32), ("tri", 272, BF), ("hrow", 272, F16),
+    ("wx", 128, F16), ("ta", 128, BF), ("tb", 120, BF), ("tc", 64, BF), ("rst", 120, F32),
+    ("ends", 8, U16), ("val", 8, BF), ("lst", 8, F32), ("tri", 272, BF), ("hrow", 272, F16),
     ("win", 16, BF), ("fsel", 256, BF), ("thr", 8, BF), ("hc", 32, F16), ("aq", 16, BF), ("ay", 8, F32), ("aj", 16, F32),
 ]:
     _sb(_n, _w, _d)
 for _h in range(2):
     for _n, _w, _d in [
-        ("ld", 128, I32), ("lu", 128 * STEPS, U16), ("su", 128 * STEPS, U16), ("home", 256, F32), ("a", 2048, BF),
+        ("ld", 256, I32), ("lu", 128 * STEPS, U16), ("su", 128 * STEPS, U16), ("home", 256, F32), ("a", 2048, BF),
         ("at", 2048, F16), ("f", 1920, BF), ("d", 1920, F16), ("ab", 1920, F16), ("cl", 1920, BF), ("lall", 1088, I32),
-        ("w4", 256, F16), ("w2", 256, I32), ("w3", 384, BF), ("hu", 128, U16), ("sc", 240, I32), ("k", 48, I32),
-        ("m", 16, F32), ("ou", 64, U16), ("eq", TOT[_h], BF), ("es", TOT[_h], BF), ("msk", TOT[_h], BF),
-        ("snd", 8 * STEPS, I32), ("rcv", 8 * STEPS, I32), ("fo", 128, F32), ("sl", 16, U16), ("own", 64, I32),
+        ("w4", 256, F16), ("w2", 256, I32), ("w3", 384, BF), ("hu", 128, U16), ("sc", 248, I32), ("k", 48, I32),
+        ("sp", 120, BF), ("ou", 64, U16), ("eq", TOT[_h], BF), ("es", TOT[_h], BF), ("msk", TOT[_h], BF),
+        ("snd", 8 * STEPS, I32), ("rcv", 8 * STEPS + 8, I32), ("fo", 128, F32), ("sl", 16, U16), ("own", 192, I32), ("rr", 480, BF), ("cd", 120, BF),
     ]:
         _o = SCRATCH[_n][1][1] if _h else 0
         PART[_n + str(_h)] = (_n, _o, _w)
@@ -54,8 +56,8 @@ for _n in ("pn", "pf"):
 
 SEMAPHORES = ["sv", "sa", "sp", "sg", "gone"] + ["dm%d" % i for i in range(50)] + ["arr%d" % i for i in range(6 * STEPS)]
 
-CYC, PCYC = 1.04, 0.56
-MIDDLE, CAUTIOUS = (1.56, 3.8, 130.0, 90.0, 2400.0), (1.62, 4.1, 140.0, 95.0, 2800.0)
+COSTS = [(1.1, 1.65, 4.0, 280.0, 200.0, 2800.0, 0.9, 0.51), (0.85, 1.56, 3.8, 240.0, 170.0, 3000.0, 0.8, 0.51),
+         (1.05, 1.3, 3.0, 180.0, 120.0, 2400.0, 0.7, 0.72), (1.22, 2.0, 5.2, 240.0, 160.0, 3400.0, 1.0, 0.51)]
 SIZE = {F32: 4, I32: 4, BF: 2, F16: 2, U16: 2}
 
 
@@ -64,8 +66,8 @@ def A(name, lo=0, hi=None, step=1, part=None):
     return ("A", name, o + lo, o + (w if hi is None else hi), step, part)
 
 
-def rows(name, lo, w):
-    return ("A", name, lo, lo + 240, (w,), None)
+def rows(name, lo, w, n=15):
+    return ("A", name, lo, lo + 16 * n, (w, n), None)
 
 
 def IX(name, lo, hi, off, c, d):
@@ -77,7 +79,7 @@ def count(a):
     if a[0] == "I":
         return 16 * (a[6] - a[5])
     if isinstance(a[4], tuple):
-        return 15 * a[4][0]
+        return a[4][0] * a[4][1]
     return len(range(a[2], a[3], abs(a[4])))
 
 
@@ -95,8 +97,9 @@ def narrow(*xs):
     return all(SIZE[SCRATCH[a[1]][2]] == 2 for a in xs)
 
 
-def plan(costs=MIDDLE):
-    GATHER, SCATTER = costs[:2]
+def plan(costs=COSTS[0]):
+    CYC, GATHER, SCATTER = costs[:3]
+    PCYC = costs[7] * CYC
     ops = []
     acc = {}
     tag = [-9, 0, "c"]
@@ -131,6 +134,7 @@ def plan(costs=MIDDLE):
                     old.append((i, lo, hi, w))
         for j in after:
             deps[j] = True
+        cost = costs[5] + cost if kind == "r" else cost * costs[6] if kind == "d" else cost
         ops.append(dict(eng=eng, cost=cost, call=call, deps=deps, kind=kind, tag=tuple(tag), alt=alt))
         return i
 
@@ -201,8 +205,7 @@ def plan(costs=MIDDLE):
 
     al = slice(None)
     dma("Y", A("lan"), H("lanes", al, al), 2700)
-    first = [dma("S", A("xs", 0, 2048), H("x", al, slice(0, 2048)), 5900),
-             dma("Y", A("xs", 2048, 4096), H("x", al, slice(2048, 4096)), 5900)]
+    first = [dma("S", A("xs"), H("x", al, al), 5900)]
     iota(A("s0w"), [[0, 256]], 0, 0)
     dma("Y", A("wti", 0, 1), H("wt", al, al), 2000)
     dma("Y", A("s0w", part=slice(0, 128, 16)), H("s0", al, al), 2000)
@@ -215,10 +218,15 @@ def plan(costs=MIDDLE):
     iota(A("t1", 128, 256), [[0, 16], [1, 8]], 0, 0)
     iota(A("t3", 0, 128), [[1, 8], [0, 16]], 0, 0)
     iota(A("t3", 128, 136), [[16, 8]], 0, 0)
-    iota(A("t3", 136, 144), [[3840, 2], [944, 4]], -128, 0)
-    iota(A("mtab", 0, 120), [[0, 8], [1, 15]], 1, 0)
-    iota(A("mtab", 120, 128), [[0, 8]], 0, 0)
+    iota(A("t3", 136, 144), [[960, 2], [236, 4]], -32, 0)
+    iota(A("t4", 0, 120), [[0, 2], [2, 4], [8, 15]], 17, 0)
+    iota(A("t4", 120, 128), [[128, 2], [1, 4]], 264, 0)
+    iota(A("tb"), [[0, 8], [64, 15]], 12288 + 64, 0)
     iota(A("ctab"), [[1, 4240]], -2176, 0)
+    if OPT["two"]:
+        ms(A("lall0", 0, 272), 2 ** 24)
+        add("Y", 4000, ("dmas", [(A("lall", 272 * i, 272 * i + 272), A("lall", 0, 272)) for i in range(1, 8)]),
+            [A("lall", 0, 272)], [A("lall", 272, 2176)], kind="d", after=first)
     ts(col("ci", 1), col("ci", 0), 15, ALU.bitwise_and)
     ts(col("ci", 2), col("ci", 0), 4, ALU.arith_shift_right)
     ts(col("ci", 3), col("ci", 0), 7, ALU.bitwise_and)
@@ -232,28 +240,28 @@ def plan(costs=MIDDLE):
     tt(A("wme"), A("t2", 256, 384), A("t2", 0, 128), ALU.mult)
     lin("S", A("wx"), A("wme"), 1.0, 1024.0)
     lin("S", A("nwm"), A("wx"), -1.0, 1024.0)
-    for name, f in (("c31", 2.0 ** 31), ("n31", -2.0 ** 31), ("c43", 1.5 * 2.0 ** 43), ("n43", -1.5 * 2.0 ** 43),
-                    ("nid", -1.0), ("idh", 1.0), ("i19", 2.0 ** 19)):
+    for name, f in (("c31", 2.0 ** 31), ("n31", -2.0 ** 31), ("c45", 1.5 * 2.0 ** 45), ("n45", (-1.125 if OPT["wrap"] == "P" else -1.5) * 2.0 ** 45),
+                    ("n43", -1.5 * 2.0 ** 43), ("nid", -1.0), ("idh", 1.0), ("i15", 29952.0), ("i24", 2.0 ** 24)):
         lin("S", A(name), A("idb"), f)
     ms(A("one"), 1.0)
     lin("S", col("cf", 8), col("wti", 0))
     lin("S", col("cf", 7), G_, 16.0, 15.0)
     ts(A("selb"), A("t0"), col("cf", 7), ALU.is_equal)
     ts(A("selw"), A("selb"), col("cf", 8), ALU.mult)
-    lin("S", A("sel"), A("selb"), 2.0 ** 16)
+    lin("S", A("sel"), A("selb"), 2.0 ** 18)
     lin("S", A("selk"), A("selb"), 1024.0)
     ts(col("cf", 16), J_, 8.0, ALU.is_ge, 65280.0, ALU.mult)
     lin("S", A("tc"), A("one", 0, 64), 256.0, col("cf", 16))
-    lin("S", A("ta", 0, 120), A("t0", 0, 120), 4096.0, 2048.0)
-    lin("S", A("tb", 0, 120), A("mtab", 0, 120), 64.0, 12288.0)
+    lin("S", A("ta", 0, 120), A("t4", 0, 120), 4096.0)
     ts(A("blk"), A("t3", 0, 128), G_, ALU.is_equal)
-    ts(A("rst"), A("mtab", 0, 120), 1.0, ALU.is_equal, 2.0 ** 25, ALU.mult)
+    ms(A("rst"), 0.0)
+    lin("S", A("rst", 0, 120, 15), A("t4", 120, 128), 8192.0, 6144.0)
+    ts(A("rsf"), A("rst"), 1.0, ALU.is_ge, 2.0 ** 25, ALU.mult)
+    ts(A("cont"), A("rst"), 1.0, ALU.is_lt)
+    ms(A("sp"), -1.0)
     ms(col("thr", 0), 2.5)
-    lin("S", col("cf", 9), J_, 1.0 / 15.0, 0.5 / 15.0 - 0.5)
-    lin("S", A("ti"), A("t3", 128, 136), 1.0 / 15.0, col("cf", 9))
-    ts(A("ltl"), A("ti"), C - 1.0, ALU.min)
     lin("S", A("val"), A("t3", 128, 136), 1.0, J_)
-    ts(A("lst"), A("t3", 136, 144), J_, ALU.subtract)
+    lin("S", A("lst"), A("t3", 136, 144), 1.0, J_)
     ts(A("tri", 0, 16), A("t0", 0, 16), J_, ALU.is_le, 8192.0, ALU.mult)
     lin("S", A("tri", 16, 272), A("one", 0, 256), 0.0)
     lin("S", A("hrow", 256, 272), A("one", 0, 16), 2048.0)
@@ -271,7 +279,7 @@ def plan(costs=MIDDLE):
     lin("S", A("srow"), A("s0w", 0, 256, -1))
     mm(group(A("pn", 0, 16), [(A("selb", 15 - j, 143 - j), A("srow", j, 256, 16)) for j in range(16)]))
     for h in range(2):
-        lin("S", A("rcv%d" % h, 0, C), A("pn", Q0[h], Q0[h] + C))
+        lin("S", A("sp%d" % h, 0, 120, 15), A("pn", Q0[h], Q0[h] + C), 1.0, 16.0)
 
     def prints(t, h):
         s = str(h)
@@ -285,19 +293,26 @@ def plan(costs=MIDDLE):
                 tag[:] = [t, h, "f%d" % (2 * pc + u)]
                 pt, bk = "pt%d" % u, "px%d" % (2 * pc + u)
                 o = 1024 * pc + 512 * u
-                if pc or not u:
-                    n = 32 if pc else 64
+                if pc or not u or h in OPT["fine"]:
+                    n = 32 if pc or h in OPT["fine"] else 64
                     lin("S", A("a" + s, o, o + 16 * n), IX("xs", 0, 4096, "lu" + s, l0 + o // 16, l0 + o // 16 + n))
                 lst = [("T", A(pt, 128 * i, 128 * i + 128), A("a" + s, o + 128 * i, o + 128 * i + 128)) for i in range(4)]
                 add("P", 512 * PCYC, ("tr", lst), [m[2] for m in lst] + [A("idb")], [m[1] for m in lst])
-                lin("V", A("at" + s, o, o + 512), A(pt, 0, 512), 1.0, 272.0)
+                off = (h, 2 * pc + u) in OPT["off"]
+                lin("V", A("at" + s, o, o + 512), A(pt, 0, 512), 1.0, 288.0 if off else 272.0)
 
                 def blocks(w, last):
                     return [(rows(bk, 240 * (i // 2) + 8 * (i % 2), 8), A("at" + s, o + 128 * i, o + 128 * i + 128), A(w, 8, 128),
-                             False, last and i == 3) for i in range(4)]
-                mm([(A(bk, 0, 480), A("c31"), A("one"), True, False)])
-                mm(blocks("wme", False) + [(A(bk, 0, 480), A("n31"), A("one"), False, False)] + blocks("nwm", True))
-                lin("S", A("f" + s, 960 * pc + 480 * u, 960 * pc + 480 * u + 480), A(bk, 0, 480), -1.0, 128.0)
+                             off, off or last and i == 3) for i in range(4)]
+                out = A("f" + s, 960 * pc + 480 * u, 960 * pc + 480 * u + 480)
+                if off:
+                    mm(blocks("nwm", True))
+                    lin("S", A("rr" + s), A(bk, 0, 480), 1.0, 127.5)
+                    tt(out, A("rr" + s), A(bk, 0, 480), ALU.subtract)
+                else:
+                    mm([(A(bk, 0, 480), A("c31"), A("one"), True, False)])
+                    mm(blocks("wme", False) + [(A(bk, 0, 480), A("n31"), A("one"), False, False)] + blocks("nwm", True))
+                    lin("S", out, A(bk, 0, 480), -1.0, 128.0)
             tag[:] = [t, h, "u%d" % pc]
             a, b = 60 * pc, 60 * pc + 60
             pu = rows(bk, 0, 4)
@@ -309,50 +324,72 @@ def plan(costs=MIDDLE):
             lin("V", A("hu" + s, a, b), A(w2, 128 + a, 128 + b))
             lin("S", A(w4, 128 + a, 128 + b), A(w2, 128 + a, 128 + b), 1.0, -2048.0)
         tag[:] = [t, h, "key"]
-        tt(A(w3, 0, 128), IX("rcv" + s, 8 * t, 8 * t + 8, "ltl", 0, 8), A("mtab"), ALU.is_gt)
+        if t:
+            lin("S", A("sp" + s, 0, 120, 15), A("rcv" + s, 8 * t, 8 * t + 8), 1.0, 16.0)
+        if OPT["wrap"] == "P":
+            scan(A(w3, 0, 120), A("cont"), A("sp" + s), ALU.mult, ALU.add)
+        else:
+            scan(A("cd" + s), A("cont"), A("sp" + s), ALU.mult, ALU.add)
+            ts(A(w3, 0, 120), A("cd" + s), 17.5, ALU.is_gt, 2.0 ** 20, ALU.mult)
         lin("S", A(w3, 256, 376), A(w4, 0, 120), 1.0, 12288.0 - 31.5)
         tag[:] = [t, h, "flip"]
-        lin("S", A("own" + s), A("lu" + s, l0 + 64, l0 + 128), 4096.0)
-        tt(A(lall, 0, 64), A("own" + s), A("lu" + s, l0, l0 + 64), ALU.add)
-        dma("Y", A("dl" + s), A(lall, 0, 64), 3500)
-        for w in (64, 256):
-            add("Y", 3500, ("dmas", [(A(lall, w * i, w * i + w), A(lall, 0, w)) for i in (1, 2, 3)]),
-                [A(lall, 0, w)], [A(lall, w, 4 * w)], kind="d")
+        if OPT["two"]:
+            lin("S", A("own" + s, 0, 64), A("lu" + s, l0 + 64, l0 + 128), 4096.0, -2.0 ** 24)
+            tt(A("own" + s, 64, 128), A("own" + s, 0, 64), A("lu" + s, l0, l0 + 64), ALU.add)
+            lin("S", A("own" + s, 128, 192), A("lu" + s, l0 + 64, l0 + 128), 4096.0)
+            dma("Y", A("dl" + s), A("own" + s, 64, 128), 3000)
+        else:
+            lin("S", A("own" + s, 0, 64), A("lu" + s, l0 + 64, l0 + 128), 4096.0)
+            tt(A(lall, 0, 64), A("own" + s, 0, 64), A("lu" + s, l0, l0 + 64), ALU.add)
+            dma("Y", A("dl" + s), A(lall, 0, 64), 3500)
+            for w in (64, 256):
+                add("Y", 3500, ("dmas", [(A(lall, w * i, w * i + w), A(lall, 0, w)) for i in (1, 2, 3)]),
+                    [A(lall, 0, w)], [A(lall, w, 4 * w)], kind="d")
         moves = [(A(lall, 64 * max(k, 1) + 64, 1088, part=slice(k, 128, 16)), A("dl" + s, 64 * (k == 0), 1024 - 64 * k))
                  for k in range(16)]
         add("Y", 6000, ("dmas", moves), [A("dl" + s)], [A(lall, 128, 1088)], kind="d")
 
     def send(sem, src, dst):
         sent = add("G", 300, ("send", "arr%d" % sem, 0, src, dst), [src], [], kind="s")
-        add("R", 0, ("arr", "arr%d" % sem), [], [dst], kind="r", after=[sent])
+        add("R", 1200 if sem == 4 * STEPS else 600 if count(dst) == 128 else 0, ("arr", "arr%d" % sem), [], [dst], kind="r", after=[sent])
 
     def decide(t, h):
         s = str(h)
         B, cut = 16 * Q0[h], sum(SEG[h][4:])
-        w3, w4, k, m_, ou, ld, sc = "w3" + s, "w4" + s, "k" + s, "m" + s, "ou" + s, "ld" + s, "sc" + s
-        for q0, q1 in ((4, 8), (0, 4)) if t < STEPS - 1 else ((0, 8),):
+        w3, w4, k, ou, ld, sc = "w3" + s, "w4" + s, "k" + s, "ou" + s, "ld" + s, "sc" + s
+        for q0, q1 in ((4, 8), (0, 4)) if t < STEPS - 1 or h in OPT["split"] else ((0, 8),):
             c0, c1, early = 15 * q0, 15 * q1, q0 // 4
             tag[:] = [t, h, "near"]
-            mm(group(A("pn", c0, c1), [(A("c43"), A("one", c0, c1))], last=False))
+            mm(group(A("pn", c0, c1), [(A("c45"), A("one", c0, c1))], last=False))
             for pc in range(q1 // 4 - 1, q0 // 4 - 1, -1):
                 for pi in (2 * pc, 2 * pc + 1):
                     tag[:] = [t, h, "d%d" % pi]
                     a, b = 480 * pi, 480 * pi + 480
-                    tt(A("d" + s, a, b), IX("vs", 128, 4224, "hu" + s, 30 * pi, 30 * pi + 30), A("f" + s, a, b), ALU.subtract)
-                    act(A("ab" + s, a, b), A("d" + s, a, b), AF.Abs)
+                    marks = IX("vs", 128, 4224, "hu" + s, 30 * pi, 30 * pi + 30)
+                    if (t, h, pi) in OPT["tensor"]:
+                        lin("S", A("d" + s, a, b), marks)
+                        bk = A("px%d" % pi, 0, 480)
+                        mm(group(bk, [(A("nid"), A("f" + s, a, b)), (A("idh"), A("d" + s, a, b))]))
+                        act(A("ab" + s, a, b), bk, AF.Abs)
+                    else:
+                        tt(A("d" + s, a, b), marks, A("f" + s, a, b), ALU.subtract)
+                        act(A("ab" + s, a, b), A("d" + s, a, b), AF.Abs)
                     ts(A("cl" + s, a, b), A("ab" + s, a, b), col("thr", 0), ALU.is_le, -3.5 / 16, ALU.add)
                 mm(group(A("pn", 60 * pc, 60 * pc + 60), sums("sel", "cl" + s, pc), False, False))
             tag[:] = [t, h, "pick"]
-            mm(group(A("pn", c0, c1), [(A("n43"), A("one", c0, c1)), (A("idb"), A("ta", c0, c1)),
-                                       (A("idh"), A(w4, 128 + c0, 128 + c1)), (A("i19"), A(w3, c0, c1))], first=False))
-            scan(A(sc, c0, c1), A("rst", c0, c1), A("pn", c0, c1), ALU.add, ALU.min)
+            if OPT["wrap"] == "P":
+                wrap = [(A("n45"), A("one", c0, c1)), (A("i15"), A(w3, c0, c1)), (A("n43"), A("one", c0, c1))]
+            else:
+                wrap = [(A("n45"), A("one", c0, c1)), (A("idb"), A(w3, c0, c1))]
+            mm(group(A("pn", c0, c1), wrap + [(A("idb"), A("ta", c0, c1)), (A("idh"), A(w4, 128 + c0, 128 + c1))], first=False))
+            scan(A(sc, c0, c1), A("rst", c0, c1), A("pn", c0, c1), ALU.max, ALU.min)
             k1 = A(sc, c0 + 14, c1, 15)
-            ts(A(k, 16 + q0, 16 + q1), k1, 0x100FFF, ALU.bitwise_and)
-            ts(A(ou, q0, q1), A(k, 16 + q0, 16 + q1), 4096.0, ALU.min, 128.0, ALU.add)
+            ts(A(k, 16 + q0, 16 + q1), k1, 8191, ALU.bitwise_and)
+            lin("V", A(ou, q0, q1), A(k, 16 + q0, 16 + q1), 1.0, -1920.0)
             lin("S", A("hrow", B + 16 * q0, B + 16 * q1), IX("ctab", 0, 4240, ou, q0, q1))
-            lin("V", A("hc", 16 * h + q0, 16 * h + q1), A(ou, q0, q1), 1.0, -2176.0)
-            ts(A(k, 24 + q0, 24 + q1), k1, 6, ALU.arith_shift_right, 127 * 64, ALU.bitwise_and)
-            tt(A(ou, 8 + q0, 8 + q1), A(k, 24 + q0, 24 + q1), A("lst", q0, q1), ALU.subtract)
+            lin("V", A("hc", 16 * h + q0, 16 * h + q1), A(k, 16 + q0, 16 + q1), 1.0, -4096.0)
+            ts(A(k, 24 + q0, 24 + q1), k1, 11, ALU.arith_shift_right, 127 * 4, ALU.bitwise_and)
+            lin("S", A(ou, 8 + q0, 8 + q1), A(k, 24 + q0, 24 + q1), 4.0, J_)
             tag[:] = [t, h, "win"]
             for q in range(q0, q1):
                 o, w = seg0(h, q), SEG[h][q]
@@ -363,34 +400,56 @@ def plan(costs=MIDDLE):
             a = 32 + 16 * early
             tt(A(ou, a, a + 16), IX("es" + s, 0, b, "ends", 4 * early + 2 * h, 4 * early + 2 * h + 1), A(ou, 0, 16), ALU.min)
             for q in range(q0, q1, 4):
-                ts(A(ld, 16 * q, 16 * q + 64), IX("lall" + s, 0, 1088, ou, a + 8 + q, a + 12 + q),
-                   *((12, ALU.arith_shift_right) if q else (4095, ALU.bitwise_and)))
+                turned = IX("lall" + s, 0, 1088, ou, a + 8 + q, a + 12 + q)
+                if OPT["two"]:
+                    tt(A(ld, 128 + 16 * q, 192 + 16 * q), turned,
+                       A("own" + s, 128, 192) if q else A("lu" + s, 128 * t, 128 * t + 64), ALU.min)
+                    turned = A(ld, 128 + 16 * q, 192 + 16 * q)
+                ts(A(ld, 16 * q, 16 * q + 64), turned,
+                   *((12, ALU.arith_shift_right, 4095, ALU.bitwise_and) if q else (4095, ALU.bitwise_and)))
             if t < STEPS - 1:
                 o = 128 * t + 16 * q0
                 src, dst = A("su" + s, o, o + 64), A("lu" + s, o + 128, o + 192)
                 lin("V", src, A(ld, 16 * q0, 16 * q1))
             else:
                 src, dst = A("home" + s, 0, 128), A("home" + s, 128, 256)
-                lin("V", src, A(ld, 0, 128, -1))
-            send(2 * t + h + 4 * STEPS * early, src, dst)
+                lin("V", A("home" + s, 128 - 16 * q1, 128 - 16 * q0), A(ld, 16 * q0, 16 * q1, -1))
+            if t < STEPS - 1 or not q0:
+                send(2 * t + h + 4 * STEPS * early, src, dst)
         tag[:] = [t, h, "mark"]
-        lin("S", A(ou, 16, 24), A(k, 24, 32), 0.25, J_)
+        tt(A(ou, 16, 24), A(k, 24, 32), A("lst"), ALU.add)
         lin("S", A("fsel", B, B + 128), IX("f" + s, 0, 1920, ou, 16, 24))
         tag[:] = [t, h, "far"]
-        mm(group(A("pf", 0, 120), [(A("idb"), A("tb", 0, 120)), (A("idh"), A(w4, 0, 120)), (A("nid"), A(w3, 256, 376))], last=False))
-        for pc in (1, 0):
-            mm(group(A("pf", 60 * pc, 60 * pc + 60), sums("selk", "ab" + s, pc), False, pc == 0))
-        scan(A(sc, 120, 240), A("rst"), A("pf", 0, 120), ALU.add, ALU.min)
-        ts(A(k, 32, 40), A(sc, 134, 240, 15), 15, ALU.bitwise_and)
-        tt(A(m_, 0, 8), A("rcv" + s, 8 * t, 8 * t + 8), A(k, 32, 40), ALU.subtract)
+        mm(group(A("pf", 0, 120), [(A("idb"), A("tb")), (A("idh"), A(w4, 0, 120)), (A("nid"), A(w3, 256, 376))], last=False))
+        far = [(A("selk", 15 - j, 143 - j), A("ab" + s, j, 1920, 16)) for j in range(16)]
+        for j in range(0, 16, 4):
+            mm(group(A("pf", 0, 120), far[j:j + 4], False, j == 12))
+        scan(A(sc, 120, 240), A("rsf"), A("pf", 0, 120), ALU.add, ALU.min)
         tag[:] = [t, h, "s"]
-        wn = A("win", Q0[h], Q0[h] + C)
-        ts(wn, A(ou, 32, 40), 127.5, ALU.is_gt)
-        tt(A(m_, 8, 16), A(m_, 0, 8), wn, ALU.mult)
+        lost, near = A("win", Q0[h], Q0[h] + C), A(sc, 134, 240, 15)
         src, dst = A("snd" + s, 8 * t, 8 * t + 8), A("rcv" + s, 8 * t + 8, 8 * t + 16)
-        if t == STEPS - 1:
+        ts(lost, A(ou, 32, 40), 127.5, ALU.is_le, 2.0 ** 24 if OPT["cand"] == "V" else 1.0, ALU.mult)
+        if t < STEPS - 1 and OPT["cand"] == "V":
+            tt(A(k, 40, 48), A("sp" + s, 0, 120, 15), lost, ALU.max)
+            tt(A(k, 32, 40), A(k, 40, 48), near, ALU.min)
+            ts(src, A(k, 32, 40), 15, ALU.bitwise_and)
+        elif OPT["cand"] == "V":
+            tt(A(k, 40, 48), A("rcv" + s, 8 * t, 8 * t + 8), lost, ALU.max)
+            tt(A(k, 32, 40), A(k, 40, 48), near, ALU.min)
+            ts(src, A(k, 32, 40), 15, ALU.bitwise_and)
+            lin("V", A("sl" + s, 0, 8), src)
             src, dst = A("sl" + s, 0, 8), A("sl" + s, 8, 16)
-        tt(src, A(m_, 8, 16), A(k, 32, 40), ALU.add)
+        elif t < STEPS - 1:
+            mm(group(A("pf", 128, 136), [(A("idb"), A("sp" + s, 0, 120, 15)), (A("i24"), lost)]))
+            tt(A(k, 32, 40), A("pf", 128, 136), near, ALU.min)
+            ts(src, A(k, 32, 40), 15, ALU.bitwise_and)
+        else:
+            old = A("rcv" + s, 8 * t, 8 * t + 8)
+            ts(src, near, 15, ALU.bitwise_and)
+            tt(A(k, 32, 40), src, old, ALU.subtract)
+            tt(A(k, 40, 48), A(k, 32, 40), lost, ALU.mult)
+            src, dst = A("sl" + s, 0, 8), A("sl" + s, 8, 16)
+            tt(src, A(k, 40, 48), old, ALU.add)
         send(2 * (STEPS + t) + h, src, dst)
 
     def close_step(t):
@@ -399,7 +458,7 @@ def plan(costs=MIDDLE):
             cp(IX("vs", 0, 4224, "ou%d" % h, 32, 40), A("fsel", 16 * Q0[h], 16 * Q0[h] + 128))
         if t < STEPS - 1:
             mm(group(A("pn", 256, 272), [(A("blk"), A("win"))]))
-            act(A("aj"), A("pn", 256, 272), scale=-1.0, bias=48.40625, accum=col("ay", 0))
+            act(A("aj"), A("pn", 256, 272), scale=2.0 ** -24 if OPT["cand"] == "V" else 1.0, bias=32.40625, accum=col("ay", 0))
             lin("S", col("aq", 0), col("ay", 0), 1.0, -4.0)
             lin("S", col("thr", 0), col("aq", 0), -1.0, col("ay", 0))
 
@@ -410,8 +469,8 @@ def plan(costs=MIDDLE):
             decide(t, h)
         close_step(t)
     tag[:] = [99, 9, "out"]
-    cut = [0, 920, 1840, ROT, 4096]
-    for k in range(4):
+    cut = [0, ROT, 4096]
+    for k in range(2):
         o = (cut[k] - ROT) % 4096
         dma("YS"[k % 2], H("yv", al, slice(o, o + cut[k + 1] - cut[k])), A("vs", 128 + cut[k], 128 + cut[k + 1]), 4800)
     for h in range(2):
@@ -424,11 +483,11 @@ def plan(costs=MIDDLE):
 
 def first_order(ops):
     n = len(ops)
-    LAT_X, LAT_S, LAT_R = MIDDLE[2:]
+    LAT_X = 130.0
     tail = [0.0] * n
     for i in range(n - 1, -1, -1):
         o = ops[i]
-        tail[i] += LAT_R if o["kind"] == "r" else o["cost"]
+        tail[i] += o["cost"]
         for j in o["deps"]:
             tail[j] = max(tail[j], tail[i] + LAT_X)
     tail = [tail[i] + (OPT["lead"] if o["tag"][1] == 0 and 0 <= o["tag"][0] < STEPS else 0) for i, o in enumerate(ops)]
@@ -449,7 +508,7 @@ def first_order(ops):
                 t = max(t, b[k][1])
                 k += 1
             b.insert(k, (t, t + hold))
-        st[i], end[i] = t, t + (LAT_R if o["kind"] == "r" else o["cost"])
+        st[i], end[i] = t, t + o["cost"]
     return sorted(range(n), key=lambda i: (st[i], i))
 
 
@@ -457,13 +516,13 @@ def swap(o):
     (o["eng"], o["cost"], o["call"]), o["alt"] = o["alt"], (o["eng"], o["cost"], o["call"])
 
 
-def improve(ops, seq, tries, temp, costs=MIDDLE):
+def improve(plans, costs, seq, tries, temp):
+    ops, K = plans[0], range(len(costs))
     n = len(ops)
-    LAT_X, LAT_S, LAT_R = costs[2:]
     eng = [o["eng"] for o in ops]
-    lat = [LAT_R if o["kind"] == "r" else o["cost"] for o in ops]
-    hold = [60 if o["kind"] == "d" else o["cost"] for o in ops]
-    other = [o["alt"][:2] if o["alt"] else None for o in ops]
+    lats = [[o["cost"] for o in plans[c]] for c in K]
+    holds = [[60 if o["kind"] == "d" else o["cost"] for o in plans[c]] for c in K]
+    other = [(o["alt"][0], [plans[c][i]["alt"][1] for c in K]) if o["alt"] else None for i, o in enumerate(ops)]
     keep, anc, succ = [], [], [[] for _ in ops]
     for i, o in enumerate(ops):
         a, k = 0, []
@@ -475,9 +534,9 @@ def improve(ops, seq, tries, temp, costs=MIDDLE):
         anc.append(a)
         keep.append(k)
 
-    def waits(i):
-        return [(j, lat[j] + ((LAT_S if eng[j] == eng[i] else LAT_X) if ops[i]["deps"][j] else 0)) for j in keep[i]]
-    pred = [waits(i) for i in range(n)]
+    def waits(c, i):
+        return [(j, lats[c][j] + (costs[c][4 if eng[j] == eng[i] else 3] if ops[i]["deps"][j] else 0)) for j in keep[i]]
+    preds = [[waits(c, i) for i in range(n)] for c in K]
     order = list(seq)
     prev, nxt, last = [None] * n, [None] * n, {}
 
@@ -491,9 +550,10 @@ def improve(ops, seq, tries, temp, costs=MIDDLE):
         if eng[i] != "R":
             link(last.get(eng[i]), i)
             last[eng[i]] = i
-    st, why = [0.0] * n, [None] * n
+    sts, whys = [[0.0] * n for c in K], [[None] * n for c in K]
 
-    def starts(k0, k1=n):
+    def starts(c, k0, k1=n):
+        st, why, hold, pred, lat = sts[c], whys[c], holds[c], preds[c], lats[c]
         run, by = 0, 0.0
         for k in range(k0, n):
             i = order[k]
@@ -516,8 +576,9 @@ def improve(ops, seq, tries, temp, costs=MIDDLE):
 
     def hand(i):
         link(prev[i], nxt[i])
-        (eng[i], lat[i]), other[i] = other[i], (eng[i], lat[i])
-        hold[i] = lat[i]
+        (eng[i], new), other[i] = other[i], (eng[i], [lats[c][i] for c in K])
+        for c in K:
+            lats[c][i] = holds[c][i] = new[c]
         a = b = pos[i]
         while a >= 0 and (order[a] == i or eng[order[a]] != eng[i]):
             a -= 1
@@ -525,14 +586,19 @@ def improve(ops, seq, tries, temp, costs=MIDDLE):
             b += 1
         link(order[a] if a >= 0 else None, i, order[b] if b < n else None)
         for e in [i] + succ[i]:
-            pred[e] = waits(e)
+            for c in K:
+                preds[c][e] = waits(c, e)
     ends = [i for i in range(n) if ops[i]["tag"][0] == 99]
     either = [i for i in range(n) if other[i]]
-    cur = starts(0)
-    best, x, moves = (cur, list(order), list(eng)), OPT["seed"], []
+    ways = [starts(c, 0) for c in K]
+    share = [ways[0] / w / len(K) for w in ways]
+    cur = ways[0]
+    best, x, moves = (cur, list(order), list(eng), ways), OPT["seed"], []
     pos = {i: k for k, i in enumerate(order)}
     for it in range(tries):
         if not moves:
+            c = (x >> 16) % len(K)
+            st, why, lat = sts[c], whys[c], lats[c]
             i = max(ends, key=lambda e: st[e] + lat[e])
             while why[i] is not None:
                 w = why[i]
@@ -582,19 +648,26 @@ def improve(ops, seq, tries, temp, costs=MIDDLE):
             else:
                 link(i, j, nxt[i])
             order[a:b + 1] = [e for e in seg if (e in mark) == ahead] + [e for e in seg if (e in mark) != ahead]
-        old = st[:], why[:]
-        new = starts(a, b)
         x = (x * 1103515245 + 12345) % 2147483648
-        if new <= cur or x / 2147483648.0 < math.exp((cur - new) / (temp * (1 - it / tries) + 1)):
+        bound = cur - math.log((x + 1) / 2147483649.0) * (temp * (1 - it / tries) + 1)
+        old, got, new = [], [], cur
+        for c in K:
+            old.append((sts[c][:], whys[c][:]))
+            got.append(starts(c, a, b))
+            new += (got[c] - ways[c]) * share[c]
+            if new > bound + temp:
+                break
+        if new <= bound:
             if abs(new - cur) > 0.01 or x % 4 == 0:
                 moves = []
-            cur = new
+            cur, ways = new, got
             for k in range(a, b + 1):
                 pos[order[k]] = k
             if cur < best[0] or x % 64 == 0:
-                cur = starts(0)
+                ways = [starts(c, 0) for c in K]
+                cur = sum(w * f for w, f in zip(ways, share))
             if cur < best[0]:
-                best = (cur, list(order), list(eng))
+                best = (cur, list(order), list(eng), ways)
         else:
             if i == j:
                 hand(i)
@@ -602,23 +675,296 @@ def improve(ops, seq, tries, temp, costs=MIDDLE):
                 order[a:b + 1] = seg
                 link(prev[e0], nxt[e0])
                 link(p, e0, q)
-            st[:], why[:] = old
-    for o, e in zip(ops, best[2]):
-        if e != o["eng"]:
-            swap(o)
-    return best[:2]
+            for c, (st, why) in enumerate(old):
+                sts[c], whys[c] = st, why
+    for i, e in enumerate(best[2]):
+        if e != ops[i]["eng"]:
+            for p in plans:
+                swap(p[i])
+    return best
+
+
+def justify(ops, costs, seq, rounds, noise):
+    n = len(ops)
+    hold = [0 if o["kind"] == "r" else 60 if o["kind"] == "d" else o["cost"] for o in ops]
+    fw = [[(j, ops[j]["cost"] + (costs[4 if ops[j]["eng"] == o["eng"] else 3] if w else 0)) for j, w in o["deps"].items()] for o in ops]
+    bw = [[] for _ in ops]
+    for i in range(n):
+        for j, d in fw[i]:
+            bw[j].append((i, d + hold[i] - hold[j]))
+
+    def place(key, pred, st):
+        busy, done = {}, [False] * n
+        for top in sorted(range(n), key=key.get):
+            stack = [top]
+            while stack:
+                i = stack[-1]
+                first = [j for j, d in pred[i] if not done[j]]
+                if first:
+                    stack += first
+                    continue
+                stack.pop()
+                if done[i]:
+                    continue
+                done[i] = True
+                t = max([st[i]] + [st[j] + d for j, d in pred[i]])
+                if hold[i]:
+                    b = busy.setdefault(ops[i]["eng"], [])
+                    k = len(b)
+                    while k and b[k - 1][1] > t:
+                        k -= 1
+                    while k < len(b) and b[k][0] < t + hold[i]:
+                        t = max(t, b[k][1])
+                        k += 1
+                    b.insert(k, (t, t + hold[i]))
+                st[i] = t
+        return st
+    x = [OPT["seed"]]
+
+    def turn(st, by):
+        key = {}
+        for i in range(n):
+            x[0] = (x[0] * 1103515245 + 12345) % 2147483648
+            key[i] = by * x[0] / 2147483648.0 - st[i] - hold[i]
+        return key
+    st = place({i: k for k, i in enumerate(seq)}, fw, [0.0] * n)
+    best = cur = (max(st[i] + ops[i]["cost"] for i in range(n)), st)
+    for r in range(rounds):
+        left = 1 - r / rounds
+        back = place(turn(cur[1], noise * left), bw, [o["cost"] - h for o, h in zip(ops, hold)])
+        st = place(turn(back, noise * left), fw, [0.0] * n)
+        new = (max(st[i] + ops[i]["cost"] for i in range(n)), st)
+        if new[0] < cur[0] + 300 * left:
+            cur = new
+        if new[0] < best[0]:
+            best = new
+    return sorted(range(n), key=lambda i: (best[1][i], i))
+
+
+def better(plans, costs, seq, sweeps, tries, temp, width):
+    ops, K = plans[0], range(len(costs))
+    n = len(ops)
+    eng = [o["eng"] for o in ops]
+    lats = [[o["cost"] for o in plans[c]] for c in K]
+    holds = [[60 if o["kind"] == "d" else o["cost"] for o in plans[c]] for c in K]
+    other = [(o["alt"][0], [plans[c][i]["alt"][1] for c in K]) if o["alt"] else None for i, o in enumerate(ops)]
+    keep, anc, succ = [], [], [[] for _ in ops]
+    for i, o in enumerate(ops):
+        a, k = 0, []
+        for j in sorted(o["deps"], reverse=True):
+            if not (a >> j) & 1:
+                k.append(j)
+                succ[j].append(i)
+            a |= anc[j] | (1 << j)
+        anc.append(a)
+        keep.append(k)
+
+    def gap(c, j, i):
+        return lats[c][j] + (costs[c][4 if eng[j] == eng[i] else 3] if ops[i]["deps"][j] else 0)
+    preds = [[[(j, gap(c, j, i)) for j in keep[i]] for i in range(n)] for c in K]
+    order = list(seq)
+    prev, nxt, last = [None] * n, [None] * n, {}
+
+    def link(*row):
+        for a, b in zip(row, row[1:]):
+            if a is not None:
+                nxt[a] = b
+            if b is not None:
+                prev[b] = a
+    for i in order:
+        if eng[i] != "R":
+            link(last.get(eng[i]), i)
+            last[eng[i]] = i
+    sts, whys, tails, exits = ([[0.0] * n for c in K] for _ in range(4))
+    tops = [[(0.0, None)] * (n + 1) for c in K]
+    pos = [0] * n
+
+    def starts(c, k0, k1):
+        st, why, hold, pred, tail, out, top = sts[c], whys[c], holds[c], preds[c], tails[c], exits[c], tops[c]
+        way, at = top[k0]
+        for k in range(k0, k1):
+            i = order[k]
+            w = prev[i]
+            t = 0.0 if w is None else st[w] + hold[w]
+            for j, d in pred[i]:
+                if st[j] + d >= t:
+                    t, w = st[j] + d, -1 - j
+            st[i], why[i] = t, w
+            e, q = out[i], nxt[i]
+            if q is not None and pos[q] >= k1 and hold[i] + tail[q] > e:
+                e = hold[i] + tail[q]
+            if t + e > way:
+                way, at = t + e, i
+            top[k + 1] = way, at
+        return way
+
+    def leave(c, i, k1):
+        return max([lats[c][i]] + [gap(c, i, j) + tails[c][j] for j in succ[i] if pos[j] >= k1])
+
+    def hand(i, k1):
+        link(prev[i], nxt[i])
+        (eng[i], new), other[i] = other[i], (eng[i], [lats[c][i] for c in K])
+        a = b = pos[i]
+        while a >= 0 and (order[a] == i or eng[order[a]] != eng[i]):
+            a -= 1
+        while b < n and (order[b] == i or eng[order[b]] != eng[i]):
+            b += 1
+        link(order[a] if a >= 0 else None, i, order[b] if b < n else None)
+        for c in K:
+            lats[c][i] = holds[c][i] = new[c]
+            exits[c][i] = leave(c, i, k1)
+            for e in [i] + succ[i]:
+                preds[c][e] = [(j, gap(c, j, e)) for j in keep[e]]
+        return max(a, 0)
+
+    def whole():
+        for k, i in enumerate(order):
+            pos[i] = k
+        for c in K:
+            exits[c][:] = lats[c]
+            tops[c][0] = (0.0, None)
+        return [starts(c, 0, n) for c in K]
+    ways = whole()
+    share = [ways[0] / w / len(K) for w in ways]
+    best, x = (ways[0], list(order), list(eng), ways), OPT["seed"]
+    for sweep in range(sweeps):
+        heat = temp * (1 - sweep / sweeps) + 1
+        order.sort(key=lambda i: (sts[0][i], pos[i]))
+        whole()
+        for w0 in range(-(x >> 8) % width // 2 - width // 2, n - 20, width // 2):
+            w0, w1 = max(w0, 0), min(w0 + width, n)
+            for c in K:
+                st, tail, hold = sts[c], tails[c], holds[c]
+                for i in reversed(order[w1:]):
+                    q = nxt[i]
+                    tail[i] = max(leave(c, i, 0), 0.0 if q is None else hold[i] + tail[q])
+                for i in order[w0:w1]:
+                    exits[c][i] = leave(c, i, w1)
+                tops[c][w0] = (max([st[i] + leave(c, i, w1) for i in order[:w0]]
+                                   + [st[i] + hold[i] + tail[nxt[i]] for i in order[:w0] if nxt[i] is not None and pos[nxt[i]] >= w1]
+                                   + [tail[i] for i in order[w1:] if prev[i] is None and not keep[i]] + [0.0]), None)
+            ways = [starts(c, w0, w1) for c in K]
+            cur, moves = sum(w * f for w, f in zip(ways, share)), []
+            either = [i for i in order[w0 + 8:w1 - 8] if other[i]]
+            for it in range(tries):
+                x = (x * 1103515245 + 12345) % 2147483648
+                if not moves:
+                    c = (x >> 16) % len(K)
+                    why, i = whys[c], tops[c][w1][1]
+                    while i is not None and pos[i] >= w0:
+                        w = why[i]
+                        if w is not None and w >= 0 and pos[w] >= w0 and not (anc[i] >> w) & 1:
+                            moves.append((w, i))
+                        if other[i] and w0 + 8 <= pos[i] < w1 - 8:
+                            moves.append((i, i))
+                        i = w if w is None or w >= 0 else -1 - w
+                    if not moves:
+                        continue
+                j, i = moves[x * len(moves) >> 31]
+                if it % 10 == 0 and either:
+                    i = j = either[x * len(either) >> 31]
+                far, ahead = (x >> 8) % 3, (x >> 12) & 1
+                if i != j:
+                    if nxt[j] != i:
+                        moves = []
+                        continue
+                    for _ in range(far):
+                        if ahead and prev[j] is not None and pos[prev[j]] >= w0:
+                            j = prev[j]
+                        if not ahead and nxt[i] is not None and pos[nxt[i]] < w1:
+                            i = nxt[i]
+                a, b = pos[j], pos[i]
+                seg = order[a:b + 1]
+                if i == j:
+                    p = prev[i]
+                    a = max(w0, min(hand(i, w1), a if p is None else pos[p]))
+                else:
+                    e0, way, deps = (i, prev, keep) if ahead else (j, nxt, succ)
+                    mark = {e0}
+                    for e in (reversed(seg) if ahead else seg):
+                        if e in mark:
+                            if e != e0 and eng[e] == eng[e0]:
+                                break
+                            mark.update(deps[e])
+                            if e != e0:
+                                mark.add(way[e])
+                    else:
+                        e = None
+                    if e is not None:
+                        continue
+                    p, q = prev[e0], nxt[e0]
+                    link(p, q)
+                    if ahead:
+                        link(prev[j], i, j)
+                    else:
+                        link(i, j, nxt[i])
+                    order[a:b + 1] = [e for e in seg if (e in mark) == ahead] + [e for e in seg if (e in mark) != ahead]
+                x = (x * 1103515245 + 12345) % 2147483648
+                bound = cur - math.log((x + 1) / 2147483649.0) * heat
+                old, got, new, part = [], [], cur, order[a:w1]
+                for c in K:
+                    st, why = sts[c], whys[c]
+                    old.append(([st[e] for e in part], [why[e] for e in part], tops[c][a:w1 + 1]))
+                    got.append(starts(c, a, w1))
+                    new += (got[c] - ways[c]) * share[c]
+                    if new > bound + heat:
+                        break
+                if new <= bound:
+                    if abs(new - cur) > 0.01 or x % 4 == 0:
+                        moves = []
+                    cur, ways = new, got
+                    if i != j:
+                        for k in range(a, b + 1):
+                            pos[order[k]] = k
+                else:
+                    if i == j:
+                        hand(i, w1)
+                    else:
+                        order[a:b + 1] = seg
+                        link(prev[e0], nxt[e0])
+                        link(p, e0, q)
+                    for c, (s0, w_, top) in enumerate(old):
+                        st, why = sts[c], whys[c]
+                        for e, u, v in zip(part, s0, w_):
+                            st[e], why[e] = u, v
+                        tops[c][a:w1 + 1] = top
+        ways = whole()
+        cur = sum(w * f for w, f in zip(ways, share))
+        if cur < best[0]:
+            best = (cur, list(order), list(eng), ways)
+    for i, e in enumerate(best[2]):
+        if e != ops[i]["eng"]:
+            for p in plans:
+                swap(p[i])
+    return best
 
 
 def program():
-    ops = plan()
-    seq = first_order(ops)
-    for tries, temp in OPT["passes"]:
-        seq = improve(ops, seq, tries, temp)[1]
-    slow = plan(CAUTIOUS)
-    for o, first in zip(slow, ops):
-        if o["eng"] != first["eng"]:
-            swap(o)
-    return slow, improve(slow, seq, 150000, 40, CAUTIOUS)[1]
+    plans = [plan(c) for c in COSTS]
+    seq = justify(plans[0], COSTS[0], first_order(plans[0]), 500, 600)
+    for sets, sweeps, temp in OPT["passes"]:
+        seq = better(plans, COSTS[:sets], seq, sweeps, 250, temp, 80)[1]
+    return plans[0], seq
+
+
+def view(T, a):
+    if not isinstance(a, tuple):
+        return a
+    if a[0] == "H":
+        return T[a[1]][a[2]]
+    if a[0] == "I":
+        return T[a[1]][:, a[2]:a[3]].indirect(T[a[4]][:, a[5]:a[6]])
+    p = a[5] if a[5] is not None else slice(None)
+    if isinstance(a[4], tuple):
+        r, c = divmod(a[2], 16)
+        return T[a[1]][p, r:r + a[4][1], c:c + a[4][0]]
+    if len(SCRATCH[a[1]][1]) == 3:
+        return T[a[1]][p, a[2] // 16:a[3] // 16, :]
+    if a[4] == 1:
+        return T[a[1]][p, a[2]:a[3]]
+    if a[4] < 0:
+        return T[a[1]][p, a[3] - 1:(a[2] - 1 if a[2] else None):a[4]]
+    return T[a[1]][p, a[2]:a[3]:a[4]]
 
 
 _PLAN = []
@@ -640,22 +986,7 @@ def rank_program(g, core, T, topo):
     esem = {"V": "sv", "S": "sa", "P": "sp", "G": "sg"}
 
     def ap(a):
-        if not isinstance(a, tuple):
-            return a
-        if a[0] == "H":
-            return T[a[1]][a[2]]
-        if a[0] == "I":
-            return T[a[1]][:, a[2]:a[3]].indirect(T[a[4]][:, a[5]:a[6]])
-        p = a[5] if a[5] is not None else slice(None)
-        if isinstance(a[4], tuple):
-            return T[a[1]][p, a[2] // 16:a[2] // 16 + 15, a[2] % 16:a[2] % 16 + a[4][0]]
-        if len(SCRATCH[a[1]][1]) == 3:
-            return T[a[1]][p, a[2] // 16:a[3] // 16, :]
-        if a[4] == 1:
-            return T[a[1]][p, a[2]:a[3]]
-        if a[4] < 0:
-            return T[a[1]][p, a[3] - 1:(a[2] - 1 if a[2] else None):a[4]]
-        return T[a[1]][p, a[2]:a[3]:a[4]]
+        return view(T, a)
 
     needed = set()
     for o in ops:

import math

from concourse.mybir import AluOpType, ActivationFunctionType

ALU = AluOpType
AF = ActivationFunctionType
F32, BF, F16, I32, U16 = "float32", "bfloat16", "float16", "int32", "uint16"
STEPS = 4
ROT = 2760
C = 8
Q0 = (8, 0)
SEG = [[16 * (16 - (Q0[h] + q)) + 2 for q in range(C)] for h in range(2)]
TOT = [sum(s) for s in SEG]
OPT = dict(lead=3000.0, seed=1, passes=((1, 40, 300), (4, 190, 150)), split=(0, 1), tensor=(), fine=(0, 1), two=False,
           off=((1, 0),), wrap="P", cand="P")

SCRATCH = {}
PART = {}


def _sb(name, n, d):
    SCRATCH[name] = ("sbuf", [128, n], d)


for _n, _w, _d in [
    ("xs", 4096, BF), ("vs", 4224, BF), ("ctab", 4240, F32), ("lan", 256, I32), ("s0w", 256, I32), ("wti", 8, I32),
    ("srow", 256, BF), ("ci", 16, I32), ("cf", 32, F32), ("t0", 144, F32), ("t1", 256, F32), ("t2", 384, F32),
    ("t3", 144, F32), ("t4", 128, F32), ("idb", 128, BF), ("idh", 128, F16), ("nid", 128, BF), ("c31", 128, BF),
    ("n31", 128, BF), ("c45", 128, BF), ("n45", 128, BF), ("n43", 128, BF), ("i15", 128, BF), ("i24", 128, BF),
    ("one", 480, BF), ("blk", 128, BF), ("cont", 120, BF), ("rsf", 120, F32),
    ("sel", 144, BF), ("selk", 144, F16), ("selw", 144, BF), ("selb", 144, BF), ("wme", 128, F16), ("nwm", 128, F16),
    ("wx", 128, F16), ("ta", 128, BF), ("tb", 120, BF), ("tc", 64, BF), ("rst", 120, F32),
    ("ends", 8, U16), ("val", 8, BF), ("lst", 8, F32), ("tri", 272, BF), ("hrow", 272, F16),
    ("win", 16, BF), ("fsel", 256, BF), ("thr", 8, BF), ("hc", 32, F16), ("aq", 16, BF), ("ay", 8, F32), ("aj", 16, F32),
]:
    _sb(_n, _w, _d)
for _h in range(2):
    for _n, _w, _d in [
        ("ld", 256, I32), ("lu", 128 * STEPS, U16), ("su", 128 * STEPS, U16), ("home", 256, F32), ("a", 2048, BF),
        ("at", 2048, F16), ("f", 1920, BF), ("d", 1920, F16), ("ab", 1920, F16), ("cl", 1920, BF), ("lall", 1088, I32),
        ("w4", 256, F16), ("w2", 256, I32), ("w3", 384, BF), ("hu", 128, U16), ("sc", 248, I32), ("k", 48, I32),
        ("sp", 120, BF), ("ou", 64, U16), ("eq", TOT[_h], BF), ("es", TOT[_h], BF), ("msk", TOT[_h], BF),
        ("snd", 8 * STEPS, I32), ("rcv", 8 * STEPS + 8, I32), ("fo", 128, F32), ("sl", 16, U16), ("own", 192, I32), ("rr", 480, BF), ("cd", 120, BF),
    ]:
        _o = SCRATCH[_n][1][1] if _h else 0
        PART[_n + str(_h)] = (_n, _o, _w)
        _sb(_n, _o + _w + (-_w) % 32, _d)
for _n in ("dl0", "dl1"):
    SCRATCH[_n] = ("dram", [8, 1024], I32)
for _n in ("pt0", "pt1"):
    SCRATCH[_n] = ("psum", [128, 1024], BF)
for _n in ("px0", "px1", "px2", "px3"):
    SCRATCH[_n] = ("psum", [128, 32, 16], F32)
for _n in ("pn", "pf"):
    SCRATCH[_n] = ("psum", [128, 512], F32)

SEMAPHORES = ["sv", "sa", "sp", "sg", "gone"] + ["dm%d" % i for i in range(50)] + ["arr%d" % i for i in range(6 * STEPS)]

COSTS = [(1.1, 1.65, 4.0, 280.0, 200.0, 2800.0, 0.9, 0.51), (0.85, 1.56, 3.8, 240.0, 170.0, 3000.0, 0.8, 0.51),
         (1.05, 1.3, 3.0, 180.0, 120.0, 2400.0, 0.7, 0.72), (1.22, 2.0, 5.2, 240.0, 160.0, 3400.0, 1.0, 0.51)]
SIZE = {F32: 4, I32: 4, BF: 2, F16: 2, U16: 2}


def A(name, lo=0, hi=None, step=1, part=None):
    name, o, w = PART.get(name) or (name, 0, SCRATCH[name][1][1])
    return ("A", name, o + lo, o + (w if hi is None else hi), step, part)


def rows(name, lo, w, n=15):
    return ("A", name, lo, lo + 16 * n, (w, n), None)


def IX(name, lo, hi, off, c, d):
    w, l = A(name, lo, hi), A(off, c, d)
    return ("I", w[1], w[2], w[3], l[1], l[2], l[3])


def count(a):
    if a[0] == "I":
        return 16 * (a[6] - a[5])
    if isinstance(a[4], tuple):
        return a[4][0] * a[4][1]
    return len(range(a[2], a[3], abs(a[4])))


def spans(a):
    if a[0] == "I":
        return [(a[1], a[2], a[3]), (a[4], a[5], a[6])]
    return [(a[1], a[2], a[3])]


def psum(a):
    return SCRATCH[a[1]][0] == "psum"


def narrow(*xs):
    return all(SIZE[SCRATCH[a[1]][2]] == 2 for a in xs)


def plan(costs=COSTS[0]):
    CYC, GATHER, SCATTER = costs[:3]
    PCYC = costs[7] * CYC
    ops = []
    acc = {}
    tag = [-9, 0, "c"]

    def add(eng, cost, call, reads, writes, kind="c", after=(), alt=None):
        i = len(ops)
        deps = {}
        user = i if alt else eng
        for lst, wr in ((reads, False), (writes, True)):
            for a in lst:
                for n, (name, lo, hi) in enumerate(spans(a)):
                    w = wr and n == 0
                    if SCRATCH[name][0] == "psum":
                        st = acc.setdefault(name, [user, [], []])
                        if st[0] != user:
                            st[:] = [user, [], st[1]]
                        for j in st[2]:
                            deps[j] = True
                        if eng == "P":
                            for j in st[1][-2:]:
                                if j != i:
                                    deps.setdefault(j, False)
                        if i not in st[1]:
                            st[1].append(i)
                        continue
                    old = acc.setdefault(name, [])
                    for (j, l2, h2, w2) in old:
                        if j != i and (w or w2) and lo < h2 and l2 < hi:
                            deps[j] = True
                    if w:
                        old[:] = [o for o in old if not (lo <= o[1] and o[2] <= hi)]
                    old.append((i, lo, hi, w))
        for j in after:
            deps[j] = True
        cost = costs[5] + cost if kind == "r" else cost * costs[6] if kind == "d" else cost
        ops.append(dict(eng=eng, cost=cost, call=call, deps=deps, kind=kind, tag=tuple(tag), alt=alt))
        return i

    def aps(*xs):
        return [x for x in xs if isinstance(x, tuple)]

    def vcost(out, ins, two=False):
        n = count(out)
        if out[0] == "I":
            return (60 + SCATTER * n) * CYC
        if ins[0][0] == "I":
            return (60 + GATHER * n) * CYC
        if two:
            return max(64, n * (1 if any(psum(a) for a in ins) else 2)) * CYC
        return max(64, n * (0.5 if narrow(out, *ins) else 1)) * CYC

    def scost(out, in_):
        return ((78 + GATHER * count(out)) if in_[0] == "I" else max(64, count(out))) * CYC

    def cp(out, in_):
        return add("V", vcost(out, [in_]), ("cp", out, in_), [in_], [out])

    def ts(out, in_, s1, op0, s2=None, op1=None):
        return add("V", vcost(out, [in_] + aps(s1, s2)), ("ts", out, in_, s1, s2, op0, op1), [in_] + aps(s1, s2), [out])

    def tt(out, a, b, op):
        return add("V", vcost(out, [a, b], True), ("tt", out, a, b, op), [a, b], [out])

    def scan(out, a, b, op0, op1):
        return add("V", vcost(out, [a, b]), ("scan", out, a, b, op0, op1), [a, b], [out])

    def ms(out, v):
        return add("V", vcost(out, [out]), ("ms", out, v), [], [out])

    def act(out, in_, f=AF.Identity, bias=0.0, scale=1.0, accum=None):
        return add("S", scost(out, in_), ("act", out, in_, f, bias, scale, accum), [in_] + aps(bias, scale), [out] + aps(accum))

    def lin(eng, out, in_, scale=1.0, bias=0.0):
        ins = [in_] + aps(bias)
        v = ("cp", out, in_) if (scale, bias) == (1.0, 0.0) else ("ts", out, in_, scale, bias, ALU.mult, ALU.add)
        ways = {"V": ("V", vcost(out, ins), v), "S": ("S", scost(out, in_), ("act", out, in_, AF.Identity, bias, scale, None))}
        return add(*ways[eng], ins, [out], alt=ways["V" if eng == "S" else "S"])

    def mm(lst):
        c = sum(max(64, count(m[0])) for m in lst)
        return add("P", c * PCYC, ("mm", lst), [a for m in lst for a in m[1:3]], [m[0] for m in lst])

    def group(out, pairs, first=True, last=True):
        return [(out, l, r, first and k == 0, last and k == len(pairs) - 1) for k, (l, r) in enumerate(pairs)]

    def sums(name, src, pc):
        return [(A(name, 15 - j, 143 - j), A(src, 960 * pc + j, 960 * pc + 960, 16)) for j in range(16)]

    def iota(out, pat, base, cm):
        return add("G", 130 + 2 * count(out) * CYC, ("iota", out, pat, base, cm), [], [out])

    def dma(eng, out, in_, ns, after=()):
        return add(eng, ns, ("dma", out, in_), [in_] if in_[0] != "H" else [], [out] if out[0] != "H" else [], kind="d", after=after)

    def H(name, *ix):
        return ("H", name, ix)

    def col(b, j):
        return A(b, j, j + 1)

    def seg0(h, q):
        return (sum(SEG[h][:q]) - sum(SEG[h][:4])) % TOT[h]

    al = slice(None)
    dma("Y", A("lan"), H("lanes", al, al), 2700)
    first = [dma("S", A("xs"), H("x", al, al), 5900)]
    iota(A("s0w"), [[0, 256]], 0, 0)
    dma("Y", A("wti", 0, 1), H("wt", al, al), 2000)
    dma("Y", A("s0w", part=slice(0, 128, 16)), H("s0", al, al), 2000)
    dma("Y", A("vs", 128, 128 + ROT), H("v", al, slice(4096 - ROT, 4096)), 5900, first)
    dma("Y", A("vs", 128 + ROT, 4224), H("v", al, slice(0, 4096 - ROT)), 5900, first)

    iota(col("ci", 0), [[0, 1]], 0, 1)
    iota(A("t0"), [[1, 144]], 0, 0)
    iota(A("t1", 0, 128), [[1, 16], [0, 8]], 0, 0)
    iota(A("t1", 128, 256), [[0, 16], [1, 8]], 0, 0)
    iota(A("t3", 0, 128), [[1, 8], [0, 16]], 0, 0)
    iota(A("t3", 128, 136), [[16, 8]], 0, 0)
    iota(A("t3", 136, 144), [[960, 2], [236, 4]], -32, 0)
    iota(A("t4", 0, 120), [[0, 2], [2, 4], [8, 15]], 17, 0)
    iota(A("t4", 120, 128), [[128, 2], [1, 4]], 264, 0)
    iota(A("tb"), [[0, 8], [64, 15]], 12288 + 64, 0)
    iota(A("ctab"), [[1, 4240]], -2176, 0)
    if OPT["two"]:
        ms(A("lall0", 0, 272), 2 ** 24)
        add("Y", 4000, ("dmas", [(A("lall", 272 * i, 272 * i + 272), A("lall", 0, 272)) for i in range(1, 8)]),
            [A("lall", 0, 272)], [A("lall", 272, 2176)], kind="d", after=first)
    ts(col("ci", 1), col("ci", 0), 15, ALU.bitwise_and)
    ts(col("ci", 2), col("ci", 0), 4, ALU.arith_shift_right)
    ts(col("ci", 3), col("ci", 0), 7, ALU.bitwise_and)
    cp(A("cf", 0, 4), A("ci", 0, 4))
    P_, J_, G_, J8 = (col("cf", j) for j in range(4))
    ts(A("idb"), A("t0", 0, 128), P_, ALU.is_equal)
    ts(A("t2", 0, 128), A("t1", 0, 128), J_, ALU.subtract, 2.0 ** -10, ALU.max)
    ts(A("t2", 128, 256), A("t1", 0, 128), J_, ALU.is_lt, J_, ALU.mult)
    tt(A("t2", 256, 384), A("t2", 0, 128), A("t2", 128, 256), ALU.max)
    ts(A("t2", 0, 128), A("t1", 128, 256), G_, ALU.is_equal)
    tt(A("wme"), A("t2", 256, 384), A("t2", 0, 128), ALU.mult)
    lin("S", A("wx"), A("wme"), 1.0, 1024.0)
    lin("S", A("nwm"), A("wx"), -1.0, 1024.0)
    for name, f in (("c31", 2.0 ** 31), ("n31", -2.0 ** 31), ("c45", 1.5 * 2.0 ** 45), ("n45", (-1.125 if OPT["wrap"] == "P" else -1.5) * 2.0 ** 45),
                    ("n43", -1.5 * 2.0 ** 43), ("nid", -1.0), ("idh", 1.0), ("i15", 29952.0), ("i24", 2.0 ** 24)):
        lin("S", A(name), A("idb"), f)
    ms(A("one"), 1.0)
    lin("S", col("cf", 8), col("wti", 0))
    lin("S", col("cf", 7), G_, 16.0, 15.0)
    ts(A("selb"), A("t0"), col("cf", 7), ALU.is_equal)
    ts(A("selw"), A("selb"), col("cf", 8), ALU.mult)
    lin("S", A("sel"), A("selb"), 2.0 ** 18)
    lin("S", A("selk"), A("selb"), 1024.0)
    ts(col("cf", 16), J_, 8.0, ALU.is_ge, 65280.0, ALU.mult)
    lin("S", A("tc"), A("one", 0, 64), 256.0, col("cf", 16))
    lin("S", A("ta", 0, 120), A("t4", 0, 120), 4096.0)
    ts(A("blk"), A("t3", 0, 128), G_, ALU.is_equal)
    ms(A("rst"), 0.0)
    lin("S", A("rst", 0, 120, 15), A("t4", 120, 128), 8192.0, 6144.0)
    ts(A("rsf"), A("rst"), 1.0, ALU.is_ge, 2.0 ** 25, ALU.mult)
    ts(A("cont"), A("rst"), 1.0, ALU.is_lt)
    ms(A("sp"), -1.0)
    ms(col("thr", 0), 2.5)
    lin("S", A("val"), A("t3", 128, 136), 1.0, J_)
    lin("S", A("lst"), A("t3", 136, 144), 1.0, J_)
    ts(A("tri", 0, 16), A("t0", 0, 16), J_, ALU.is_le, 8192.0, ALU.mult)
    lin("S", A("tri", 16, 272), A("one", 0, 256), 0.0)
    lin("S", A("hrow", 256, 272), A("one", 0, 16), 2048.0)
    for h in range(2):
        s = str(h)
        lin("S", col("cf", 18 + h), J8, -8.0, float(SEG[h][0]))
        ts(col("cf", 22 + h), J8, 1.0, ALU.add, col("cf", 18 + h), ALU.mult)
        ts(A("ends", 4 + 2 * h, 5 + 2 * h), col("cf", 22 + h), -1.0 - sum(SEG[h][:4]), ALU.add, 0.0, ALU.max)
        ts(col("cf", 24 + h), J8, 4.0, ALU.is_lt, float(TOT[h]), ALU.mult)
        ts(A("ends", 2 * h, 2 * h + 1), col("cf", 22 + h), -1.0 - sum(SEG[h][:4]), ALU.add, col("cf", 24 + h), ALU.add)
        ms(A("ou" + s, 0, 16), 0)
        for q in range(C):
            o = seg0(h, q)
            ts(A("msk" + s, o, o + SEG[h][q]), A("tri", 0, SEG[h][q]), col("val", q), ALU.max)
    lin("S", A("srow"), A("s0w", 0, 256, -1))
    mm(group(A("pn", 0, 16), [(A("selb", 15 - j, 143 - j), A("srow", j, 256, 16)) for j in range(16)]))
    for h in range(2):
        lin("S", A("sp%d" % h, 0, 120, 15), A("pn", Q0[h], Q0[h] + C), 1.0, 16.0)

    def prints(t, h):
        s = str(h)
        l0 = 128 * t
        w2, w3, w4, lall = "w2" + s, "w3" + s, "w4" + s, "lall" + s
        tag[:] = [t, h, "list"]
        if t == 0:
            lin("V", A("lu" + s, 0, 128), A("lan", 128 * h, 128 * h + 128, -1))
        for pc in (1, 0):
            for u in range(2):
                tag[:] = [t, h, "f%d" % (2 * pc + u)]
                pt, bk = "pt%d" % u, "px%d" % (2 * pc + u)
                o = 1024 * pc + 512 * u
                if pc or not u or h in OPT["fine"]:
                    n = 32 if pc or h in OPT["fine"] else 64
                    lin("S", A("a" + s, o, o + 16 * n), IX("xs", 0, 4096, "lu" + s, l0 + o // 16, l0 + o // 16 + n))
                lst = [("T", A(pt, 128 * i, 128 * i + 128), A("a" + s, o + 128 * i, o + 128 * i + 128)) for i in range(4)]
                add("P", 512 * PCYC, ("tr", lst), [m[2] for m in lst] + [A("idb")], [m[1] for m in lst])
                off = (h, 2 * pc + u) in OPT["off"]
                lin("V", A("at" + s, o, o + 512), A(pt, 0, 512), 1.0, 288.0 if off else 272.0)

                def blocks(w, last):
                    return [(rows(bk, 240 * (i // 2) + 8 * (i % 2), 8), A("at" + s, o + 128 * i, o + 128 * i + 128), A(w, 8, 128),
                             off, off or last and i == 3) for i in range(4)]
                out = A("f" + s, 960 * pc + 480 * u, 960 * pc + 480 * u + 480)
                if off:
                    mm(blocks("nwm", True))
                    lin("S", A("rr" + s), A(bk, 0, 480), 1.0, 127.5)
                    tt(out, A("rr" + s), A(bk, 0, 480), ALU.subtract)
                else:
                    mm([(A(bk, 0, 480), A("c31"), A("one"), True, False)])
                    mm(blocks("wme", False) + [(A(bk, 0, 480), A("n31"), A("one"), False, False)] + blocks("nwm", True))
                    lin("S", out, A(bk, 0, 480), -1.0, 128.0)
            tag[:] = [t, h, "u%d" % pc]
            a, b = 60 * pc, 60 * pc + 60
            pu = rows(bk, 0, 4)
            mm(group(pu, [(A("blk"), A("tc", 0, 60))] + sums("selw", "f" + s, pc)))
            lin("S", A(w3, 128 + a, 128 + b), pu, 1.0, 0.5)
            tt(A(w4, a, b), pu, A(w3, 128 + a, 128 + b), ALU.subtract)
            act(A(w2, a, b), A(w4, a, b), AF.Square, bias=2640.0)
            ts(A(w2, 128 + a, 128 + b), A(w2, a, b), 5, ALU.arith_shift_right, 4095, ALU.bitwise_and)
            lin("V", A("hu" + s, a, b), A(w2, 128 + a, 128 + b))
            lin("S", A(w4, 128 + a, 128 + b), A(w2, 128 + a, 128 + b), 1.0, -2048.0)
        tag[:] = [t, h, "key"]
        if t:
            lin("S", A("sp" + s, 0, 120, 15), A("rcv" + s, 8 * t, 8 * t + 8), 1.0, 16.0)
        if OPT["wrap"] == "P":
            scan(A(w3, 0, 120), A("cont"), A("sp" + s), ALU.mult, ALU.add)
        else:
            scan(A("cd" + s), A("cont"), A("sp" + s), ALU.mult, ALU.add)
            ts(A(w3, 0, 120), A("cd" + s), 17.5, ALU.is_gt, 2.0 ** 20, ALU.mult)
        lin("S", A(w3, 256, 376), A(w4, 0, 120), 1.0, 12288.0 - 31.5)
        tag[:] = [t, h, "flip"]
        if OPT["two"]:
            lin("S", A("own" + s, 0, 64), A("lu" + s, l0 + 64, l0 + 128), 4096.0, -2.0 ** 24)
            tt(A("own" + s, 64, 128), A("own" + s, 0, 64), A("lu" + s, l0, l0 + 64), ALU.add)
            lin("S", A("own" + s, 128, 192), A("lu" + s, l0 + 64, l0 + 128), 4096.0)
            dma("Y", A("dl" + s), A("own" + s, 64, 128), 3000)
        else:
            lin("S", A("own" + s, 0, 64), A("lu" + s, l0 + 64, l0 + 128), 4096.0)
            tt(A(lall, 0, 64), A("own" + s, 0, 64), A("lu" + s, l0, l0 + 64), ALU.add)
            dma("Y", A("dl" + s), A(lall, 0, 64), 3500)
            for w in (64, 256):
                add("Y", 3500, ("dmas", [(A(lall, w * i, w * i + w), A(lall, 0, w)) for i in (1, 2, 3)]),
                    [A(lall, 0, w)], [A(lall, w, 4 * w)], kind="d")
        moves = [(A(lall, 64 * max(k, 1) + 64, 1088, part=slice(k, 128, 16)), A("dl" + s, 64 * (k == 0), 1024 - 64 * k))
                 for k in range(16)]
        add("Y", 6000, ("dmas", moves), [A("dl" + s)], [A(lall, 128, 1088)], kind="d")

    def send(sem, src, dst):
        sent = add("G", 300, ("send", "arr%d" % sem, 0, src, dst), [src], [], kind="s")
        add("R", 1200 if sem == 4 * STEPS else 600 if count(dst) == 128 else 0, ("arr", "arr%d" % sem), [], [dst], kind="r", after=[sent])

    def decide(t, h):
        s = str(h)
        B, cut = 16 * Q0[h], sum(SEG[h][4:])
        w3, w4, k, ou, ld, sc = "w3" + s, "w4" + s, "k" + s, "ou" + s, "ld" + s, "sc" + s
        for q0, q1 in ((4, 8), (0, 4)) if t < STEPS - 1 or h in OPT["split"] else ((0, 8),):
            c0, c1, early = 15 * q0, 15 * q1, q0 // 4
            tag[:] = [t, h, "near"]
            mm(group(A("pn", c0, c1), [(A("c45"), A("one", c0, c1))], last=False))
            for pc in range(q1 // 4 - 1, q0 // 4 - 1, -1):
                for pi in (2 * pc, 2 * pc + 1):
                    tag[:] = [t, h, "d%d" % pi]
                    a, b = 480 * pi, 480 * pi + 480
                    marks = IX("vs", 128, 4224, "hu" + s, 30 * pi, 30 * pi + 30)
                    if (t, h, pi) in OPT["tensor"]:
                        lin("S", A("d" + s, a, b), marks)
                        bk = A("px%d" % pi, 0, 480)
                        mm(group(bk, [(A("nid"), A("f" + s, a, b)), (A("idh"), A("d" + s, a, b))]))
                        act(A("ab" + s, a, b), bk, AF.Abs)
                    else:
                        tt(A("d" + s, a, b), marks, A("f" + s, a, b), ALU.subtract)
                        act(A("ab" + s, a, b), A("d" + s, a, b), AF.Abs)
                    ts(A("cl" + s, a, b), A("ab" + s, a, b), col("thr", 0), ALU.is_le, -3.5 / 16, ALU.add)
                mm(group(A("pn", 60 * pc, 60 * pc + 60), sums("sel", "cl" + s, pc), False, False))
            tag[:] = [t, h, "pick"]
            if OPT["wrap"] == "P":
                wrap = [(A("n45"), A("one", c0, c1)), (A("i15"), A(w3, c0, c1)), (A("n43"), A("one", c0, c1))]
            else:
                wrap = [(A("n45"), A("one", c0, c1)), (A("idb"), A(w3, c0, c1))]
            mm(group(A("pn", c0, c1), wrap + [(A("idb"), A("ta", c0, c1)), (A("idh"), A(w4, 128 + c0, 128 + c1))], first=False))
            scan(A(sc, c0, c1), A("rst", c0, c1), A("pn", c0, c1), ALU.max, ALU.min)
            k1 = A(sc, c0 + 14, c1, 15)
            ts(A(k, 16 + q0, 16 + q1), k1, 8191, ALU.bitwise_and)
            lin("V", A(ou, q0, q1), A(k, 16 + q0, 16 + q1), 1.0, -1920.0)
            lin("S", A("hrow", B + 16 * q0, B + 16 * q1), IX("ctab", 0, 4240, ou, q0, q1))
            lin("V", A("hc", 16 * h + q0, 16 * h + q1), A(k, 16 + q0, 16 + q1), 1.0, -4096.0)
            ts(A(k, 24 + q0, 24 + q1), k1, 11, ALU.arith_shift_right, 127 * 4, ALU.bitwise_and)
            lin("S", A(ou, 8 + q0, 8 + q1), A(k, 24 + q0, 24 + q1), 4.0, J_)
            tag[:] = [t, h, "win"]
            for q in range(q0, q1):
                o, w = seg0(h, q), SEG[h][q]
                ts(A("eq" + s, o, o + w), A("hrow", 258 - w, 258), col("hc", 16 * h + q), ALU.not_equal, 8192.0, ALU.mult)
            a, b = 0 if q1 == 8 else cut, cut if early else TOT[h]
            scan(A("es" + s, a, b), A("eq" + s, a, b), A("msk" + s, a, b), ALU.min, ALU.max)
            tag[:] = [t, h, "send"]
            a = 32 + 16 * early
            tt(A(ou, a, a + 16), IX("es" + s, 0, b, "ends", 4 * early + 2 * h, 4 * early + 2 * h + 1), A(ou, 0, 16), ALU.min)
            for q in range(q0, q1, 4):
                turned = IX("lall" + s, 0, 1088, ou, a + 8 + q, a + 12 + q)
                if OPT["two"]:
                    tt(A(ld, 128 + 16 * q, 192 + 16 * q), turned,
                       A("own" + s, 128, 192) if q else A("lu" + s, 128 * t, 128 * t + 64), ALU.min)
                    turned = A(ld, 128 + 16 * q, 192 + 16 * q)
                ts(A(ld, 16 * q, 16 * q + 64), turned,
                   *((12, ALU.arith_shift_right, 4095, ALU.bitwise_and) if q else (4095, ALU.bitwise_and)))
            if t < STEPS - 1:
                o = 128 * t + 16 * q0
                src, dst = A("su" + s, o, o + 64), A("lu" + s, o + 128, o + 192)
                lin("V", src, A(ld, 16 * q0, 16 * q1))
            else:
                src, dst = A("home" + s, 0, 128), A("home" + s, 128, 256)
                lin("V", A("home" + s, 128 - 16 * q1, 128 - 16 * q0), A(ld, 16 * q0, 16 * q1, -1))
            if t < STEPS - 1 or not q0:
                send(2 * t + h + 4 * STEPS * early, src, dst)
        tag[:] = [t, h, "mark"]
        tt(A(ou, 16, 24), A(k, 24, 32), A("lst"), ALU.add)
        lin("S", A("fsel", B, B + 128), IX("f" + s, 0, 1920, ou, 16, 24))
        tag[:] = [t, h, "far"]
        mm(group(A("pf", 0, 120), [(A("idb"), A("tb")), (A("idh"), A(w4, 0, 120)), (A("nid"), A(w3, 256, 376))], last=False))
        far = [(A("selk", 15 - j, 143 - j), A("ab" + s, j, 1920, 16)) for j in range(16)]
        for j in range(0, 16, 4):
            mm(group(A("pf", 0, 120), far[j:j + 4], False, j == 12))
        scan(A(sc, 120, 240), A("rsf"), A("pf", 0, 120), ALU.add, ALU.min)
        tag[:] = [t, h, "s"]
        lost, near = A("win", Q0[h], Q0[h] + C), A(sc, 134, 240, 15)
        src, dst = A("snd" + s, 8 * t, 8 * t + 8), A("rcv" + s, 8 * t + 8, 8 * t + 16)
        ts(lost, A(ou, 32, 40), 127.5, ALU.is_le, 2.0 ** 24 if OPT["cand"] == "V" else 1.0, ALU.mult)
        if t < STEPS - 1 and OPT["cand"] == "V":
            tt(A(k, 40, 48), A("sp" + s, 0, 120, 15), lost, ALU.max)
            tt(A(k, 32, 40), A(k, 40, 48), near, ALU.min)
            ts(src, A(k, 32, 40), 15, ALU.bitwise_and)
        elif OPT["cand"] == "V":
            tt(A(k, 40, 48), A("rcv" + s, 8 * t, 8 * t + 8), lost, ALU.max)
            tt(A(k, 32, 40), A(k, 40, 48), near, ALU.min)
            ts(src, A(k, 32, 40), 15, ALU.bitwise_and)
            lin("V", A("sl" + s, 0, 8), src)
            src, dst = A("sl" + s, 0, 8), A("sl" + s, 8, 16)
        elif t < STEPS - 1:
            mm(group(A("pf", 128, 136), [(A("idb"), A("sp" + s, 0, 120, 15)), (A("i24"), lost)]))
            tt(A(k, 32, 40), A("pf", 128, 136), near, ALU.min)
            ts(src, A(k, 32, 40), 15, ALU.bitwise_and)
        else:
            old = A("rcv" + s, 8 * t, 8 * t + 8)
            ts(src, near, 15, ALU.bitwise_and)
            tt(A(k, 32, 40), src, old, ALU.subtract)
            tt(A(k, 40, 48), A(k, 32, 40), lost, ALU.mult)
            src, dst = A("sl" + s, 0, 8), A("sl" + s, 8, 16)
            tt(src, A(k, 40, 48), old, ALU.add)
        send(2 * (STEPS + t) + h, src, dst)

    def close_step(t):
        tag[:] = [t, 9, "close"]
        for h in range(2):
            cp(IX("vs", 0, 4224, "ou%d" % h, 32, 40), A("fsel", 16 * Q0[h], 16 * Q0[h] + 128))
        if t < STEPS - 1:
            mm(group(A("pn", 256, 272), [(A("blk"), A("win"))]))
            act(A("aj"), A("pn", 256, 272), scale=2.0 ** -24 if OPT["cand"] == "V" else 1.0, bias=32.40625, accum=col("ay", 0))
            lin("S", col("aq", 0), col("ay", 0), 1.0, -4.0)
            lin("S", col("thr", 0), col("aq", 0), -1.0, col("ay", 0))

    for t in range(STEPS):
        for h in range(2):
            prints(t, h)
        for h in range(2):
            decide(t, h)
        close_step(t)
    tag[:] = [99, 9, "out"]
    cut = [0, ROT, 4096]
    for k in range(2):
        o = (cut[k] - ROT) % 4096
        dma("YS"[k % 2], H("yv", al, slice(o, o + cut[k + 1] - cut[k])), A("vs", 128 + cut[k], 128 + cut[k + 1]), 4800)
    for h in range(2):
        s, l0 = str(h), 128 * h
        dma("Y", H("yl", al, slice(l0, l0 + 128)), A("home" + s, 128, 256), 2400)
        lin("S", A("fo" + s, 0, 128, -1), IX("ctab", 0, 4240, "sl" + s, 8, 16), 1.0, 2176.0)
        dma("S", H("ys", al, slice(l0, l0 + 128)), A("fo" + s, 0, 128, part=slice(0, 128, 16)), 2000)
    return ops


def first_order(ops):
    n = len(ops)
    LAT_X = 130.0
    tail = [0.0] * n
    for i in range(n - 1, -1, -1):
        o = ops[i]
        tail[i] += o["cost"]
        for j in o["deps"]:
            tail[j] = max(tail[j], tail[i] + LAT_X)
    tail = [tail[i] + (OPT["lead"] if o["tag"][1] == 0 and 0 <= o["tag"][0] < STEPS else 0) for i, o in enumerate(ops)]
    for i in range(n - 1, -1, -1):
        for j in ops[i]["deps"]:
            tail[j] = max(tail[j], tail[i] + 1)
    busy, st, end = {}, {}, {}
    for i in sorted(range(n), key=lambda i: (-tail[i], i)):
        o = ops[i]
        t = max([end[j] + LAT_X for j in o["deps"]] or [0.0])
        hold = 60 if o["kind"] == "d" else o["cost"]
        if o["kind"] != "r":
            b = busy.setdefault(o["eng"], [])
            k = len(b)
            while k and b[k - 1][1] > t:
                k -= 1
            while k < len(b) and b[k][0] < t + hold:
                t = max(t, b[k][1])
                k += 1
            b.insert(k, (t, t + hold))
        st[i], end[i] = t, t + o["cost"]
    return sorted(range(n), key=lambda i: (st[i], i))


def swap(o):
    (o["eng"], o["cost"], o["call"]), o["alt"] = o["alt"], (o["eng"], o["cost"], o["call"])


def improve(plans, costs, seq, tries, temp):
    ops, K = plans[0], range(len(costs))
    n = len(ops)
    eng = [o["eng"] for o in ops]
    lats = [[o["cost"] for o in plans[c]] for c in K]
    holds = [[60 if o["kind"] == "d" else o["cost"] for o in plans[c]] for c in K]
    other = [(o["alt"][0], [plans[c][i]["alt"][1] for c in K]) if o["alt"] else None for i, o in enumerate(ops)]
    keep, anc, succ = [], [], [[] for _ in ops]
    for i, o in enumerate(ops):
        a, k = 0, []
        for j in sorted(o["deps"], reverse=True):
            if not (a >> j) & 1:
                k.append(j)
                succ[j].append(i)
            a |= anc[j] | (1 << j)
        anc.append(a)
        keep.append(k)

    def waits(c, i):
        return [(j, lats[c][j] + (costs[c][4 if eng[j] == eng[i] else 3] if ops[i]["deps"][j] else 0)) for j in keep[i]]
    preds = [[waits(c, i) for i in range(n)] for c in K]
    order = list(seq)
    prev, nxt, last = [None] * n, [None] * n, {}

    def link(*row):
        for a, b in zip(row, row[1:]):
            if a is not None:
                nxt[a] = b
            if b is not None:
                prev[b] = a
    for i in order:
        if eng[i] != "R":
            link(last.get(eng[i]), i)
            last[eng[i]] = i
    sts, whys = [[0.0] * n for c in K], [[None] * n for c in K]

    def starts(c, k0, k1=n):
        st, why, hold, pred, lat = sts[c], whys[c], holds[c], preds[c], lats[c]
        run, by = 0, 0.0
        for k in range(k0, n):
            i = order[k]
            p = prev[i]
            t, w = (0.0, None) if p is None else (st[p] + hold[p], p)
            for j, d in pred[i]:
                if st[j] + d >= t:
                    t, w = st[j] + d, -1 - j
            if -0.01 < t - st[i] - by < 0.01:
                run += 1
                if run > 40 and k > k1:
                    if by:
                        for e in order[k:]:
                            st[e] += by
                    break
            else:
                run, by = 0, t - st[i]
            st[i], why[i] = t, w
        return max(st[e] + lat[e] for e in ends)

    def hand(i):
        link(prev[i], nxt[i])
        (eng[i], new), other[i] = other[i], (eng[i], [lats[c][i] for c in K])
        for c in K:
            lats[c][i] = holds[c][i] = new[c]
        a = b = pos[i]
        while a >= 0 and (order[a] == i or eng[order[a]] != eng[i]):
            a -= 1
        while b < n and (order[b] == i or eng[order[b]] != eng[i]):
            b += 1
        link(order[a] if a >= 0 else None, i, order[b] if b < n else None)
        for e in [i] + succ[i]:
            for c in K:
                preds[c][e] = waits(c, e)
    ends = [i for i in range(n) if ops[i]["tag"][0] == 99]
    either = [i for i in range(n) if other[i]]
    ways = [starts(c, 0) for c in K]
    share = [ways[0] / w / len(K) for w in ways]
    cur = ways[0]
    best, x, moves = (cur, list(order), list(eng), ways), OPT["seed"], []
    pos = {i: k for k, i in enumerate(order)}
    for it in range(tries):
        if not moves:
            c = (x >> 16) % len(K)
            st, why, lat = sts[c], whys[c], lats[c]
            i = max(ends, key=lambda e: st[e] + lat[e])
            while why[i] is not None:
                w = why[i]
                if w >= 0 and not (anc[i] >> w) & 1:
                    moves.append((w, i))
                if other[i]:
                    moves.append((i, i))
                i = w if w >= 0 else -1 - w
        x = (x * 1103515245 + 12345) % 2147483648
        j, i = moves[x * len(moves) >> 31]
        if it % 10 == 0:
            i = j = either[x * len(either) >> 31]
            if eng[i] == "S" and x % 4:
                continue
        far, ahead = (x >> 8) % 3, (x >> 12) & 1
        if i != j:
            if nxt[j] != i:
                moves = []
                continue
            for _ in range(far):
                if ahead and prev[j] is not None:
                    j = prev[j]
                if not ahead and nxt[i] is not None:
                    i = nxt[i]
        a, b = pos[j], pos[i]
        seg = order[a:b + 1]
        if i == j:
            hand(i)
        else:
            e0, way, deps = (i, prev, keep) if ahead else (j, nxt, succ)
            mark = {e0}
            for e in (reversed(seg) if ahead else seg):
                if e in mark:
                    if e != e0 and eng[e] == eng[e0]:
                        break
                    mark.update(deps[e])
                    if e != e0:
                        mark.add(way[e])
            else:
                e = None
            if e is not None:
                continue
            p, q = prev[e0], nxt[e0]
            link(p, q)
            if ahead:
                link(prev[j], i, j)
            else:
                link(i, j, nxt[i])
            order[a:b + 1] = [e for e in seg if (e in mark) == ahead] + [e for e in seg if (e in mark) != ahead]
        x = (x * 1103515245 + 12345) % 2147483648
        bound = cur - math.log((x + 1) / 2147483649.0) * (temp * (1 - it / tries) + 1)
        old, got, new = [], [], cur
        for c in K:
            old.append((sts[c][:], whys[c][:]))
            got.append(starts(c, a, b))
            new += (got[c] - ways[c]) * share[c]
            if new > bound + temp:
                break
        if new <= bound:
            if abs(new - cur) > 0.01 or x % 4 == 0:
                moves = []
            cur, ways = new, got
            for k in range(a, b + 1):
                pos[order[k]] = k
            if cur < best[0] or x % 64 == 0:
                ways = [starts(c, 0) for c in K]
                cur = sum(w * f for w, f in zip(ways, share))
            if cur < best[0]:
                best = (cur, list(order), list(eng), ways)
        else:
            if i == j:
                hand(i)
            else:
                order[a:b + 1] = seg
                link(prev[e0], nxt[e0])
                link(p, e0, q)
            for c, (st, why) in enumerate(old):
                sts[c], whys[c] = st, why
    for i, e in enumerate(best[2]):
        if e != ops[i]["eng"]:
            for p in plans:
                swap(p[i])
    return best


def justify(ops, costs, seq, rounds, noise):
    n = len(ops)
    hold = [0 if o["kind"] == "r" else 60 if o["kind"] == "d" else o["cost"] for o in ops]
    fw = [[(j, ops[j]["cost"] + (costs[4 if ops[j]["eng"] == o["eng"] else 3] if w else 0)) for j, w in o["deps"].items()] for o in ops]
    bw = [[] for _ in ops]
    for i in range(n):
        for j, d in fw[i]:
            bw[j].append((i, d + hold[i] - hold[j]))

    def place(key, pred, st):
        busy, done = {}, [False] * n
        for top in sorted(range(n), key=key.get):
            stack = [top]
            while stack:
                i = stack[-1]
                first = [j for j, d in pred[i] if not done[j]]
                if first:
                    stack += first
                    continue
                stack.pop()
                if done[i]:
                    continue
                done[i] = True
                t = max([st[i]] + [st[j] + d for j, d in pred[i]])
                if hold[i]:
                    b = busy.setdefault(ops[i]["eng"], [])
                    k = len(b)
                    while k and b[k - 1][1] > t:
                        k -= 1
                    while k < len(b) and b[k][0] < t + hold[i]:
                        t = max(t, b[k][1])
                        k += 1
                    b.insert(k, (t, t + hold[i]))
                st[i] = t
        return st
    x = [OPT["seed"]]

    def turn(st, by):
        key = {}
        for i in range(n):
            x[0] = (x[0] * 1103515245 + 12345) % 2147483648
            key[i] = by * x[0] / 2147483648.0 - st[i] - hold[i]
        return key
    st = place({i: k for k, i in enumerate(seq)}, fw, [0.0] * n)
    best = cur = (max(st[i] + ops[i]["cost"] for i in range(n)), st)
    for r in range(rounds):
        left = 1 - r / rounds
        back = place(turn(cur[1], noise * left), bw, [o["cost"] - h for o, h in zip(ops, hold)])
        st = place(turn(back, noise * left), fw, [0.0] * n)
        new = (max(st[i] + ops[i]["cost"] for i in range(n)), st)
        if new[0] < cur[0] + 300 * left:
            cur = new
        if new[0] < best[0]:
            best = new
    return sorted(range(n), key=lambda i: (best[1][i], i))


def better(plans, costs, seq, sweeps, tries, temp, width):
    ops, K = plans[0], range(len(costs))
    n = len(ops)
    eng = [o["eng"] for o in ops]
    lats = [[o["cost"] for o in plans[c]] for c in K]
    holds = [[60 if o["kind"] == "d" else o["cost"] for o in plans[c]] for c in K]
    other = [(o["alt"][0], [plans[c][i]["alt"][1] for c in K]) if o["alt"] else None for i, o in enumerate(ops)]
    keep, anc, succ = [], [], [[] for _ in ops]
    for i, o in enumerate(ops):
        a, k = 0, []
        for j in sorted(o["deps"], reverse=True):
            if not (a >> j) & 1:
                k.append(j)
                succ[j].append(i)
            a |= anc[j] | (1 << j)
        anc.append(a)
        keep.append(k)

    def gap(c, j, i):
        return lats[c][j] + (costs[c][4 if eng[j] == eng[i] else 3] if ops[i]["deps"][j] else 0)
    preds = [[[(j, gap(c, j, i)) for j in keep[i]] for i in range(n)] for c in K]
    order = list(seq)
    prev, nxt, last = [None] * n, [None] * n, {}

    def link(*row):
        for a, b in zip(row, row[1:]):
            if a is not None:
                nxt[a] = b
            if b is not None:
                prev[b] = a
    for i in order:
        if eng[i] != "R":
            link(last.get(eng[i]), i)
            last[eng[i]] = i
    sts, whys, tails, exits = ([[0.0] * n for c in K] for _ in range(4))
    tops = [[(0.0, None)] * (n + 1) for c in K]
    pos = [0] * n

    def starts(c, k0, k1):
        st, why, hold, pred, tail, out, top = sts[c], whys[c], holds[c], preds[c], tails[c], exits[c], tops[c]
        way, at = top[k0]
        for k in range(k0, k1):
            i = order[k]
            w = prev[i]
            t = 0.0 if w is None else st[w] + hold[w]
            for j, d in pred[i]:
                if st[j] + d >= t:
                    t, w = st[j] + d, -1 - j
            st[i], why[i] = t, w
            e, q = out[i], nxt[i]
            if q is not None and pos[q] >= k1 and hold[i] + tail[q] > e:
                e = hold[i] + tail[q]
            if t + e > way:
                way, at = t + e, i
            top[k + 1] = way, at
        return way

    def leave(c, i, k1):
        return max([lats[c][i]] + [gap(c, i, j) + tails[c][j] for j in succ[i] if pos[j] >= k1])

    def hand(i, k1):
        link(prev[i], nxt[i])
        (eng[i], new), other[i] = other[i], (eng[i], [lats[c][i] for c in K])
        a = b = pos[i]
        while a >= 0 and (order[a] == i or eng[order[a]] != eng[i]):
            a -= 1
        while b < n and (order[b] == i or eng[order[b]] != eng[i]):
            b += 1
        link(order[a] if a >= 0 else None, i, order[b] if b < n else None)
        for c in K:
            lats[c][i] = holds[c][i] = new[c]
            exits[c][i] = leave(c, i, k1)
            for e in [i] + succ[i]:
                preds[c][e] = [(j, gap(c, j, e)) for j in keep[e]]
        return max(a, 0)

    def whole():
        for k, i in enumerate(order):
            pos[i] = k
        for c in K:
            exits[c][:] = lats[c]
            tops[c][0] = (0.0, None)
        return [starts(c, 0, n) for c in K]
    ways = whole()
    share = [ways[0] / w / len(K) for w in ways]
    best, x = (ways[0], list(order), list(eng), ways), OPT["seed"]
    for sweep in range(sweeps):
        heat = temp * (1 - sweep / sweeps) + 1
        order.sort(key=lambda i: (sts[0][i], pos[i]))
        whole()
        for w0 in range(-(x >> 8) % width // 2 - width // 2, n - 20, width // 2):
            w0, w1 = max(w0, 0), min(w0 + width, n)
            for c in K:
                st, tail, hold = sts[c], tails[c], holds[c]
                for i in reversed(order[w1:]):
                    q = nxt[i]
                    tail[i] = max(leave(c, i, 0), 0.0 if q is None else hold[i] + tail[q])
                for i in order[w0:w1]:
                    exits[c][i] = leave(c, i, w1)
                tops[c][w0] = (max([st[i] + leave(c, i, w1) for i in order[:w0]]
                                   + [st[i] + hold[i] + tail[nxt[i]] for i in order[:w0] if nxt[i] is not None and pos[nxt[i]] >= w1]
                                   + [tail[i] for i in order[w1:] if prev[i] is None and not keep[i]] + [0.0]), None)
            ways = [starts(c, w0, w1) for c in K]
            cur, moves = sum(w * f for w, f in zip(ways, share)), []
            either = [i for i in order[w0 + 8:w1 - 8] if other[i]]
            for it in range(tries):
                x = (x * 1103515245 + 12345) % 2147483648
                if not moves:
                    c = (x >> 16) % len(K)
                    why, i = whys[c], tops[c][w1][1]
                    while i is not None and pos[i] >= w0:
                        w = why[i]
                        if w is not None and w >= 0 and pos[w] >= w0 and not (anc[i] >> w) & 1:
                            moves.append((w, i))
                        if other[i] and w0 + 8 <= pos[i] < w1 - 8:
                            moves.append((i, i))
                        i = w if w is None or w >= 0 else -1 - w
                    if not moves:
                        continue
                j, i = moves[x * len(moves) >> 31]
                if it % 10 == 0 and either:
                    i = j = either[x * len(either) >> 31]
                far, ahead = (x >> 8) % 3, (x >> 12) & 1
                if i != j:
                    if nxt[j] != i:
                        moves = []
                        continue
                    for _ in range(far):
                        if ahead and prev[j] is not None and pos[prev[j]] >= w0:
                            j = prev[j]
                        if not ahead and nxt[i] is not None and pos[nxt[i]] < w1:
                            i = nxt[i]
                a, b = pos[j], pos[i]
                seg = order[a:b + 1]
                if i == j:
                    p = prev[i]
                    a = max(w0, min(hand(i, w1), a if p is None else pos[p]))
                else:
                    e0, way, deps = (i, prev, keep) if ahead else (j, nxt, succ)
                    mark = {e0}
                    for e in (reversed(seg) if ahead else seg):
                        if e in mark:
                            if e != e0 and eng[e] == eng[e0]:
                                break
                            mark.update(deps[e])
                            if e != e0:
                                mark.add(way[e])
                    else:
                        e = None
                    if e is not None:
                        continue
                    p, q = prev[e0], nxt[e0]
                    link(p, q)
                    if ahead:
                        link(prev[j], i, j)
                    else:
                        link(i, j, nxt[i])
                    order[a:b + 1] = [e for e in seg if (e in mark) == ahead] + [e for e in seg if (e in mark) != ahead]
                x = (x * 1103515245 + 12345) % 2147483648
                bound = cur - math.log((x + 1) / 2147483649.0) * heat
                old, got, new, part = [], [], cur, order[a:w1]
                for c in K:
                    st, why = sts[c], whys[c]
                    old.append(([st[e] for e in part], [why[e] for e in part], tops[c][a:w1 + 1]))
                    got.append(starts(c, a, w1))
                    new += (got[c] - ways[c]) * share[c]
                    if new > bound + heat:
                        break
                if new <= bound:
                    if abs(new - cur) > 0.01 or x % 4 == 0:
                        moves = []
                    cur, ways = new, got
                    if i != j:
                        for k in range(a, b + 1):
                            pos[order[k]] = k
                else:
                    if i == j:
                        hand(i, w1)
                    else:
                        order[a:b + 1] = seg
                        link(prev[e0], nxt[e0])
                        link(p, e0, q)
                    for c, (s0, w_, top) in enumerate(old):
                        st, why = sts[c], whys[c]
                        for e, u, v in zip(part, s0, w_):
                            st[e], why[e] = u, v
                        tops[c][a:w1 + 1] = top
        ways = whole()
        cur = sum(w * f for w, f in zip(ways, share))
        if cur < best[0]:
            best = (cur, list(order), list(eng), ways)
    for i, e in enumerate(best[2]):
        if e != ops[i]["eng"]:
            for p in plans:
                swap(p[i])
    return best


def program():
    plans = [plan(c) for c in COSTS]
    seq = justify(plans[0], COSTS[0], first_order(plans[0]), 500, 600)
    for sets, sweeps, temp in OPT["passes"]:
        seq = better(plans, COSTS[:sets], seq, sweeps, 250, temp, 80)[1]
    return plans[0], seq


def view(T, a):
    if not isinstance(a, tuple):
        return a
    if a[0] == "H":
        return T[a[1]][a[2]]
    if a[0] == "I":
        return T[a[1]][:, a[2]:a[3]].indirect(T[a[4]][:, a[5]:a[6]])
    p = a[5] if a[5] is not None else slice(None)
    if isinstance(a[4], tuple):
        r, c = divmod(a[2], 16)
        return T[a[1]][p, r:r + a[4][1], c:c + a[4][0]]
    if len(SCRATCH[a[1]][1]) == 3:
        return T[a[1]][p, a[2] // 16:a[3] // 16, :]
    if a[4] == 1:
        return T[a[1]][p, a[2]:a[3]]
    if a[4] < 0:
        return T[a[1]][p, a[3] - 1:(a[2] - 1 if a[2] else None):a[4]]
    return T[a[1]][p, a[2]:a[3]:a[4]]


_PLAN = []


def rank_program(g, core, T, topo):
    rank = T.rank_of(core)
    if rank is None:
        return
    if not _PLAN:
        _PLAN.append(program())
    ops, seq = _PLAN[0]
    N = len(T.cores)
    nxt, prv = T.cores[(rank + 1) % N], T.cores[(rank - 1) % N]
    rid, pid, _se = topo.addr(nxt)
    mask = topo.mask(core, nxt)
    n_out, n_in = len(topo.engines(core, nxt)), len(topo.engines(prv, core))
    Q = {"V": g.vector, "S": g.scalar, "P": g.tensor, "G": g, "Y": g.sync}
    esem = {"V": "sv", "S": "sa", "P": "sp", "G": "sg"}

    def ap(a):
        return view(T, a)

    needed = set()
    for o in ops:
        if o["kind"] != "r":
            needed.update(j for j, w in o["deps"].items() if w)
    mark, cnt, seen, known, clock = {}, {}, {}, {}, {}
    pos = {i: n for n, i in enumerate(seq)}
    ndma = [0]
    for i in seq:
        o = ops[i]
        e, c = o["eng"], o["call"]
        if o["kind"] == "r":
            mark[i] = (c[1], n_in)
            cnt[mark[i][0]] = n_in
            continue
        q = Q[e]
        want = {}
        kn = known.setdefault(e, {})
        for j, w in o["deps"].items():
            if w and mark[j][1] > want.get(mark[j][0], (0, 0))[0]:
                want[mark[j][0]] = (mark[j][1], j)
        for s_, (v, j) in sorted(want.items(), key=lambda x: -pos[x[1][1]]):
            if kn.get(s_, 0) < v:
                q.wait_ge(T.sem[s_], v)
                seen[s_] = max(seen.get(s_, 0), v)
                kn[s_] = v
                for s2, v2 in clock.get(j, {}).items():
                    kn[s2] = max(kn.get(s2, 0), v2)
        clock[i] = dict(kn)
        k = c[0]
        if k == "cp":
            r = q.tensor_copy(ap(c[1]), ap(c[2]))
        elif k == "ts":
            if c[6] is None:
                r = q.tensor_scalar(ap(c[1]), ap(c[2]), ap(c[3]), None, c[5])
            else:
                r = q.tensor_scalar(ap(c[1]), ap(c[2]), ap(c[3]), ap(c[4]), c[5], c[6])
        elif k == "tt":
            r = q.tensor_tensor(ap(c[1]), ap(c[2]), ap(c[3]), c[4])
        elif k == "scan":
            r = q.tensor_tensor_scan(ap(c[1]), ap(c[2]), ap(c[3]), 0.0, c[4], c[5])
        elif k == "ms":
            r = q.memset(ap(c[1]), c[2])
        elif k == "act":
            r = q.activation(ap(c[1]), ap(c[2]), c[3], bias=ap(c[4]), scale=ap(c[5]), accum_out=ap(c[6]))
        elif k == "mm":
            for m in c[1]:
                r = q.matmul(ap(m[0]), ap(m[1]), ap(m[2]), m[3], m[4])
        elif k == "tr":
            for m in c[1]:
                r = q.transpose(ap(m[1]), ap(m[2]), T["idb"][:])
        elif k == "iota":
            if SCRATCH[c[1][1]][2] == I32:
                r = q.iota(ap(c[1]), c[2], c[3], c[4])
            else:
                r = q.iota(ap(c[1]), c[2], c[3], c[4], allow_small_or_imprecise_dtypes=True)
        elif k in ("dma", "dmas"):
            s_ = "dm%d" % ndma[0]
            ndma[0] += 1
            moves = c[1] if k == "dmas" else [c[1:3]]
            for out, in_ in moves:
                q.dma_start(ap(out), ap(in_)).then_inc(T.sem[s_], 16)
            cnt[s_] = 16 * len(moves)
            mark[i] = (s_, cnt[s_])
            continue
        elif k == "send":
            q.remote_dma(ap(c[4]), ap(c[3]), T.sem[c[1]], T.sem["gone"], pid, rid, mask)
            cnt["gone"] = cnt.get("gone", 0) + n_out
            continue
        if i in needed:
            s_ = esem[e]
            cnt[s_] = cnt.get(s_, 0) + 1
            r.then_inc(T.sem[s_], 1)
            mark[i] = (s_, cnt[s_])
    for s_, v in sorted(cnt.items()):
        if seen.get(s_, 0) < v:
            g.wait_ge(T.sem[s_], v)
